import numpy as np, ml_dtypes
CORES = [3,11,19,27,35,43,51,59]
N = 8
BF = ml_dtypes.bfloat16
V, TY, LN, SL, RT, RO, ST = 2048, 1024, 512, 128, 64, 3, 896
WT = 1 + 10 * np.arange(16)
def cand(u):
    return ((u * u >> 5) + u + np.arange(16)[:, None] * (2 * u + 1)) & (V - 1)
def pack(w, x, q, s, h, v, t):
    i = lambda a, n: np.ascontiguousarray(a).reshape(N, -1, n).astype(np.int32)
    b = lambda a, n: np.ascontiguousarray(a).reshape(N, -1, n).astype(np.float32).astype(BF)
    return {"wd": i(w, V), "xs": b(x, V), "rq": i(q, TY), "sg": b(s, TY), "hy": i(h, V), "vf": i(v, V), "th": i(t, 1)}
def world(rng, A, top, size, twin, noise, pw, wrong, harm):
    w = np.zeros((N, 8, 16, V), np.int64); x = w.copy(); q = np.zeros((N, 8, 16, TY), np.int64); s = q.copy(); h = np.zeros((N, 8, V), np.int64); tt = h.copy()
    for r in range(N):
        for g in range(8):
            live = rng.permutation(TY)[:A]
            sa = rng.integers(0, top + 1, (16, TY)) >> rng.integers(0, size + 1, (1, TY))
            sa[:, live[1::2]] = np.clip(sa[:, live[0::2]] + rng.integers(-twin, twin + 1, (16, A // 2)), 0, 255)
            qa = np.where(rng.random((16, TY)) < rng.random((1, TY)), live[(A * rng.random((16, TY)) ** pw).astype(np.int64)], TY)
            k = rng.permutation(np.concatenate([np.arange(A), (A * rng.random(V - A) ** pw).astype(np.int64)]))
            o = np.argsort(k, kind="stable"); n = np.bincount(k, minlength=A); b = np.add.accumulate(n) - n
            back = np.zeros(TY + 1, np.int64); back[live] = np.arange(A)
            need = qa[:, live[k]]; kk = back[need]
            wa = o[b[kk] + (n[kk] * rng.random((16, V)) ** pw).astype(np.int64)]
            p = rng.choice(np.array([0.0, 0.0, 0.0, 0.0, 0.0, 0.0, 0.15, 0.15, 0.15, 0.5]), V) * harm
            wa = np.where((need == TY) | (rng.random((16, V)) < p), rng.integers(0, V, (16, V)), wa)
            off = np.where(rng.random(V) < 0.5, live[rng.integers(0, A, V)], rng.integers(0, TY, V))
            h[r, g] = np.where(rng.random(V) < wrong[r, g], off, live[k]); tt[r, g] = live[k]
            x[r, g] = np.clip(sa[:, live[k]] + rng.integers(-noise, noise + 1, (16, V)), 0, 255)
            w[r, g], q[r, g], s[r, g] = wa, qa, sa
    return w, x, q, s, h, tt
def setup_inputs(rng):
    wrong = rng.choice(np.array([0.004, 0.02, 0.06, 0.15]), (N, 8))
    w, x, q, s, h, tt = world(rng, min(V, TY) // 2, 255, 0, 3, 4, 1, wrong, 1.0)
    v = rng.random((N, 8, V)) < rng.choice(np.array([0.02, 0.2, 0.5, 0.85]), (N, 8, 1))
    t = 40 + (1200 * rng.random((N, 8, 16)) ** 2).astype(np.int64)
    return pack(w, x, q, s, h, v, t)
def setup_inputs_spread(rng):
    w, x, q, s, h, tt = world(rng, min(V, TY) // 2, 255, 7, 2, 4, 3, 0.2 * rng.random((N, 8)), 1.0)
    v = rng.random((N, 8, V)) < rng.random((N, 8, 1))
    t = np.minimum(np.exp2(12 * rng.random((N, 8, 16))).astype(np.int64) - 1, 4080)
    return pack(w, x, q, s, h, v, t)
def setup_inputs_ties(rng):
    w, x, q, s, h, tt = world(rng, 8, 150, 0, 0, 0, 1, rng.choice(np.array([0.1, 0.3, 0.5]), (N, 8)), 0.5)
    near = np.array([49, 50, 51])
    x = np.take_along_axis(s, np.broadcast_to(tt[:, :, None, :], (N, 8, 16, V)), 3)
    x = x + (np.arange(16)[:, None] == rng.integers(0, 16, (N, 8, 1, V))) * rng.choice(near, (N, 8, 1, V))
    v = rng.random((N, 8, V)) < rng.choice(np.array([0.1, 0.4, 0.6]), (N, 8, 1))
    return pack(w, x, q, s, h, v, rng.choice(near, (N, 8, 16)))
def setup_inputs_ends(rng):
    def two(lo, hi, *sh): return np.where(rng.random(sh) < 0.5, lo, hi)
    x = np.where(rng.random((N, 8, 1, V)) < 0.5, two(0, 255, N, 8, 1, V), two(0, 255, N, 8, 16, V))
    s = np.where(rng.random((N, 8, 1, TY)) < 0.5, two(0, 255, N, 8, 1, TY), two(0, 255, N, 8, 16, TY))
    h = np.where(rng.random((N, 8, V)) < 0.9, two(0, TY - 1, N, 8, V), rng.integers(0, TY, (N, 8, V)))
    v = (rng.random((N, 8, V)) < 0.4).astype(np.int64)
    w = np.where(rng.random((N, 8, 16, V)) < 0.8, two(0, V - 1, N, 8, 16, V), rng.integers(0, V, (N, 8, 16, V)))
    q = np.where(rng.random((N, 8, 16, TY)) < 0.7, two(0, TY, N, 8, 16, TY), TY - 1)
    for c in (0, TY - 1): q[..., c] = np.where(rng.random((N, 8, 16)) < 0.85, two(0, TY - 1, N, 8, 16), TY)
    z = np.stack([rng.permutation(np.array([2, 3, 4, 5, 6, 8, 12, 16])) for r in range(N)]); z[:, 7] = 5
    t = np.where(np.argsort(rng.random((N, 8, 16)), axis=-1) < z[..., None], 0, 4080)
    c = cand(np.array([(255 * 1216) & (V - 1)]))[:, 0]
    v[:, 7, 0] = 1; v[:, 7, V - 1] = 0; v[:, 7, c[:2]] = 0; v[:, 7, c[2]] = 1; v[:, 7, c[15]] = 1
    x[:, 7] = np.where(v[:, 7] == 1, 0, 255)[:, None, :]
    lo = two(0, 255, N, 8, 1); lo[:, 7] = 0
    x[..., 0] = lo; x[..., V - 1] = 255 - lo; s[..., 0] = 255 - lo
    s[..., TY - 1] = np.where(rng.random((N, 8, 1)) < 0.5, lo, 255 - lo); s[:, 7, :, TY - 1] = 0
    h[..., 0] = TY - 1; h[..., V - 1] = 0
    q[0, :, 0] = TY; t[0] = 4080; t[0, :, 0] = 0
    return pack(w, x, q, s, h, v, t)
def setup_inputs_corners(rng):
    w0 = np.zeros((N, 8, 16, V), np.int64); x0 = w0.copy(); q0 = np.zeros((N, 8, 16, TY), np.int64); s0 = q0.copy(); h0 = np.zeros((N, 8, V), np.int64); v0 = h0.copy()
    all_ = V - 16
    plan_u = (all_, LN, LN + 1, LN - 1, 1, 0, all_, all_); plan_p = (SL, SL + 1, SL - 1, LN, 1, 0, 0, SL); plan_t = (RT, RT + 1, RT - 1, 0, 0, 0, LN, RT)
    for r in range(N):
        for g in range(8):
            live = rng.permutation(TY)[:32]; s = rng.integers(0, 256, (16, TY)); s[:, live[1::2]] = s[:, live[0::2]]
            q = np.where(rng.random((16, TY)) < 0.6, live[rng.integers(0, 32, (16, TY))], TY)
            q[np.array([0, 3, 7, 11])] = live[rng.integers(0, 32, (4, TY))]; q[15, live] = live
            z = 1 + rng.permutation(V - 2)[:16]; reg = np.setdiff1d(np.arange(V), z)
            k = rng.permutation(np.concatenate([np.arange(32), rng.integers(0, 32, V - 48)]))
            o = np.argsort(k, kind="stable"); n = np.bincount(k, minlength=32); b = np.add.accumulate(n) - n
            back = np.zeros(TY + 1, np.int64); back[live] = np.arange(32)
            pairs = np.arange(16)
            h = np.zeros(V, np.int64); h[reg] = live[k]; h[z] = live[(2 * pairs + 2) % 32]
            x = np.zeros((16, V), np.int64); x[:, reg] = np.clip(s[:, live[k]] + rng.integers(-3, 4, (16, V - 16)), 0, 255); x[:, z] = s[:, live[2 * pairs]]
            w = rng.integers(0, V, (16, V)); need = q[:, h[reg]]; kk = back[need]
            wr = np.where(need == TY, w[:, reg], reg[o[b[kk] + (n[kk] * rng.random(kk.shape)).astype(np.int64)]])
            wr[15] = np.where(rng.random(V - 16) < 0.5, reg, wr[15])
            for e in (0, V - 17): wr = np.where((need < TY) & (kk == k[e]) & (rng.random(kk.shape) < 0.3), reg[e], wr)
            w[:, reg] = wr
            if r == 0: nu, n1, n2 = plan_u[g], plan_p[g], plan_t[g]
            else:
                nu = int(rng.choice(np.array([0, 1, LN - 1, LN, LN, LN + 1, all_, all_])))
                n1 = int(rng.choice(np.array([0, 1, SL - 1, SL, SL + 1, LN - RT - 1]))); n2 = int(rng.choice(np.array([0, 1, RT - 1, RT, RT + 1, LN])))
            on = np.sort(rng.permutation(reg)[:nu]); v = np.ones(V, np.int64); v[on] = 0
            la = rng.permutation(on[:LN]); m = len(la); n1 = min(n1, m); n2 = min(n2, m - n1); n3 = min(m - n1 - n2, int(rng.integers(0, 40)))
            nd = np.zeros(m, np.int64); nd[:n1] = rng.integers(1, 4, n1); nd[n1 + n2:n1 + n2 + n3] = rng.integers(4, 6, n3)
            need = q[:, h[la]]; kk = back[need]
            at = np.argsort(np.argsort(np.where(need < TY, rng.random(need.shape), 2.0), axis=0), axis=0)
            kb = 2 * ((kk // 2 + 1 + rng.integers(0, 15, kk.shape)) % 16) + rng.integers(0, 2, kk.shape)
            new = np.where(at < nd, reg[o[b[kb] + (n[kb] * rng.random(kb.shape)).astype(np.int64)]], w[:, la])
            re_ = (np.arange(m) >= n1) & (np.arange(m) < n1 + n2)
            w[:, la] = np.where((at == 0) & re_, z[kk // 2], new)
            w0[r, g], x0[r, g], q0[r, g], s0[r, g], h0[r, g], v0[r, g] = w, x, q, s, h, v
    return pack(w0, x0, q0, s0, h0, v0, rng.choice(np.array([0, 1, 30, 60]), (N, 8, 16)))
def setup_inputs_full(rng):
    w = rng.integers(0, V, (N, 8, 16, V)); x = np.zeros((N, 8, 16, V), np.int64); q = np.full((N, 8, 16, TY), TY); s = rng.integers(0, 256, (N, 8, 16, TY))
    h = np.zeros((N, 8, V), np.int64); v = h.copy(); M = TY - 24; i = np.arange(V); edge = max(ST, LN) + LN; first = int(rng.integers(0, N))
    for a in range(N):
        r = (first + a) % N; role = a % 4; lo, hi = ((200, 241), (10, 41), (40, 121), (40, 121))[role]
        for g in range(8):
            ty = rng.permutation(TY); rest = ty[24:]
            b = rng.integers(lo, hi, (16, 1)); x[r, g] = b + rng.integers(-2, 3, (16, V))
            far = rng.integers(0, 21, (16, 8)); s[r, g][:, ty[:8]] = far if role == 0 else 255 - far
            s[r, g][:, ty[8:16]] = b + (2 * rng.integers(0, 2, (16, 8)) - 1) * rng.integers(5, 8, (16, 8)); s[r, g][:, ty[16:24]] = b
            sort = np.arange(M) % 4; at = np.argsort(rng.random((16, M)), axis=0)
            cnt = np.where(sort == 1, rng.integers(1, 4, M), np.where(sort == 2, rng.integers(1, 9, M), np.where(sort == 3, 1, 0)))
            pick = np.where(sort == 3, np.arange(M) // 4 % 8, rng.integers(0, 8, (16, M)))
            q[r, g][:, rest] = np.where(at < cnt, ty[8 * np.maximum(sort - 1, 0) + pick], TY)
            c = rng.integers(0, 4, V)
            if role == 0:
                c[:LN] = 1; v[r, g, LN:] = rng.random(V - LN) < 0.5
                if g % 4 == 3: c[:256] = 0
            elif role == 1: v[r, g] = rng.random(V) < 0.85
            elif role == 2: c = np.where(i < LN, 0, 2)
            else: c = np.where(i < edge, 1, 2); c[rng.permutation(LN)[:int(rng.integers(20, 29))]] = 0
            y = 4 * rng.integers(0, M // 4, V) + c
            if role == 2:
                o = np.arange(256, LN - 1, 4); goal = LN + rng.permutation(V - LN)[:len(o)]
                for k in (0, 1):
                    y[o + k] = 4 * (2 * rng.integers(0, M // 8, len(o)) + k) + 3
                    w[r, g, np.argmin(at[:, y[o + k]], axis=0), o + k] = goal
            h[r, g] = rest[y]
    for a in range(0, N - 1, 4):
        r, e = (first + a) % N, (first + a + 1) % N
        for g in (3, 7):
            k = np.arange(255 + SL, 255, -1); c = cand(np.add.reduce(WT[:, None] * x[r, g][:, k], axis=0) & (V - 1))
            top = np.max(x[e, g], axis=1) + 1; used = np.zeros(V, bool)
            for b in range(SL):
                if np.any(used[c[:, b]]): continue
                used[c[:, b]] = True; v[e, g, c[0, b]] = 1; v[e, g, c[15, b]] = 1
                x[e, g][:, c[0, b]] = top - (np.arange(16) == rng.integers(0, 16)); x[e, g][:, c[15, b]] = top
    return pack(w, x, q, s, h, v, 32 + rng.integers(0, 9, (N, 8, 16)))
def check_inputs(d):
    bad = []
    for k, lo, hi in (("wd", 0, V - 1), ("xs", 0, 255), ("rq", 0, TY), ("sg", 0, 255), ("hy", 0, TY - 1), ("vf", 0, 1), ("th", 0, 4080)):
        a = np.asarray(d[k]).astype(np.float64)
        if not (np.min(a) >= lo and np.max(a) <= hi): bad.append("range of " + k)
        elif np.any(a != np.floor(a)): bad.append("whole numbers of " + k)
    return bad
def reference(wd, xs, rq, sg, hy, vf, th):
    m = wd.astype(np.int64).reshape(N, 8, 16, V); x = xs.astype(np.float32).astype(np.int64).reshape(N, 8, 16, V)
    q = rq.astype(np.int64).reshape(N, 8, 16, TY); s = sg.astype(np.float32).astype(np.int64).reshape(N, 8, 16, TY)
    h = hy.astype(np.int64).reshape(N, 8, V); v = vf.reshape(N, 8, V) == 1; lim = th.astype(np.int64).reshape(N, 8, 16, 1)
    last = np.zeros(N, np.int64)
    for t in range(RO):
        d = 1 + t % (N - 1); order = (ST * t + np.arange(V)) % V
        m1, h1, v1 = m.copy(), h.copy(), v.copy(); now = np.zeros(N, np.int64)
        for r in range(N):
            e = (r + d) % N
            for g in range(8):
                a = order[~v[r, g][order]][:LN]
                w = m[r, g][:, a]; need = q[r, g][:, h[r, g][a]]
                other = (need < TY) & (h[r, g][w] != need)
                far = np.add.reduce(np.abs(x[r, g][:, w] - s[r, g][:, np.minimum(need, TY - 1)]), axis=0)
                fail = other & (far > lim[r, g] + (last[r] & 255))
                n = np.add.reduce(fail.astype(np.int64), axis=0); good = n == 0; much = n > 3
                now[r] += np.count_nonzero(good)
                v1[r, g, a[good]] = True
                y = h[r, g][a[much]]; h1[r, g, a[much]] = ((y * y >> 4) + 5 * y + n[much]) & (TY - 1)
                i = np.flatnonzero((n > 0) & (n < 4))[:SL]
                if len(i) > 0:
                    z = x[r, g][:, a[i]]; u = np.add.reduce(WT[:, None] * z, axis=0) & (V - 1); c = cand(u); k = np.arange(len(i))
                    gap = np.add.reduce(np.abs(x[e, g][:, c] - z[:, None, :]), axis=0)
                    gap = np.where(v[e, g][c], gap, 4096); b = np.argmin(gap, axis=0)
                    take = fail[:, i] & (gap[b, k] < 4096)
                    m1[r, g][:, a[i]] = np.where(take, m[e, g][:, c[b, k]], w[:, i])
                j = np.flatnonzero(good & np.any(other, axis=0))[:RT]
                if len(j) > 0:
                    p = np.argmax(other[:, j], axis=0); name, one = np.unique(w[p, j], return_index=True)
                    h1[r, g, name] = need[p, j][one]; v1[r, g, name] = False
        m, h, v, last = m1, h1, v1, now
    return {"ym": m.reshape(N, 128, V).astype(np.float32), "yh": h.astype(np.float32), "yv": v.astype(np.float32)}

@@ -1,0 +1,834 @@
+from concourse.mybir import AluOpType as A, AxisListType, ActivationFunctionType as F
+
+PATIENCE = 0.5
+SCRATCH = {}
+SEMAPHORES = ["cV", "cS", "cP", "cG"]
+
+
+PLACE = {}
+_POOLED = ("BO", "LT", "EQ0", "GT", "ID", "TRI", "LPA", "LPB", "UW", "BOI", "BC", "ON", "D0", "D1", "X2D", "K34", "R1", "RD0", "RI",
+           "RC", "RH", "RX", "RD2", "R2", "RN", "RH12", "C1", "MK", "COLS", "CR", "MG", "MI", "BOf", "R1f", "R0f", "SW", "W8", "JW",
+           "J192", "DD", "LIM", "JC", "NI", "RU", "RH8", "UD")
+
+
+def _buf(name, cols, dtype, where="sbuf"):
+    if name in _POOLED:
+        pool = "PB" if dtype == "bfloat16" else "PF"
+        at = SCRATCH[pool][1][1] if pool in SCRATCH else 0
+        PLACE[name] = (pool, at, cols, dtype)
+        SCRATCH[pool] = ("sbuf", [128, at + (cols + 15) // 16 * 16], dtype)
+    else:
+        PLACE[name] = (name, 0, cols, dtype)
+        SCRATCH[name] = (where, [128, cols], dtype)
+
+
+for _n, _c, _d in (
+        ("X", 2560, "bfloat16"), ("WD", 2560, "float32"), ("RQ", 1032, "float32"), ("SG", 1040, "bfloat16"),
+        ("TB", 2640, "bfloat16"), ("SXT", 2048, "bfloat16"), ("WI", 2048, "int32"), ("RI32", 1024, "int32"), ("NI", 128, "bfloat16"),
+        ("FOf", 512, "float32"), ("RU", 144, "bfloat16"), ("UD", 128, "bfloat16"),
+        ("hyb", 128, "int32"), ("vfb", 128, "int32"), ("x2b", 128, "bfloat16"),
+        ("thi", 1, "int32"), ("KI", 4, "int32"), ("COLS", 32, "float32"), ("CR", 256, "float32"), ("MG", 128, "float32"),
+        ("MI", 128, "float32"), ("BO", 128, "bfloat16"), ("BOf", 128, "float32"), ("LT", 128, "bfloat16"), ("EQ0", 128, "bfloat16"),
+        ("GT", 128, "bfloat16"), ("ID", 128, "bfloat16"), ("TRI", 128, "bfloat16"), ("LPA", 128, "bfloat16"), ("LPB", 128, "bfloat16"),
+        ("UW", 128, "bfloat16"), ("BOI", 128, "bfloat16"), ("BC", 128, "bfloat16"), ("ON", 128, "bfloat16"),
+        ("D0", 128, "bfloat16"), ("D1", 128, "bfloat16"), ("X2D", 128, "bfloat16"), ("K34", 128, "bfloat16"),
+        ("R1", 144, "bfloat16"), ("RD0", 144, "bfloat16"), ("RI", 144, "bfloat16"), ("RC", 144, "bfloat16"), ("RH", 144, "bfloat16"),
+        ("RX", 144, "bfloat16"), ("RD2", 144, "bfloat16"), ("R2", 144, "bfloat16"), ("RN", 144, "bfloat16"),
+        ("R1f", 144, "float32"), ("R0f", 144, "float32"), ("SW", 512, "float32"), ("RH12", 16, "bfloat16"),
+        ("W8", 24, "float32"), ("C1", 128, "bfloat16"), ("JI", 512, "float32"), ("JW", 32, "float32"), ("J192", 32, "float32"), ("DD", 64, "float32"),
+        ("LIM", 64, "float32"), ("JC", 64, "float32"), ("MK", 256, "bfloat16"), ("ZR", 512, "bfloat16"), ("ZF", 128, "float32"),
+        ("U0", 2064, "bfloat16"), ("UH", 2048, "bfloat16"), ("UL", 2048, "bfloat16"), ("UG", 2048, "bfloat16"),
+        ("NW", 128, "bfloat16"), ("CUM", 128, "float32"), ("POS", 128, "float32"), ("TTB", 384, "bfloat16"),
+        ("OF", 24, "float32"), ("OFu", 8, "uint16"), ("CW", 4352, "bfloat16"), ("CC", 512, "bfloat16"), ("CLu", 32, "uint16"),
+        ("OH", 512, "bfloat16"), ("EX", 64, "float32"), ("Li", 64, "int32"), ("Lu", 32, "uint16"), ("TBL", 512, "bfloat16"),
+        ("Wu", 512, "uint16"), ("Ku", 512, "uint16"), ("STu", 32, "uint16"), ("TY", 64, "int32"),
+        ("PM", 512, "bfloat16"), ("W4", 512, "float32"), ("W4K", 512, "float32"), ("KX", 512, "float32"),
+        ("P2", 512, "float32"), ("FT", 1024, "bfloat16"),
+        ("ED", 320, "int32"), ("GA", 160, "bfloat16"), ("O0", 160, "bfloat16"),
+        ("sg0", 2560, "bfloat16"), ("sg1", 2560, "bfloat16"), ("mm0", 2560, "bfloat16"), ("mm1", 2560, "bfloat16"),
+        ("hg0", 2560, "bfloat16"), ("hg1", 2560, "bfloat16"),
+        ("LW", 416, "float32"), ("HLi", 192, "int32"), ("HLb", 64, "bfloat16"), ("RP", 64, "bfloat16"), ("GM", 32, "bfloat16"),
+        ("PFu", 32, "uint16"), ("P1W", 704, "float32"), ("P2W", 704, "float32"), ("TBn", 512, "bfloat16"), ("thB", 4, "float32"),
+        ("CN", 4, "int32"), ("AI", 512, "int32"), ("AF", 640, "float32"), ("AB", 704, "bfloat16"), ("AU", 8, "uint16"),
+        ("BI", 1200, "int32"), ("BF2", 560, "float32"), ("BU", 320, "uint16"), ("FL0", 128, "bfloat16"), ("FL1", 128, "bfloat16"),
+        ("FL2", 128, "bfloat16"), ("DW0", 136, "float32"), ("DW1", 136, "float32"), ("DW2", 136, "float32")):
+    _buf(_n, _c, _d)
+for _t in range(3):
+    _buf("XE%d" % _t, 2048, "bfloat16")
+    _buf("WE%d" % _t, 2176, "float32")
+    _buf("FI%d" % _t, 128, "bfloat16")
+for _n in ("i01", "i02", "i12"):
+    _buf("D" + _n, 136, "float32")
+for _b in range(8):
+    _buf("q%d" % _b, 512, "float32", "psum")
+_NDMA, _NREM = 40, 15
+SEMAPHORES += ["d%d" % k for k in range(_NDMA)] + ["l%d" % k for k in range(_NREM)] + ["r%d" % k for k in range(_NREM)]
+
+
+def relay_of(core, T, topo):
+    return [c for c in topo.cores_of(core) if T.rank_of(c) is None and topo.die(c) != topo.die(core)
+            and all(topo.may_write(c, d) for d in T.cores)][0]
+
+
+def lanes_of(src, dst, T, topo):
+    far = [d for d in T.cores if topo.chip(d) != topo.chip(src)][0]
+    e = [k for k in topo.engines(src, dst) if k in topo.engines(src, far)]
+    return sum(1 << k for k in e), len(e)
+
+
+def relay_program(g, core, T, topo):
+    own = [c for c in T.cores if topo.chip(c) == topo.chip(core)]
+    if not own or relay_of(own[0], T, topo) != core:
+        return
+    rank, sent = T.rank_of(own[0]), []
+    n_on = lanes_of(own[0], core, T, topo)[1]
+    for slot, d, name, lo, hi, src in ((14, 1, "WE0", 1024, 2048, "WD"), (1, 2, "XE1", 0, 2048, "X"), (4, 2, "WE1", 0, 2048, "WD"), (2, 3, "XE2", 0, 2048, "X")):
+        if slot == 14:
+            g.wait_ge(T.sem.r13, n_on)
+        if slot == 1:
+            g.wait_ge(T.sem.r12, n_on)
+        dst = T.cores[(rank - d) % len(T.cores)]
+        mask, n = lanes_of(core, dst, T, topo)
+        rid, pid, _ = topo.addr(dst)
+        g.remote_dma(T[name][:, lo:hi], T[src][:, lo:hi], T.sem["r%d" % slot], T.sem["l%d" % slot], pid, rid, mask)
+        sent.append((slot, n))
+    for slot, n in sent:
+        g.wait_ge(T.sem["l%d" % slot], n)
+
+
+def rank_program(g, core, T, topo):
+    rank = T.rank_of(core)
+    if rank is None:
+        relay_program(g, core, T, topo)
+        return
+    N = len(T.cores)
+    GQ = ("gq", 0, 1, 1, None)
+    eng = {"V": g.vector, "S": g.scalar, "P": g.tensor, "G": g, "Y": g.sync}
+    cnt = {"cV": 0, "cS": 0, "cP": 0, "cG": 0}
+    known = {e: {} for e in eng}
+    acc = {}
+    nd, sent, fin = [0], [], []
+    psum = {"q%d" % b for b in range(8)}
+
+    def v(name, lo=0, hi=None, step=1, rows=None):
+        buf, at, cols, _ = PLACE[name]
+        return (buf, at + lo, at + (cols if hi is None else hi), step, rows)
+
+    def ap(x):
+        name, lo, hi, step, rows = x
+        r = slice(None) if rows is None else rows
+        return T[name][r, lo:hi] if step == 1 else T[name][r, lo:hi:step]
+
+    def wait(e, sem, val, clock):
+        k = known[e]
+        if k.get(sem, 0) < val:
+            eng[e].wait_ge(T.sem[sem], val)
+            k[sem] = val
+        for s, c in clock.items():
+            if k.get(s, 0) < c:
+                k[s] = c
+
+    def deps(e, reads, writes):
+        need = []
+        for lst, wr in ((reads, False), (writes, True)):
+            for x in lst:
+                ex = x[0] in psum
+                for a in acc.get(x[0], ()):
+                    if ex and e == "P" and a[4] == "P":
+                        continue
+                    if ex and a[4] != e:
+                        need.append(a)
+                    elif a[1] < x[2] and x[1] < a[2] and (wr or a[3]) and (a[0] is None or x[4] is None or a[0] == x[4]):
+                        need.append(a)
+        need.sort(key=lambda a: -a[6])
+        for a in need:
+            wait(e, a[5], a[6], a[7])
+
+    def note(e, reads, writes, sem, val, clock):
+        for lst, wr in ((reads, False), (writes, True)):
+            for x in lst:
+                old = acc.setdefault(x[0], [])
+                if x[0] in psum:
+                    keep = [a for a in old if a[4] == e and not (wr and x[1] <= a[1] and a[2] <= x[2])]
+                elif wr and x[3] == 1:
+                    keep = [a for a in old if not (x[1] <= a[1] and a[2] <= x[2] and (x[4] is None or a[0] == x[4]))]
+                else:
+                    keep = [a for a in old if a[3] or a[4] != e or a[1:3] != (x[1], x[2]) or a[0] != x[4] or wr]
+                keep.append((x[4], x[1], x[2], wr, e, sem, val, clock))
+                acc[x[0]] = keep
+
+    prog = []
+
+    def call(e, emit, reads, writes, cost, lat=0.0):
+        prog.append({"e": e, "emit": emit, "r": reads, "w": writes, "cost": cost, "lat": lat})
+
+    def op(e, fn, reads, writes, cost=0.1):
+        def emit():
+            deps(e, reads, writes)
+            sem = "c" + e
+            cnt[sem] += 1
+            fn().then_inc(T.sem[sem], 1)
+            clock = dict(known[e])
+            clock[sem] = cnt[sem]
+            note(e, reads, writes, sem, cnt[sem], clock)
+        call(e, emit, reads, writes, cost)
+
+    def mms(*parts):
+        for n, lst in enumerate(parts):
+            first, last = n == 0, n == len(parts) - 1
+            cyc = sum(max(64, (r[2] - r[1]) // r[3]) * (4 if r[0] in ("AF", "BF2", "P2W") else 1) for _, _, r in lst)
+
+            def emit(lst=lst, first=first, last=last):
+                sem = "cP"
+                val = cnt[sem] + 1
+                for k, (o, l, r) in enumerate(lst):
+                    deps("P", [l, r], [o] if k == 0 else [])
+                    m = g.tensor.matmul(ap(o), ap(l), ap(r), first and k == 0, last and k == len(lst) - 1)
+                m.then_inc(T.sem[sem], 1)
+                cnt[sem] = val
+                clock = dict(known["P"])
+                clock[sem] = val
+                note("P", [x[1] for x in lst] + [x[2] for x in lst], [x[0] for x in lst], sem, val, clock)
+            call("P", emit, [x[1] for x in lst] + [x[2] for x in lst], [x[0] for x in lst], cyc * 0.7e-3)
+
+    def dma(e, out, in_, o=None, i=None):
+        sem = "d%d" % nd[0]
+        nd[0] += 1
+        rd, wr = ([] if in_ is None else [in_]), ([] if out is None else [out])
+
+        def emit():
+            deps(e, rd, wr)
+            eng[e].dma_start(ap(out) if o is None else o, ap(in_) if i is None else i).then_inc(T.sem[sem], 16)
+            clock = dict(known[e])
+            clock[sem] = 16
+            note("D" + sem, rd, wr, sem, 16, clock)
+        big = (out or in_)[4] is None and (out or in_)[2] - (out or in_)[1] > 512
+        call(e, emit, rd, wr, 0.06, 5.0 if big else 2.3)
+        return sem
+
+    def send(slot, to, out, in_):
+        dst = relay_of(core, T, topo) if to is None else T.cores[to % N]
+        mask, n = lanes_of(core, dst, T, topo)
+        sent.append(("l%d" % slot, n))
+
+        def emit():
+            deps("G", [in_], [])
+            rid, pid, _ = topo.addr(dst)
+            g.remote_dma(ap(out), ap(in_), T.sem["r%d" % slot], T.sem["l%d" % slot], pid, rid, mask)
+            note("Dl%d" % slot, [in_], [], "l%d" % slot, n, {"l%d" % slot: n})
+        call("G", emit, [in_], [(slot, 0, 1, 1, None), GQ], 1.2, 0.0)
+
+    def arrive(slot, buf, left, way):
+        n = lanes_of(T.cores[(rank + 1) % N], core, T, topo)[1]
+        call("R", lambda: note("Dr%d" % slot, [], [buf], "r%d" % slot, n, {"r%d" % slot: n}), [(left, 0, 1, 1, None)], [buf], way)
+
+    def issue():
+        hist, pred = {}, []
+        for k, c in enumerate(prog):
+            ps = {}
+            for lst, wr in ((c["r"], False), (c["w"], True)):
+                for x in lst:
+                    h = hist.setdefault(x[0], [])
+                    for a in h:
+                        if a[0] == k:
+                            continue
+                        if x[0] in psum:
+                            hit = wr or a[4] or a[5] != c["e"]
+                        else:
+                            hit = (wr or a[4]) and a[1] < x[2] and x[1] < a[2] and (a[3] is None or x[4] is None or a[3] == x[4])
+                        if hit:
+                            ps[a[0]] = max(ps.get(a[0], 0.0), 0.0 if x == GQ else prog[a[0]]["lat"] + 0.1)
+            for lst, wr in ((c["r"], False), (c["w"], True)):
+                for x in lst:
+                    h = hist[x[0]]
+                    if wr and x[3] == 1:
+                        if x[0] in psum:
+                            h[:] = [a for a in h if a[0] == k]
+                        else:
+                            h[:] = [a for a in h if not (x[1] <= a[1] and a[2] <= x[2] and (x[4] is None or a[3] == x[4]))]
+                    e = (k, x[1], x[2], x[4], wr, c["e"])
+                    if e not in h:
+                        h.append(e)
+            pred.append(ps)
+        n = len(prog)
+        rank_, succ = [0.0] * n, [[] for _ in range(n)]
+        for k in range(n):
+            for p in pred[k]:
+                succ[p].append(k)
+        for k in range(n - 1, -1, -1):
+            rank_[k] = prog[k]["cost"] + max([rank_[s] + pred[s][k] for s in succ[k]] or [0.0])
+        left = [len(p) for p in pred]
+        at, free, done = [0.0] * n, {}, [0.0] * n
+        ready = {k for k in range(n) if left[k] == 0}
+        while ready:
+            best = None
+            for k in ready:
+                e = prog[k]["e"]
+                t0 = at[k] if e == "R" else max(at[k], free.get(e, 0.0))
+                key = (t0, -rank_[k], k)
+                if best is None or key < best:
+                    best = key
+            t0, _, k = best
+            e, late = prog[k]["e"], t0 + PATIENCE * prog[k]["cost"]
+            if e in ("V", "S", "P"):
+                for j in ready:
+                    if prog[j]["e"] == e and at[j] < late and (rank_[j], -j) > (rank_[k], -k):
+                        k = j
+                t0 = max(at[k], free.get(e, 0.0))
+            ready.remove(k)
+            c = prog[k]
+            c["emit"]()
+            done[k] = t0 + c["cost"]
+            free[c["e"]] = done[k]
+            for s in succ[k]:
+                at[s] = max(at[s], done[k] + pred[s][k])
+                left[s] -= 1
+                if left[s] == 0:
+                    ready.add(s)
+
+    def wid(x):
+        return (x[2] - x[1] + x[3] - 1) // x[3]
+
+    def half(*xs):
+        return 0.5 if all(x[0] in two for x in xs) else 1.0
+
+    two = {p[0] for p in PLACE.values() if p[3] in ("bfloat16", "uint16")}
+
+    def ew(w, f=1.0):
+        return 0.03 + max(64, w * f) * 1.04e-3
+
+    def ind(win, off):
+        return ap(win).indirect(ap(off))
+
+    def tt(o, a, b, f):
+        k = 1 if a[0] in psum or b[0] in psum else 2 * half(o, a, b)
+        op("V", lambda: g.vector.tensor_tensor(ap(o), ap(a), ap(b), f), [a, b], [o], ew(wid(o), k))
+
+    def ts(o, a, s1, f, s2=None, f2=None):
+        rd = [a] + [x for x in (s1, s2) if isinstance(x, tuple)]
+        p1 = ap(s1) if isinstance(s1, tuple) else s1
+        p2 = ap(s2) if isinstance(s2, tuple) else s2
+        w = ew(wid(o), half(o, a))
+        if f2 is None:
+            op("V", lambda: g.vector.tensor_scalar(ap(o), ap(a), p1, None, f), rd, [o], w)
+        else:
+            op("V", lambda: g.vector.tensor_scalar(ap(o), ap(a), p1, p2, f, f2), rd, [o], w)
+
+    def cp(o, a):
+        op("V", lambda: g.vector.tensor_copy(ap(o), ap(a)), [a], [o], ew(wid(o), half(o, a)))
+
+    def ms(o, c):
+        op("V", lambda: g.vector.memset(ap(o), c), [], [o], ew(wid(o), half(o)))
+
+    def red(o, a):
+        op("V", lambda: g.vector.tensor_reduce(ap(o), ap(a), AxisListType.X, A.add), [a], [o], ew(wid(a)))
+
+    def asel(o, a, pattern, base):
+        op("G", lambda: g.affine_select(ap(o), ap(a), pattern, A.is_equal, 0.0, base, 1), [a], [o, GQ], 0.2 + 2.1e-3 * wid(o))
+
+    def gat(o, win, off):
+        op("V", lambda: g.vector.tensor_copy(ap(o), ind(win, off)), [win, off], [o], ew(wid(o), 1.5))
+
+    def sca(win, off, a):
+        op("V", lambda: g.vector.tensor_copy(ind(win, off), ap(a)), [a, off], [win], ew(wid(a), 3.5))
+
+    def gtt(o, win, off, b, f):
+        op("V", lambda: g.vector.tensor_tensor(ap(o), ind(win, off), ap(b), f), [win, off, b], [o], ew(wid(o), 1.6))
+
+    def scan(o, a, z, f):
+        w = ew(wid(o), half(o, a))
+        op("V", lambda: g.vector.tensor_tensor_scan(ap(o), ap(a), ap(z), 0.0, f, A.add), [a, z], [o], w)
+
+    def act(o, a, func=F.Copy, bias=None, scale=None, accum_out=None):
+        kw = {}
+        rd = [a]
+        for k, x in (("bias", bias), ("scale", scale)):
+            if isinstance(x, tuple):
+                rd += [x]
+                kw[k] = ap(x)
+            elif x is not None:
+                kw[k] = x
+        if accum_out is not None:
+            kw["accum_out"] = ap(accum_out)
+        op("S", lambda: g.scalar.activation(ap(o), ap(a), func, **kw), rd, [o] + ([] if accum_out is None else [accum_out]), ew(wid(o)))
+
+    def sgat(o, win, off, scale=1.0):
+        op("S", lambda: g.scalar.activation(ap(o), ind(win, off), F.Copy, scale=scale), [win, off], [o], ew(wid(o), 1.5))
+
+    def iota(o, pattern, base, ch=0):
+        if SCRATCH[o[0]][2] == "int32":
+            op("G", lambda: g.iota(ap(o), pattern, base, ch), [], [o], 0.2)
+        else:
+            op("G", lambda: g.iota(ap(o), pattern, base, ch, allow_small_or_imprecise_dtypes=True), [], [o], 0.2 + 2.1e-3 * wid(o))
+
+    def win(R, i):
+        return v(R, 15 - i, 143 - i)
+
+    dma("Y", v("vfb"), None, i=T.vf[:])
+    dma("S", v("hyb"), None, i=T.hy[:])
+    dma("Y", v("x2b"), None, i=T.xs[2:128:16, :])
+    dma("S", v("X", 0, 2048), None, i=T.xs[:])
+    dma("Y", v("WI"), None, i=T.wd[:])
+    dma("S", v("RI32"), None, i=T.rq[:])
+    dma("Y", v("SG", 0, 1024), None, i=T.sg[:])
+    dma("S", v("thi"), None, i=T.th[:])
+
+    iota(v("KI", 0, 1), [[1, 1]], 0, 1)
+    iota(v("CR"), [[1, 256]], 0)
+    iota(v("MG"), [[1, 8], [0, 16]], 0)
+    iota(v("MI"), [[0, 8], [1, 16]], 0)
+    iota(v("C1"), [[1, 128]], 0)
+    iota(v("JI"), [[1, 512]], 4097)
+    iota(v("JC", 0, 32), [[16, 32]], 0)
+    col = {}
+
+    def newcol(name):
+        k = len(col)
+        col[name] = v("COLS", k, k + 1)
+        return col[name]
+
+    ms(v("TB"), 0.0)
+    kif, kgf, kf = newcol("ki"), newcol("kg"), newcol("k")
+    ts(v("KI", 1, 2), v("KI", 0, 1), 4, A.arith_shift_right)
+    ts(v("KI", 2, 3), v("KI", 0, 1), 15, A.bitwise_and)
+    ts(v("KI", 3, 4), v("KI", 1, 2), 1, A.bitwise_and)
+    cp(kif, v("KI", 2, 3))
+    cp(kgf, v("KI", 1, 2))
+    cp(kf, v("KI", 0, 1))
+    odd, even = newcol("odd"), newcol("even")
+    cp(odd, v("KI", 3, 4))
+    ts(newcol("g15"), kgf, 16.0, A.mult, 15.0, A.add)
+    for q in range(8):
+        ts(newcol("q%d" % q), kif, float(q), A.is_equal)
+    ts(even, odd, 0.0, A.is_equal)
+    ts(newcol("c16"), col["q0"], 16.0, A.mult)
+    ts(newcol("c32"), col["q0"], 32.0, A.mult)
+    ts(newcol("x64"), col["q3"], -64.0, A.mult)
+    ts(newcol("b2"), col["q2"], 8192.0, A.mult)
+    ts(newcol("uw"), kif, 10.0, A.mult, 1.0, A.add)
+    ts(newcol("u32"), col["q5"], 32.0 * 4096.0, A.mult)
+    ts(newcol("u1"), col["q6"], 4096.0, A.mult)
+    tt(newcol("ud"), col["u32"], col["u1"], A.add)
+    ts(newcol("m2"), kif, 2.0, A.mult, 1.0, A.add)
+    ts(newcol("km"), kf, -16.0, A.add)
+    ts(newcol("kp"), kf, 16.0, A.add)
+    ts(newcol("k5"), kf, -5.0, A.add)
+    tt(newcol("h"), col["c32"], col["q1"], A.add)
+    ts(newcol("keep"), kif, 2.5, A.is_gt)
+    ts(newcol("sx"), col["h"], 8192.0, A.mult)
+    tt(col["sx"], col["sx"], col["x64"], A.add)
+    tt(col["sx"], col["sx"], col["q4"], A.subtract)
+    ts(v("R1", 0, 143), v("CR", 0, 143), col["g15"], A.is_equal)
+    ts(v("BI", 0, 128), v("hyb"), 5, A.arith_shift_right)
+    ts(v("BI", 128, 256), v("hyb"), 31, A.bitwise_and)
+    ts(v("BF2", 0, 128), v("vfb"), -8192.0, A.mult, 8192.0, A.add)
+    tt(v("FL0"), v("BF2", 0, 128), v("x2b"), A.add)
+    dma("Y", v("TB", 0, 2048, 1, slice(2, 128, 16)), v("FL0"))
+    cp(v("AB", 0, 256), v("BI", 0, 256))
+    dma("Y", v("TB", 0, 2048, 1, slice(0, 128, 16)), v("AB", 0, 128))
+    dma("Y", v("TB", 0, 2048, 1, slice(1, 128, 16)), v("AB", 128, 256))
+    ts(v("BO"), v("MG"), kgf, A.is_equal)
+    ts(v("RD2", 0, 143), v("R1", 0, 143), col["q2"], A.mult)
+    ts(v("GT"), v("MI"), kif, A.is_lt)
+    ts(v("EQ0"), v("MI"), kif, A.is_equal)
+    ts(v("LT"), v("MI"), kif, A.is_gt)
+    tt(v("ID"), v("BO"), v("EQ0"), A.mult)
+    tt(v("GT"), v("GT"), v("BO"), A.mult)
+    ts(v("LPA"), v("ID"), 4096.0, A.mult)
+    tt(v("LPA"), v("LPA"), v("GT"), A.subtract)
+    ts(v("LPB"), v("ID"), -4096.0, A.mult)
+    tt(v("LPB"), v("LPB"), v("GT"), A.subtract)
+    ts(v("RH12", 0, 8), v("CR", 0, 8), kgf, A.is_gt)
+    ts(v("RH12", 8, 16), v("CR", 0, 8), kgf, A.is_equal)
+    ms(v("ZF"), 0.0)
+    ms(v("ZR"), 0.0)
+    ms(v("X", 2048, 2560), 0.0)
+    ms(v("WD", 2048, 2560), 0.0)
+    for t in range(3):
+        ms(v("WE%d" % t, 2048, 2176), 0.0)
+    ms(v("RQ", 1024, 1032), 1024.0)
+    ms(v("SG", 1024, 1040), 0.0)
+    ms(v("CW", 0, 512), 0.0)
+    ts(v("TB", 2048, 2560), v("ZR"), col["c32"], A.add)
+    ts(v("JW"), v("JC", 0, 32), kif, A.add)
+    ts(v("W8", 0, 8), v("JW", 0, 8), 2048.0, A.add)
+    ts(v("W8", 8, 12), v("JW", 0, 4), 2560.0, A.add)
+    ts(v("JC", 32, 64), v("JW"), 2048.0, A.add)
+    for n_, c_ in (("RD0", "q0"), ("RI", "ki"), ("RC", "c16"), ("RH", "h"), ("RX", "sx"), ("R0f", "q0"), ("RU", "uw")):
+        act(v(n_, 0, 143), v("R1", 0, 143), scale=col[c_])
+    dma("Y", v("TB", 0, 2048, 1, slice(7, 128, 16)), v("x2b"))
+    mms([(v("q7", 0, 128), win("R1", b), v("X", 128 * b, 128 * b + 128)) for b in range(16)])
+    mms([(v("q7", 128, 256), win("RU", b), v("X", 128 * b, 128 * b + 128)) for b in range(16)])
+    cp(v("BI", 256, 512), v("q7", 0, 256))
+    ts(v("BI", 512, 640), v("BI", 256, 384), 6, A.arith_shift_right)
+    ts(v("BI", 640, 768), v("BI", 256, 384), 63, A.bitwise_and)
+    ts(v("BI", 768, 896), v("BI", 384, 512), 5, A.arith_shift_right, 63, A.bitwise_and)
+    ts(v("BI", 896, 1024), v("BI", 384, 512), 31, A.bitwise_and)
+    cp(v("CW", 512, 1024), v("BI", 512, 1024))
+    for q in range(3, 7):
+        dma("Y", v("TB", 0, 2048, 1, slice(q, 128, 16)), v("CW", 128 * q + 128, 128 * q + 256))
+    cp(v("SXT"), v("TB", 0, 2048))
+    cp(v("RQ", 0, 1024), v("RI32"))
+    cp(v("WD", 0, 2048), v("WI"))
+    send(6, rank - 1, v("FI0"), v("FL0"))
+    send(0, rank - 1, v("XE0"), v("X", 0, 2048))
+    send(13, None, v("WD", 0, 2048), v("WD", 0, 2048))
+    send(3, rank - 1, v("WE0", 0, 1024), v("WD", 0, 1024))
+    send(12, None, v("X", 0, 2048), v("X", 0, 2048))
+    send(5, rank - 3, v("WE2", 0, 2048), v("WD", 0, 2048))
+    arrive(6, v("FI0"), 6, 4.0)
+    arrive(0, v("XE0"), 0, 20.0)
+    arrive(3, v("WE0", 0, 1024), 3, 30.0)
+    arrive(14, v("WE0", 1024, 2048), 13, 30.0)
+    arrive(1, v("XE1"), 12, 40.0)
+    arrive(4, v("WE1", 0, 2048), 12, 60.0)
+    arrive(2, v("XE2"), 12, 80.0)
+    arrive(5, v("WE2", 0, 2048), 5, 70.0)
+
+    def late_constants():
+        ts(v("R2", 0, 143), v("R1", 0, 143), 2.0, A.mult)
+        ts(v("RN", 0, 143), v("R1", 0, 143), -1.0, A.mult)
+        act(v("R1f", 0, 143), v("R1", 0, 143))
+        act(v("BOf"), v("BO"))
+        for n_, c_ in (("UD", "ud"), ("BOI", "ki"), ("BC", "c16")):
+            act(v(n_), v("BO"), scale=col[c_])
+        for n_, c_ in (("D0", "q0"), ("D1", "q1"), ("K34", "keep")):
+            act(v(n_), v("ID"), scale=col[c_])
+        ts(v("NI"), v("ID"), -1.0, A.mult)
+        ts(v("X2D"), v("CR", 0, 128), col["k5"], A.is_equal, col["q7"], A.mult)
+        tt(v("X2D"), v("X2D"), v("K34"), A.add)
+
+    def last_constants():
+        cp(v("thB", 0, 1), v("thi"))
+        cp(v("thB", 1, 2), v("thB", 0, 1))
+        tt(v("TRI"), v("BO"), v("LT"), A.mult)
+        ms(v("ON"), 1.0)
+        ts(v("J192"), v("JW"), 192.0, A.add)
+        ts(v("DD", 0, 32), v("JW"), 192.0 - 4095.0, A.add)
+        ts(v("DD", 32, 64), v("JW"), 64.0 - 4095.0, A.add)
+        ms(v("LIM", 0, 32), 128.0 - 4095.0)
+        ms(v("LIM", 32, 64), 64.0 - 4095.0)
+        for k, (c_, m_) in enumerate(((kf, even), (col["kp"], even), (col["km"], odd), (kf, odd))):
+            ts(v("SW", 128 * k, 128 * k + 128), v("CR", 0, 128), c_, A.is_equal, m_, A.mult)
+        for c in range(4):
+            ts(v("AF", 64 * c, 64 * c + 64), v("CR", 0, 64), -1.0, A.mult, 16.0 * c - 0.5, A.add)
+        ts(v("MK"), v("AF", 0, 256), kif, A.add, 0.0, A.is_gt)
+        ms(v("U0"), 0.0)
+        ms(v("U0", 0, 2064, 16), 1.0)
+        for q, n_ in enumerate(("UH", "UL", "UG")):
+            asel(v(n_), v("U0", 16 - q, 2064 - q), [[-1, 16], [-1, 128]], q)
+
+    def lanes(t):
+        c0 = 896 * t % 2048 // 16
+        mms([(v("q2", 0, 128), win("RD2", i), v("TB", i, 2048, 16)) for i in range(16)])
+        ts(v("NW", 0, 128 - c0), v("q2", c0, 128), 4096.0, A.is_ge)
+        if c0:
+            ts(v("NW", 128 - c0, 128), v("q2", 0, c0), 4096.0, A.is_ge)
+        mms([(v("q3", 0, 128), v("BO"), v("NW"))])
+        mms([(v("q4", 0, 128), v("NW"), v("BO"))])
+        mms([(v("q3", 128, 256), v("LPA"), v("NW"))])
+        act(v("TTB", 0, 128), v("q4", 0, 128))
+        scan(v("CUM"), v("q3", 0, 128), v("ZF"), A.add)
+        tt(v("TTB", 256, 384), v("q4", 0, 128), v("EQ0"), A.mult)
+        tt(v("TTB", 128, 256), v("q4", 0, 128), v("LT"), A.mult)
+        mms([(v("q5", 8, 16), v("TTB", 256, 384), v("RH12", 8, 16))])
+        mms([(v("q5", 0, 8), v("TTB", 0, 128), v("RH12", 0, 8)), (v("q5", 0, 8), v("TTB", 128, 256), v("RH12", 8, 16))])
+        tt(v("POS"), v("q3", 128, 256), v("CUM"), A.add)
+        ts(v("OF", 0, 8), v("q5", 8, 16), 0.5, A.is_lt)
+        tt(v("OF", 8, 16), v("OF", 0, 8), v("W8", 0, 8), A.mult)
+        tt(v("OF", 16, 24), v("q5", 0, 8), v("OF", 8, 16), A.add)
+        cp(v("OFu"), v("OF", 16, 24))
+        sca(v("CW"), v("OFu"), v("C1"))
+        ts(v("EX", 0, 32), v("JW"), v("CUM", 127, 128), A.is_ge)
+        tt(v("EX", 32, 64), v("EX", 0, 32), v("JC", 32, 64), A.mult)
+        scan(v("CC"), v("CW", 0, 512), v("ZR"), A.max)
+        mms([(v("q5", 32, 64), win("RD0", i), v("CC", i, 512, 16)) for i in range(16)])
+        cp(v("CLu"), v("q5", 32, 64))
+        gtt(v("OH"), v("POS"), v("CLu"), v("JI"), A.is_equal)
+        mms([(v("q6", 0, 32), win("RC", i), v("CC", i, 512, 16)) for i in range(16)],
+            [(v("q6", 0, 32), win("RI", i), v("OH", i, 512, 16)) for i in range(16)])
+        ts(v("Li", 0, 32), v("q6", 0, 32), float(16 * c0), A.add)
+        ts(v("Li", 32, 64), v("Li", 0, 32), 2047, A.bitwise_and)
+        tt(v("Li", 0, 32), v("Li", 32, 64), v("EX", 32, 64), A.max)
+        cp(v("Lu"), v("Li", 0, 32))
+
+    def fetch(t):
+        sgat(v("TBL"), v("TB"), v("Lu"))
+        gat(v("Wu"), v("WD"), v("Lu"))
+        mms([(v("q5", 64, 96), win("RH", i), v("TBL", i, 512, 16)) for i in range(16)])
+        cp(v("STu"), v("q5", 64, 96))
+        gat(v("Ku"), v("RQ"), v("STu"))
+        sgat(v("KX"), v("RQ"), v("STu"), 8192.0)
+        sgat(v("W4"), v("WD"), v("Lu"), 4.0)
+
+    CH = (0, 160, 320, 448, 512)
+
+    def check(t):
+        def ch(x, k):
+            return v(x, CH[k], CH[k + 1])
+
+        def sig(k):
+            sgat(tile("sg", k), v("SG"), ch("Ku", k))
+
+        def tile(x, k, p=None):
+            n = 16 * (CH[k + 1] - CH[k])
+            name = "%s%d" % (x, k & 1)
+            return v(name, 0, n) if p is None else v(name, p, n, 16)
+
+        def typ(k, e):
+            (gat if e == "V" else sgat)(tile("hg", k), v("TB"), ch("Wu", k))
+
+        def val(k):
+            gtt(tile("mm", k), v("X"), ch("Wu", k), tile("sg", k), A.max)
+
+        def sums(k):
+            q, n = ("q0", "q1", "q7", "q0")[k], CH[k + 1] - CH[k]
+            parts = [[(v(q, 0, n), win(R, p), tile(x, k, p)) for p in range(16)] for R, x in (("RX", "hg"), ("RN", "sg"), ("R2", "mm"))]
+            mms(*(parts if k < 3 else (parts[1], parts[0], parts[2])))
+
+        def small(k):
+            q, n = ("q0", "q1", "q7", "q0")[k], CH[k + 1] - CH[k]
+            tt(v("ED", 0, n), v(q, 0, n), ch("KX", k), A.subtract)
+            ts(v("ED", 160, 160 + n), v("ED", 0, n), 8191, A.bitwise_and)
+            tt(v("O0", 0, n), v("ED", 160, 160 + n), v("ED", 0, n), A.not_equal)
+            ts(v("GA", 0, n), v("ED", 160, 160 + n), v("thB", 1, 2), A.is_gt, 2.0, A.add)
+            tt(v("FT", 512 + CH[k], 512 + CH[k + 1]), v("O0", 0, n), ch("PM", k), A.mult)
+            tt(ch("FT", k), v("FT", 512 + CH[k], 512 + CH[k + 1]), v("GA", 0, n), A.mult)
+            act(ch("FOf", k), ch("FT", k))
+
+        sig(0)
+        typ(0, "V")
+        val(0)
+        sums(0)
+        if t == 0:
+            last_constants()
+        sig(1)
+        typ(1, "S")
+        ts(v("PM"), v("Ku"), 1024.0, A.is_lt)
+        val(1)
+        sums(1)
+        sig(2)
+        typ(2, "S")
+        tt(v("W4K"), v("W4"), v("KX"), A.add)
+        small(0)
+        mms([(v("q6"), v("BC"), v("CC")), (v("q6"), v("BOI"), v("OH")), (v("q6"), v("UD"), v("TBL"))])
+        act(v("P2"), v("q6"), F.Identity, bias=float(896 * t % 2048))
+        val(2)
+        sums(2)
+        sig(3)
+        typ(3, "S")
+        small(1)
+        cp(v("TY", 0, 32), v("q5", 64, 96))
+        tt(v("HLi", 0, 32), v("TY", 0, 32), v("TY", 0, 32), A.mult)
+        ts(v("HLi", 0, 32), v("HLi", 0, 32), 4, A.arith_shift_right)
+        ts(v("HLi", 32, 64), v("TY", 0, 32), 5.0, A.mult)
+        tt(v("TY", 32, 64), v("HLi", 0, 32), v("HLi", 32, 64), A.add)
+        ms(v("P1W", 0, 192), 0.0)
+        ms(v("P2W", 0, 128), 8388608.0)
+        ms(v("CW", 0, 512), 0.0)
+        val(3)
+        sums(3)
+        small(2)
+        small(3)
+
+    def post(t):
+        last = t == 2
+        c16 = 896 * t % 2048
+        lw = lambda k: v("LW", 32 * k, 32 * k + 32)
+        mms([(v("q3", 0, 64), win("R1", i), v("FT", i, 1024, 16)) for i in range(16)])
+        ts(lw(0), v("q3", 32, 64), -2.0, A.mult)
+        tt(lw(1), v("q3", 0, 32), lw(0), A.add)
+        ts(lw(4), lw(0), -1.0, A.is_lt)
+        ts(lw(2), lw(1), 0.5, A.is_lt)
+        ts(lw(3), lw(1), 3.5, A.is_lt)
+        tt(v("RP", 0, 32), lw(3), lw(2), A.subtract)
+        tt(v("RP", 32, 64), lw(4), lw(2), A.mult)
+        mms([(v("q4", 0, 64), v("BO"), v("RP"))])
+        mms([(v("q4", 64, 128), v("LPB"), v("RP"))])
+        mm = [(v("q6"), v("X2D"), v("TBL"))]
+        tt(v("HLi", 64, 96), v("TY", 32, 64), lw(1), A.add)
+        scan(lw(5), v("q4", 0, 32), v("ZF", 0, 32), A.add)
+        scan(lw(6), v("q4", 32, 64), v("ZF", 0, 32), A.add)
+        ts(v("HLi", 64, 96), v("HLi", 64, 96), 1023, A.bitwise_and)
+        tt(v("LW", 224, 288), v("q4", 64, 128), v("LW", 160, 224), A.add)
+        ts(v("GM"), lw(2), -8192.0, A.mult)
+        tt(v("LW", 288, 352), v("LW", 224, 288), v("LIM"), A.is_lt)
+        tt(v("LW", 352, 416), v("LW", 224, 288), v("DD"), A.subtract)
+        tt(v("HLi", 64, 96), v("HLi", 64, 96), v("TY", 0, 32), A.subtract)
+        tt(v("LW", 352, 416), v("LW", 352, 416), v("LW", 288, 352), A.mult)
+        ts(lw(4), lw(3), 0.5, A.is_lt)
+        tt(lw(9), lw(11), lw(12), A.add)
+        tt(v("HLi", 64, 96), v("HLi", 64, 96), lw(4), A.mult)
+        tt(lw(9), lw(9), v("J192"), A.add)
+        tt(v("HLi", 64, 96), v("HLi", 64, 96), v("TY", 0, 32), A.add)
+        cp(v("PFu"), lw(9))
+        op("V", lambda: g.vector.tensor_tensor(ind(v("P1W"), v("PFu")), ap(v("W4K")), ap(v("FOf")), A.add),
+           [v("W4K"), v("FOf"), v("PFu")], [v("P1W")], ew(512, 3.5))
+        ts(v("HLi", 128, 160), v("HLi", 64, 96), 5, A.arith_shift_right)
+        ts(v("HLi", 160, 192), v("HLi", 64, 96), 31, A.bitwise_and)
+        cp(v("HLb"), v("HLi", 128, 192))
+        ai = lambda lo, hi: v("AI", lo, hi)
+        af = lambda lo, hi: v("AF", lo, hi)
+        ab = lambda lo, hi: v("AB", lo, hi)
+        cp(ai(0, 64), v("P1W", 128, 192))
+        ts(ai(64, 128), ai(0, 64), 2, A.bitwise_and)
+        ts(ab(0, 64), ai(64, 128), 0.5, A.mult)
+        mms([(v("q4", 0, 64), v("TRI"), ab(0, 64))])
+        sca(v("P2W"), v("PFu"), v("P2"))
+        for i in range(16):
+            for U, d in (("UH", v("HLb", 0, 32)), ("UL", v("HLb", 32, 64)), ("UG", v("GM"))):
+                mm.append((v("q6", i, 512, 16), v(U, 128 * i, 128 * i + 128), d))
+        ts(af(0, 64), v("q4", 0, 64), 0.5, A.is_lt)
+        tt(af(0, 64), af(0, 64), ab(0, 64), A.mult)
+        tt(af(64, 128), v("P1W", 128, 192), af(0, 64), A.mult)
+        mms([(v("q4", 0, 64), v("BOf"), af(64, 128))])
+        mms(mm[:1], mm[1:])
+        act(v("TBn"), v("q6"), F.Identity, bias=col["b2"])
+        bi = lambda k: v("BI", 128 * k, 128 * k + 128)
+        cp(bi(0), v("P2W", 0, 128))
+        tt(af(216, 280), v("q4", 0, 64), v("EQ0", 0, 64), A.mult)
+        cp(ai(128, 192), v("q4", 0, 64))
+        tt(af(280, 312), v("AF", 216, 280, 2), v("AF", 217, 280, 2), A.add)
+        tt(af(312, 328), v("AF", 280, 312, 2), v("AF", 281, 312, 2), A.add)
+        tt(af(328, 336), v("AF", 312, 328, 2), v("AF", 313, 328, 2), A.add)
+        tt(ai(192, 196), v("AF", 328, 336, 2), v("AF", 329, 336, 2), A.add)
+        ts(bi(1), bi(0), 2047, A.bitwise_and)
+        ts(ai(196, 264), ai(128, 196), 2, A.arith_shift_right, 2047, A.bitwise_and)
+        cp(af(128, 196), ai(196, 264))
+        cp(v("AU", 0, 4), ai(260, 264))
+        cp(v("BU", 0, 128), bi(1))
+        sgat(ab(320, 384), v("SXT"), v("AU", 0, 4))
+        for h in (0, 1):
+            sgat(v("sg0", 1024 * h, 1024 * h + 1024), v("X"), v("BU", 64 * h, 64 * h + 64))
+        ts(bi(2), bi(0), 12, A.arith_shift_right, 2047, A.bitwise_and)
+        for c in range(4):
+            ts(ab(64 + 64 * c, 128 + 64 * c), af(128, 192), af(192 + c, 193 + c), A.is_equal)
+        tt(bi(3), bi(2), bi(2), A.mult)
+        ts(bi(4), bi(2), col["m2"], A.mult, kif, A.add)
+        tt(ab(64, 320), ab(64, 320), v("MK"), A.mult)
+        ts(bi(3), bi(3), 5, A.arith_shift_right)
+        for c in range(4):
+            act(ab(64 + 64 * c, 128 + 64 * c), ab(64 + 64 * c, 128 + 64 * c), accum_out=af(200 + c, 201 + c))
+        tt(bi(3), bi(3), bi(4), A.add)
+        ts(ai(264, 268), ai(192, 196), 2, A.bitwise_and)
+        ts(bi(3), bi(3), 2047, A.bitwise_and)
+        ts(af(204, 208), af(200, 204), 0.5, A.is_gt)
+        ts(af(208, 212), ai(264, 268), 0.5, A.is_lt)
+        cp(v("BU", 128, 256), bi(3))
+        tt(af(204, 208), af(204, 208), af(208, 212), A.max)
+        ts(ai(272, 336), ai(128, 192), 18, A.arith_shift_right)
+        tt(af(204, 208), af(204, 208), v("W8", 8, 12), A.mult)
+        ts(ai(336, 400), ai(128, 192), 13, A.arith_shift_right, 31, A.bitwise_and)
+        tt(af(204, 208), af(204, 208), af(192, 196), A.max)
+        cp(ab(384, 512), ai(272, 400))
+        cp(v("AU", 4, 8), af(204, 208))
+        mms([(v("q2", 0, 64), v("K34"), ab(320, 384)), (v("q2", 0, 64), v("D0"), ab(384, 448)), (v("q2", 0, 64), v("D1"), ab(448, 512))])
+        act(ab(512, 576), v("q2", 0, 64), F.Identity, bias=col["b2"])
+        sca(v("TB"), v("Lu"), v("TBn"))
+        sca(v("TB"), v("AU", 4, 8), ab(512, 576))
+        if not last:
+            dma("Y", v("FL%d" % (t + 1)), v("TB", 0, 2048, 1, slice(2, 128, 16)))
+            send(7 + t, rank - 2 - t, v("FI%d" % (t + 1)), v("FL%d" % (t + 1)))
+            arrive(7 + t, v("FI%d" % (t + 1)), 7 + t, 4.0)
+            ts(v("EX", 0, 32), v("EX", 0, 32), 0.5, A.is_lt)
+            tt(v("EX", 0, 32), v("EX", 0, 32), lw(2), A.mult)
+            red(v("thB", 2, 3), v("EX", 0, 32))
+            cp(ab(576, 577), v("thB", 2, 3))
+
+    def bsum(t):
+        mms([(v("q3", 500, 501), v("ON"), v("AB", 576, 577))])
+        cp(v("CN", 0, 1), v("q3", 500, 501))
+        ts(v("CN", 1, 2), v("CN", 0, 1), 255, A.bitwise_and)
+        tt(v("thB", 1, 2), v("thB", 0, 1), v("CN", 1, 2), A.add)
+
+    def repairs(t):
+        bi = lambda k: v("BI", 128 * k, 128 * k + 128)
+        bf = lambda lo, hi: v("BF2", lo, hi)
+        sm = lambda k: v("BI", 1024 + 8 * k, 1032 + 8 * k)
+        xe, c16 = "XE%d" % t, 896 * t % 2048
+        mms([(v("q5", 0, 8), win("R0f", i), v("P2W", i, 128, 16)) for i in range(16)])
+        for h in (0, 1):
+            sgat(v("mm0", 1024 * h, 1024 * h + 1024), v(xe), v("BU", 128 + 64 * h, 192 + 64 * h))
+            for b in (2 * h, 2 * h + 1):
+                q, lo, hi = "q%d" % (b & 1), 512 * b, 512 * b + 512
+                mms([(v(q), v("NI"), v("sg0", lo, hi)), (v(q), v("ID"), v("mm0", lo, hi))])
+                act(v("hg0", lo, hi), v(q), F.Abs)
+            mms([(v("q7", 64 * h, 64 * h + 64), win("R1", m), v("hg0", 1024 * h + m, 1024 * h + 1024, 16)) for m in range(16)])
+        cp(sm(0), v("q5", 0, 8))
+        cp(bi(4), v("P1W", 0, 128))
+        ts(sm(1), sm(0), 2047, A.bitwise_and)
+        ts(sm(2), sm(0), 12, A.arith_shift_right, 2047, A.bitwise_and)
+        ts(bi(5), bi(4), 1, A.bitwise_and)
+        ts(bi(6), bi(4), 2, A.arith_shift_right, 2047, A.bitwise_and)
+        tt(sm(3), sm(2), sm(2), A.mult)
+        ts(sm(4), sm(2), 2.0, A.mult, 1.0, A.add)
+        ts(sm(3), sm(3), 5, A.arith_shift_right)
+        tt(sm(3), sm(3), sm(2), A.add)
+        ts(bf(520, 528), sm(0), 8388608.0, A.is_ge)
+        ts(bf(0, 128), v("q7", 0, 128), 16.0, A.mult, kif, A.add)
+        op("V", lambda: g.vector.transpose(ap(bf(128, 256)), ap(bf(0, 128))), [bf(0, 128)], [bf(128, 256)])
+        lo, n, o = 128, 128, 256
+        while n > 8:
+            tt(bf(o, o + n // 2), v("BF2", lo, lo + n, 2), v("BF2", lo + 1, lo + n, 2), A.min)
+            lo, n, o = o, n // 2, o + n // 2
+        for s1 in (0, 1):
+            mms([(v("q7", 256 + s1, 264, 2), v("SW", 256 * s1 + 128 * g2, 256 * s1 + 128 * g2 + 128), v("BF2", lo + g2, lo + 8, 2)) for g2 in (0, 1)])
+        cp(sm(6), v("q7", 256, 264))
+        ts(bf(528, 536), v("q7", 256, 264), 65400.0, A.is_gt)
+        ts(sm(7), sm(6), 15, A.bitwise_and)
+        tt(bf(528, 536), bf(528, 536), bf(520, 528), A.max)
+        tt(sm(7), sm(7), sm(4), A.mult)
+        tt(bf(528, 536), bf(528, 536), v("W8", 0, 8), A.mult)
+        tt(sm(7), sm(7), sm(3), A.add)
+        dw = "DW%d" % t
+        tt(v(dw, 128, 136), bf(528, 536), sm(1), A.max)
+        ts(sm(7), sm(7), 2047, A.bitwise_and)
+        cp(v("BU", 264, 272), v(dw, 128, 136))
+        cp(v("BU", 256, 264), sm(7))
+        gat(bf(384, 512), v("WE%d" % t), v("BU", 256, 264))
+        tt(bf(384, 512), bf(384, 512), bi(6), A.subtract)
+        tt(bf(384, 512), bf(384, 512), bi(5), A.mult)
+        tt(v(dw, 0, 128), bf(384, 512), bi(6), A.add)
+        sca(v("WD"), v("BU", 264, 272), v(dw, 0, 128))
+        if t == 2:
+            fin.append(dma("Y", None, v("WD", 0, 2048), o=T.ym[:]))
+            return
+        for t2 in range(t + 1, 3):
+            slot = 9 + t + t2 - 1
+            send(slot, rank - 1 - t2, v("Di%d%d" % (t, t2)), v(dw))
+            arrive(slot, v("Di%d%d" % (t, t2)), slot, 4.0)
+
+    def helper(t):
+        dma("Y", v("XE%d" % t, 0, 2048, 1, slice(2, 128, 16)), v("FI%d" % t))
+        for s in range(t):
+            b = "Di%d%d" % (s, t)
+            cp(v("BU", 272, 280), v(b, 128, 136))
+            sca(v("WE%d" % t), v("BU", 272, 280), v(b, 0, 128))
+
+    def flags_out():
+        mms([(v("q2", 0, 128), win("RH", b), v("TB", 128 * b, 128 * b + 128)) for b in range(16)])
+        mms([(v("q2", 128, 256), win("RD2", b), v("TB", 128 * b, 128 * b + 128)) for b in range(16)])
+        cp(v("CUM"), v("q2", 0, 128))
+        ts(v("POS"), v("q2", 128, 256), 4096.0, A.is_lt)
+        fin.append(dma("Y", None, v("CUM"), o=T.yh[:]))
+        fin.append(dma("Y", None, v("POS"), o=T.yv[:]))
+
+    late_constants()
+    for t in range(3):
+        lanes(t)
+        fetch(t)
+        check(t)
+        helper(t)
+        post(t)
+        if t == 2:
+            flags_out()
+        repairs(t)
+        if t < 2:
+            bsum(t)
+    issue()
+    for sem in fin:
+        wait("Y", sem, 16, {})
+    for sem, n in sent:
+        wait("G", sem, n, {})
+    for sem in cnt:
+        wait("G", sem, cnt[sem], {})

@@ -1,19 +1,20 @@
 from concourse.mybir import AluOpType as A, AxisListType, ActivationFunctionType as F
 
 PATIENCE = 0.5
+CH = (0, 160, 320, 448, 512)
+TYP = ("SVSS", "SVSS", "SVSS")
+CAND = ("SS", "SS", "SV")
+LATE = 2.0
+SMALL = 0.0
 SCRATCH = {}
 SEMAPHORES = ["cV", "cS", "cP", "cG"]
 
-
 PLACE = {}
-_POOLED = ("BO", "LT", "EQ0", "GT", "ID", "TRI", "LPA", "LPB", "UW", "BOI", "BC", "ON", "D0", "D1", "X2D", "K34", "R1", "RD0", "RI",
-           "RC", "RH", "RX", "RD2", "R2", "RN", "RH12", "C1", "MK", "COLS", "CR", "MG", "MI", "BOf", "R1f", "R0f", "SW", "W8", "JW",
-           "J192", "DD", "LIM", "JC", "NI", "RU", "RH8", "UD")
+BF, FP, I32, U16, H16 = "bfloat16", "float32", "int32", "uint16", "float16"
 
 
-def _buf(name, cols, dtype, where="sbuf"):
-    if name in _POOLED:
-        pool = "PB" if dtype == "bfloat16" else "PF"
+def _buf(name, cols, dtype, where="sbuf", pool=None):
+    if pool:
         at = SCRATCH[pool][1][1] if pool in SCRATCH else 0
         PLACE[name] = (pool, at, cols, dtype)
         SCRATCH[pool] = ("sbuf", [128, at + (cols + 15) // 16 * 16], dtype)
@@ -22,76 +23,87 @@ def _buf(name, cols, dtype, where="sbuf"):
         SCRATCH[name] = (where, [128, cols], dtype)
 
 
+for _n in ("BO", "NBO", "LT", "EQH", "GT", "ID", "NI", "LPA", "LPB", "NLP", "ZT", "X2D", "K34", "D0", "D1", "B128", "BQ0", "IDK", "ID24",
+           "IDF", "ON", "ONS", "CWM", "MK12", "C10", "C11", "C12"):
+    _buf(_n, 128, BF, pool="PB")
+for _n in ("R1", "RD0", "RD2", "RI", "RC", "RH", "RX", "R2", "RN", "RU", "RL", "RO", "RB", "RS", "R16"):
+    _buf(_n, 144, BF, pool="PB")
+for _n, _c in (("RH3", 24), ("SWB", 512), ("SC", 64), ("KIB", 128)):
+    _buf(_n, _c, BF, pool="PB")
+for _n, _c in (("COLS", 128), ("QH", 16), ("CR", 144), ("MG", 128), ("MI", 128), ("SW", 512), ("JW", 32), ("JC", 32), ("JD", 32), ("J16", 32),
+               ("W8", 8), ("W4", 4), ("S4", 4), ("RM", 64), ("DF", 192), ("ZF", 128), ("TMP", 128)):
+    _buf(_n, _c, FP, pool="PF")
 for _n, _c, _d in (
-        ("X", 2560, "bfloat16"), ("WD", 2560, "float32"), ("RQ", 1032, "float32"), ("SG", 1040, "bfloat16"),
-        ("TB", 2640, "bfloat16"), ("SXT", 2048, "bfloat16"), ("WI", 2048, "int32"), ("RI32", 1024, "int32"), ("NI", 128, "bfloat16"),
-        ("FOf", 512, "float32"), ("RU", 144, "bfloat16"), ("UD", 128, "bfloat16"),
-        ("hyb", 128, "int32"), ("vfb", 128, "int32"), ("x2b", 128, "bfloat16"),
-        ("thi", 1, "int32"), ("KI", 4, "int32"), ("COLS", 32, "float32"), ("CR", 256, "float32"), ("MG", 128, "float32"),
-        ("MI", 128, "float32"), ("BO", 128, "bfloat16"), ("BOf", 128, "float32"), ("LT", 128, "bfloat16"), ("EQ0", 128, "bfloat16"),
-        ("GT", 128, "bfloat16"), ("ID", 128, "bfloat16"), ("TRI", 128, "bfloat16"), ("LPA", 128, "bfloat16"), ("LPB", 128, "bfloat16"),
-        ("UW", 128, "bfloat16"), ("BOI", 128, "bfloat16"), ("BC", 128, "bfloat16"), ("ON", 128, "bfloat16"),
-        ("D0", 128, "bfloat16"), ("D1", 128, "bfloat16"), ("X2D", 128, "bfloat16"), ("K34", 128, "bfloat16"),
-        ("R1", 144, "bfloat16"), ("RD0", 144, "bfloat16"), ("RI", 144, "bfloat16"), ("RC", 144, "bfloat16"), ("RH", 144, "bfloat16"),
-        ("RX", 144, "bfloat16"), ("RD2", 144, "bfloat16"), ("R2", 144, "bfloat16"), ("RN", 144, "bfloat16"),
-        ("R1f", 144, "float32"), ("R0f", 144, "float32"), ("SW", 512, "float32"), ("RH12", 16, "bfloat16"),
-        ("W8", 24, "float32"), ("C1", 128, "bfloat16"), ("JI", 512, "float32"), ("JW", 32, "float32"), ("J192", 32, "float32"), ("DD", 64, "float32"),
-        ("LIM", 64, "float32"), ("JC", 64, "float32"), ("MK", 256, "bfloat16"), ("ZR", 512, "bfloat16"), ("ZF", 128, "float32"),
-        ("U0", 2064, "bfloat16"), ("UH", 2048, "bfloat16"), ("UL", 2048, "bfloat16"), ("UG", 2048, "bfloat16"),
-        ("NW", 128, "bfloat16"), ("CUM", 128, "float32"), ("POS", 128, "float32"), ("TTB", 384, "bfloat16"),
-        ("OF", 24, "float32"), ("OFu", 8, "uint16"), ("CW", 4352, "bfloat16"), ("CC", 512, "bfloat16"), ("CLu", 32, "uint16"),
-        ("OH", 512, "bfloat16"), ("EX", 64, "float32"), ("Li", 64, "int32"), ("Lu", 32, "uint16"), ("TBL", 512, "bfloat16"),
-        ("Wu", 512, "uint16"), ("Ku", 512, "uint16"), ("STu", 32, "uint16"), ("TY", 64, "int32"),
-        ("PM", 512, "bfloat16"), ("W4", 512, "float32"), ("W4K", 512, "float32"), ("KX", 512, "float32"),
-        ("P2", 512, "float32"), ("FT", 1024, "bfloat16"),
-        ("ED", 320, "int32"), ("GA", 160, "bfloat16"), ("O0", 160, "bfloat16"),
-        ("sg0", 2560, "bfloat16"), ("sg1", 2560, "bfloat16"), ("mm0", 2560, "bfloat16"), ("mm1", 2560, "bfloat16"),
-        ("hg0", 2560, "bfloat16"), ("hg1", 2560, "bfloat16"),
-        ("LW", 416, "float32"), ("HLi", 192, "int32"), ("HLb", 64, "bfloat16"), ("RP", 64, "bfloat16"), ("GM", 32, "bfloat16"),
-        ("PFu", 32, "uint16"), ("P1W", 704, "float32"), ("P2W", 704, "float32"), ("TBn", 512, "bfloat16"), ("thB", 4, "float32"),
-        ("CN", 4, "int32"), ("AI", 512, "int32"), ("AF", 640, "float32"), ("AB", 704, "bfloat16"), ("AU", 8, "uint16"),
-        ("BI", 1200, "int32"), ("BF2", 560, "float32"), ("BU", 320, "uint16"), ("FL0", 128, "bfloat16"), ("FL1", 128, "bfloat16"),
-        ("FL2", 128, "bfloat16"), ("DW0", 136, "float32"), ("DW1", 136, "float32"), ("DW2", 136, "float32")):
+        ("X", 2064, BF), ("WD", 2560, FP), ("WI", 2560, I32), ("W16", 2048, H16), ("RI32", 1032, I32), ("SG", 1040, BF), ("TB", 2688, BF),
+        ("Z", 640, BF), ("ZU", 2048, BF), ("PW", 64, FP), ("UH", 2048, BF), ("UL", 2048, BF), ("UG", 2048, BF), ("JI", 512, FP), ("JB", 512, BF),
+        ("hyb", 128, I32), ("vfb", 128, I32), ("x2b", 128, BF), ("thi", 1, I32), ("KI", 4, I32), ("ST", 1024, BF), ("SI", 1280, I32),
+        ("NW", 128, BF), ("NT", 256, BF), ("CUM", 128, FP), ("POS", 128, FP), ("TTB", 384, BF), ("OF", 8, FP), ("OFu", 8, U16),
+        ("CW", 2176, BF), ("CC", 512, BF), ("CLu", 32, U16), ("OH", 512, BF), ("EX", 32, BF), ("Lf", 32, FP), ("Lu", 32, U16),
+        ("TBL", 528, BF), ("Wu", 512, U16), ("Wf", 512, H16), ("Ku", 512, U16), ("KF", 512, H16), ("PM", 512, BF), ("STu", 32, U16),
+        ("HI", 256, I32), ("HF", 64, FP), ("FT", 1024, BF), ("FO", 512, BF), ("RD", 256, I32), ("GA", 256, BF), ("PAY", 512, FP),
+        ("sig", 8192, BF), ("mm0", 2560, BF), ("mm1", 2560, BF), ("hg0", 2560, BF), ("hg1", 2560, BF),
+        ("RP", 96, BF), ("LW", 192, FP), ("PFu", 32, U16), ("DL", 160, BF), ("P1W", 1536, FP), ("TBn", 512, BF),
+        ("thB", 4, FP), ("CN", 4, I32), ("BS", 32, FP),
+        ("AI", 256, I32), ("AH", 192, H16), ("AF", 288, FP), ("AB", 128, BF), ("AU", 8, U16),
+        ("BI", 640, I32), ("FB", 256, BF), ("TBS", 128, BF), ("LX", 128, BF), ("OLD", 128, FP), ("BF2", 512, FP), ("SM", 64, I32),
+        ("BU", 256, U16), ("HU", 8, U16), ("WE", 2176, FP), ("OUT", 256, FP),
+        ("FL0", 128, BF), ("FL1", 128, BF), ("FL2", 128, BF), ("DW0", 136, FP), ("DW1", 136, FP), ("DW2", 136, FP)):
     _buf(_n, _c, _d)
 for _t in range(3):
-    _buf("XE%d" % _t, 2048, "bfloat16")
-    _buf("WE%d" % _t, 2176, "float32")
-    _buf("FI%d" % _t, 128, "bfloat16")
+    _buf("XE%d" % _t, 2048, BF)
+    _buf("WH%d" % _t, 2048, H16)
+    _buf("FI%d" % _t, 128, BF)
 for _n in ("i01", "i02", "i12"):
-    _buf("D" + _n, 136, "float32")
+    _buf("D" + _n, 136, FP)
 for _b in range(8):
-    _buf("q%d" % _b, 512, "float32", "psum")
-_NDMA, _NREM = 40, 15
+    _buf("q%d" % _b, 512, FP, "psum")
+_NDMA, _NREM = 40, 17
 SEMAPHORES += ["d%d" % k for k in range(_NDMA)] + ["l%d" % k for k in range(_NREM)] + ["r%d" % k for k in range(_NREM)]
 
 
-def relay_of(core, T, topo):
-    return [c for c in topo.cores_of(core) if T.rank_of(c) is None and topo.die(c) != topo.die(core)
-            and all(topo.may_write(c, d) for d in T.cores)][0]
+def relays_of(core, T, topo):
+    free = [c for c in topo.cores_of(core) if T.rank_of(c) is None and all(topo.may_write(c, d) for d in T.cores)]
+    return ([c for c in free if topo.die(c) != topo.die(core)][0], [c for c in free if topo.die(c) == topo.die(core)][0])
 
 
 def lanes_of(src, dst, T, topo):
-    far = [d for d in T.cores if topo.chip(d) != topo.chip(src)][0]
-    e = [k for k in topo.engines(src, dst) if k in topo.engines(src, far)]
+    far = topo.engines(src, [d for d in T.cores if topo.chip(d) != topo.chip(src)][0])
+    e = [k for k in topo.engines(src, dst) if topo.chip(src) != topo.chip(dst) or k not in far]
     return sum(1 << k for k in e), len(e)
 
 
 def relay_program(g, core, T, topo):
     own = [c for c in T.cores if topo.chip(c) == topo.chip(core)]
-    if not own or relay_of(own[0], T, topo) != core:
+    if not own or core not in relays_of(own[0], T, topo):
         return
     rank, sent = T.rank_of(own[0]), []
+    far, near = relays_of(own[0], T, topo)
     n_on = lanes_of(own[0], core, T, topo)[1]
-    for slot, d, name, lo, hi, src in ((14, 1, "WE0", 1024, 2048, "WD"), (1, 2, "XE1", 0, 2048, "X"), (4, 2, "WE1", 0, 2048, "WD"), (2, 3, "XE2", 0, 2048, "X")):
-        if slot == 14:
-            g.wait_ge(T.sem.r13, n_on)
-        if slot == 1:
-            g.wait_ge(T.sem.r12, n_on)
-        dst = T.cores[(rank - d) % len(T.cores)]
+
+    def send(slot, dst, name, src, lo=0, hi=2048):
         mask, n = lanes_of(core, dst, T, topo)
         rid, pid, _ = topo.addr(dst)
         g.remote_dma(T[name][:, lo:hi], T[src][:, lo:hi], T.sem["r%d" % slot], T.sem["l%d" % slot], pid, rid, mask)
         sent.append((slot, n))
+        return n
+
+    def served(d):
+        return T.cores[(rank - d) % len(T.cores)]
+
+    if core == far:
+        g.wait_ge(T.sem.r3, n_on)
+        n = send(10, served(1), "WH0", "W16", 1024, 2048)
+        g.wait_ge(T.sem.r12, n_on)
+        send(13, served(2), "XE1", "X")
+        send(14, served(2), "WH1", "W16")
+        g.wait_ge(T.sem.l10, n)
+        send(11, near, "W16", "W16")
+    else:
+        g.wait_ge(T.sem.r2, n_on)
+        send(12, far, "X", "X")
+        g.wait_ge(T.sem.r11, n_on)
+        send(15, served(3), "XE2", "X")
+        send(16, served(3), "WH2", "W16")
     for slot, n in sent:
         g.wait_ge(T.sem["l%d" % slot], n)
 
@@ -107,7 +119,7 @@ def rank_program(g, core, T, topo):
     cnt = {"cV": 0, "cS": 0, "cP": 0, "cG": 0}
     known = {e: {} for e in eng}
     acc = {}
-    nd, sent, fin = [0], [], []
+    nd, sent, fin, bias = [0], [], [], [0.0]
     psum = {"q%d" % b for b in range(8)}
 
     def v(name, lo=0, hi=None, step=1, rows=None):
@@ -157,10 +169,10 @@ def rank_program(g, core, T, topo):
                 keep.append((x[4], x[1], x[2], wr, e, sem, val, clock))
                 acc[x[0]] = keep
 
-    prog = []
+    prog, hold = [], []
 
     def call(e, emit, reads, writes, cost, lat=0.0):
-        prog.append({"e": e, "emit": emit, "r": reads, "w": writes, "cost": cost, "lat": lat})
+        prog.append({"e": e, "emit": emit, "r": reads + hold, "w": writes, "cost": cost, "lat": lat, "bias": bias[0]})
 
     def op(e, fn, reads, writes, cost=0.1):
         def emit():
@@ -173,25 +185,27 @@ def rank_program(g, core, T, topo):
             note(e, reads, writes, sem, cnt[sem], clock)
         call(e, emit, reads, writes, cost)
 
+    def mm(lst, first=True, last=True, each=0):
+        cyc = sum(max(64, wid(r)) * (4 if SCRATCH[r[0]][2] == FP else 1) for _, _, r in lst)
+        n = each or len(lst)
+
+        def emit():
+            val = cnt["cP"] + 1
+            for k, (o, l, r) in enumerate(lst):
+                deps("P", [l, r], [o] if k == 0 else [])
+                m = g.tensor.matmul(ap(o), ap(l), ap(r), first and k % n == 0, last and k % n == n - 1)
+            m.then_inc(T.sem["cP"], 1)
+            cnt["cP"] = val
+            clock = dict(known["P"])
+            clock["cP"] = val
+            note("P", [x[1] for x in lst] + [x[2] for x in lst], [x[0] for x in lst], "cP", val, clock)
+        call("P", emit, [x[1] for x in lst] + [x[2] for x in lst], [x[0] for x in lst], cyc * 0.6e-3)
+
     def mms(*parts):
         for n, lst in enumerate(parts):
-            first, last = n == 0, n == len(parts) - 1
-            cyc = sum(max(64, (r[2] - r[1]) // r[3]) * (4 if r[0] in ("AF", "BF2", "P2W") else 1) for _, _, r in lst)
+            mm(lst, n == 0, n == len(parts) - 1)
 
-            def emit(lst=lst, first=first, last=last):
-                sem = "cP"
-                val = cnt[sem] + 1
-                for k, (o, l, r) in enumerate(lst):
-                    deps("P", [l, r], [o] if k == 0 else [])
-                    m = g.tensor.matmul(ap(o), ap(l), ap(r), first and k == 0, last and k == len(lst) - 1)
-                m.then_inc(T.sem[sem], 1)
-                cnt[sem] = val
-                clock = dict(known["P"])
-                clock[sem] = val
-                note("P", [x[1] for x in lst] + [x[2] for x in lst], [x[0] for x in lst], sem, val, clock)
-            call("P", emit, [x[1] for x in lst] + [x[2] for x in lst], [x[0] for x in lst], cyc * 0.7e-3)
-
-    def dma(e, out, in_, o=None, i=None):
+    def dma(e, out, in_, o=None, i=None, lat=None):
         sem = "d%d" % nd[0]
         nd[0] += 1
         rd, wr = ([] if in_ is None else [in_]), ([] if out is None else [out])
@@ -202,12 +216,10 @@ def rank_program(g, core, T, topo):
             clock = dict(known[e])
             clock[sem] = 16
             note("D" + sem, rd, wr, sem, 16, clock)
-        big = (out or in_)[4] is None and (out or in_)[2] - (out or in_)[1] > 512
-        call(e, emit, rd, wr, 0.06, 5.0 if big else 2.3)
+        call(e, emit, rd, wr, 0.06, lat or 2.3)
         return sem
 
-    def send(slot, to, out, in_):
-        dst = relay_of(core, T, topo) if to is None else T.cores[to % N]
+    def send(slot, dst, out, in_):
         mask, n = lanes_of(core, dst, T, topo)
         sent.append(("l%d" % slot, n))
 
@@ -218,8 +230,11 @@ def rank_program(g, core, T, topo):
             note("Dl%d" % slot, [in_], [], "l%d" % slot, n, {"l%d" % slot: n})
         call("G", emit, [in_], [(slot, 0, 1, 1, None), GQ], 1.2, 0.0)
 
+    def served(d):
+        return T.cores[(rank - d) % N]
+
     def arrive(slot, buf, left, way):
-        n = lanes_of(T.cores[(rank + 1) % N], core, T, topo)[1]
+        n = lanes_of(served(-1), core, T, topo)[1]
         call("R", lambda: note("Dr%d" % slot, [], [buf], "r%d" % slot, n, {"r%d" % slot: n}), [(left, 0, 1, 1, None)], [buf], way)
 
     def issue():
@@ -256,7 +271,8 @@ def rank_program(g, core, T, topo):
             for p in pred[k]:
                 succ[p].append(k)
         for k in range(n - 1, -1, -1):
-            rank_[k] = prog[k]["cost"] + max([rank_[s] + pred[s][k] for s in succ[k]] or [0.0])
+            rank_[k] = prog[k]["cost"] + max([rank_[s] + pred[s][k] for s in succ[k]] or [prog[k]["lat"]])
+        rank_ = [r + c["bias"] for r, c in zip(rank_, prog)]
         left = [len(p) for p in pred]
         at, free, done = [0.0] * n, {}, [0.0] * n
         ready = {k for k in range(n) if left[k] == 0}
@@ -270,7 +286,7 @@ def rank_program(g, core, T, topo):
                     best = key
             t0, _, k = best
             e, late = prog[k]["e"], t0 + PATIENCE * prog[k]["cost"]
-            if e in ("V", "S", "P"):
+            if e in ("V", "S", "P", "G"):
                 for j in ready:
                     if prog[j]["e"] == e and at[j] < late and (rank_[j], -j) > (rank_[k], -k):
                         k = j
@@ -290,12 +306,10 @@ def rank_program(g, core, T, topo):
         return (x[2] - x[1] + x[3] - 1) // x[3]
 
     def half(*xs):
-        return 0.5 if all(x[0] in two for x in xs) else 1.0
-
-    two = {p[0] for p in PLACE.values() if p[3] in ("bfloat16", "uint16")}
+        return 0.5 if all(SCRATCH[x[0]][2] in (BF, U16, H16) for x in xs) else 1.0
 
     def ew(w, f=1.0):
-        return 0.03 + max(64, w * f) * 1.04e-3
+        return 0.04 + max(64, w * f) * 0.95e-3
 
     def ind(win, off):
         return ap(win).indirect(ap(off))
@@ -314,30 +328,35 @@ def rank_program(g, core, T, topo):
         else:
             op("V", lambda: g.vector.tensor_scalar(ap(o), ap(a), p1, p2, f, f2), rd, [o], w)
 
+    def bits(o, a, shift, mask):
+        if shift:
+            ts(o, a, shift, A.arith_shift_right, mask, A.bitwise_and)
+        else:
+            ts(o, a, mask, A.bitwise_and)
+
     def cp(o, a):
         op("V", lambda: g.vector.tensor_copy(ap(o), ap(a)), [a], [o], ew(wid(o), half(o, a)))
 
     def ms(o, c):
         op("V", lambda: g.vector.memset(ap(o), c), [], [o], ew(wid(o), half(o)))
 
-    def red(o, a):
-        op("V", lambda: g.vector.tensor_reduce(ap(o), ap(a), AxisListType.X, A.add), [a], [o], ew(wid(a)))
+    def least(o, a):
+        op("V", lambda: g.vector.tensor_reduce(ap(o), ap(a), AxisListType.X, A.min), [a], [o], ew(wid(a)))
 
-    def asel(o, a, pattern, base):
-        op("G", lambda: g.affine_select(ap(o), ap(a), pattern, A.is_equal, 0.0, base, 1), [a], [o, GQ], 0.2 + 2.1e-3 * wid(o))
+    def turn(o, a):
+        op("V", lambda: g.vector.transpose(ap(o), ap(a)), [a], [o], ew(wid(o), half(o, a)))
 
     def gat(o, win, off):
-        op("V", lambda: g.vector.tensor_copy(ap(o), ind(win, off)), [win, off], [o], ew(wid(o), 1.5))
+        op("V", lambda: g.vector.tensor_copy(ap(o), ind(win, off)), [win, off], [o], ew(wid(o), 1.56))
 
     def sca(win, off, a):
-        op("V", lambda: g.vector.tensor_copy(ind(win, off), ap(a)), [a, off], [win], ew(wid(a), 3.5))
+        op("V", lambda: g.vector.tensor_copy(ind(win, off), ap(a)), [a, off], [win], ew(wid(a), 3.8))
 
     def gtt(o, win, off, b, f):
-        op("V", lambda: g.vector.tensor_tensor(ap(o), ind(win, off), ap(b), f), [win, off, b], [o], ew(wid(o), 1.6))
+        op("V", lambda: g.vector.tensor_tensor(ap(o), ind(win, off), ap(b), f), [win, off, b], [o], ew(wid(o), 1.56))
 
-    def scan(o, a, z, f):
-        w = ew(wid(o), half(o, a))
-        op("V", lambda: g.vector.tensor_tensor_scan(ap(o), ap(a), ap(z), 0.0, f, A.add), [a, z], [o], w)
+    def scan(o, a, z, f, first=0.0):
+        op("V", lambda: g.vector.tensor_tensor_scan(ap(o), ap(a), ap(z), first, f, A.add), [a, z], [o], ew(wid(o), half(o, a)))
 
     def act(o, a, func=F.Copy, bias=None, scale=None, accum_out=None):
         kw = {}
@@ -352,479 +371,479 @@ def rank_program(g, core, T, topo):
             kw["accum_out"] = ap(accum_out)
         op("S", lambda: g.scalar.activation(ap(o), ap(a), func, **kw), rd, [o] + ([] if accum_out is None else [accum_out]), ew(wid(o)))
 
-    def sgat(o, win, off, scale=1.0):
-        op("S", lambda: g.scalar.activation(ap(o), ind(win, off), F.Copy, scale=scale), [win, off], [o], ew(wid(o), 1.5))
+    def sgat(o, win, off):
+        op("S", lambda: g.scalar.activation(ap(o), ind(win, off), F.Copy), [win, off], [o], ew(wid(o), 1.56))
+
+    def pick(e):
+        return gat if e == "V" else sgat
 
     def iota(o, pattern, base, ch=0):
-        if SCRATCH[o[0]][2] == "int32":
-            op("G", lambda: g.iota(ap(o), pattern, base, ch), [], [o], 0.2)
+        if SCRATCH[o[0]][2] == I32:
+            op("G", lambda: g.iota(ap(o), pattern, base, ch), [], [o], 0.13 + 1.9e-3 * wid(o))
         else:
-            op("G", lambda: g.iota(ap(o), pattern, base, ch, allow_small_or_imprecise_dtypes=True), [], [o], 0.2 + 2.1e-3 * wid(o))
+            op("G", lambda: g.iota(ap(o), pattern, base, ch, allow_small_or_imprecise_dtypes=True), [], [o], 0.13 + 1.9e-3 * wid(o))
+
+    def gcp(o, a):
+        op("G", lambda: g.affine_select(ap(o), ap(a), [[0, wid(o)]], A.is_equal, 0.0, 0, 0), [a], [o, GQ], 0.17 + 1.9e-3 * wid(o))
 
     def win(R, i):
         return v(R, 15 - i, 143 - i)
 
+    def wrap(o, R, x, lo, hi):
+        return [(o, win(R, i), v(x, lo + i, hi, 16)) for i in range(16)]
+
+    def row(name, q):
+        return v(name, 0, 2048, 1, slice(q, 128, 16))
+
+    bias[0] = 50.0
     dma("Y", v("vfb"), None, i=T.vf[:])
     dma("S", v("hyb"), None, i=T.hy[:])
     dma("Y", v("x2b"), None, i=T.xs[2:128:16, :])
-    dma("S", v("X", 0, 2048), None, i=T.xs[:])
-    dma("Y", v("WI"), None, i=T.wd[:])
-    dma("S", v("RI32"), None, i=T.rq[:])
-    dma("Y", v("SG", 0, 1024), None, i=T.sg[:])
-    dma("S", v("thi"), None, i=T.th[:])
+    bias[0] = 40.0
+    dma("S", v("X", 0, 2048), None, i=T.xs[:], lat=4.0)
+    dma("Y", v("WI", 0, 2048), None, i=T.wd[:], lat=9.5)
+    bias[0] = 30.0
+    dma("S", v("RI32", 0, 1024), None, i=T.rq[:], lat=9.5)
+    dma("Y", v("SG", 0, 1024), None, i=T.sg[:], lat=10.5)
+    dma("S", v("thi"), None, i=T.th[:], lat=11.0)
+    bias[0] = 0.0
 
     iota(v("KI", 0, 1), [[1, 1]], 0, 1)
-    iota(v("CR"), [[1, 256]], 0)
+    iota(v("CR"), [[1, 144]], 0)
     iota(v("MG"), [[1, 8], [0, 16]], 0)
     iota(v("MI"), [[0, 8], [1, 16]], 0)
-    iota(v("C1"), [[1, 128]], 0)
+    iota(v("J16"), [[16, 32]], 0)
     iota(v("JI"), [[1, 512]], 4097)
-    iota(v("JC", 0, 32), [[16, 32]], 0)
-    col = {}
+    iota(v("WI", 2048, 2560), [[0, 512]], 0)
+    col, ncol = {}, [0]
 
-    def newcol(name):
-        k = len(col)
-        col[name] = v("COLS", k, k + 1)
+    def newcol(name=None):
+        ncol[0] += 1
+        col[name] = v("COLS", ncol[0] - 1, ncol[0])
         return col[name]
 
-    ms(v("TB"), 0.0)
-    kif, kgf, kf = newcol("ki"), newcol("kg"), newcol("k")
-    ts(v("KI", 1, 2), v("KI", 0, 1), 4, A.arith_shift_right)
-    ts(v("KI", 2, 3), v("KI", 0, 1), 15, A.bitwise_and)
-    ts(v("KI", 3, 4), v("KI", 1, 2), 1, A.bitwise_and)
-    cp(kif, v("KI", 2, 3))
-    cp(kgf, v("KI", 1, 2))
-    cp(kf, v("KI", 0, 1))
-    odd, even = newcol("odd"), newcol("even")
-    cp(odd, v("KI", 3, 4))
-    ts(newcol("g15"), kgf, 16.0, A.mult, 15.0, A.add)
-    for q in range(8):
-        ts(newcol("q%d" % q), kif, float(q), A.is_equal)
-    ts(even, odd, 0.0, A.is_equal)
-    ts(newcol("c16"), col["q0"], 16.0, A.mult)
-    ts(newcol("c32"), col["q0"], 32.0, A.mult)
-    ts(newcol("x64"), col["q3"], -64.0, A.mult)
-    ts(newcol("b2"), col["q2"], 8192.0, A.mult)
-    ts(newcol("uw"), kif, 10.0, A.mult, 1.0, A.add)
-    ts(newcol("u32"), col["q5"], 32.0 * 4096.0, A.mult)
-    ts(newcol("u1"), col["q6"], 4096.0, A.mult)
-    tt(newcol("ud"), col["u32"], col["u1"], A.add)
-    ts(newcol("m2"), kif, 2.0, A.mult, 1.0, A.add)
-    ts(newcol("km"), kf, -16.0, A.add)
-    ts(newcol("kp"), kf, 16.0, A.add)
-    ts(newcol("k5"), kf, -5.0, A.add)
-    tt(newcol("h"), col["c32"], col["q1"], A.add)
-    ts(newcol("keep"), kif, 2.5, A.is_gt)
-    ts(newcol("sx"), col["h"], 8192.0, A.mult)
-    tt(col["sx"], col["sx"], col["x64"], A.add)
-    tt(col["sx"], col["sx"], col["q4"], A.subtract)
-    ts(v("R1", 0, 143), v("CR", 0, 143), col["g15"], A.is_equal)
-    ts(v("BI", 0, 128), v("hyb"), 5, A.arith_shift_right)
-    ts(v("BI", 128, 256), v("hyb"), 31, A.bitwise_and)
-    ts(v("BF2", 0, 128), v("vfb"), -8192.0, A.mult, 8192.0, A.add)
-    tt(v("FL0"), v("BF2", 0, 128), v("x2b"), A.add)
-    dma("Y", v("TB", 0, 2048, 1, slice(2, 128, 16)), v("FL0"))
-    cp(v("AB", 0, 256), v("BI", 0, 256))
-    dma("Y", v("TB", 0, 2048, 1, slice(0, 128, 16)), v("AB", 0, 128))
-    dma("Y", v("TB", 0, 2048, 1, slice(1, 128, 16)), v("AB", 128, 256))
-    ts(v("BO"), v("MG"), kgf, A.is_equal)
-    ts(v("RD2", 0, 143), v("R1", 0, 143), col["q2"], A.mult)
-    ts(v("GT"), v("MI"), kif, A.is_lt)
-    ts(v("EQ0"), v("MI"), kif, A.is_equal)
-    ts(v("LT"), v("MI"), kif, A.is_gt)
-    tt(v("ID"), v("BO"), v("EQ0"), A.mult)
-    tt(v("GT"), v("GT"), v("BO"), A.mult)
-    ts(v("LPA"), v("ID"), 4096.0, A.mult)
-    tt(v("LPA"), v("LPA"), v("GT"), A.subtract)
-    ts(v("LPB"), v("ID"), -4096.0, A.mult)
-    tt(v("LPB"), v("LPB"), v("GT"), A.subtract)
-    ts(v("RH12", 0, 8), v("CR", 0, 8), kgf, A.is_gt)
-    ts(v("RH12", 8, 16), v("CR", 0, 8), kgf, A.is_equal)
+    def q(k):
+        return v("QH", k, k + 1)
+
+    def weights(name, w):
+        last = None
+        for r, x in w.items():
+            c = newcol(name)
+            if last is None:
+                act(c, q(r), scale=float(x))
+            else:
+                act(c, q(r), F.Identity, bias=last, scale=float(x))
+            last = c
+        return last
+
+    bias[0] = 30.0
+    ms(v("TB", 0, 2048), 0.0)
+    ms(v("Z"), 0.0)
     ms(v("ZF"), 0.0)
-    ms(v("ZR"), 0.0)
-    ms(v("X", 2048, 2560), 0.0)
-    ms(v("WD", 2048, 2560), 0.0)
+    bias[0] = 0.0
+    ki, kg, kf, odd, even = newcol("ki"), newcol("kg"), newcol("k"), newcol("odd"), newcol("even")
+    ts(v("KI", 1, 2), v("KI", 0, 1), 4, A.arith_shift_right)
+    bits(v("KI", 2, 3), v("KI", 0, 1), 0, 15)
+    bits(v("KI", 3, 4), v("KI", 0, 1), 4, 1)
+    cp(ki, v("KI", 2, 3))
+    cp(kg, v("KI", 1, 2))
+    cp(kf, v("KI", 0, 1))
+    cp(odd, v("KI", 3, 4))
+    ts(v("QH"), v("CR", 0, 16), ki, A.is_equal)
+    for name, src, a, b in (("even2", odd, -1.0, 1.0), ("g15", kg, 16.0, 15.0), ("g16", kg, 16.0, 0.0), ("g17", kg, 16.0, 1.0), ("km", kf, 1.0, -16.0),
+                            ("kp", kf, 1.0, 16.0), ("k5", kf, 1.0, -5.0), ("uw", ki, 10.0, 1.0), ("n2", q(2), -1.0, 1.0)):
+        act(newcol(name), src, F.Identity, bias=b, scale=a)
+    even = col["even2"]
+    ts(v("R1", 0, 143), v("CR", 0, 143), col["g15"], A.is_equal)
+    ts(v("BO"), v("MG"), kg, A.is_equal)
+    ts(v("ID"), v("CR", 0, 128), kf, A.is_equal)
+    ts(v("LT"), v("MI"), ki, A.is_gt)
+    ts(v("EQH"), v("MI"), ki, A.is_equal, 0.5, A.mult)
+    ts(v("GT"), v("MI"), ki, A.is_lt)
+    tt(v("GT"), v("GT"), v("BO"), A.mult)
+    act(v("LPA"), v("ID"), scale=4096.0)
+    tt(v("LPA"), v("LPA"), v("GT"), A.subtract)
+    ts(v("RH3", 0, 8), v("CR", 0, 8), kg, A.is_gt)
+    ts(v("RH3", 8, 16), v("CR", 0, 8), kg, A.is_equal)
+    ts(v("RH3", 16, 24), v("CR", 0, 8), kg, A.is_equal, 4096.0, A.mult)
+    for k, (c_, m_) in enumerate(((kf, even), (col["kp"], even), (col["km"], odd), (kf, odd))):
+        ts(v("SWB", 128 * k, 128 * k + 128), v("CR", 0, 128), c_, A.is_equal, m_, A.mult)
+    act(v("JW"), v("J16"), F.Identity, bias=ki)
+    for name, n, a, b in (("JC", 32, 1.0, 2048.0), ("W8", 8, 1.0, 2048.0), ("JD", 32, 1.0, 1024.0), ("W4", 4, 2.0, 2560.0), ("S4", 4, 1.0, 0.25)):
+        act(v(name), v("JW", 0, n), F.Identity, bias=b, scale=a)
     for t in range(3):
-        ms(v("WE%d" % t, 2048, 2176), 0.0)
-    ms(v("RQ", 1024, 1032), 1024.0)
+        c0 = 896 * t % 2048 // 16
+        act(v("C1%d" % t), v("CR", 0, 128), F.Relu, bias=weights("c1", {1: c0 - 127, 2: c0, 3: c0 - 128} if t else {1: -127, 3: -128}),
+            scale=col["n2"])
+    ts(v("PW", 0, 16), v("ZF", 0, 16), 2.0, A.add)
+    scan(v("PW", 16, 32), v("PW", 0, 16), v("ZF", 0, 16), A.mult, 0.5)
+    tt(v("PW", 32, 48), v("PW", 16, 32), v("QH"), A.mult)
+    op("V", lambda: g.vector.tensor_reduce(ap(v("PW", 48, 49)), ap(v("PW", 32, 48)), AxisListType.X, A.add), [v("PW", 32, 48)], [v("PW", 48, 49)])
+    for name, c in (("RD0", q(0)), ("RI", ki), ("RC", weights("rc", {0: 16, 1: -2048, 2: 16, 3: 2048})), ("RH", weights("h", {0: 32, 1: 1})),
+                    ("RU", col["uw"]), ("RX", weights("sx", {0: 1 / 64, 1: 1 / 2048, 3: -64, 4: -1})), ("R2", 2.0), ("RN", -1.0), ("RD2", q(2)),
+                    ("R16", 16.0), ("RO", weights("ro", {10: 128, 11: 1})), ("RB", weights("rb", {8: 32, 9: 1})),
+                    ("RS", weights("rs", {5: 64, 6: 2, 12: 1})), ("RL", v("PW", 48, 49))):
+        act(v(name, 0, 143), v("R1", 0, 143), scale=c)
+    act(v("ON"), v("Z", 0, 128), F.Identity, bias=1.0)
+    dma("Y", row("TB", 12), v("ON"))
+    ts(v("TB", 2048, 2688), v("Z", 0, 640), weights("tb", {0: 32}), A.add)
+    act(v("CW", 0, 512), v("Z", 0, 512))
+    act(v("TBL", 512, 528), v("Z", 0, 16), F.Identity, bias=weights("tl", {10: 16}))
+    ms(v("X", 2048, 2064), 16384.0)
+    ms(v("RI32", 1024, 1032), 1024)
     ms(v("SG", 1024, 1040), 0.0)
-    ms(v("CW", 0, 512), 0.0)
-    ts(v("TB", 2048, 2560), v("ZR"), col["c32"], A.add)
-    ts(v("JW"), v("JC", 0, 32), kif, A.add)
-    ts(v("W8", 0, 8), v("JW", 0, 8), 2048.0, A.add)
-    ts(v("W8", 8, 12), v("JW", 0, 4), 2560.0, A.add)
-    ts(v("JC", 32, 64), v("JW"), 2048.0, A.add)
-    for n_, c_ in (("RD0", "q0"), ("RI", "ki"), ("RC", "c16"), ("RH", "h"), ("RX", "sx"), ("R0f", "q0"), ("RU", "uw")):
-        act(v(n_, 0, 143), v("R1", 0, 143), scale=col[c_])
-    dma("Y", v("TB", 0, 2048, 1, slice(7, 128, 16)), v("x2b"))
-    mms([(v("q7", 0, 128), win("R1", b), v("X", 128 * b, 128 * b + 128)) for b in range(16)])
-    mms([(v("q7", 128, 256), win("RU", b), v("X", 128 * b, 128 * b + 128)) for b in range(16)])
-    cp(v("BI", 256, 512), v("q7", 0, 256))
-    ts(v("BI", 512, 640), v("BI", 256, 384), 6, A.arith_shift_right)
-    ts(v("BI", 640, 768), v("BI", 256, 384), 63, A.bitwise_and)
-    ts(v("BI", 768, 896), v("BI", 384, 512), 5, A.arith_shift_right, 63, A.bitwise_and)
-    ts(v("BI", 896, 1024), v("BI", 384, 512), 31, A.bitwise_and)
-    cp(v("CW", 512, 1024), v("BI", 512, 1024))
-    for q in range(3, 7):
-        dma("Y", v("TB", 0, 2048, 1, slice(q, 128, 16)), v("CW", 128 * q + 128, 128 * q + 256))
-    cp(v("SXT"), v("TB", 0, 2048))
-    cp(v("RQ", 0, 1024), v("RI32"))
-    cp(v("WD", 0, 2048), v("WI"))
-    send(6, rank - 1, v("FI0"), v("FL0"))
-    send(0, rank - 1, v("XE0"), v("X", 0, 2048))
-    send(13, None, v("WD", 0, 2048), v("WD", 0, 2048))
-    send(3, rank - 1, v("WE0", 0, 1024), v("WD", 0, 1024))
-    send(12, None, v("X", 0, 2048), v("X", 0, 2048))
-    send(5, rank - 3, v("WE2", 0, 2048), v("WD", 0, 2048))
-    arrive(6, v("FI0"), 6, 4.0)
-    arrive(0, v("XE0"), 0, 20.0)
-    arrive(3, v("WE0", 0, 1024), 3, 30.0)
-    arrive(14, v("WE0", 1024, 2048), 13, 30.0)
-    arrive(1, v("XE1"), 12, 40.0)
-    arrive(4, v("WE1", 0, 2048), 12, 60.0)
-    arrive(2, v("XE2"), 12, 80.0)
-    arrive(5, v("WE2", 0, 2048), 5, 70.0)
+    ts(v("NT", 0, 128), v("vfb"), 0.5, A.is_lt)
+    ts(v("SI", 0, 128), v("hyb"), 5, A.arith_shift_right)
+    bits(v("SI", 128, 256), v("hyb"), 0, 31)
+    cp(v("ST", 0, 256), v("SI", 0, 256))
+    dma("Y", row("TB", 0), v("ST", 0, 128))
+    dma("Y", row("TB", 1), v("ST", 128, 256))
+    act(v("TMP"), v("NT", 0, 128), scale=8192.0)
+    tt(v("FL0"), v("TMP"), v("x2b"), A.add)
+    dma("Y", row("TB", 2), v("FL0"))
+    dma("Y", row("TB", 7), None, i=T.xs[2:128:16, :])
+    act(v("KIB"), v("Z", 0, 128), F.Identity, bias=ki)
+    dma("Y", row("TB", 10), v("KIB"))
+    act(v("BQ0"), v("CR", 0, 128))
+    dma("Y", row("TB", 11), v("BQ0"))
+    mm([(v("q6", 0, 128), win("R1", b), v("X", 128 * b, 128 * b + 128)) for b in range(16)])
+    mm([(v("q6", 128, 256), win("RU", b), v("X", 128 * b, 128 * b + 128)) for b in range(16)])
+    si = lambda k: v("SI", 128 * k, 128 * k + 128)
+    cp(v("SI", 256, 512), v("q6", 0, 256))
+    ts(si(4), si(2), 6, A.arith_shift_right)
+    bits(si(5), si(2), 0, 63)
+    cp(v("ST", 256, 512), v("SI", 512, 768))
+    for r in (3, 4):
+        dma("Y", row("TB", r), v("ST", 128 * r - 128, 128 * r))
+    bits(si(2), si(3), 0, 2047)
+    ts(si(3), si(2), 32.0, A.add)
+    ts(si(6), si(2), 5, A.arith_shift_right)
+    tt(si(3), si(3), si(2), A.mult)
+    bits(si(7), si(2), 0, 31)
+    bits(si(8), si(3), 10, 63)
+    bits(si(9), si(3), 5, 31)
+    cp(v("ST", 512, 1024), v("SI", 768, 1280))
+    for k, r in enumerate((5, 6, 8, 9)):
+        dma("Y", row("TB", r), v("ST", 512 + 128 * k, 640 + 128 * k))
+    for k in range(4):
+        cp(v("W16", 512 * k, 512 * k + 512), v("WI", 512 * k, 512 * k + 512))
+    far, near = relays_of(core, T, topo)
+    send(1, served(1), v("XE0"), v("X", 0, 2048))
+    send(2, near, v("X", 0, 2048), v("X", 0, 2048))
+    send(3, far, v("W16"), v("W16"))
+    send(4, served(1), v("WH0", 0, 1024), v("W16", 0, 1024))
+    send(0, served(1), v("FI0"), v("FL0"))
+    arrive(0, v("FI0"), 0, 4.0)
+    arrive(1, v("XE0"), 1, 18.0)
+    arrive(4, v("WH0", 0, 1024), 4, 20.0)
+    arrive(10, v("WH0", 1024, 2048), 3, 20.0)
+    arrive(13, v("XE1"), 3, 35.0)
+    arrive(14, v("WH1"), 3, 50.0)
+    arrive(15, v("XE2"), 3, 40.0)
+    arrive(16, v("WH2"), 3, 55.0)
+    op("G", lambda: g.iota(ap(v("ZU")), [[0, 2048]], 0, 0, allow_small_or_imprecise_dtypes=True), [], [v("ZU"), GQ], 4.1)
+    for k, (n_, w_) in enumerate((("UH", 32.0), ("UL", 1.0), ("UG", 8192.0))):
+        op("G", lambda n_=n_, w_=w_, k=k: g.affine_select(ap(v(n_)), ap(v("ZU")), [[-1, 16], [-16, 8], [1000, 16]], A.not_equal, w_,
+                                                          -1000 * k, 1), [v("ZU")], [v(n_), GQ], 4.1)
+    gcp(v("WD", 0, 2048), v("W16"))
+    gcp(v("WD", 2048, 2560), v("Z", 0, 512))
+    gcp(v("WE", 2048, 2176), v("Z", 0, 128))
 
     def late_constants():
-        ts(v("R2", 0, 143), v("R1", 0, 143), 2.0, A.mult)
-        ts(v("RN", 0, 143), v("R1", 0, 143), -1.0, A.mult)
-        act(v("R1f", 0, 143), v("R1", 0, 143))
-        act(v("BOf"), v("BO"))
-        for n_, c_ in (("UD", "ud"), ("BOI", "ki"), ("BC", "c16")):
-            act(v(n_), v("BO"), scale=col[c_])
-        for n_, c_ in (("D0", "q0"), ("D1", "q1"), ("K34", "keep")):
-            act(v(n_), v("ID"), scale=col[c_])
-        ts(v("NI"), v("ID"), -1.0, A.mult)
-        ts(v("X2D"), v("CR", 0, 128), col["k5"], A.is_equal, col["q7"], A.mult)
-        tt(v("X2D"), v("X2D"), v("K34"), A.add)
+        for n_, src, c in (("NI", "ID", -1.0), ("IDK", "ID", -8388608.0), ("ID24", "ID", 24.0), ("IDF", "ID", 2048.0), ("NBO", "BO", -1.0),
+                           ("B128", "BO", 128.0), ("BQ0", "BO", q(0))):
+            act(v(n_), v(src), scale=c)
+        act(v("SW"), v("SWB"))
+        act(v("NLP"), v("ID"), scale=4096.0)
+        tt(v("NLP"), v("NLP"), v("GT"), A.add)
+        act(v("LPB"), v("NLP"), scale=-1.0)
+        ts(v("ZT"), v("LT"), -2.0, A.mult)
+        tt(v("ZT"), v("ZT"), v("BO"), A.mult)
+        tt(v("ZT"), v("ZT"), v("ID"), A.add)
+        ts(newcol("keep"), ki, 2.5, A.is_gt)
+        act(v("K34"), v("ID"), scale=col["keep"])
+        ts(v("X2D"), v("CR", 0, 128), col["k5"], A.is_equal, q(7), A.mult)
+        act(v("D0"), v("ID"), scale=col["n2"])
+        tt(v("X2D"), v("X2D"), v("D0"), A.add)
+        ts(v("D0"), v("CR", 0, 128), col["g16"], A.is_equal)
+        ts(v("D1"), v("CR", 0, 128), col["g17"], A.is_equal)
+        act(v("ONS"), v("Z", 0, 128), F.Identity, bias=1.0 / 4096)
+        act(v("TMP"), v("MI"), F.Identity, bias=col["rb"], scale=col["rs"])
+        tt(v("CWM"), v("TMP"), v("BO"), A.mult)
+        act(v("TMP"), v("MI"), scale=q(12))
+        tt(v("MK12"), v("TMP"), v("BO"), A.mult)
+        act(v("SC", 0, 32), v("Z", 0, 32), F.Identity, bias=weights("sc", {0: 4096, 1: -1}))
+        act(v("SC", 32, 64), v("Z", 0, 32), F.Identity, bias=weights("sc", {0: 4608, 1: -1}))
+        ts(v("RM"), v("CR", 0, 64), 32.0, A.not_equal)
+        act(v("DF", 0, 128), v("ZF"), F.Identity, bias=weights("df", {9: 1 << 22}))
+        act(v("DF", 128, 192), v("CR", 0, 64), F.Identity, bias=weights("df", {0: (1 << 23) + 2560}), scale=weights("d2", {0: 2}))
+        weights("b2", {2: 8192})
+        ts(v("thB", 0, 1), v("thi"), 0.5, A.add)
+        ts(v("thB", 1, 2), v("thi"), 0.5, A.add)
+        bias[0] = 12.0
+        inv = v("PW", 56, 57)
+        op("V", lambda: g.vector.reciprocal(ap(inv), ap(v("PW", 48, 49))), [v("PW", 48, 49)], [inv], 0.25)
+        act(newcol("cut"), inv, F.Identity, bias=0.499, scale=4097.0)
+        ts(v("SI", 0, 512), v("JI"), inv, A.mult, col["cut"], A.subtract)
+        bits(v("SI", 0, 512), v("SI", 0, 512), 0, 1)
+        ts(v("JB"), v("SI", 0, 512), 4194304.0, A.mult)
+        bias[0] = 0.0
 
-    def last_constants():
-        cp(v("thB", 0, 1), v("thi"))
-        cp(v("thB", 1, 2), v("thB", 0, 1))
-        tt(v("TRI"), v("BO"), v("LT"), A.mult)
-        ms(v("ON"), 1.0)
-        ts(v("J192"), v("JW"), 192.0, A.add)
-        ts(v("DD", 0, 32), v("JW"), 192.0 - 4095.0, A.add)
-        ts(v("DD", 32, 64), v("JW"), 64.0 - 4095.0, A.add)
-        ms(v("LIM", 0, 32), 128.0 - 4095.0)
-        ms(v("LIM", 32, 64), 64.0 - 4095.0)
-        for k, (c_, m_) in enumerate(((kf, even), (col["kp"], even), (col["km"], odd), (kf, odd))):
-            ts(v("SW", 128 * k, 128 * k + 128), v("CR", 0, 128), c_, A.is_equal, m_, A.mult)
-        for c in range(4):
-            ts(v("AF", 64 * c, 64 * c + 64), v("CR", 0, 64), -1.0, A.mult, 16.0 * c - 0.5, A.add)
-        ts(v("MK"), v("AF", 0, 256), kif, A.add, 0.0, A.is_gt)
-        ms(v("U0"), 0.0)
-        ms(v("U0", 0, 2064, 16), 1.0)
-        for q, n_ in enumerate(("UH", "UL", "UG")):
-            asel(v(n_), v("U0", 16 - q, 2064 - q), [[-1, 16], [-1, 128]], q)
+    def slots_reset():
+        gcp(v("P1W", 0, 128), v("DF", 0, 128))
+        gcp(v("P1W", 512, 576), v("DF", 128, 192))
 
     def lanes(t):
         c0 = 896 * t % 2048 // 16
-        mms([(v("q2", 0, 128), win("RD2", i), v("TB", i, 2048, 16)) for i in range(16)])
-        ts(v("NW", 0, 128 - c0), v("q2", c0, 128), 4096.0, A.is_ge)
-        if c0:
-            ts(v("NW", 128 - c0, 128), v("q2", 0, c0), 4096.0, A.is_ge)
-        mms([(v("q3", 0, 128), v("BO"), v("NW"))])
-        mms([(v("q4", 0, 128), v("NW"), v("BO"))])
-        mms([(v("q3", 128, 256), v("LPA"), v("NW"))])
-        act(v("TTB", 0, 128), v("q4", 0, 128))
-        scan(v("CUM"), v("q3", 0, 128), v("ZF"), A.add)
-        tt(v("TTB", 256, 384), v("q4", 0, 128), v("EQ0"), A.mult)
-        tt(v("TTB", 128, 256), v("q4", 0, 128), v("LT"), A.mult)
-        mms([(v("q5", 8, 16), v("TTB", 256, 384), v("RH12", 8, 16))])
-        mms([(v("q5", 0, 8), v("TTB", 0, 128), v("RH12", 0, 8)), (v("q5", 0, 8), v("TTB", 128, 256), v("RH12", 8, 16))])
-        tt(v("POS"), v("q3", 128, 256), v("CUM"), A.add)
-        ts(v("OF", 0, 8), v("q5", 8, 16), 0.5, A.is_lt)
-        tt(v("OF", 8, 16), v("OF", 0, 8), v("W8", 0, 8), A.mult)
-        tt(v("OF", 16, 24), v("q5", 0, 8), v("OF", 8, 16), A.add)
-        cp(v("OFu"), v("OF", 16, 24))
-        sca(v("CW"), v("OFu"), v("C1"))
-        ts(v("EX", 0, 32), v("JW"), v("CUM", 127, 128), A.is_ge)
-        tt(v("EX", 32, 64), v("EX", 0, 32), v("JC", 32, 64), A.mult)
-        scan(v("CC"), v("CW", 0, 512), v("ZR"), A.max)
-        mms([(v("q5", 32, 64), win("RD0", i), v("CC", i, 512, 16)) for i in range(16)])
-        cp(v("CLu"), v("q5", 32, 64))
+        if t == 0:
+            turn(v("NT", 128, 256), v("NT", 0, 128))
+            mm([(v("q3", 2 * b + s1, 128, 8), v("SWB", 256 * s1 + 128 * g2, 256 * s1 + 128 * g2 + 128), v("NT", 128 + 32 * b + 16 * g2, 144 + 32 * b + 16 * g2))
+                for b in range(4) for s1 in (0, 1) for g2 in (0, 1)], each=2)
+            ts(v("NW"), v("q3", 0, 128), 0.5, A.is_ge)
+        else:
+            mm(wrap(v("q3", 0, 128), "RD2", "TB", 0, 2048))
+            ts(v("NW", 0, 128 - c0), v("q3", c0, 128), 4096.0, A.is_ge)
+            ts(v("NW", 128 - c0, 128), v("q3", 0, c0), 4096.0, A.is_ge)
+        mm([(v("q3", 128, 256), v("NW"), v("BO"))])
+        mm([(v("q5", 0, 128), v("BO"), v("NW")), (v("q5", 128, 256), v("LPA"), v("NW"))], each=1)
+        cp(v("TTB", 0, 128), v("q3", 128, 256))
+        tt(v("TTB", 128, 256), v("q3", 128, 256), v("LT"), A.mult)
+        tt(v("TTB", 256, 384), v("q3", 128, 256), v("EQH"), A.is_lt)
+        mm([(v("q3", 256, 264), v("TTB", 128 * k, 128 * k + 128), v("RH3", 8 * k, 8 * k + 8)) for k in range(3)])
+        scan(v("CUM"), v("q5", 0, 128), v("ZF"), A.add)
+        tt(v("OF"), v("q3", 256, 264), v("W8"), A.min)
+        cp(v("OFu"), v("OF"))
+        sca(v("CW"), v("OFu"), v("C1%d" % t))
+        tt(v("POS"), v("q5", 128, 256), v("CUM"), A.add)
+        ts(v("EX"), v("JW"), v("CUM", 127, 128), A.is_ge, 4096.0, A.mult)
+        scan(v("CC"), v("CW", 0, 512), v("Z", 0, 512), A.max)
+        mm(wrap(v("q3", 288, 320), "RD0", "CC", 0, 512))
+        cp(v("CLu"), v("q3", 288, 320))
         gtt(v("OH"), v("POS"), v("CLu"), v("JI"), A.is_equal)
-        mms([(v("q6", 0, 32), win("RC", i), v("CC", i, 512, 16)) for i in range(16)],
-            [(v("q6", 0, 32), win("RI", i), v("OH", i, 512, 16)) for i in range(16)])
-        ts(v("Li", 0, 32), v("q6", 0, 32), float(16 * c0), A.add)
-        ts(v("Li", 32, 64), v("Li", 0, 32), 2047, A.bitwise_and)
-        tt(v("Li", 0, 32), v("Li", 32, 64), v("EX", 32, 64), A.max)
-        cp(v("Lu"), v("Li", 0, 32))
+        mms(wrap(v("q4", 0, 32), "RC", "CC", 0, 512) + [(v("q4", 0, 32), v("ID"), v("EX"))], wrap(v("q4", 0, 32), "RI", "OH", 0, 512))
+        tt(v("Lf"), v("q4", 0, 32), v("JC"), A.min)
+        cp(v("Lu"), v("Lf"))
 
     def fetch(t):
-        sgat(v("TBL"), v("TB"), v("Lu"))
-        gat(v("Wu"), v("WD"), v("Lu"))
-        mms([(v("q5", 64, 96), win("RH", i), v("TBL", i, 512, 16)) for i in range(16)])
-        cp(v("STu"), v("q5", 64, 96))
-        gat(v("Ku"), v("RQ"), v("STu"))
-        sgat(v("KX"), v("RQ"), v("STu"), 8192.0)
-        sgat(v("W4"), v("WD"), v("Lu"), 4.0)
-
-    CH = (0, 160, 320, 448, 512)
+        gat(v("TBL", 0, 512), v("TB"), v("Lu"))
+        mm(wrap(v("q5", 256, 288), "RH", "TBL", 0, 512))
+        cp(v("STu"), v("q5", 256, 288))
+        gat(v("Ku"), v("RI32"), v("STu"))
 
     def check(t):
-        def ch(x, k):
-            return v(x, CH[k], CH[k + 1])
+        nch = len(CH) - 1
+        banks = ("q5", "q3", "q0", "q1")
 
-        def sig(k):
-            sgat(tile("sg", k), v("SG"), ch("Ku", k))
+        def ch(x, k, at=0):
+            return v(x, at + CH[k], at + CH[k + 1])
 
         def tile(x, k, p=None):
             n = 16 * (CH[k + 1] - CH[k])
-            name = "%s%d" % (x, k & 1)
-            return v(name, 0, n) if p is None else v(name, p, n, 16)
+            name, at = ("sig", 16 * CH[k]) if x == "sg" else ("%s%d" % (x, k & 1), 0)
+            return v(name, at, at + n) if p is None else v(name, at + p, at + n, 16)
 
-        def typ(k, e):
-            (gat if e == "V" else sgat)(tile("hg", k), v("TB"), ch("Wu", k))
+        def part(R, x, k):
+            return [(v(banks[k], 0, CH[k + 1] - CH[k]), win(R, p), tile(x, k, p)) for p in range(16)]
 
-        def val(k):
+        for k in range(nch):
+            sgat(tile("sg", k), v("SG"), ch("Ku", k))
+        ts(v("KF"), v("Ku"), -1.0 / 2048, A.mult)
+        ts(v("PM"), v("Ku"), 1024.0, A.is_ge, 4194304.0, A.mult)
+        gat(v("Wu"), v("WI" if t == 0 else "WD"), v("Lu"))
+        bias[0] = 20.0
+        cp(v("Wf"), v("Wu"))
+        mm([(v("q2"), v("ID"), v("JB")), (v("q2"), v("IDK"), v("KF")), (v("q2"), v("NI"), v("PM")), (v("q2"), v("ID"), v("Wf"))], last=False)
+        bias[0] = 0.0
+        hi = lambda k: v("HI", 32 * k, 32 * k + 32)
+        cp(hi(0), v("STu"))
+        ts(hi(1), hi(0), 80.0, A.add)
+        tt(hi(1), hi(1), hi(0), A.mult)
+        bits(hi(2), hi(1), 4, 1023)
+        tt(hi(3), hi(2), hi(0), A.subtract)
+        ts(v("HF", 0, 32), hi(2), 1024.0, A.subtract, -1.0, A.mult)
+        ts(hi(4), hi(3), 5, A.arith_shift_right)
+        bits(hi(5), hi(3), 0, 31)
+        ts(v("HF", 32, 64), hi(4), 1.0 / 32, A.mult)
+        for k in range(nch):
+            b, n = banks[k], CH[k + 1] - CH[k]
+            e = v(b, 0, n)
+            pick(TYP[t][k])(tile("hg", k), v("TB"), ch("Wu", k))
             gtt(tile("mm", k), v("X"), ch("Wu", k), tile("sg", k), A.max)
-
-        def sums(k):
-            q, n = ("q0", "q1", "q7", "q0")[k], CH[k + 1] - CH[k]
-            parts = [[(v(q, 0, n), win(R, p), tile(x, k, p)) for p in range(16)] for R, x in (("RX", "hg"), ("RN", "sg"), ("R2", "mm"))]
-            mms(*(parts if k < 3 else (parts[1], parts[0], parts[2])))
-
-        def small(k):
-            q, n = ("q0", "q1", "q7", "q0")[k], CH[k + 1] - CH[k]
-            tt(v("ED", 0, n), v(q, 0, n), ch("KX", k), A.subtract)
-            ts(v("ED", 160, 160 + n), v("ED", 0, n), 8191, A.bitwise_and)
-            tt(v("O0", 0, n), v("ED", 160, 160 + n), v("ED", 0, n), A.not_equal)
-            ts(v("GA", 0, n), v("ED", 160, 160 + n), v("thB", 1, 2), A.is_gt, 2.0, A.add)
-            tt(v("FT", 512 + CH[k], 512 + CH[k + 1]), v("O0", 0, n), ch("PM", k), A.mult)
-            tt(ch("FT", k), v("FT", 512 + CH[k], 512 + CH[k + 1]), v("GA", 0, n), A.mult)
-            act(ch("FOf", k), ch("FT", k))
-
-        sig(0)
-        typ(0, "V")
-        val(0)
-        sums(0)
-        if t == 0:
-            last_constants()
-        sig(1)
-        typ(1, "S")
-        ts(v("PM"), v("Ku"), 1024.0, A.is_lt)
-        val(1)
-        sums(1)
-        sig(2)
-        typ(2, "S")
-        tt(v("W4K"), v("W4"), v("KX"), A.add)
-        small(0)
-        mms([(v("q6"), v("BC"), v("CC")), (v("q6"), v("BOI"), v("OH")), (v("q6"), v("UD"), v("TBL"))])
-        act(v("P2"), v("q6"), F.Identity, bias=float(896 * t % 2048))
-        val(2)
-        sums(2)
-        sig(3)
-        typ(3, "S")
-        small(1)
-        cp(v("TY", 0, 32), v("q5", 64, 96))
-        tt(v("HLi", 0, 32), v("TY", 0, 32), v("TY", 0, 32), A.mult)
-        ts(v("HLi", 0, 32), v("HLi", 0, 32), 4, A.arith_shift_right)
-        ts(v("HLi", 32, 64), v("TY", 0, 32), 5.0, A.mult)
-        tt(v("TY", 32, 64), v("HLi", 0, 32), v("HLi", 32, 64), A.add)
-        ms(v("P1W", 0, 192), 0.0)
-        ms(v("P2W", 0, 128), 8388608.0)
-        ms(v("CW", 0, 512), 0.0)
-        val(3)
-        sums(3)
-        small(2)
-        small(3)
+            ends = [part("RX", "hg", k), part("R2", "mm", k)]
+            mms(part("RN", "sg", k) + [(e, v("ID"), ch("KF", k)), (e, v("ID24"), ch("PM", k))], *(ends if TYP[t][k] == "V" else ends[::-1]))
+            bias[0] = SMALL
+            cp(v("RD", 0, n), e)
+            tt(ch("FT", k, 512), e, v("RD", 0, n), A.not_equal)
+            mm([(v(b, 256, 256 + n), v("ZT"), ch("FT", k, 512))])
+            ts(v("GA", 0, n), v("RD", 0, n), v("thB", 1, 2), A.is_gt)
+            tt(ch("FT", k), ch("FT", k, 512), v("GA", 0, n), A.mult)
+            act(ch("FO", k), v(b, 256, 256 + n), F.Relu, scale=8388608.0)
+            mm([(ch("q2", k), v("IDF"), ch("FT", k)), (ch("q2", k), v("ID"), ch("FO", k))], first=False, last=k == nch - 1)
+            bias[0] = 0.0
+        act(v("PAY"), v("q2"))
 
     def post(t):
-        last = t == 2
-        c16 = 896 * t % 2048
-        lw = lambda k: v("LW", 32 * k, 32 * k + 32)
-        mms([(v("q3", 0, 64), win("R1", i), v("FT", i, 1024, 16)) for i in range(16)])
-        ts(lw(0), v("q3", 32, 64), -2.0, A.mult)
-        tt(lw(1), v("q3", 0, 32), lw(0), A.add)
-        ts(lw(4), lw(0), -1.0, A.is_lt)
-        ts(lw(2), lw(1), 0.5, A.is_lt)
-        ts(lw(3), lw(1), 3.5, A.is_lt)
-        tt(v("RP", 0, 32), lw(3), lw(2), A.subtract)
-        tt(v("RP", 32, 64), lw(4), lw(2), A.mult)
-        mms([(v("q4", 0, 64), v("BO"), v("RP"))])
-        mms([(v("q4", 64, 128), v("LPB"), v("RP"))])
-        mm = [(v("q6"), v("X2D"), v("TBL"))]
-        tt(v("HLi", 64, 96), v("TY", 32, 64), lw(1), A.add)
-        scan(lw(5), v("q4", 0, 32), v("ZF", 0, 32), A.add)
-        scan(lw(6), v("q4", 32, 64), v("ZF", 0, 32), A.add)
-        ts(v("HLi", 64, 96), v("HLi", 64, 96), 1023, A.bitwise_and)
-        tt(v("LW", 224, 288), v("q4", 64, 128), v("LW", 160, 224), A.add)
-        ts(v("GM"), lw(2), -8192.0, A.mult)
-        tt(v("LW", 288, 352), v("LW", 224, 288), v("LIM"), A.is_lt)
-        tt(v("LW", 352, 416), v("LW", 224, 288), v("DD"), A.subtract)
-        tt(v("HLi", 64, 96), v("HLi", 64, 96), v("TY", 0, 32), A.subtract)
-        tt(v("LW", 352, 416), v("LW", 352, 416), v("LW", 288, 352), A.mult)
-        ts(lw(4), lw(3), 0.5, A.is_lt)
-        tt(lw(9), lw(11), lw(12), A.add)
-        tt(v("HLi", 64, 96), v("HLi", 64, 96), lw(4), A.mult)
-        tt(lw(9), lw(9), v("J192"), A.add)
-        tt(v("HLi", 64, 96), v("HLi", 64, 96), v("TY", 0, 32), A.add)
-        cp(v("PFu"), lw(9))
-        op("V", lambda: g.vector.tensor_tensor(ind(v("P1W"), v("PFu")), ap(v("W4K")), ap(v("FOf")), A.add),
-           [v("W4K"), v("FOf"), v("PFu")], [v("P1W")], ew(512, 3.5))
-        ts(v("HLi", 128, 160), v("HLi", 64, 96), 5, A.arith_shift_right)
-        ts(v("HLi", 160, 192), v("HLi", 64, 96), 31, A.bitwise_and)
-        cp(v("HLb"), v("HLi", 128, 192))
-        ai = lambda lo, hi: v("AI", lo, hi)
-        af = lambda lo, hi: v("AF", lo, hi)
-        ab = lambda lo, hi: v("AB", lo, hi)
-        cp(ai(0, 64), v("P1W", 128, 192))
-        ts(ai(64, 128), ai(0, 64), 2, A.bitwise_and)
-        ts(ab(0, 64), ai(64, 128), 0.5, A.mult)
-        mms([(v("q4", 0, 64), v("TRI"), ab(0, 64))])
-        sca(v("P2W"), v("PFu"), v("P2"))
-        for i in range(16):
-            for U, d in (("UH", v("HLb", 0, 32)), ("UL", v("HLb", 32, 64)), ("UG", v("GM"))):
-                mm.append((v("q6", i, 512, 16), v(U, 128 * i, 128 * i + 128), d))
-        ts(af(0, 64), v("q4", 0, 64), 0.5, A.is_lt)
-        tt(af(0, 64), af(0, 64), ab(0, 64), A.mult)
-        tt(af(64, 128), v("P1W", 128, 192), af(0, 64), A.mult)
-        mms([(v("q4", 0, 64), v("BOf"), af(64, 128))])
-        mms(mm[:1], mm[1:])
-        act(v("TBn"), v("q6"), F.Identity, bias=col["b2"])
-        bi = lambda k: v("BI", 128 * k, 128 * k + 128)
-        cp(bi(0), v("P2W", 0, 128))
-        tt(af(216, 280), v("q4", 0, 64), v("EQ0", 0, 64), A.mult)
-        cp(ai(128, 192), v("q4", 0, 64))
-        tt(af(280, 312), v("AF", 216, 280, 2), v("AF", 217, 280, 2), A.add)
-        tt(af(312, 328), v("AF", 280, 312, 2), v("AF", 281, 312, 2), A.add)
-        tt(af(328, 336), v("AF", 312, 328, 2), v("AF", 313, 328, 2), A.add)
-        tt(ai(192, 196), v("AF", 328, 336, 2), v("AF", 329, 336, 2), A.add)
-        ts(bi(1), bi(0), 2047, A.bitwise_and)
-        ts(ai(196, 264), ai(128, 196), 2, A.arith_shift_right, 2047, A.bitwise_and)
-        cp(af(128, 196), ai(196, 264))
-        cp(v("AU", 0, 4), ai(260, 264))
-        cp(v("BU", 0, 128), bi(1))
-        sgat(ab(320, 384), v("SXT"), v("AU", 0, 4))
-        for h in (0, 1):
-            sgat(v("sg0", 1024 * h, 1024 * h + 1024), v("X"), v("BU", 64 * h, 64 * h + 64))
-        ts(bi(2), bi(0), 12, A.arith_shift_right, 2047, A.bitwise_and)
-        for c in range(4):
-            ts(ab(64 + 64 * c, 128 + 64 * c), af(128, 192), af(192 + c, 193 + c), A.is_equal)
-        tt(bi(3), bi(2), bi(2), A.mult)
-        ts(bi(4), bi(2), col["m2"], A.mult, kif, A.add)
-        tt(ab(64, 320), ab(64, 320), v("MK"), A.mult)
-        ts(bi(3), bi(3), 5, A.arith_shift_right)
-        for c in range(4):
-            act(ab(64 + 64 * c, 128 + 64 * c), ab(64 + 64 * c, 128 + 64 * c), accum_out=af(200 + c, 201 + c))
-        tt(bi(3), bi(3), bi(4), A.add)
-        ts(ai(264, 268), ai(192, 196), 2, A.bitwise_and)
-        ts(bi(3), bi(3), 2047, A.bitwise_and)
-        ts(af(204, 208), af(200, 204), 0.5, A.is_gt)
-        ts(af(208, 212), ai(264, 268), 0.5, A.is_lt)
-        cp(v("BU", 128, 256), bi(3))
-        tt(af(204, 208), af(204, 208), af(208, 212), A.max)
-        ts(ai(272, 336), ai(128, 192), 18, A.arith_shift_right)
-        tt(af(204, 208), af(204, 208), v("W8", 8, 12), A.mult)
-        ts(ai(336, 400), ai(128, 192), 13, A.arith_shift_right, 31, A.bitwise_and)
-        tt(af(204, 208), af(204, 208), af(192, 196), A.max)
-        cp(ab(384, 512), ai(272, 400))
-        cp(v("AU", 4, 8), af(204, 208))
-        mms([(v("q2", 0, 64), v("K34"), ab(320, 384)), (v("q2", 0, 64), v("D0"), ab(384, 448)), (v("q2", 0, 64), v("D1"), ab(448, 512))])
-        act(ab(512, 576), v("q2", 0, 64), F.Identity, bias=col["b2"])
+        n_, much, some = v("q3", 0, 32), v("RP", 0, 32), v("RP", 32, 64)
+        dl = lambda k: v("DL", 32 * k, 32 * k + 32)
+        mm(wrap(v("q3", 0, 64), "R1", "FT", 0, 1024))
+        ts(v("RP", 32, 96), v("q3", 0, 64), 0.5, A.is_gt)
+        ts(much, n_, 3.5, A.is_gt)
+        mm([(v("q5", 0, 64), v("BO"), v("RP", 32, 96)), (v("q5", 0, 64), v("NBO"), v("RP", 0, 64))])
+        mm([(v("q5", 64, 128), v("BO"), v("SC")), (v("q5", 64, 128), v("LPB"), v("RP", 32, 96)), (v("q5", 64, 128), v("NLP"), v("RP", 0, 64))])
+        tt(dl(0), n_, v("HF", 0, 32), A.is_ge)
+        tt(dl(2), n_, v("HI", 160, 192), A.add)
+        scan(v("LW", 0, 64), v("RM"), v("q5", 0, 64), A.mult)
+        tt(v("LW", 64, 128), v("q5", 64, 128), v("LW", 0, 64), A.add)
+        tt(v("LW", 128, 160), v("LW", 64, 96), v("LW", 96, 128), A.min)
+        tt(v("LW", 160, 192), v("LW", 128, 160), v("JD"), A.min)
+        cp(v("PFu"), v("LW", 160, 192))
+        tt(dl(1), v("HF", 32, 64), dl(0), A.subtract)
+        tt(dl(3), dl(1), much, A.mult)
+        tt(dl(4), dl(2), much, A.mult)
+        sca(v("P1W"), v("PFu"), v("PAY"))
+        mms([(v("q4"), v("X2D"), v("TBL", 0, 512))],
+            [(v("q4", i, 512, 16), v(U, 128 * i, 128 * i + 128), d) for U, d in (("UG", some), ("UH", dl(3)), ("UL", dl(4))) for i in range(16)])
+        act(v("TBn"), v("q4"))
+        if t < 2:
+            mm([(v("q2", 0, 32), v("ON"), some), (v("q2", 0, 32), v("ONS"), v("EX"))])
+            act(v("BS"), v("q2", 0, 32), scale=-1.0, accum_out=v("thB", 2, 3))
+            ts(v("CN", 0, 1), v("thB", 2, 3), 4096.0, A.add)
+            bits(v("CN", 1, 2), v("CN", 0, 1), 0, 255)
+            tt(v("thB", 1, 2), v("thB", 0, 1), v("CN", 1, 2), A.add)
+        bias[0] = 2.0
+        ts(v("AI", 0, 64), v("P1W", 512, 576), 8388608.0, A.subtract, 0.0, A.max)
+        bits(v("AI", 64, 128), v("AI", 0, 64), 0, 4095)
+        cp(v("AH", 0, 64), v("AI", 64, 128))
+        bias[0] = 0.0
+        to = v("q5", 128, 132)
+        mm(wrap(to, "R1", "AH", 0, 64))
+        mm([(v("q3", 64, 128), v("B128"), v("AH", 0, 64)), (v("q3", 64, 128), v("BQ0"), v("C10", 0, 64))])
+        bits(v("AI", 128, 192), v("AI", 0, 64), 17, 31)
+        bits(v("AI", 192, 256), v("AI", 0, 64), 12, 31)
+        cp(v("AH", 64, 192), v("AI", 128, 256))
         sca(v("TB"), v("Lu"), v("TBn"))
-        sca(v("TB"), v("AU", 4, 8), ab(512, 576))
-        if not last:
-            dma("Y", v("FL%d" % (t + 1)), v("TB", 0, 2048, 1, slice(2, 128, 16)))
-            send(7 + t, rank - 2 - t, v("FI%d" % (t + 1)), v("FL%d" % (t + 1)))
-            arrive(7 + t, v("FI%d" % (t + 1)), 7 + t, 4.0)
-            ts(v("EX", 0, 32), v("EX", 0, 32), 0.5, A.is_lt)
-            tt(v("EX", 0, 32), v("EX", 0, 32), lw(2), A.mult)
-            red(v("thB", 2, 3), v("EX", 0, 32))
-            cp(ab(576, 577), v("thB", 2, 3))
-
-    def bsum(t):
-        mms([(v("q3", 500, 501), v("ON"), v("AB", 576, 577))])
-        cp(v("CN", 0, 1), v("q3", 500, 501))
-        ts(v("CN", 1, 2), v("CN", 0, 1), 255, A.bitwise_and)
-        tt(v("thB", 1, 2), v("thB", 0, 1), v("CN", 1, 2), A.add)
+        ts(v("AF", 256, 260), to, -128.0, A.mult, 0.5, A.add)
+        cp(v("AU", 0, 4), to)
+        for c in range(4):
+            act(v("AF", 64 * c, 64 * c + 64), v("q3", 64, 128), F.Abs, bias=v("AF", 256 + c, 257 + c))
+            least(v("AF", 260 + c, 261 + c), v("AF", 64 * c, 64 * c + 64))
+        tt(v("AF", 264, 268), v("AF", 260, 264), v("S4"), A.is_lt)
+        tt(v("AF", 268, 272), v("AF", 264, 268), v("W4"), A.mult)
+        tt(v("AF", 272, 276), to, v("AF", 268, 272), A.max)
+        cp(v("AU", 4, 8), v("AF", 272, 276))
+        sgat(v("AB", 0, 64), v("TB"), v("AU", 0, 4))
+        mm([(v("q4", 0, 64), v("D0"), v("AH", 64, 128)), (v("q4", 0, 64), v("D1"), v("AH", 128, 192)), (v("q4", 0, 64), v("K34"), v("AB", 0, 64))])
+        act(v("AB", 64, 128), v("q4", 0, 64), F.Identity, bias=col["b2"])
+        sca(v("TB"), v("AU", 4, 8), v("AB", 64, 128))
+        if t < 2:
+            dma("Y", v("FL%d" % (t + 1)), row("TB", 2))
+            send(5 + t, served(2 + t), v("FI%d" % (t + 1)), v("FL%d" % (t + 1)))
+            arrive(5 + t, v("FI%d" % (t + 1)), 5 + t, 4.0)
 
     def repairs(t):
         bi = lambda k: v("BI", 128 * k, 128 * k + 128)
         bf = lambda lo, hi: v("BF2", lo, hi)
-        sm = lambda k: v("BI", 1024 + 8 * k, 1032 + 8 * k)
-        xe, c16 = "XE%d" % t, 896 * t % 2048
-        mms([(v("q5", 0, 8), win("R0f", i), v("P2W", i, 128, 16)) for i in range(16)])
+        sm = lambda k: v("SM", 8 * k, 8 * k + 8)
+        dw = "DW%d" % t
+        cp(bi(0), v("P1W", 0, 128))
+        bits(bi(1), bi(0), 22, 1)
+        bits(bi(2), bi(0), 11, 1)
+        cp(v("FB"), v("BI", 128, 384))
+        mm(wrap(v("q6", 0, 8), "RL", "FB", 0, 128))
+        cp(v("BU", 0, 8), v("q6", 0, 8))
+        sgat(v("TBS"), v("TBL"), v("BU", 0, 8))
+        mm([(v("q6", 128, 256), v("CWM"), v("TBS"))])
+        mm(wrap(v("q7", 264, 272), "RO", "TBS", 0, 128))
+        cp(bi(3), v("q6", 128, 256))
+        bits(bi(4), bi(3), 0, 2047)
+        cp(v("BU", 128, 256), bi(4))
+        cp(v("BU", 8, 16), v("q7", 264, 272))
+        sgat(v("LX"), v("X"), v("BU", 8, 16))
+        for k, R in enumerate(("RO", "RB", "RS")):
+            mm(wrap(v("q6", 8 + 8 * k, 16 + 8 * k), R, "TBS", 0, 128))
         for h in (0, 1):
-            sgat(v("mm0", 1024 * h, 1024 * h + 1024), v(xe), v("BU", 128 + 64 * h, 192 + 64 * h))
-            for b in (2 * h, 2 * h + 1):
-                q, lo, hi = "q%d" % (b & 1), 512 * b, 512 * b + 512
-                mms([(v(q), v("NI"), v("sg0", lo, hi)), (v(q), v("ID"), v("mm0", lo, hi))])
-                act(v("hg0", lo, hi), v(q), F.Abs)
-            mms([(v("q7", 64 * h, 64 * h + 64), win("R1", m), v("hg0", 1024 * h + m, 1024 * h + 1024, 16)) for m in range(16)])
-        cp(sm(0), v("q5", 0, 8))
-        cp(bi(4), v("P1W", 0, 128))
-        ts(sm(1), sm(0), 2047, A.bitwise_and)
-        ts(sm(2), sm(0), 12, A.arith_shift_right, 2047, A.bitwise_and)
-        ts(bi(5), bi(4), 1, A.bitwise_and)
-        ts(bi(6), bi(4), 2, A.arith_shift_right, 2047, A.bitwise_and)
-        tt(sm(3), sm(2), sm(2), A.mult)
-        ts(sm(4), sm(2), 2.0, A.mult, 1.0, A.add)
-        ts(sm(3), sm(3), 5, A.arith_shift_right)
-        tt(sm(3), sm(3), sm(2), A.add)
-        ts(bf(520, 528), sm(0), 8388608.0, A.is_ge)
-        ts(bf(0, 128), v("q7", 0, 128), 16.0, A.mult, kif, A.add)
-        op("V", lambda: g.vector.transpose(ap(bf(128, 256)), ap(bf(0, 128))), [bf(0, 128)], [bf(128, 256)])
-        lo, n, o = 128, 128, 256
+            pick(CAND[t][h])(v("mm0", 1024 * h, 1024 * h + 1024), v("XE%d" % t), v("BU", 128 + 64 * h, 192 + 64 * h))
+        for h in (0, 1):
+            for b in (0, 1):
+                qb, lo = "q%d" % b, 1024 * h + 512 * b
+                lst = []
+                for m in range(8):
+                    o = v(qb, 64 * m, 64 * m + 64)
+                    lst += [(o, v("NI"), v("LX", 64 * h, 64 * h + 64)), (o, v("ID"), v("mm0", 1024 * h + 8 * b + m, 1024 * h + 1024, 16))]
+                mm(lst, each=2)
+                act(v("hg0", lo, lo + 512), v(qb), F.Abs)
+            o = v("q7", 64 * h, 64 * h + 64)
+            mms([(o, v("MK12"), v("TBS", 64 * h, 64 * h + 64))] + [(o, win("R16", m), v("hg0", 1024 * h + 64 * m, 1024 * h + 64 * m + 64)) for m in range(8)],
+                [(o, win("R16", m), v("hg0", 1024 * h + 64 * m, 1024 * h + 64 * m + 64)) for m in range(8, 16)])
+        sgat(v("OLD"), v("WD"), v("BU", 8, 16))
+        turn(bf(0, 128), v("q7", 0, 128))
+        lo, n, o = 0, 128, 128
         while n > 8:
             tt(bf(o, o + n // 2), v("BF2", lo, lo + n, 2), v("BF2", lo + 1, lo + n, 2), A.min)
             lo, n, o = o, n // 2, o + n // 2
-        for s1 in (0, 1):
-            mms([(v("q7", 256 + s1, 264, 2), v("SW", 256 * s1 + 128 * g2, 256 * s1 + 128 * g2 + 128), v("BF2", lo + g2, lo + 8, 2)) for g2 in (0, 1)])
-        cp(sm(6), v("q7", 256, 264))
-        ts(bf(528, 536), v("q7", 256, 264), 65400.0, A.is_gt)
-        ts(sm(7), sm(6), 15, A.bitwise_and)
-        tt(bf(528, 536), bf(528, 536), bf(520, 528), A.max)
-        tt(sm(7), sm(7), sm(4), A.mult)
-        tt(bf(528, 536), bf(528, 536), v("W8", 0, 8), A.mult)
-        tt(sm(7), sm(7), sm(3), A.add)
-        dw = "DW%d" % t
-        tt(v(dw, 128, 136), bf(528, 536), sm(1), A.max)
-        ts(sm(7), sm(7), 2047, A.bitwise_and)
-        cp(v("BU", 264, 272), v(dw, 128, 136))
-        cp(v("BU", 256, 264), sm(7))
-        gat(bf(384, 512), v("WE%d" % t), v("BU", 256, 264))
-        tt(bf(384, 512), bf(384, 512), bi(6), A.subtract)
-        tt(bf(384, 512), bf(384, 512), bi(5), A.mult)
-        tt(v(dw, 0, 128), bf(384, 512), bi(6), A.add)
-        sca(v("WD"), v("BU", 264, 272), v(dw, 0, 128))
+        mm([(v("q7", 256 + s1, 264, 2), v("SW", 256 * s1 + 128 * g2, 256 * s1 + 128 * g2 + 128), v("BF2", lo + g2, lo + 8, 2))
+            for s1 in (0, 1) for g2 in (0, 1)], each=2)
+        cp(sm(0), v("q7", 256, 264))
+        bits(sm(1), sm(0), 0, 15)
+        tt(sm(2), v("q6", 24, 32), sm(1), A.mult)
+        tt(sm(3), v("q6", 16, 24), sm(2), A.add)
+        bits(sm(4), sm(3), 0, 2047)
+        cp(v("BU", 24, 32), sm(4))
+        gtt(bf(256, 384), v("WE"), v("BU", 24, 32), v("OLD"), A.subtract)
+        ts(bf(248, 256), sm(0), 65400.0, A.is_gt)
+        tt(bf(248, 256), bf(248, 256), v("W8"), A.mult)
+        tt(v(dw, 128, 136), v("q6", 8, 16), bf(248, 256), A.max)
+        cp(v("BU", 16, 24), v(dw, 128, 136))
+        tt(bf(384, 512), bf(256, 384), v("FB", 128, 256), A.mult)
         if t == 2:
-            fin.append(dma("Y", None, v("WD", 0, 2048), o=T.ym[:]))
+            op("V", lambda: g.vector.tensor_tensor(ind(v("WD"), v("BU", 16, 24)), ap(bf(384, 512)), ap(v("OLD")), A.add),
+               [bf(384, 512), v("OLD"), v("BU", 16, 24)], [v("WD")], ew(128, 3.8))
+            fin.append(dma("Y", None, v("WD", 0, 2048), o=T.ym[:], lat=6.0))
             return
+        tt(v(dw, 0, 128), bf(384, 512), v("OLD"), A.add)
+        sca(v("WD"), v("BU", 16, 24), v(dw, 0, 128))
         for t2 in range(t + 1, 3):
-            slot = 9 + t + t2 - 1
-            send(slot, rank - 1 - t2, v("Di%d%d" % (t, t2)), v(dw))
+            slot = 6 + t + t2
+            send(slot, served(1 + t2), v("Di%d%d" % (t, t2)), v(dw))
             arrive(slot, v("Di%d%d" % (t, t2)), slot, 4.0)
 
     def helper(t):
-        dma("Y", v("XE%d" % t, 0, 2048, 1, slice(2, 128, 16)), v("FI%d" % t))
+        gcp(v("WE", 0, 2048), v("WH%d" % t))
+        hold.append(v("FT", CH[1], CH[2]))
+        dma("Y", row("XE%d" % t, 2), v("FI%d" % t))
         for s in range(t):
             b = "Di%d%d" % (s, t)
-            cp(v("BU", 272, 280), v(b, 128, 136))
-            sca(v("WE%d" % t), v("BU", 272, 280), v(b, 0, 128))
+            cp(v("HU"), v(b, 128, 136))
+            sca(v("WE"), v("HU"), v(b, 0, 128))
+        hold.pop()
 
     def flags_out():
-        mms([(v("q2", 0, 128), win("RH", b), v("TB", 128 * b, 128 * b + 128)) for b in range(16)])
-        mms([(v("q2", 128, 256), win("RD2", b), v("TB", 128 * b, 128 * b + 128)) for b in range(16)])
-        cp(v("CUM"), v("q2", 0, 128))
-        ts(v("POS"), v("q2", 128, 256), 4096.0, A.is_lt)
-        fin.append(dma("Y", None, v("CUM"), o=T.yh[:]))
-        fin.append(dma("Y", None, v("POS"), o=T.yv[:]))
+        mm([(v("q3", 0, 128), win("RH", b), v("TB", 128 * b, 128 * b + 128)) for b in range(16)])
+        mm([(v("q5", 0, 128), win("RD2", b), v("TB", 128 * b, 128 * b + 128)) for b in range(16)])
+        act(v("OUT", 0, 128), v("q3", 0, 128))
+        ts(v("OUT", 128, 256), v("q5", 0, 128), 4096.0, A.is_lt)
+        fin.append(dma("Y", None, v("OUT", 0, 128), o=T.yh[:]))
+        fin.append(dma("Y", None, v("OUT", 128, 256), o=T.yv[:]))
 
     late_constants()
+    lanes(0)
+    fetch(0)
     for t in range(3):
-        lanes(t)
-        fetch(t)
+        slots_reset()
+        if t < 2:
+            gcp(v("CW", 0, 512), v("Z", 0, 512))
         check(t)
         helper(t)
         post(t)
-        if t == 2:
-            flags_out()
-        repairs(t)
         if t < 2:
-            bsum(t)
+            lanes(t + 1)
+            bias[0] = -LATE
+            repairs(t)
+            bias[0] = 0.0
+            fetch(t + 1)
+        else:
+            repairs(t)
+            flags_out()
     issue()
     for sem in fin:
         wait("Y", sem, 16, {})

@@ -1,11 +1,23 @@
+from concourse.bass import DstId, RemoteDMATransfer
 from concourse.mybir import AluOpType as A, AxisListType, ActivationFunctionType as F
 
 PATIENCE = 0.5
 CH = (0, 160, 320, 448, 512)
-TYP = ("SVSS", "SVSS", "SVSS")
+TYP = ("SSVS", "SSVS", "SSVS")
 CAND = ("SS", "SS", "SV")
 LATE = 2.0
 SMALL = 0.0
+LOADS = ("X", "RI32", "SG", "WI")
+TBLQ = "S"
+LAST = 3.0
+PASSES, WAKE, PE = 3, 0.18, 0.48e-3
+GATHER, SCATTER = 1.56, 3.8
+SPEEDS = ((0.9e-3, 1.25, 3.0), (0.9e-3, 1.5, 3.5), (1.0e-3, 2.0, 5.0))
+PLAN = SPEEDS + ((0.95e-3, 1.56, 3.8), (0.95e-3, 1.4, 3.0), (1.0e-3, 1.7, 4.0))
+ORDER, EST = [], []
+PACE, CUT = 1, 896
+FIRST = 160
+BANKS = ("q5", "q3", "q0", "q1")
 SCRATCH = {}
 SEMAPHORES = ["cV", "cS", "cP", "cG"]
 
@@ -24,40 +36,41 @@ def _buf(name, cols, dtype, where="sbuf", pool=None):
 
 
 for _n in ("BO", "NBO", "LT", "EQH", "GT", "ID", "NI", "LPA", "LPB", "NLP", "ZT", "X2D", "K34", "D0", "D1", "B128", "BQ0", "IDK", "ID24",
-           "IDF", "ON", "ONS", "CWM", "MK12", "C10", "C11", "C12"):
+           "IDF", "IDQ", "ON", "ONS", "CWM", "MK12", "C1"):
     _buf(_n, 128, BF, pool="PB")
-for _n in ("R1", "RD0", "RD2", "RI", "RC", "RH", "RX", "R2", "RN", "RU", "RL", "RO", "RB", "RS", "R16"):
+for _n in ("R1", "RD0", "RI", "RH", "RX", "R2", "RN", "RU", "RO", "R16"):
     _buf(_n, 144, BF, pool="PB")
-for _n, _c in (("RH3", 24), ("SWB", 512), ("SC", 64), ("KIB", 128)):
+for _n, _c in (("RH3", 32), ("UT", 128), ("SWB", 512), ("SC", 64), ("KIB", 128)):
     _buf(_n, _c, BF, pool="PB")
-for _n, _c in (("COLS", 128), ("QH", 16), ("CR", 144), ("MG", 128), ("MI", 128), ("SW", 512), ("JW", 32), ("JC", 32), ("JD", 32), ("J16", 32),
+for _n, _c in (("COLS", 128), ("QH", 16), ("CR", 144), ("MG", 128), ("MI", 128), ("JW", 32), ("JC", 32), ("JD", 32), ("J16", 32),
                ("W8", 8), ("W4", 4), ("S4", 4), ("RM", 64), ("DF", 192), ("ZF", 128), ("TMP", 128)):
     _buf(_n, _c, FP, pool="PF")
 for _n, _c, _d in (
         ("X", 2064, BF), ("WD", 2560, FP), ("WI", 2560, I32), ("W16", 2048, H16), ("RI32", 1032, I32), ("SG", 1040, BF), ("TB", 2688, BF),
         ("Z", 640, BF), ("ZU", 2048, BF), ("PW", 64, FP), ("UH", 2048, BF), ("UL", 2048, BF), ("UG", 2048, BF), ("JI", 512, FP), ("JB", 512, BF),
-        ("hyb", 128, I32), ("vfb", 128, I32), ("x2b", 128, BF), ("thi", 1, I32), ("KI", 4, I32), ("ST", 1024, BF), ("SI", 1280, I32),
-        ("NW", 128, BF), ("NT", 256, BF), ("CUM", 128, FP), ("POS", 128, FP), ("TTB", 384, BF), ("OF", 8, FP), ("OFu", 8, U16),
-        ("CW", 2176, BF), ("CC", 512, BF), ("CLu", 32, U16), ("OH", 512, BF), ("EX", 32, BF), ("Lf", 32, FP), ("Lu", 32, U16),
+        ("hyb", 128, I32), ("vfb", 128, I32), ("thi", 1, I32), ("KI", 4, I32), ("ST", 1024, BF), ("SI", 1280, I32),
+        ("NW", 128, BF), ("NT", 128, BF), ("VB", 256, H16), ("HW", 128, FP), ("TY", 512, H16), ("POS", 128, FP), ("TTB", 384, BF), ("OFu", 8, U16),
+        ("CW", 4224, BF), ("CC", 512, BF), ("CLu", 32, U16), ("OH", 512, BF), ("EX", 32, BF), ("Lf", 32, FP), ("Lu", 32, U16),
         ("TBL", 528, BF), ("Wu", 512, U16), ("Wf", 512, H16), ("Ku", 512, U16), ("KF", 512, H16), ("PM", 512, BF), ("STu", 32, U16),
-        ("HI", 256, I32), ("HF", 64, FP), ("FT", 1024, BF), ("FO", 512, BF), ("RD", 256, I32), ("GA", 256, BF), ("PAY", 512, FP),
+        ("HI", 256, I32), ("HF", 64, FP), ("HY", 64, FP), ("TS", 2688, BF), ("FT", 1024, BF), ("FO", 512, BF), ("RD", 256, I32), ("GA", 256, BF), ("PAY", 512, FP),
         ("sig", 8192, BF), ("mm0", 2560, BF), ("mm1", 2560, BF), ("hg0", 2560, BF), ("hg1", 2560, BF),
         ("RP", 96, BF), ("LW", 192, FP), ("PFu", 32, U16), ("DL", 160, BF), ("P1W", 1536, FP), ("TBn", 512, BF),
         ("thB", 4, FP), ("CN", 4, I32), ("BS", 32, FP),
-        ("AI", 256, I32), ("AH", 192, H16), ("AF", 288, FP), ("AB", 128, BF), ("AU", 8, U16),
-        ("BI", 640, I32), ("FB", 256, BF), ("TBS", 128, BF), ("LX", 128, BF), ("OLD", 128, FP), ("BF2", 512, FP), ("SM", 64, I32),
+        ("AI", 256, I32), ("AH", 320, H16), ("T3", 384, BF), ("WB", 24, FP), ("MB", 16, BF), ("Li", 64, I32), ("AF", 352, FP), ("AB", 128, BF), ("AU", 8, U16),
+        ("BI", 640, I32), ("FB", 128, BF), ("TBS", 128, BF), ("LX", 128, BF), ("OLD", 128, FP), ("BF2", 512, FP), ("SM", 64, I32),
         ("BU", 256, U16), ("HU", 8, U16), ("WE", 2176, FP), ("OUT", 256, FP),
-        ("FL0", 128, BF), ("FL1", 128, BF), ("FL2", 128, BF), ("DW0", 136, FP), ("DW1", 136, FP), ("DW2", 136, FP)):
+        ("DW0", 136, FP), ("DW1", 136, FP), ("DW2", 136, FP)):
     _buf(_n, _c, _d)
 for _t in range(3):
     _buf("XE%d" % _t, 2048, BF)
     _buf("WH%d" % _t, 2048, H16)
-    _buf("FI%d" % _t, 128, BF)
+    _buf("FL%d" % _t, 128, BF, "dram")
+    _buf("FI%d" % _t, 128, BF, "dram")
 for _n in ("i01", "i02", "i12"):
     _buf("D" + _n, 136, FP)
 for _b in range(8):
     _buf("q%d" % _b, 512, FP, "psum")
-_NDMA, _NREM = 40, 17
+_NDMA, _NREM = 40, 22
 SEMAPHORES += ["d%d" % k for k in range(_NDMA)] + ["l%d" % k for k in range(_NREM)] + ["r%d" % k for k in range(_NREM)]
 
 
@@ -72,13 +85,18 @@ def lanes_of(src, dst, T, topo):
     return sum(1 << k for k in e), len(e)
 
 
+def piece(k, h):
+    cut = 1024 if k < 2 else CUT
+    return (cut, 2048) if h else (0, cut)
+
+
 def relay_program(g, core, T, topo):
     own = [c for c in T.cores if topo.chip(c) == topo.chip(core)]
     if not own or core not in relays_of(own[0], T, topo):
         return
     rank, sent = T.rank_of(own[0]), []
     far, near = relays_of(own[0], T, topo)
-    n_on = lanes_of(own[0], core, T, topo)[1]
+    n_on = len(topo.engines(own[0], core)) // 2
 
     def send(slot, dst, name, src, lo=0, hi=2048):
         mask, n = lanes_of(core, dst, T, topo)
@@ -90,20 +108,14 @@ def relay_program(g, core, T, topo):
     def served(d):
         return T.cores[(rank - d) % len(T.cores)]
 
-    if core == far:
-        g.wait_ge(T.sem.r3, n_on)
-        n = send(10, served(1), "WH0", "W16", 1024, 2048)
-        g.wait_ge(T.sem.r12, n_on)
-        send(13, served(2), "XE1", "X")
-        send(14, served(2), "WH1", "W16")
-        g.wait_ge(T.sem.l10, n)
-        send(11, near, "W16", "W16")
-    else:
-        g.wait_ge(T.sem.r2, n_on)
-        send(12, far, "X", "X")
-        g.wait_ge(T.sem.r11, n_on)
-        send(15, served(3), "XE2", "X")
-        send(16, served(3), "WH2", "W16")
+    h = 1 if core == far else 0
+    for k in range(6):
+        t, name, src = k // 2, ("XE%d", "WH%d")[k & 1] % (k // 2), ("X", "W16")[k & 1]
+        if k < 2:
+            g.wait_ge(T.sem["r%d" % (1 + 2 * k + h)], n_on)
+        elif core == near and k >= PACE:
+            g.wait_ge(T.sem["l%d" % (10 + 2 * (k - PACE) + h)], n)
+        n = send(10 + 2 * k + h, served(1 + t), name, src, *piece(k, h))
     for slot, n in sent:
         g.wait_ge(T.sem["l%d" % slot], n)
 
@@ -115,6 +127,7 @@ def rank_program(g, core, T, topo):
         return
     N = len(T.cores)
     GQ = ("gq", 0, 1, 1, None)
+    LQ = ("lq", 0, 1, 1, None)
     eng = {"V": g.vector, "S": g.scalar, "P": g.tensor, "G": g, "Y": g.sync}
     cnt = {"cV": 0, "cS": 0, "cP": 0, "cG": 0}
     known = {e: {} for e in eng}
@@ -199,7 +212,7 @@ def rank_program(g, core, T, topo):
             clock = dict(known["P"])
             clock["cP"] = val
             note("P", [x[1] for x in lst] + [x[2] for x in lst], [x[0] for x in lst], "cP", val, clock)
-        call("P", emit, [x[1] for x in lst] + [x[2] for x in lst], [x[0] for x in lst], cyc * 0.6e-3)
+        call("P", emit, [x[1] for x in lst] + [x[2] for x in lst], [x[0] for x in lst], cyc * PE)
 
     def mms(*parts):
         for n, lst in enumerate(parts):
@@ -216,10 +229,22 @@ def rank_program(g, core, T, topo):
             clock = dict(known[e])
             clock[sem] = 16
             note("D" + sem, rd, wr, sem, 16, clock)
-        call(e, emit, rd, wr, 0.06, lat or 2.3)
+        call(e, emit, rd, wr + ([] if i is None else [LQ]), 0.06, lat or 2.3)
         return sem
 
-    def send(slot, dst, out, in_):
+    def gadd(out, in_):
+        sem = "d%d" % nd[0]
+        nd[0] += 1
+
+        def emit():
+            deps("G", [in_], [out])
+            g.dma_start(ap(out), ap(in_), accum_op=A.add).then_inc(T.sem[sem], 16)
+            clock = dict(known["G"])
+            clock[sem] = 16
+            note("D" + sem, [in_], [out], sem, 16, clock)
+        call("G", emit, [in_], [out, GQ], 1.0, 2.3)
+
+    def send(slot, dst, out, in_, cost=1.2):
         mask, n = lanes_of(core, dst, T, topo)
         sent.append(("l%d" % slot, n))
 
@@ -228,7 +253,24 @@ def rank_program(g, core, T, topo):
             rid, pid, _ = topo.addr(dst)
             g.remote_dma(ap(out), ap(in_), T.sem["r%d" % slot], T.sem["l%d" % slot], pid, rid, mask)
             note("Dl%d" % slot, [in_], [], "l%d" % slot, n, {"l%d" % slot: n})
-        call("G", emit, [in_], [(slot, 0, 1, 1, None), GQ], 1.2, 0.0)
+        call("G", emit, [in_], [(slot, 0, 1, 1, None), GQ], cost, 0.0)
+
+    def hand_on(slot, name, cost=1.2):
+        wide = 2048 - CUT
+        far, near = relays_of(core, T, topo)
+        e = topo.engines(core, near)
+        sent.append(("l%d" % slot, len(e)))
+
+        def emit():
+            deps("G", [v(name, 0, 2048)], [])
+            tr = []
+            for h, (dst, lo) in enumerate(((near, 0), (far, CUT))):
+                rid, pid, _ = topo.addr(dst)
+                tr.append(RemoteDMATransfer(dst_ids=[DstId(rid=rid, pnc=pid)], dma_engine_mask=sum(1 << k for k in e[h * len(e) // 2:(h + 1) * len(e) // 2]),
+                                            remote_sem=T.sem["r%d" % (slot + h)], src=ap(v(name, lo, lo + wide)), dst=ap(v(name, lo, lo + wide))))
+            g.remote_dma_fused(tr, local_sem=T.sem["l%d" % slot])
+            note("Dl%d" % slot, [v(name, 0, 2048)], [], "l%d" % slot, len(e), {"l%d" % slot: len(e)})
+        call("G", emit, [v(name, 0, 2048)], [(slot, 0, 1, 1, None), GQ], cost, 0.0)
 
     def served(d):
         return T.cores[(rank - d) % N]
@@ -252,7 +294,7 @@ def rank_program(g, core, T, topo):
                         else:
                             hit = (wr or a[4]) and a[1] < x[2] and x[1] < a[2] and (a[3] is None or x[4] is None or a[3] == x[4])
                         if hit:
-                            ps[a[0]] = max(ps.get(a[0], 0.0), 0.0 if x == GQ else prog[a[0]]["lat"] + 0.1)
+                            ps[a[0]] = max(ps.get(a[0], 0.0), 0.0 if x in (GQ, LQ) else prog[a[0]]["lat"] + WAKE)
             for lst, wr in ((c["r"], False), (c["w"], True)):
                 for x in lst:
                     h = hist[x[0]]
@@ -266,41 +308,85 @@ def rank_program(g, core, T, topo):
                         h.append(e)
             pred.append(ps)
         n = len(prog)
-        rank_, succ = [0.0] * n, [[] for _ in range(n)]
+        rank_, cost, succ = [0.0] * n, [0.0] * n, [[] for _ in range(n)]
         for k in range(n):
             for p in pred[k]:
                 succ[p].append(k)
-        for k in range(n - 1, -1, -1):
-            rank_[k] = prog[k]["cost"] + max([rank_[s] + pred[s][k] for s in succ[k]] or [prog[k]["lat"]])
-        rank_ = [r + c["bias"] for r, c in zip(rank_, prog)]
-        left = [len(p) for p in pred]
-        at, free, done = [0.0] * n, {}, [0.0] * n
-        ready = {k for k in range(n) if left[k] == 0}
-        while ready:
-            best = None
-            for k in ready:
+
+        def assume(speed):
+            cyc, ga, sc = speed
+            for k in range(n - 1, -1, -1):
+                c = prog[k]["cost"]
+                if isinstance(c, tuple):
+                    c = 0.05 + c[0] * cyc * (ga if c[1] == GATHER else sc) if c[1] in (GATHER, SCATTER) else 0.03 + max(64, c[0] * c[1]) * cyc
+                cost[k] = c
+                rank_[k] = c + max([rank_[s] + pred[s][k] for s in succ[k]] or [prog[k]["lat"]])
+            for k in range(n):
+                rank_[k] += prog[k]["bias"]
+
+        def length(order):
+            free, done = {}, [0.0] * n
+            for k in order:
                 e = prog[k]["e"]
-                t0 = at[k] if e == "R" else max(at[k], free.get(e, 0.0))
-                key = (t0, -rank_[k], k)
-                if best is None or key < best:
-                    best = key
-            t0, _, k = best
-            e, late = prog[k]["e"], t0 + PATIENCE * prog[k]["cost"]
-            if e in ("V", "S", "P", "G"):
-                for j in ready:
-                    if prog[j]["e"] == e and at[j] < late and (rank_[j], -j) > (rank_[k], -k):
-                        k = j
-                t0 = max(at[k], free.get(e, 0.0))
-            ready.remove(k)
-            c = prog[k]
-            c["emit"]()
-            done[k] = t0 + c["cost"]
-            free[c["e"]] = done[k]
-            for s in succ[k]:
-                at[s] = max(at[s], done[k] + pred[s][k])
-                left[s] -= 1
-                if left[s] == 0:
-                    ready.add(s)
+                t0 = max([done[p] + x for p, x in pred[k].items()] + [0.0 if e == "R" else free.get(e, 0.0)])
+                done[k] = free[e] = t0 + cost[k]
+            return max(done[k] + prog[k]["lat"] for k in range(n))
+
+        def place(order, before, lag, head):
+            start, busy = [0.0] * n, {}
+            for k in order:
+                t0 = max([start[p] + cost[p] + lag(p, k) for p in before[k]] or [head[k]])
+                if prog[k]["e"] != "R":
+                    iv = busy.setdefault(prog[k]["e"], [])
+                    j = len(iv)
+                    while j > 0 and iv[j - 1][1] > t0:
+                        j -= 1
+                    while j < len(iv) and iv[j][0] < t0 + cost[k] - 1e-9:
+                        t0 = max(t0, iv[j][1])
+                        j += 1
+                    iv.insert(j, (t0, t0 + cost[k]))
+                start[k] = t0
+            return start
+
+        def greedy():
+            left = [len(p) for p in pred]
+            at, free, start = [0.0] * n, {}, [0.0] * n
+            ready = {k for k in range(n) if left[k] == 0}
+            while ready:
+                t0, _, k = min((at[k] if prog[k]["e"] == "R" else max(at[k], free.get(prog[k]["e"], 0.0)), -rank_[k], k) for k in ready)
+                e, late = prog[k]["e"], t0 + PATIENCE * cost[k]
+                if e in ("V", "S", "P", "G"):
+                    for j in ready:
+                        if prog[j]["e"] == e and at[j] < late and (rank_[j], -j) > (rank_[k], -k):
+                            k = j
+                    t0 = max(at[k], free.get(e, 0.0))
+                ready.remove(k)
+                start[k] = t0
+                free[e] = t0 + cost[k]
+                for s in succ[k]:
+                    at[s] = max(at[s], t0 + cost[k] + pred[s][k])
+                    left[s] -= 1
+                    if left[s] == 0:
+                        ready.add(s)
+            return start
+
+        if not ORDER:
+            orders = []
+            for speed in PLAN:
+                assume(speed)
+                fore = greedy()
+                for _ in range(PASSES + 1):
+                    orders.append(sorted(range(n), key=lambda k: (fore[k], k)))
+                    back = place(sorted(range(n), key=lambda k: (-fore[k] - cost[k], -k)), succ, lambda p, k: pred[p][k], [c["lat"] for c in prog])
+                    fore = place(sorted(range(n), key=lambda k: (-back[k] - cost[k], k)), pred, lambda p, k: pred[k][p], [0.0] * n)
+            total = [1.0] * len(orders)
+            for speed in SPEEDS:
+                assume(speed)
+                total = [x * length(o) for x, o in zip(total, orders)]
+            ORDER[:] = orders[total.index(min(total))]
+            EST.append((total.index(min(total)), min(total) ** (1 / len(SPEEDS))))
+        for k in ORDER:
+            prog[k]["emit"]()
 
     def wid(x):
         return (x[2] - x[1] + x[3] - 1) // x[3]
@@ -309,7 +395,7 @@ def rank_program(g, core, T, topo):
         return 0.5 if all(SCRATCH[x[0]][2] in (BF, U16, H16) for x in xs) else 1.0
 
     def ew(w, f=1.0):
-        return 0.04 + max(64, w * f) * 0.95e-3
+        return (w, f)
 
     def ind(win, off):
         return ap(win).indirect(ap(off))
@@ -395,18 +481,23 @@ def rank_program(g, core, T, topo):
     def row(name, q):
         return v(name, 0, 2048, 1, slice(q, 128, 16))
 
-    bias[0] = 50.0
+    bias[0] = 500.0
     dma("Y", v("vfb"), None, i=T.vf[:])
     dma("S", v("hyb"), None, i=T.hy[:])
-    dma("Y", v("x2b"), None, i=T.xs[2:128:16, :])
-    bias[0] = 40.0
-    dma("S", v("X", 0, 2048), None, i=T.xs[:], lat=4.0)
-    dma("Y", v("WI", 0, 2048), None, i=T.wd[:], lat=9.5)
-    bias[0] = 30.0
-    dma("S", v("RI32", 0, 1024), None, i=T.rq[:], lat=9.5)
-    dma("Y", v("SG", 0, 1024), None, i=T.sg[:], lat=10.5)
-    dma("S", v("thi"), None, i=T.th[:], lat=11.0)
+    at = 3.0
+    for k, name in enumerate(LOADS):
+        src, n, us = {"X": (T.xs, 2048, 1.8), "WI": (T.wd, 2048, 3.6), "RI32": (T.rq, 1024, 1.8), "SG": (T.sg, 1024, 0.9)}[name]
+        at += us
+        bias[0] = 400.0 - 50 * k
+        dma("SY"[k & 1], v(name, 0, n), None, i=src[:], lat=at)
+    bias[0] = 10.0
+    dma("Y", v("FL0"), None, i=T.xs[2:128:16, :], lat=at)
+    dma("S", v("thi"), None, i=T.th[:], lat=at)
     bias[0] = 0.0
+    hold.append(v("WI", 0, 2048))
+    for t in (1, 2):
+        dma("Y", v("FL%d" % t), None, i=T.xs[2:128:16, :])
+    hold.pop()
 
     iota(v("KI", 0, 1), [[1, 1]], 0, 1)
     iota(v("CR"), [[1, 144]], 0)
@@ -451,7 +542,7 @@ def rank_program(g, core, T, topo):
     cp(odd, v("KI", 3, 4))
     ts(v("QH"), v("CR", 0, 16), ki, A.is_equal)
     for name, src, a, b in (("even2", odd, -1.0, 1.0), ("g15", kg, 16.0, 15.0), ("g16", kg, 16.0, 0.0), ("g17", kg, 16.0, 1.0), ("km", kf, 1.0, -16.0),
-                            ("kp", kf, 1.0, 16.0), ("k5", kf, 1.0, -5.0), ("uw", ki, 10.0, 1.0), ("n2", q(2), -1.0, 1.0)):
+                            ("kp", kf, 1.0, 16.0), ("uw", ki, 10.0, 1.0), ("n2", q(2), -1.0, 1.0), ("c40", ki, 0.0, 40.0)):
         act(newcol(name), src, F.Identity, bias=b, scale=a)
     even = col["even2"]
     ts(v("R1", 0, 143), v("CR", 0, 143), col["g15"], A.is_equal)
@@ -465,25 +556,25 @@ def rank_program(g, core, T, topo):
     tt(v("LPA"), v("LPA"), v("GT"), A.subtract)
     ts(v("RH3", 0, 8), v("CR", 0, 8), kg, A.is_gt)
     ts(v("RH3", 8, 16), v("CR", 0, 8), kg, A.is_equal)
-    ts(v("RH3", 16, 24), v("CR", 0, 8), kg, A.is_equal, 4096.0, A.mult)
+    act(v("RH3", 16, 24), v("RH3", 8, 16), scale=2048.0)
+    act(v("RH3", 24, 32), v("RH3", 8, 16), scale=kf)
+    ts(v("UT"), v("CR", 0, 128), kf, A.is_ge)
     for k, (c_, m_) in enumerate(((kf, even), (col["kp"], even), (col["km"], odd), (kf, odd))):
         ts(v("SWB", 128 * k, 128 * k + 128), v("CR", 0, 128), c_, A.is_equal, m_, A.mult)
     act(v("JW"), v("J16"), F.Identity, bias=ki)
-    for name, n, a, b in (("JC", 32, 1.0, 2048.0), ("W8", 8, 1.0, 2048.0), ("JD", 32, 1.0, 1024.0), ("W4", 4, 2.0, 2560.0), ("S4", 4, 1.0, 0.25)):
+    for name, n, a, b in (("JC", 32, 1.0, 2048.0), ("W8", 8, 1.0, 2048.0), ("JD", 32, 1.0, 1024.0), ("W4", 4, 2.0, 2560.0), ("S4", 4, 4096.0, 1024.0)):
         act(v(name), v("JW", 0, n), F.Identity, bias=b, scale=a)
-    for t in range(3):
-        c0 = 896 * t % 2048 // 16
-        act(v("C1%d" % t), v("CR", 0, 128), F.Relu, bias=weights("c1", {1: c0 - 127, 2: c0, 3: c0 - 128} if t else {1: -127, 3: -128}),
-            scale=col["n2"])
+    act(v("C1"), v("CR", 0, 128))
     ts(v("PW", 0, 16), v("ZF", 0, 16), 2.0, A.add)
     scan(v("PW", 16, 32), v("PW", 0, 16), v("ZF", 0, 16), A.mult, 0.5)
     tt(v("PW", 32, 48), v("PW", 16, 32), v("QH"), A.mult)
     op("V", lambda: g.vector.tensor_reduce(ap(v("PW", 48, 49)), ap(v("PW", 32, 48)), AxisListType.X, A.add), [v("PW", 32, 48)], [v("PW", 48, 49)])
-    for name, c in (("RD0", q(0)), ("RI", ki), ("RC", weights("rc", {0: 16, 1: -2048, 2: 16, 3: 2048})), ("RH", weights("h", {0: 32, 1: 1})),
-                    ("RU", col["uw"]), ("RX", weights("sx", {0: 1 / 64, 1: 1 / 2048, 3: -64, 4: -1})), ("R2", 2.0), ("RN", -1.0), ("RD2", q(2)),
-                    ("R16", 16.0), ("RO", weights("ro", {10: 128, 11: 1})), ("RB", weights("rb", {8: 32, 9: 1})),
-                    ("RS", weights("rs", {5: 64, 6: 2, 12: 1})), ("RL", v("PW", 48, 49))):
+    for name, c in (("RD0", q(0)), ("RI", ki), ("RH", weights("h", {0: 32, 1: 1, 2: 0.25})),
+                    ("RU", col["uw"]), ("RX", weights("sx", {0: 1 / 64, 1: 1 / 2048, 3: -64, 4: -1})), ("R2", 2.0), ("RN", -1.0),
+                    ("R16", 16.0), ("RO", weights("ro", {10: 128, 11: 1}))):
         act(v(name, 0, 143), v("R1", 0, 143), scale=c)
+    weights("rb", {8: 32, 9: 1})
+    weights("rs", {5: 64, 6: 2, 12: 1})
     act(v("ON"), v("Z", 0, 128), F.Identity, bias=1.0)
     dma("Y", row("TB", 12), v("ON"))
     ts(v("TB", 2048, 2688), v("Z", 0, 640), weights("tb", {0: 32}), A.add)
@@ -492,20 +583,19 @@ def rank_program(g, core, T, topo):
     ms(v("X", 2048, 2064), 16384.0)
     ms(v("RI32", 1024, 1032), 1024)
     ms(v("SG", 1024, 1040), 0.0)
-    ts(v("NT", 0, 128), v("vfb"), 0.5, A.is_lt)
+    ts(v("TMP"), v("vfb"), -2048.0, A.mult)
+    tt(v("VB", 0, 128), v("TMP"), v("hyb"), A.add)
+    act(v("IDQ"), v("ID"), scale=0.25)
     ts(v("SI", 0, 128), v("hyb"), 5, A.arith_shift_right)
     bits(v("SI", 128, 256), v("hyb"), 0, 31)
     cp(v("ST", 0, 256), v("SI", 0, 256))
     dma("Y", row("TB", 0), v("ST", 0, 128))
     dma("Y", row("TB", 1), v("ST", 128, 256))
-    act(v("TMP"), v("NT", 0, 128), scale=8192.0)
-    tt(v("FL0"), v("TMP"), v("x2b"), A.add)
-    dma("Y", row("TB", 2), v("FL0"))
-    dma("Y", row("TB", 7), None, i=T.xs[2:128:16, :])
+    act(v("NT"), v("TMP"), F.Identity, bias=8192.0, scale=4.0)
+    dma("Y", row("TB", 2), v("NT"))
     act(v("KIB"), v("Z", 0, 128), F.Identity, bias=ki)
     dma("Y", row("TB", 10), v("KIB"))
-    act(v("BQ0"), v("CR", 0, 128))
-    dma("Y", row("TB", 11), v("BQ0"))
+    dma("Y", row("TB", 11), v("C1"))
     mm([(v("q6", 0, 128), win("R1", b), v("X", 128 * b, 128 * b + 128)) for b in range(16)])
     mm([(v("q6", 128, 256), win("RU", b), v("X", 128 * b, 128 * b + 128)) for b in range(16)])
     si = lambda k: v("SI", 128 * k, 128 * k + 128)
@@ -525,26 +615,26 @@ def rank_program(g, core, T, topo):
     cp(v("ST", 512, 1024), v("SI", 768, 1280))
     for k, r in enumerate((5, 6, 8, 9)):
         dma("Y", row("TB", r), v("ST", 512 + 128 * k, 640 + 128 * k))
+    dma("Y", v("TS"), v("TB"), lat=4.0)
     for k in range(4):
         cp(v("W16", 512 * k, 512 * k + 512), v("WI", 512 * k, 512 * k + 512))
-    far, near = relays_of(core, T, topo)
-    send(1, served(1), v("XE0"), v("X", 0, 2048))
-    send(2, near, v("X", 0, 2048), v("X", 0, 2048))
-    send(3, far, v("W16"), v("W16"))
-    send(4, served(1), v("WH0", 0, 1024), v("W16", 0, 1024))
-    send(0, served(1), v("FI0"), v("FL0"))
-    arrive(0, v("FI0"), 0, 4.0)
-    arrive(1, v("XE0"), 1, 18.0)
-    arrive(4, v("WH0", 0, 1024), 4, 20.0)
-    arrive(10, v("WH0", 1024, 2048), 3, 20.0)
-    arrive(13, v("XE1"), 3, 35.0)
-    arrive(14, v("WH1"), 3, 50.0)
-    arrive(15, v("XE2"), 3, 40.0)
-    arrive(16, v("WH2"), 3, 55.0)
+    hand_on(1, "X", 4.0)
     op("G", lambda: g.iota(ap(v("ZU")), [[0, 2048]], 0, 0, allow_small_or_imprecise_dtypes=True), [], [v("ZU"), GQ], 4.1)
-    for k, (n_, w_) in enumerate((("UH", 32.0), ("UL", 1.0), ("UG", 8192.0))):
-        op("G", lambda n_=n_, w_=w_, k=k: g.affine_select(ap(v(n_)), ap(v("ZU")), [[-1, 16], [-16, 8], [1000, 16]], A.not_equal, w_,
-                                                          -1000 * k, 1), [v("ZU")], [v(n_), GQ], 4.1)
+    hand_on(3, "W16")
+
+    def unwrap(k, name, w):
+        op("G", lambda: g.affine_select(ap(v(name)), ap(v("ZU")), [[-1, 16], [-16, 8], [1000, 16]], A.not_equal, w, -1000 * k, 1),
+           [v("ZU")], [v(name), GQ], 4.1)
+
+    unwrap(0, "UH", 32.0)
+    unwrap(1, "UL", 1.0)
+    gadd(v("FL0"), row("TB", 2))
+    unwrap(2, "UG", 8192.0)
+    send(0, served(1), v("FI0"), v("FL0"))
+    arrive(0, v("FI0"), 0, 10.0)
+    for k in range(6):
+        for h in (0, 1):
+            arrive(10 + 2 * k + h, v(("XE%d", "WH%d")[k & 1] % (k // 2), *piece(k, h)), 3, 12.0 + 12.0 * k)
     gcp(v("WD", 0, 2048), v("W16"))
     gcp(v("WD", 2048, 2560), v("Z", 0, 512))
     gcp(v("WE", 2048, 2176), v("Z", 0, 128))
@@ -553,7 +643,6 @@ def rank_program(g, core, T, topo):
         for n_, src, c in (("NI", "ID", -1.0), ("IDK", "ID", -8388608.0), ("ID24", "ID", 24.0), ("IDF", "ID", 2048.0), ("NBO", "BO", -1.0),
                            ("B128", "BO", 128.0), ("BQ0", "BO", q(0))):
             act(v(n_), v(src), scale=c)
-        act(v("SW"), v("SWB"))
         act(v("NLP"), v("ID"), scale=4096.0)
         tt(v("NLP"), v("NLP"), v("GT"), A.add)
         act(v("LPB"), v("NLP"), scale=-1.0)
@@ -562,9 +651,7 @@ def rank_program(g, core, T, topo):
         tt(v("ZT"), v("ZT"), v("ID"), A.add)
         ts(newcol("keep"), ki, 2.5, A.is_gt)
         act(v("K34"), v("ID"), scale=col["keep"])
-        ts(v("X2D"), v("CR", 0, 128), col["k5"], A.is_equal, q(7), A.mult)
-        act(v("D0"), v("ID"), scale=col["n2"])
-        tt(v("X2D"), v("X2D"), v("D0"), A.add)
+        act(v("X2D"), v("ID"), scale=col["n2"])
         ts(v("D0"), v("CR", 0, 128), col["g16"], A.is_equal)
         ts(v("D1"), v("CR", 0, 128), col["g17"], A.is_equal)
         act(v("ONS"), v("Z", 0, 128), F.Identity, bias=1.0 / 4096)
@@ -596,43 +683,54 @@ def rank_program(g, core, T, topo):
     def lanes(t):
         c0 = 896 * t % 2048 // 16
         if t == 0:
-            turn(v("NT", 128, 256), v("NT", 0, 128))
-            mm([(v("q3", 2 * b + s1, 128, 8), v("SWB", 256 * s1 + 128 * g2, 256 * s1 + 128 * g2 + 128), v("NT", 128 + 32 * b + 16 * g2, 144 + 32 * b + 16 * g2))
+            turn(v("VB", 128, 256), v("VB", 0, 128))
+            mm([(v("q4", 2 * b + s1, 128, 8), v("SWB", 256 * s1 + 128 * g2, 256 * s1 + 128 * g2 + 128), v("VB", 128 + 32 * b + 16 * g2, 144 + 32 * b + 16 * g2))
                 for b in range(4) for s1 in (0, 1) for g2 in (0, 1)], each=2)
-            ts(v("NW"), v("q3", 0, 128), 0.5, A.is_ge)
+            ts(v("NW"), v("q4", 0, 128), 0.0, A.is_ge)
+            act(v("HW"), v("q4", 0, 128))
         else:
-            mm(wrap(v("q3", 0, 128), "RD2", "TB", 0, 2048))
-            ts(v("NW", 0, 128 - c0), v("q3", c0, 128), 4096.0, A.is_ge)
-            ts(v("NW", 128 - c0, 128), v("q3", 0, c0), 4096.0, A.is_ge)
+            mm(wrap(v("q4", 0, 128), "RH", "TB", 0, 2048))
+            ts(v("NW", 0, 128 - c0), v("q4", c0, 128), 2048.0, A.is_ge)
+            ts(v("NW", 128 - c0, 128), v("q4", 0, c0), 2048.0, A.is_ge)
+            act(v("HW", 0, 128 - c0), v("q4", c0, 128), F.Identity, bias=-2048.0)
+            act(v("HW", 128 - c0, 128), v("q4", 0, c0), F.Identity, bias=-2048.0)
         mm([(v("q3", 128, 256), v("NW"), v("BO"))])
-        mm([(v("q5", 0, 128), v("BO"), v("NW")), (v("q5", 128, 256), v("LPA"), v("NW"))], each=1)
         cp(v("TTB", 0, 128), v("q3", 128, 256))
         tt(v("TTB", 128, 256), v("q3", 128, 256), v("LT"), A.mult)
         tt(v("TTB", 256, 384), v("q3", 128, 256), v("EQH"), A.is_lt)
-        mm([(v("q3", 256, 264), v("TTB", 128 * k, 128 * k + 128), v("RH3", 8 * k, 8 * k + 8)) for k in range(3)])
-        scan(v("CUM"), v("q5", 0, 128), v("ZF"), A.add)
-        tt(v("OF"), v("q3", 256, 264), v("W8"), A.min)
-        cp(v("OFu"), v("OF"))
-        sca(v("CW"), v("OFu"), v("C1%d" % t))
-        tt(v("POS"), v("q5", 128, 256), v("CUM"), A.add)
-        ts(v("EX"), v("JW"), v("CUM", 127, 128), A.is_ge, 4096.0, A.mult)
+        mm([(v("q3", 256, 264), v("TTB", 128 * k, 128 * k + 128), v("RH3", 8 * j, 8 * j + 8)) for j, k in enumerate((0, 1, 2, 2))])
+        mm([(v("q3", 264, 265), v("TTB", 0, 128), v("ON", 0, 1))])
+        mm([(v("q5", 0, 128), v("LPA"), v("NW")), (v("q5", 0, 128), v("TTB", 0, 128), v("UT"))])
+        act(v("POS"), v("q5", 0, 128))
+        cp(v("OFu"), v("q3", 256, 264))
+        sca(v("CW"), v("OFu"), v("C1"))
+        ts(v("EX"), v("JW"), v("q3", 264, 265), A.is_ge, 4096.0, A.mult)
         scan(v("CC"), v("CW", 0, 512), v("Z", 0, 512), A.max)
         mm(wrap(v("q3", 288, 320), "RD0", "CC", 0, 512))
         cp(v("CLu"), v("q3", 288, 320))
-        gtt(v("OH"), v("POS"), v("CLu"), v("JI"), A.is_equal)
-        mms(wrap(v("q4", 0, 32), "RC", "CC", 0, 512) + [(v("q4", 0, 32), v("ID"), v("EX"))], wrap(v("q4", 0, 32), "RI", "OH", 0, 512))
-        tt(v("Lf"), v("q4", 0, 32), v("JC"), A.min)
+        for lo, hi, b in ((0, FIRST, "q5"), (FIRST, 512, "q3")):
+            a, z = lo // 16, hi // 16
+            gtt(v("OH", lo, hi), v("POS"), v("CLu", a, z), v("JI", lo, hi), A.is_equal)
+            gtt(v("TY", lo, hi), v("HW"), v("CLu", a, z), v("OH", lo, hi), A.mult)
+            mm([(v(b, 320 + a, 320 + z), v("IDQ"), v("EX", a, z))] + wrap(v(b, 320 + a, 320 + z), "R1", "TY", lo, hi))
+            cp(v("STu", a, z), v(b, 320 + a, 320 + z))
+            gat(v("Ku", lo, hi), v("RI32"), v("STu", a, z))
+            act(v("HY", a, z), v(b, 320 + a, 320 + z))
+            act(v("HY", 32 + a, 32 + z), v(b, 320 + a, 320 + z), F.Square, bias=col["c40"])
+        mm([(v("q4", 0, 32), v("ID"), v("EX"))] + wrap(v("q4", 0, 32), "RI", "OH", 0, 512))
+        ts(v("Li", 0, 32), v("CLu"), 16.0, A.mult, 16.0 * c0, A.add)
+        if t:
+            bits(v("Li", 0, 32), v("Li", 0, 32), 0, 2047)
+        tt(v("Li", 32, 64), v("q4", 0, 32), v("Li", 0, 32), A.add)
+        tt(v("Lf"), v("Li", 32, 64), v("JC"), A.min)
         cp(v("Lu"), v("Lf"))
 
     def fetch(t):
-        gat(v("TBL", 0, 512), v("TB"), v("Lu"))
-        mm(wrap(v("q5", 256, 288), "RH", "TBL", 0, 512))
-        cp(v("STu"), v("q5", 256, 288))
-        gat(v("Ku"), v("RI32"), v("STu"))
+        pick(TBLQ)(v("TBL", 0, 512), v("TB"), v("Lu"))
 
     def check(t):
         nch = len(CH) - 1
-        banks = ("q5", "q3", "q0", "q1")
+        banks = BANKS
 
         def ch(x, k, at=0):
             return v(x, at + CH[k], at + CH[k + 1])
@@ -647,19 +745,17 @@ def rank_program(g, core, T, topo):
 
         for k in range(nch):
             sgat(tile("sg", k), v("SG"), ch("Ku", k))
-        ts(v("KF"), v("Ku"), -1.0 / 2048, A.mult)
+        ts(v("KF"), v("Ku"), 1023.0, A.min, -1.0 / 2048, A.mult)
         ts(v("PM"), v("Ku"), 1024.0, A.is_ge, 4194304.0, A.mult)
         gat(v("Wu"), v("WI" if t == 0 else "WD"), v("Lu"))
         bias[0] = 20.0
         cp(v("Wf"), v("Wu"))
-        mm([(v("q2"), v("ID"), v("JB")), (v("q2"), v("IDK"), v("KF")), (v("q2"), v("NI"), v("PM")), (v("q2"), v("ID"), v("Wf"))], last=False)
+        mm([(v("q2"), v("ID"), v("JB")), (v("q2"), v("IDK"), v("KF")), (v("q2"), v("ID"), v("Wf"))], last=False)
         bias[0] = 0.0
         hi = lambda k: v("HI", 32 * k, 32 * k + 32)
-        cp(hi(0), v("STu"))
-        ts(hi(1), hi(0), 80.0, A.add)
-        tt(hi(1), hi(1), hi(0), A.mult)
+        ts(hi(1), v("HY", 32, 64), -1600.0, A.add)
         bits(hi(2), hi(1), 4, 1023)
-        tt(hi(3), hi(2), hi(0), A.subtract)
+        tt(hi(3), hi(2), v("HY", 0, 32), A.subtract)
         ts(v("HF", 0, 32), hi(2), 1024.0, A.subtract, -1.0, A.mult)
         ts(hi(4), hi(3), 5, A.arith_shift_right)
         bits(hi(5), hi(3), 0, 31)
@@ -714,29 +810,33 @@ def rank_program(g, core, T, topo):
         ts(v("AI", 0, 64), v("P1W", 512, 576), 8388608.0, A.subtract, 0.0, A.max)
         bits(v("AI", 64, 128), v("AI", 0, 64), 0, 4095)
         cp(v("AH", 0, 64), v("AI", 64, 128))
+        cp(v("BI", 0, 128), v("P1W", 0, 128))
+        bits(v("BI", 128, 256), v("BI", 0, 128), 22, 1)
+        ts(v("AH", 64, 192), v("BI", 128, 256), v("PW", 48, 49), A.mult)
         bias[0] = 0.0
         to = v("q5", 128, 132)
-        mm(wrap(to, "R1", "AH", 0, 64))
-        mm([(v("q3", 64, 128), v("B128"), v("AH", 0, 64)), (v("q3", 64, 128), v("BQ0"), v("C10", 0, 64))])
+        mm(wrap(v("q5", 128, 140), "R1", "AH", 0, 192))
+        mm([(v("q3", 64, 128), v("B128"), v("AH", 0, 64)), (v("q3", 64, 128), v("BQ0"), v("C1", 0, 64))])
+        act(v("AF", 256, 260), to, F.Identity, bias=0.5, scale=-128.0)
         bits(v("AI", 128, 192), v("AI", 0, 64), 17, 31)
         bits(v("AI", 192, 256), v("AI", 0, 64), 12, 31)
-        cp(v("AH", 64, 192), v("AI", 128, 256))
-        sca(v("TB"), v("Lu"), v("TBn"))
-        ts(v("AF", 256, 260), to, -128.0, A.mult, 0.5, A.add)
+        cp(v("AH", 192, 320), v("AI", 128, 256))
         cp(v("AU", 0, 4), to)
+        cp(v("BU", 0, 8), v("q5", 132, 140))
+        sgat(v("AB", 0, 64), v("TS"), v("AU", 0, 4))
+        sca(v("TB"), v("Lu"), v("TBn"))
         for c in range(4):
             act(v("AF", 64 * c, 64 * c + 64), v("q3", 64, 128), F.Abs, bias=v("AF", 256 + c, 257 + c))
-            least(v("AF", 260 + c, 261 + c), v("AF", 64 * c, 64 * c + 64))
-        tt(v("AF", 264, 268), v("AF", 260, 264), v("S4"), A.is_lt)
-        tt(v("AF", 268, 272), v("AF", 264, 268), v("W4"), A.mult)
+        for c in range(4):
+            act(v("AF", 288, 352), v("AF", 64 * c, 64 * c + 64), F.Relu, bias=v("S4", c, c + 1), scale=-4096.0, accum_out=v("AF", 260 + c, 261 + c))
+        mm([(v("q4", 0, 64), v("D0"), v("AH", 192, 256)), (v("q4", 0, 64), v("D1"), v("AH", 256, 320)), (v("q4", 0, 64), v("K34"), v("AB", 0, 64))])
+        act(v("AB", 64, 128), v("q4", 0, 64), F.Identity, bias=col["b2"])
+        tt(v("AF", 268, 272), v("AF", 260, 264), v("W4"), A.min)
         tt(v("AF", 272, 276), to, v("AF", 268, 272), A.max)
         cp(v("AU", 4, 8), v("AF", 272, 276))
-        sgat(v("AB", 0, 64), v("TB"), v("AU", 0, 4))
-        mm([(v("q4", 0, 64), v("D0"), v("AH", 64, 128)), (v("q4", 0, 64), v("D1"), v("AH", 128, 192)), (v("q4", 0, 64), v("K34"), v("AB", 0, 64))])
-        act(v("AB", 64, 128), v("q4", 0, 64), F.Identity, bias=col["b2"])
         sca(v("TB"), v("AU", 4, 8), v("AB", 64, 128))
         if t < 2:
-            dma("Y", v("FL%d" % (t + 1)), row("TB", 2))
+            gadd(v("FL%d" % (t + 1)), row("TB", 2))
             send(5 + t, served(2 + t), v("FI%d" % (t + 1)), v("FL%d" % (t + 1)))
             arrive(5 + t, v("FI%d" % (t + 1)), 5 + t, 4.0)
 
@@ -745,22 +845,20 @@ def rank_program(g, core, T, topo):
         bf = lambda lo, hi: v("BF2", lo, hi)
         sm = lambda k: v("SM", 8 * k, 8 * k + 8)
         dw = "DW%d" % t
-        cp(bi(0), v("P1W", 0, 128))
-        bits(bi(1), bi(0), 22, 1)
-        bits(bi(2), bi(0), 11, 1)
-        cp(v("FB"), v("BI", 128, 384))
-        mm(wrap(v("q6", 0, 8), "RL", "FB", 0, 128))
-        cp(v("BU", 0, 8), v("q6", 0, 8))
         sgat(v("TBS"), v("TBL"), v("BU", 0, 8))
         mm([(v("q6", 128, 256), v("CWM"), v("TBS"))])
-        mm(wrap(v("q7", 264, 272), "RO", "TBS", 0, 128))
+        mm(wrap(v("q7", 272, 280), "RO", "TBS", 0, 128))
         cp(bi(3), v("q6", 128, 256))
+        cp(v("BU", 8, 16), v("q7", 272, 280))
+        sgat(v("LX"), v("X"), v("BU", 8, 16))
         bits(bi(4), bi(3), 0, 2047)
         cp(v("BU", 128, 256), bi(4))
-        cp(v("BU", 8, 16), v("q7", 264, 272))
-        sgat(v("LX"), v("X"), v("BU", 8, 16))
-        for k, R in enumerate(("RO", "RB", "RS")):
-            mm(wrap(v("q6", 8 + 8 * k, 16 + 8 * k), R, "TBS", 0, 128))
+        for k, c in enumerate(("rb", "rs")):
+            act(v("T3", 128 * k, 128 * k + 128), v("TBS"), scale=col[c])
+        mm(wrap(v("q7", 280, 296), "R1", "T3", 0, 256))
+        act(v("WB"), v("q7", 272, 296))
+        bits(bi(2), bi(0), 11, 1)
+        cp(v("FB"), bi(2))
         for h in (0, 1):
             pick(CAND[t][h])(v("mm0", 1024 * h, 1024 * h + 1024), v("XE%d" % t), v("BU", 128 + 64 * h, 192 + 64 * h))
         for h in (0, 1):
@@ -776,25 +874,31 @@ def rank_program(g, core, T, topo):
             mms([(o, v("MK12"), v("TBS", 64 * h, 64 * h + 64))] + [(o, win("R16", m), v("hg0", 1024 * h + 64 * m, 1024 * h + 64 * m + 64)) for m in range(8)],
                 [(o, win("R16", m), v("hg0", 1024 * h + 64 * m, 1024 * h + 64 * m + 64)) for m in range(8, 16)])
         sgat(v("OLD"), v("WD"), v("BU", 8, 16))
+        changes(t)
         turn(bf(0, 128), v("q7", 0, 128))
         lo, n, o = 0, 128, 128
+        if t == 2:
+            for k in range(8):
+                least(bf(128 + k, 129 + k), bf(16 * k, 16 * k + 16))
+            lo, n = 128, 8
         while n > 8:
             tt(bf(o, o + n // 2), v("BF2", lo, lo + n, 2), v("BF2", lo + 1, lo + n, 2), A.min)
             lo, n, o = o, n // 2, o + n // 2
-        mm([(v("q7", 256 + s1, 264, 2), v("SW", 256 * s1 + 128 * g2, 256 * s1 + 128 * g2 + 128), v("BF2", lo + g2, lo + 8, 2))
-            for s1 in (0, 1) for g2 in (0, 1)], each=2)
-        cp(sm(0), v("q7", 256, 264))
+        cp(sm(0), bf(lo, lo + 8))
+        ts(v("MB", 8, 16), bf(lo, lo + 8), 65400.0, A.is_gt)
         bits(sm(1), sm(0), 0, 15)
-        tt(sm(2), v("q6", 24, 32), sm(1), A.mult)
-        tt(sm(3), v("q6", 16, 24), sm(2), A.add)
+        cp(v("MB", 0, 8), sm(1))
+        mm([(v("q7", 256 + s1, 272, 2), v("SWB", 256 * s1 + 128 * g2, 256 * s1 + 128 * g2 + 128), v("MB", g2, 16, 2))
+            for s1 in (0, 1) for g2 in (0, 1)], each=2)
+        tt(sm(2), v("q7", 256, 264), v("WB", 16, 24), A.mult)
+        tt(sm(3), sm(2), v("WB", 8, 16), A.add)
         bits(sm(4), sm(3), 0, 2047)
         cp(v("BU", 24, 32), sm(4))
         gtt(bf(256, 384), v("WE"), v("BU", 24, 32), v("OLD"), A.subtract)
-        ts(bf(248, 256), sm(0), 65400.0, A.is_gt)
-        tt(bf(248, 256), bf(248, 256), v("W8"), A.mult)
-        tt(v(dw, 128, 136), v("q6", 8, 16), bf(248, 256), A.max)
+        tt(bf(248, 256), v("q7", 264, 272), v("W8"), A.mult)
+        tt(v(dw, 128, 136), v("WB", 0, 8), bf(248, 256), A.max)
         cp(v("BU", 16, 24), v(dw, 128, 136))
-        tt(bf(384, 512), bf(256, 384), v("FB", 128, 256), A.mult)
+        tt(bf(384, 512), bf(256, 384), v("FB"), A.mult)
         if t == 2:
             op("V", lambda: g.vector.tensor_tensor(ind(v("WD"), v("BU", 16, 24)), ap(bf(384, 512)), ap(v("OLD")), A.add),
                [bf(384, 512), v("OLD"), v("BU", 16, 24)], [v("WD")], ew(128, 3.8))
@@ -811,6 +915,10 @@ def rank_program(g, core, T, topo):
         gcp(v("WE", 0, 2048), v("WH%d" % t))
         hold.append(v("FT", CH[1], CH[2]))
         dma("Y", row("XE%d" % t, 2), v("FI%d" % t))
+        hold.pop()
+
+    def changes(t):
+        hold.append(v("BU", 128, 256))
         for s in range(t):
             b = "Di%d%d" % (s, t)
             cp(v("HU"), v(b, 128, 136))
@@ -819,11 +927,11 @@ def rank_program(g, core, T, topo):
 
     def flags_out():
         mm([(v("q3", 0, 128), win("RH", b), v("TB", 128 * b, 128 * b + 128)) for b in range(16)])
-        mm([(v("q5", 0, 128), win("RD2", b), v("TB", 128 * b, 128 * b + 128)) for b in range(16)])
-        act(v("OUT", 0, 128), v("q3", 0, 128))
-        ts(v("OUT", 128, 256), v("q5", 0, 128), 4096.0, A.is_lt)
-        fin.append(dma("Y", None, v("OUT", 0, 128), o=T.yh[:]))
+        ts(v("OUT", 128, 256), v("q3", 0, 128), 2048.0, A.is_lt)
         fin.append(dma("Y", None, v("OUT", 128, 256), o=T.yv[:]))
+        act(v("HW"), v("OUT", 128, 256), F.Identity, bias=-2048.0, scale=2048.0)
+        tt(v("OUT", 0, 128), v("q3", 0, 128), v("HW"), A.add)
+        fin.append(dma("Y", None, v("OUT", 0, 128), o=T.yh[:]))
 
     late_constants()
     lanes(0)
@@ -842,7 +950,9 @@ def rank_program(g, core, T, topo):
             bias[0] = 0.0
             fetch(t + 1)
         else:
+            bias[0] = LAST
             repairs(t)
+            bias[0] = 0.0
             flags_out()
     issue()
     for sem in fin:

@@ -1,23 +1,23 @@
+import math
 from concourse.bass import DstId, RemoteDMATransfer
 from concourse.mybir import AluOpType as A, AxisListType, ActivationFunctionType as F
 
-PATIENCE = 0.5
 CH = (0, 160, 320, 448, 512)
-TYP = ("SSVS", "SSVS", "SSVS")
-CAND = ("SS", "SS", "SV")
-LATE = 2.0
-SMALL = 0.0
-LOADS = ("X", "RI32", "SG", "WI")
-TBLQ = "S"
-LAST = 3.0
-PASSES, WAKE, PE = 3, 0.18, 0.48e-3
-GATHER, SCATTER = 1.56, 3.8
-SPEEDS = ((0.9e-3, 1.25, 3.0), (0.9e-3, 1.5, 3.5), (1.0e-3, 2.0, 5.0))
-PLAN = SPEEDS + ((0.95e-3, 1.56, 3.8), (0.95e-3, 1.4, 3.0), (1.0e-3, 1.7, 4.0))
-ORDER, EST = [], []
-PACE, CUT = 1, 896
-FIRST = 160
 BANKS = ("q5", "q3", "q0", "q1")
+FIRST = 160
+TYP = ("SVSS", "SVSS", "SVSS")
+SHARE = (128, 112, 112)
+SIGS = 2
+CAND = ("SS", "SS", "SS")
+TBLQ = "S"
+LOADS = ("X", "RI32", "SG", "WI")
+PACE, CUT = 1, 896
+LATE, LAST, SMALL, PATIENCE, WAKE = 2.0, 3.0, 0.0, 0.5, 0.18
+GATHER, SCATTER, MATMUL = 1.56, 3.8, 0.62
+SPEEDS = ((1.1e-3, 1.15, 2.5), (1.0e-3, 1.55, 3.8), (1.0e-3, 2.0, 5.0))
+PLAN = ((1.1e-3, 1.08, 2.5), (0.9e-3, 1.45, 3.5), (1.0e-3, 2.0, 5.0)) + ((0.95e-3, 1.56, 3.8), (0.95e-3, 1.3, 3.0), (1.0e-3, 1.7, 4.0))
+PASSES, STEPS, STARTS = 3, 2000, 2
+ORDER, EST = [], []
 SCRATCH = {}
 SEMAPHORES = ["cV", "cS", "cP", "cG"]
 
@@ -35,29 +35,29 @@ def _buf(name, cols, dtype, where="sbuf", pool=None):
         SCRATCH[name] = (where, [128, cols], dtype)
 
 
-for _n in ("BO", "NBO", "LT", "EQH", "GT", "ID", "NI", "LPA", "LPB", "NLP", "ZT", "X2D", "K34", "D0", "D1", "B128", "BQ0", "IDK", "ID24",
-           "IDF", "IDQ", "ON", "ONS", "CWM", "MK12", "C1"):
+for _n in ("BO", "NBO", "LT", "EQH", "GT", "ID", "NI", "LPB", "NLP", "ZT", "X2D", "K34", "B128", "IDK",
+           "IDF", "ID22", "IDQ", "ON", "ONS", "CWM", "MK12", "C1"):
     _buf(_n, 128, BF, pool="PB")
-for _n in ("R1", "RD0", "RI", "RH", "RX", "R2", "RN", "RU", "RO", "R16"):
+for _n in ("R1", "RI", "RH", "RX", "R2", "RN", "RU", "RO", "R16"):
     _buf(_n, 144, BF, pool="PB")
-for _n, _c in (("RH3", 32), ("UT", 128), ("SWB", 512), ("SC", 64), ("KIB", 128)):
+for _n, _c in (("RH3", 32), ("DFB", 128), ("UT", 128), ("SWB", 512), ("KIB", 128)):
     _buf(_n, _c, BF, pool="PB")
 for _n, _c in (("COLS", 128), ("QH", 16), ("CR", 144), ("MG", 128), ("MI", 128), ("JW", 32), ("JC", 32), ("JD", 32), ("J16", 32),
-               ("W8", 8), ("W4", 4), ("S4", 4), ("RM", 64), ("DF", 192), ("ZF", 128), ("TMP", 128)):
+               ("W8", 8), ("W4", 4), ("S4", 4), ("K3", 3), ("DF", 192), ("ZF", 128), ("TMP", 128)):
     _buf(_n, _c, FP, pool="PF")
 for _n, _c, _d in (
         ("X", 2064, BF), ("WD", 2560, FP), ("WI", 2560, I32), ("W16", 2048, H16), ("RI32", 1032, I32), ("SG", 1040, BF), ("TB", 2688, BF),
-        ("Z", 640, BF), ("ZU", 2048, BF), ("PW", 64, FP), ("UH", 2048, BF), ("UL", 2048, BF), ("UG", 2048, BF), ("JI", 512, FP), ("JB", 512, BF),
+        ("Z", 640, BF), ("UN", 2064, BF), ("PW", 64, FP), ("JI", 512, FP), ("JB", 512, BF),
         ("hyb", 128, I32), ("vfb", 128, I32), ("thi", 1, I32), ("KI", 4, I32), ("ST", 1024, BF), ("SI", 1280, I32),
         ("NW", 128, BF), ("NT", 128, BF), ("VB", 256, H16), ("HW", 128, FP), ("TY", 512, H16), ("POS", 128, FP), ("TTB", 384, BF), ("OFu", 8, U16),
         ("CW", 4224, BF), ("CC", 512, BF), ("CLu", 32, U16), ("OH", 512, BF), ("EX", 32, BF), ("Lf", 32, FP), ("Lu", 32, U16),
         ("TBL", 528, BF), ("Wu", 512, U16), ("Wf", 512, H16), ("Ku", 512, U16), ("KF", 512, H16), ("PM", 512, BF), ("STu", 32, U16),
         ("HI", 256, I32), ("HF", 64, FP), ("HY", 64, FP), ("TS", 2688, BF), ("FT", 1024, BF), ("FO", 512, BF), ("RD", 256, I32), ("GA", 256, BF), ("PAY", 512, FP),
         ("sig", 8192, BF), ("mm0", 2560, BF), ("mm1", 2560, BF), ("hg0", 2560, BF), ("hg1", 2560, BF),
-        ("RP", 96, BF), ("LW", 192, FP), ("PFu", 32, U16), ("DL", 160, BF), ("P1W", 1536, FP), ("TBn", 512, BF),
+        ("RP", 96, BF), ("LW", 192, FP), ("PFu", 32, U16), ("DL", 224, BF), ("P1W", 1536, FP), ("TBn", 512, BF),
         ("thB", 4, FP), ("CN", 4, I32), ("BS", 32, FP),
         ("AI", 256, I32), ("AH", 320, H16), ("T3", 384, BF), ("WB", 24, FP), ("MB", 16, BF), ("Li", 64, I32), ("AF", 352, FP), ("AB", 128, BF), ("AU", 8, U16),
-        ("BI", 640, I32), ("FB", 128, BF), ("TBS", 128, BF), ("LX", 128, BF), ("OLD", 128, FP), ("BF2", 512, FP), ("SM", 64, I32),
+        ("BI", 640, I32), ("FB", 128, BF), ("TBS", 1536, BF), ("LX", 128, BF), ("OLD", 128, FP), ("BF2", 512, FP), ("SM", 64, I32),
         ("BU", 256, U16), ("HU", 8, U16), ("WE", 2176, FP), ("OUT", 256, FP),
         ("DW0", 136, FP), ("DW1", 136, FP), ("DW2", 136, FP)):
     _buf(_n, _c, _d)
@@ -212,7 +212,7 @@ def rank_program(g, core, T, topo):
             clock = dict(known["P"])
             clock["cP"] = val
             note("P", [x[1] for x in lst] + [x[2] for x in lst], [x[0] for x in lst], "cP", val, clock)
-        call("P", emit, [x[1] for x in lst] + [x[2] for x in lst], [x[0] for x in lst], cyc * PE)
+        call("P", emit, [x[1] for x in lst] + [x[2] for x in lst], [x[0] for x in lst], (cyc, MATMUL))
 
     def mms(*parts):
         for n, lst in enumerate(parts):
@@ -229,7 +229,7 @@ def rank_program(g, core, T, topo):
             clock = dict(known[e])
             clock[sem] = 16
             note("D" + sem, rd, wr, sem, 16, clock)
-        call(e, emit, rd, wr + ([] if i is None else [LQ]), 0.06, lat or 2.3)
+        call(e, emit, rd, wr + ([] if i is None else [LQ]), 0.06, lat or (4.0 if out is not None and out[0] == "TB" else 2.3))
         return sem
 
     def gadd(out, in_):
@@ -294,7 +294,7 @@ def rank_program(g, core, T, topo):
                         else:
                             hit = (wr or a[4]) and a[1] < x[2] and x[1] < a[2] and (a[3] is None or x[4] is None or a[3] == x[4])
                         if hit:
-                            ps[a[0]] = max(ps.get(a[0], 0.0), 0.0 if x in (GQ, LQ) else prog[a[0]]["lat"] + WAKE)
+                            ps[a[0]] = max(ps.get(a[0], 0.0), 0.0 if x in (GQ, LQ) or a[5] == c["e"] == "P" else prog[a[0]]["lat"] + WAKE)
             for lst, wr in ((c["r"], False), (c["w"], True)):
                 for x in lst:
                     h = hist[x[0]]
@@ -318,7 +318,12 @@ def rank_program(g, core, T, topo):
             for k in range(n - 1, -1, -1):
                 c = prog[k]["cost"]
                 if isinstance(c, tuple):
-                    c = 0.05 + c[0] * cyc * (ga if c[1] == GATHER else sc) if c[1] in (GATHER, SCATTER) else 0.03 + max(64, c[0] * c[1]) * cyc
+                    if c[1] == MATMUL:
+                        c = c[0] * cyc * MATMUL
+                    elif c[1] in (GATHER, SCATTER):
+                        c = 0.05 + c[0] * cyc * (ga if c[1] == GATHER else sc)
+                    else:
+                        c = 0.03 + max(64, c[0] * c[1]) * cyc
                 cost[k] = c
                 rank_[k] = c + max([rank_[s] + pred[s][k] for s in succ[k]] or [prog[k]["lat"]])
             for k in range(n):
@@ -370,6 +375,54 @@ def rank_program(g, core, T, topo):
                         ready.add(s)
             return start
 
+        def polish(order, costs):
+            pl, lat = [list(p.items()) for p in pred], [c["lat"] for c in prog]
+
+            def run(order, cs):
+                free, last, done, why = {}, {}, [0.0] * n, [None] * n
+                for k in order:
+                    t0, e = 0.0, prog[k]["e"]
+                    for p, x in pl[k]:
+                        if done[p] + x > t0:
+                            t0, why[k] = done[p] + x, (p, False)
+                    if e != "R":
+                        if free.get(e, 0.0) > t0:
+                            t0, why[k] = free[e], (last[e], True)
+                        last[e] = k
+                    done[k] = free[e] = t0 + cs[k]
+                end = max(range(n), key=lambda k: done[k] + lat[k])
+                return done[end] + lat[end], end, why
+
+            def ahead(order, k, j):
+                lo, hi = order.index(j), order.index(k)
+                need = {k}
+                for x in order[lo:hi + 1][::-1]:
+                    if x in need:
+                        need.update(p for p, _ in pl[x])
+                mid = order[lo:hi + 1]
+                return None if j in need else order[:lo] + [x for x in mid if x in need] + [x for x in mid if x not in need] + order[hi + 1:]
+
+            now, left = [run(order, cs) for cs in costs], STEPS
+            while left > 0:
+                moves = {}
+                for _, k, why in now:
+                    while why[k] is not None:
+                        if why[k][1]:
+                            moves[(k, why[k][0])] = True
+                        k = why[k][0]
+                for k, j in moves:
+                    left -= 1
+                    other = ahead(order, k, j)
+                    if other is not None:
+                        new = [run(other, cs) for cs in costs]
+                        if math.prod(x[0] for x in new) < math.prod(x[0] for x in now) * (1 - 1e-6):
+                            order, now = other, new
+                            break
+                else:
+                    break
+            EST.append((math.prod(x[0] for x in now) ** (1 / len(now)), left))
+            return math.prod(x[0] for x in now), list(order)
+
         if not ORDER:
             orders = []
             for speed in PLAN:
@@ -384,7 +437,13 @@ def rank_program(g, core, T, topo):
                 assume(speed)
                 total = [x * length(o) for x, o in zip(total, orders)]
             ORDER[:] = orders[total.index(min(total))]
-            EST.append((total.index(min(total)), min(total) ** (1 / len(SPEEDS))))
+            costs = []
+            for speed in SPEEDS:
+                assume(speed)
+                costs.append(list(cost))
+            some = sorted(range(len(orders)), key=lambda i: total[i])
+            some = [i for j, i in enumerate(some) if i // (PASSES + 1) not in [x // (PASSES + 1) for x in some[:j]]][:STARTS]
+            ORDER[:] = min(polish(orders[i], costs) for i in some)[1]
         for k in ORDER:
             prog[k]["emit"]()
 
@@ -442,7 +501,9 @@ def rank_program(g, core, T, topo):
         op("V", lambda: g.vector.tensor_tensor(ap(o), ind(win, off), ap(b), f), [win, off, b], [o], ew(wid(o), 1.56))
 
     def scan(o, a, z, f, first=0.0):
-        op("V", lambda: g.vector.tensor_tensor_scan(ap(o), ap(a), ap(z), first, f, A.add), [a, z], [o], ew(wid(o), half(o, a)))
+        col_ = isinstance(first, tuple)
+        op("V", lambda: g.vector.tensor_tensor_scan(ap(o), ap(a), ap(z), ap(first) if col_ else first, f, A.add), [a, z] + [first] * col_, [o],
+           ew(wid(o), half(o, a)))
 
     def act(o, a, func=F.Copy, bias=None, scale=None, accum_out=None):
         kw = {}
@@ -504,7 +565,9 @@ def rank_program(g, core, T, topo):
     iota(v("MG"), [[1, 8], [0, 16]], 0)
     iota(v("MI"), [[0, 8], [1, 16]], 0)
     iota(v("J16"), [[16, 32]], 0)
-    iota(v("JI"), [[1, 512]], 4097)
+    iota(v("K3", 0, 3), [[16, 3]], -16, 1)
+    iota(v("CW", 0, 512), [[0, 512]], 0)
+    iota(v("JI"), [[1, 512]], -4095)
     iota(v("WI", 2048, 2560), [[0, 512]], 0)
     col, ncol = {}, [0]
 
@@ -532,17 +595,16 @@ def rank_program(g, core, T, topo):
     ms(v("Z"), 0.0)
     ms(v("ZF"), 0.0)
     bias[0] = 0.0
-    ki, kg, kf, odd, even = newcol("ki"), newcol("kg"), newcol("k"), newcol("odd"), newcol("even")
+    ki, kg, odd = newcol("ki"), newcol("kg"), newcol("odd")
+    km, kf, kp = v("K3", 0, 1), v("K3", 1, 2), v("K3", 2, 3)
     ts(v("KI", 1, 2), v("KI", 0, 1), 4, A.arith_shift_right)
     bits(v("KI", 2, 3), v("KI", 0, 1), 0, 15)
     bits(v("KI", 3, 4), v("KI", 0, 1), 4, 1)
     cp(ki, v("KI", 2, 3))
     cp(kg, v("KI", 1, 2))
-    cp(kf, v("KI", 0, 1))
     cp(odd, v("KI", 3, 4))
     ts(v("QH"), v("CR", 0, 16), ki, A.is_equal)
-    for name, src, a, b in (("even2", odd, -1.0, 1.0), ("g15", kg, 16.0, 15.0), ("g16", kg, 16.0, 0.0), ("g17", kg, 16.0, 1.0), ("km", kf, 1.0, -16.0),
-                            ("kp", kf, 1.0, 16.0), ("uw", ki, 10.0, 1.0), ("n2", q(2), -1.0, 1.0), ("c40", ki, 0.0, 40.0)):
+    for name, src, a, b in (("even2", odd, -1.0, 1.0), ("g15", kg, 16.0, 15.0), ("uw", ki, 10.0, 1.0), ("n2", q(2), -1.0, 1.0), ("c40", ki, 0.0, 40.0)):
         act(newcol(name), src, F.Identity, bias=b, scale=a)
     even = col["even2"]
     ts(v("R1", 0, 143), v("CR", 0, 143), col["g15"], A.is_equal)
@@ -552,33 +614,32 @@ def rank_program(g, core, T, topo):
     ts(v("EQH"), v("MI"), ki, A.is_equal, 0.5, A.mult)
     ts(v("GT"), v("MI"), ki, A.is_lt)
     tt(v("GT"), v("GT"), v("BO"), A.mult)
-    act(v("LPA"), v("ID"), scale=4096.0)
-    tt(v("LPA"), v("LPA"), v("GT"), A.subtract)
+    act(v("LPB"), v("ID"), scale=-4096.0)
+    tt(v("LPB"), v("LPB"), v("GT"), A.subtract)
     ts(v("RH3", 0, 8), v("CR", 0, 8), kg, A.is_gt)
     ts(v("RH3", 8, 16), v("CR", 0, 8), kg, A.is_equal)
     act(v("RH3", 16, 24), v("RH3", 8, 16), scale=2048.0)
     act(v("RH3", 24, 32), v("RH3", 8, 16), scale=kf)
     ts(v("UT"), v("CR", 0, 128), kf, A.is_ge)
-    for k, (c_, m_) in enumerate(((kf, even), (col["kp"], even), (col["km"], odd), (kf, odd))):
+    for k, (c_, m_) in enumerate(((kf, even), (kp, even), (km, odd), (kf, odd))):
         ts(v("SWB", 128 * k, 128 * k + 128), v("CR", 0, 128), c_, A.is_equal, m_, A.mult)
     act(v("JW"), v("J16"), F.Identity, bias=ki)
     for name, n, a, b in (("JC", 32, 1.0, 2048.0), ("W8", 8, 1.0, 2048.0), ("JD", 32, 1.0, 1024.0), ("W4", 4, 2.0, 2560.0), ("S4", 4, 4096.0, 1024.0)):
         act(v(name), v("JW", 0, n), F.Identity, bias=b, scale=a)
-    act(v("C1"), v("CR", 0, 128))
+    act(v("C1"), v("CR", 0, 128), scale=1 / 16)
     ts(v("PW", 0, 16), v("ZF", 0, 16), 2.0, A.add)
     scan(v("PW", 16, 32), v("PW", 0, 16), v("ZF", 0, 16), A.mult, 0.5)
     tt(v("PW", 32, 48), v("PW", 16, 32), v("QH"), A.mult)
     op("V", lambda: g.vector.tensor_reduce(ap(v("PW", 48, 49)), ap(v("PW", 32, 48)), AxisListType.X, A.add), [v("PW", 32, 48)], [v("PW", 48, 49)])
-    for name, c in (("RD0", q(0)), ("RI", ki), ("RH", weights("h", {0: 32, 1: 1, 2: 0.25})),
+    for name, c in (("RI", ki), ("RH", weights("h", {0: 32, 1: 1, 2: 0.25})),
                     ("RU", col["uw"]), ("RX", weights("sx", {0: 1 / 64, 1: 1 / 2048, 3: -64, 4: -1})), ("R2", 2.0), ("RN", -1.0),
-                    ("R16", 16.0), ("RO", weights("ro", {10: 128, 11: 1}))):
+                    ("R16", 16.0), ("RO", weights("ro", {10: 128, 11: 16}))):
         act(v(name, 0, 143), v("R1", 0, 143), scale=c)
     weights("rb", {8: 32, 9: 1})
     weights("rs", {5: 64, 6: 2, 12: 1})
     act(v("ON"), v("Z", 0, 128), F.Identity, bias=1.0)
     dma("Y", row("TB", 12), v("ON"))
     ts(v("TB", 2048, 2688), v("Z", 0, 640), weights("tb", {0: 32}), A.add)
-    act(v("CW", 0, 512), v("Z", 0, 512))
     act(v("TBL", 512, 528), v("Z", 0, 16), F.Identity, bias=weights("tl", {10: 16}))
     ms(v("X", 2048, 2064), 16384.0)
     ms(v("RI32", 1024, 1032), 1024)
@@ -616,67 +677,54 @@ def rank_program(g, core, T, topo):
     for k, r in enumerate((5, 6, 8, 9)):
         dma("Y", row("TB", r), v("ST", 512 + 128 * k, 640 + 128 * k))
     dma("Y", v("TS"), v("TB"), lat=4.0)
-    for k in range(4):
-        cp(v("W16", 512 * k, 512 * k + 512), v("WI", 512 * k, 512 * k + 512))
-    hand_on(1, "X", 4.0)
-    op("G", lambda: g.iota(ap(v("ZU")), [[0, 2048]], 0, 0, allow_small_or_imprecise_dtypes=True), [], [v("ZU"), GQ], 4.1)
-    hand_on(3, "W16")
 
-    def unwrap(k, name, w):
-        op("G", lambda: g.affine_select(ap(v(name)), ap(v("ZU")), [[-1, 16], [-16, 8], [1000, 16]], A.not_equal, w, -1000 * k, 1),
-           [v("ZU")], [v(name), GQ], 4.1)
-
-    unwrap(0, "UH", 32.0)
-    unwrap(1, "UL", 1.0)
-    gadd(v("FL0"), row("TB", 2))
-    unwrap(2, "UG", 8192.0)
-    send(0, served(1), v("FI0"), v("FL0"))
-    arrive(0, v("FI0"), 0, 10.0)
-    for k in range(6):
-        for h in (0, 1):
-            arrive(10 + 2 * k + h, v(("XE%d", "WH%d")[k & 1] % (k // 2), *piece(k, h)), 3, 12.0 + 12.0 * k)
-    gcp(v("WD", 0, 2048), v("W16"))
-    gcp(v("WD", 2048, 2560), v("Z", 0, 512))
-    gcp(v("WE", 2048, 2176), v("Z", 0, 128))
+    def tables_out():
+        hand_on(1, "X", 4.0)
+        gcp(v("W16"), v("WI", 0, 2048))
+        hand_on(3, "W16")
+        op("G", lambda: g.iota(ap(v("UN")), [[0, 2064]], 0, 0, allow_small_or_imprecise_dtypes=True), [], [v("UN"), GQ], 4.1)
+        gadd(v("FL0"), row("TB", 2))
+        un = v("UN", 16, 2064)
+        op("G", lambda: g.affine_select(ap(un), ap(un), [[-1, 16], [-16, 8], [1000, 16]], A.not_equal, 1.0, 0, 1), [un], [un, GQ], 4.1)
+        send(0, served(1), v("FI0"), v("FL0"))
+        arrive(0, v("FI0"), 0, 10.0)
+        for k in range(6):
+            for h in (0, 1):
+                arrive(10 + 2 * k + h, v(("XE%d", "WH%d")[k & 1] % (k // 2), *piece(k, h)), 3, 10.0 + 12.0 * k)
 
     def late_constants():
-        for n_, src, c in (("NI", "ID", -1.0), ("IDK", "ID", -8388608.0), ("ID24", "ID", 24.0), ("IDF", "ID", 2048.0), ("NBO", "BO", -1.0),
-                           ("B128", "BO", 128.0), ("BQ0", "BO", q(0))):
+        for n_, src, c in (("NI", "ID", -1.0), ("IDK", "ID", -8388608.0), ("IDF", "ID", 2048.0), ("NBO", "BO", -1.0),
+                           ("B128", "BO", 128.0), ("NLP", "LPB", -1.0)):
             act(v(n_), v(src), scale=c)
-        act(v("NLP"), v("ID"), scale=4096.0)
-        tt(v("NLP"), v("NLP"), v("GT"), A.add)
-        act(v("LPB"), v("NLP"), scale=-1.0)
-        ts(v("ZT"), v("LT"), -2.0, A.mult)
+        tt(v("ZT"), v("EQH"), v("LT"), A.subtract)
         tt(v("ZT"), v("ZT"), v("BO"), A.mult)
-        tt(v("ZT"), v("ZT"), v("ID"), A.add)
         ts(newcol("keep"), ki, 2.5, A.is_gt)
         act(v("K34"), v("ID"), scale=col["keep"])
         act(v("X2D"), v("ID"), scale=col["n2"])
-        ts(v("D0"), v("CR", 0, 128), col["g16"], A.is_equal)
-        ts(v("D1"), v("CR", 0, 128), col["g17"], A.is_equal)
         act(v("ONS"), v("Z", 0, 128), F.Identity, bias=1.0 / 4096)
-        act(v("TMP"), v("MI"), F.Identity, bias=col["rb"], scale=col["rs"])
-        tt(v("CWM"), v("TMP"), v("BO"), A.mult)
-        act(v("TMP"), v("MI"), scale=q(12))
-        tt(v("MK12"), v("TMP"), v("BO"), A.mult)
-        act(v("SC", 0, 32), v("Z", 0, 32), F.Identity, bias=weights("sc", {0: 4096, 1: -1}))
-        act(v("SC", 32, 64), v("Z", 0, 32), F.Identity, bias=weights("sc", {0: 4608, 1: -1}))
-        ts(v("RM"), v("CR", 0, 64), 32.0, A.not_equal)
+        act(v("CWM"), v("MI"), F.Identity, bias=col["rb"], scale=col["rs"])
+        tt(v("CWM"), v("CWM"), v("BO"), A.mult)
+        act(v("MK12"), v("MI"), scale=q(12))
+        tt(v("MK12"), v("MK12"), v("BO"), A.mult)
         act(v("DF", 0, 128), v("ZF"), F.Identity, bias=weights("df", {9: 1 << 22}))
         act(v("DF", 128, 192), v("CR", 0, 64), F.Identity, bias=weights("df", {0: (1 << 23) + 2560}), scale=weights("d2", {0: 2}))
         weights("b2", {2: 8192})
+        act(v("DFB"), v("Z", 0, 128), F.Identity, bias=col["tl"])
         ts(v("thB", 0, 1), v("thi"), 0.5, A.add)
         ts(v("thB", 1, 2), v("thi"), 0.5, A.add)
         bias[0] = 12.0
         inv = v("PW", 56, 57)
         op("V", lambda: g.vector.reciprocal(ap(inv), ap(v("PW", 48, 49))), [v("PW", 48, 49)], [inv], 0.25)
-        act(newcol("cut"), inv, F.Identity, bias=0.499, scale=4097.0)
+        act(newcol("cut"), inv, F.Identity, bias=0.499, scale=-4095.0)
         ts(v("SI", 0, 512), v("JI"), inv, A.mult, col["cut"], A.subtract)
         bits(v("SI", 0, 512), v("SI", 0, 512), 0, 1)
-        ts(v("JB"), v("SI", 0, 512), 4194304.0, A.mult)
+        gcp(v("JB"), v("SI", 0, 512))
+        act(v("ID22"), v("ID"), scale=4194304.0)
         bias[0] = 0.0
 
-    def slots_reset():
+    def slots_reset(t):
+        if t == 2:
+            gcp(v("TBS", 0, 128), v("DFB"))
         gcp(v("P1W", 0, 128), v("DF", 0, 128))
         gcp(v("P1W", 512, 576), v("DF", 128, 192))
 
@@ -700,13 +748,13 @@ def rank_program(g, core, T, topo):
         tt(v("TTB", 256, 384), v("q3", 128, 256), v("EQH"), A.is_lt)
         mm([(v("q3", 256, 264), v("TTB", 128 * k, 128 * k + 128), v("RH3", 8 * j, 8 * j + 8)) for j, k in enumerate((0, 1, 2, 2))])
         mm([(v("q3", 264, 265), v("TTB", 0, 128), v("ON", 0, 1))])
-        mm([(v("q5", 0, 128), v("LPA"), v("NW")), (v("q5", 0, 128), v("TTB", 0, 128), v("UT"))])
+        mm([(v("q5", 0, 128), v("LPB"), v("NW")), (v("q5", 0, 128), v("TTB", 0, 128), v("UT"))])
         act(v("POS"), v("q5", 0, 128))
         cp(v("OFu"), v("q3", 256, 264))
         sca(v("CW"), v("OFu"), v("C1"))
         ts(v("EX"), v("JW"), v("q3", 264, 265), A.is_ge, 4096.0, A.mult)
         scan(v("CC"), v("CW", 0, 512), v("Z", 0, 512), A.max)
-        mm(wrap(v("q3", 288, 320), "RD0", "CC", 0, 512))
+        mm(wrap(v("q3", 288, 320), "R1", "CC", 0, 512))
         cp(v("CLu"), v("q3", 288, 320))
         for lo, hi, b in ((0, FIRST, "q5"), (FIRST, 512, "q3")):
             a, z = lo // 16, hi // 16
@@ -746,12 +794,17 @@ def rank_program(g, core, T, topo):
         for k in range(nch):
             sgat(tile("sg", k), v("SG"), ch("Ku", k))
         ts(v("KF"), v("Ku"), 1023.0, A.min, -1.0 / 2048, A.mult)
-        ts(v("PM"), v("Ku"), 1024.0, A.is_ge, 4194304.0, A.mult)
+        ts(v("PM"), v("Ku"), 1024.0, A.is_ge, 100663296.0, A.mult)
         gat(v("Wu"), v("WI" if t == 0 else "WD"), v("Lu"))
         bias[0] = 20.0
-        cp(v("Wf"), v("Wu"))
-        mm([(v("q2"), v("ID"), v("JB")), (v("q2"), v("IDK"), v("KF")), (v("q2"), v("ID"), v("Wf"))], last=False)
+        gcp(v("Wf"), v("Wu"))
         bias[0] = 0.0
+
+        mm([(v("q2"), v(l), v(r)) for l, r in (("ID22", "JB"), ("IDK", "KF"), ("ID", "Wf"))[t // 2:]], last=False)
+
+        def ft(k, other):
+            return ch("FT", k, 512 * other)
+
         hi = lambda k: v("HI", 32 * k, 32 * k + 32)
         ts(hi(1), v("HY", 32, 64), -1600.0, A.add)
         bits(hi(2), hi(1), 4, 1023)
@@ -763,45 +816,61 @@ def rank_program(g, core, T, topo):
         for k in range(nch):
             b, n = banks[k], CH[k + 1] - CH[k]
             e = v(b, 0, n)
-            pick(TYP[t][k])(tile("hg", k), v("TB"), ch("Wu", k))
+            cut = min(n, SHARE[t]) if TYP[t][k] == "V" else 0
+            for f, lo, hi_ in ((gat, 0, cut), (sgat, cut, n)):
+                if lo < hi_:
+                    hold[:] = [tile("sg", SIGS)] if f is sgat else []
+                    f(v("hg%d" % (k & 1), 16 * lo, 16 * hi_), v("TB"), v("Wu", CH[k] + lo, CH[k] + hi_))
+            del hold[:]
             gtt(tile("mm", k), v("X"), ch("Wu", k), tile("sg", k), A.max)
             ends = [part("RX", "hg", k), part("R2", "mm", k)]
-            mms(part("RN", "sg", k) + [(e, v("ID"), ch("KF", k)), (e, v("ID24"), ch("PM", k))], *(ends if TYP[t][k] == "V" else ends[::-1]))
+            mms(part("RN", "sg", k), [(e, v("ID"), ch("KF", k)), (e, v("ID"), ch("PM", k))], *(ends if TYP[t][k] == "V" else ends[::-1]))
             bias[0] = SMALL
             cp(v("RD", 0, n), e)
-            tt(ch("FT", k, 512), e, v("RD", 0, n), A.not_equal)
-            mm([(v(b, 256, 256 + n), v("ZT"), ch("FT", k, 512))])
+            tt(ft(k, 1), e, v("RD", 0, n), A.not_equal)
+            mm([(v(b, 256, 256 + n), v("ZT"), ft(k, 1))])
             ts(v("GA", 0, n), v("RD", 0, n), v("thB", 1, 2), A.is_gt)
-            tt(ch("FT", k), ch("FT", k, 512), v("GA", 0, n), A.mult)
-            act(ch("FO", k), v(b, 256, 256 + n), F.Relu, scale=8388608.0)
-            mm([(ch("q2", k), v("IDF"), ch("FT", k)), (ch("q2", k), v("ID"), ch("FO", k))], first=False, last=k == nch - 1)
+            tt(ft(k, 0), ft(k, 1), v("GA", 0, n), A.mult)
+            act(ch("FO", k), v(b, 256, 256 + n), F.Relu, scale=16777216.0)
+            mm([(ch("q2", k), v("IDF"), ft(k, 0)), (ch("q2", k), v("ID"), ch("FO", k))], first=False, last=k == nch - 1)
             bias[0] = 0.0
-        act(v("PAY"), v("q2"))
 
     def post(t):
-        n_, much, some = v("q3", 0, 32), v("RP", 0, 32), v("RP", 32, 64)
+        rp = lambda k, n=1: v("RP", 32 * k, 32 * (k + n))
+        lw = lambda k, n=1: v("LW", 32 * k, 32 * (k + n))
         dl = lambda k: v("DL", 32 * k, 32 * k + 32)
+        n_, much, some = v("q3", 0, 32), rp(0), rp(1)
+        act(v("PAY"), v("q2"))
         mm(wrap(v("q3", 0, 64), "R1", "FT", 0, 1024))
-        ts(v("RP", 32, 96), v("q3", 0, 64), 0.5, A.is_gt)
+        ts(rp(1, 2), v("q3", 0, 64), 0.5, A.is_gt)
         ts(much, n_, 3.5, A.is_gt)
-        mm([(v("q5", 0, 64), v("BO"), v("RP", 32, 96)), (v("q5", 0, 64), v("NBO"), v("RP", 0, 64))])
-        mm([(v("q5", 64, 128), v("BO"), v("SC")), (v("q5", 64, 128), v("LPB"), v("RP", 32, 96)), (v("q5", 64, 128), v("NLP"), v("RP", 0, 64))])
+        mm([(v("q5", 0, 64), v(l), rp(k, 2)) for l, k in (("BO", 1), ("NBO", 0), ("LPB", 1), ("NLP", 0))]
+           + [(v("q5", 32 * h + 1, 32 * h + 32), v(l), v("RP", 32 * (h + k), 32 * (h + k) + 31)) for h in (0, 1) for l, k in (("NLP", 1), ("LPB", 0))])
         tt(dl(0), n_, v("HF", 0, 32), A.is_ge)
         tt(dl(2), n_, v("HI", 160, 192), A.add)
-        scan(v("LW", 0, 64), v("RM"), v("q5", 0, 64), A.mult)
-        tt(v("LW", 64, 128), v("q5", 64, 128), v("LW", 0, 64), A.add)
-        tt(v("LW", 128, 160), v("LW", 64, 96), v("LW", 96, 128), A.min)
-        tt(v("LW", 160, 192), v("LW", 128, 160), v("JD"), A.min)
-        cp(v("PFu"), v("LW", 160, 192))
+        for k in (0, 1):
+            scan(lw(2 + k), v("q5", 32 * k, 32 * k + 32), v("ZF", 0, 32), A.add, 4095.0 + 512 * k)
+        tt(lw(4), lw(2), lw(3), A.min)
+        tt(lw(5), lw(4), v("JD"), A.min)
+        cp(v("PFu"), lw(5))
         tt(dl(1), v("HF", 32, 64), dl(0), A.subtract)
-        tt(dl(3), dl(1), much, A.mult)
+        act(dl(5), much, scale=32.0)
+        act(dl(6), some, scale=8192.0)
         tt(dl(4), dl(2), much, A.mult)
+        tt(dl(3), dl(1), dl(5), A.mult)
+        if t == 2:
+            bias[0] = LAST
+            sca(v("TBS"), v("PFu"), v("TBL", 0, 512))
+            candidates()
+            hold.append(v("BU", 128, 256))
+            bias[0] = 0.0
         sca(v("P1W"), v("PFu"), v("PAY"))
+        del hold[:]
         mms([(v("q4"), v("X2D"), v("TBL", 0, 512))],
-            [(v("q4", i, 512, 16), v(U, 128 * i, 128 * i + 128), d) for U, d in (("UG", some), ("UH", dl(3)), ("UL", dl(4))) for i in range(16)])
+            [(v("q4", i, 512, 16), v("UN", 16 + 128 * i - r, 144 + 128 * i - r), dl(k)) for r, k in ((1, 4), (2, 6), (0, 3)) for i in range(16)])
         act(v("TBn"), v("q4"))
         if t < 2:
-            mm([(v("q2", 0, 32), v("ON"), some), (v("q2", 0, 32), v("ONS"), v("EX"))])
+            mm([(v("q2", 0, 32), v("ONS"), v("EX")), (v("q2", 0, 32), v("ON"), some)])
             act(v("BS"), v("q2", 0, 32), scale=-1.0, accum_out=v("thB", 2, 3))
             ts(v("CN", 0, 1), v("thB", 2, 3), 4096.0, A.add)
             bits(v("CN", 1, 2), v("CN", 0, 1), 0, 255)
@@ -811,25 +880,28 @@ def rank_program(g, core, T, topo):
         bits(v("AI", 64, 128), v("AI", 0, 64), 0, 4095)
         cp(v("AH", 0, 64), v("AI", 64, 128))
         cp(v("BI", 0, 128), v("P1W", 0, 128))
-        bits(v("BI", 128, 256), v("BI", 0, 128), 22, 1)
-        ts(v("AH", 64, 192), v("BI", 128, 256), v("PW", 48, 49), A.mult)
+        direct = t == 2
+        if not direct:
+            bits(v("BI", 128, 256), v("BI", 0, 128), 22, 1)
+            ts(v("AH", 64, 192), v("BI", 128, 256), v("PW", 48, 49), A.mult)
         bias[0] = 0.0
         to = v("q5", 128, 132)
-        mm(wrap(v("q5", 128, 140), "R1", "AH", 0, 192))
-        mm([(v("q3", 64, 128), v("B128"), v("AH", 0, 64)), (v("q3", 64, 128), v("BQ0"), v("C1", 0, 64))])
+        mm(wrap(to, "R1", "AH", 0, 64) if direct else wrap(v("q5", 128, 140), "R1", "AH", 0, 192))
+        mm([(v("q3", 64, 128), v("B128"), v("AH", 0, 64)), (v("q3", 64, 128), v("BO"), v("C1", 0, 64))])
         act(v("AF", 256, 260), to, F.Identity, bias=0.5, scale=-128.0)
         bits(v("AI", 128, 192), v("AI", 0, 64), 17, 31)
         bits(v("AI", 192, 256), v("AI", 0, 64), 12, 31)
         cp(v("AH", 192, 320), v("AI", 128, 256))
         cp(v("AU", 0, 4), to)
-        cp(v("BU", 0, 8), v("q5", 132, 140))
+        if not direct:
+            cp(v("BU", 0, 8), v("q5", 132, 140))
         sgat(v("AB", 0, 64), v("TS"), v("AU", 0, 4))
         sca(v("TB"), v("Lu"), v("TBn"))
         for c in range(4):
             act(v("AF", 64 * c, 64 * c + 64), v("q3", 64, 128), F.Abs, bias=v("AF", 256 + c, 257 + c))
         for c in range(4):
             act(v("AF", 288, 352), v("AF", 64 * c, 64 * c + 64), F.Relu, bias=v("S4", c, c + 1), scale=-4096.0, accum_out=v("AF", 260 + c, 261 + c))
-        mm([(v("q4", 0, 64), v("D0"), v("AH", 192, 256)), (v("q4", 0, 64), v("D1"), v("AH", 256, 320)), (v("q4", 0, 64), v("K34"), v("AB", 0, 64))])
+        mm([(v("q4", 0, 64), win("R1", 0), v("AH", 192, 256)), (v("q4", 0, 64), win("R1", 1), v("AH", 256, 320)), (v("q4", 0, 64), v("K34"), v("AB", 0, 64))])
         act(v("AB", 64, 128), v("q4", 0, 64), F.Identity, bias=col["b2"])
         tt(v("AF", 268, 272), v("AF", 260, 264), v("W4"), A.min)
         tt(v("AF", 272, 276), to, v("AF", 268, 272), A.max)
@@ -840,30 +912,34 @@ def rank_program(g, core, T, topo):
             send(5 + t, served(2 + t), v("FI%d" % (t + 1)), v("FL%d" % (t + 1)))
             arrive(5 + t, v("FI%d" % (t + 1)), 5 + t, 4.0)
 
+    def candidates():
+        mm([(v("q6", 128, 256), v("CWM"), v("TBS", 0, 128))])
+        mm(wrap(v("q7", 272, 280), "RO", "TBS", 0, 128))
+        cp(v("BI", 384, 512), v("q6", 128, 256))
+        cp(v("BU", 8, 16), v("q7", 272, 280))
+        sgat(v("LX"), v("X"), v("BU", 8, 16))
+        bits(v("BI", 512, 640), v("BI", 384, 512), 0, 2047)
+        cp(v("BU", 128, 256), v("BI", 512, 640))
+
     def repairs(t):
         bi = lambda k: v("BI", 128 * k, 128 * k + 128)
         bf = lambda lo, hi: v("BF2", lo, hi)
         sm = lambda k: v("SM", 8 * k, 8 * k + 8)
         dw = "DW%d" % t
-        sgat(v("TBS"), v("TBL"), v("BU", 0, 8))
-        mm([(v("q6", 128, 256), v("CWM"), v("TBS"))])
-        mm(wrap(v("q7", 272, 280), "RO", "TBS", 0, 128))
-        cp(bi(3), v("q6", 128, 256))
-        cp(v("BU", 8, 16), v("q7", 272, 280))
-        sgat(v("LX"), v("X"), v("BU", 8, 16))
-        bits(bi(4), bi(3), 0, 2047)
-        cp(v("BU", 128, 256), bi(4))
+        if t < 2:
+            sgat(v("TBS", 0, 128), v("TBL"), v("BU", 0, 8))
+            candidates()
         for k, c in enumerate(("rb", "rs")):
-            act(v("T3", 128 * k, 128 * k + 128), v("TBS"), scale=col[c])
+            act(v("T3", 128 * k, 128 * k + 128), v("TBS", 0, 128), scale=col[c])
         mm(wrap(v("q7", 280, 296), "R1", "T3", 0, 256))
         act(v("WB"), v("q7", 272, 296))
-        bits(bi(2), bi(0), 11, 1)
-        cp(v("FB"), bi(2))
+        bits(bi(2), bi(0), 0, 2048)
+        ts(v("FB"), bi(2), -2048.0, A.add)
         for h in (0, 1):
             pick(CAND[t][h])(v("mm0", 1024 * h, 1024 * h + 1024), v("XE%d" % t), v("BU", 128 + 64 * h, 192 + 64 * h))
         for h in (0, 1):
             for b in (0, 1):
-                qb, lo = "q%d" % b, 1024 * h + 512 * b
+                qb, lo = ("q0", "q1", "q2", "q6")[2 * h + b], 1024 * h + 512 * b
                 lst = []
                 for m in range(8):
                     o = v(qb, 64 * m, 64 * m + 64)
@@ -874,6 +950,7 @@ def rank_program(g, core, T, topo):
             mms([(o, v("MK12"), v("TBS", 64 * h, 64 * h + 64))] + [(o, win("R16", m), v("hg0", 1024 * h + 64 * m, 1024 * h + 64 * m + 64)) for m in range(8)],
                 [(o, win("R16", m), v("hg0", 1024 * h + 64 * m, 1024 * h + 64 * m + 64)) for m in range(8, 16)])
         sgat(v("OLD"), v("WD"), v("BU", 8, 16))
+        tt(bf(384, 512), v("OLD"), bi(2), A.subtract)
         changes(t)
         turn(bf(0, 128), v("q7", 0, 128))
         lo, n, o = 0, 128, 128
@@ -894,17 +971,16 @@ def rank_program(g, core, T, topo):
         tt(sm(3), sm(2), v("WB", 8, 16), A.add)
         bits(sm(4), sm(3), 0, 2047)
         cp(v("BU", 24, 32), sm(4))
-        gtt(bf(256, 384), v("WE"), v("BU", 24, 32), v("OLD"), A.subtract)
+        gtt(bf(256, 384), v("WE"), v("BU", 24, 32), v("FB"), A.add)
         tt(bf(248, 256), v("q7", 264, 272), v("W8"), A.mult)
         tt(v(dw, 128, 136), v("WB", 0, 8), bf(248, 256), A.max)
         cp(v("BU", 16, 24), v(dw, 128, 136))
-        tt(bf(384, 512), bf(256, 384), v("FB"), A.mult)
         if t == 2:
-            op("V", lambda: g.vector.tensor_tensor(ind(v("WD"), v("BU", 16, 24)), ap(bf(384, 512)), ap(v("OLD")), A.add),
-               [bf(384, 512), v("OLD"), v("BU", 16, 24)], [v("WD")], ew(128, 3.8))
+            op("V", lambda: g.vector.tensor_tensor(ind(v("WD"), v("BU", 16, 24)), ap(bf(256, 384)), ap(bf(384, 512)), A.max),
+               [bf(256, 512), v("BU", 16, 24)], [v("WD")], ew(128, SCATTER))
             fin.append(dma("Y", None, v("WD", 0, 2048), o=T.ym[:], lat=6.0))
             return
-        tt(v(dw, 0, 128), bf(384, 512), v("OLD"), A.add)
+        tt(v(dw, 0, 128), bf(256, 384), bf(384, 512), A.max)
         sca(v("WD"), v("BU", 16, 24), v(dw, 0, 128))
         for t2 in range(t + 1, 3):
             slot = 6 + t + t2
@@ -912,7 +988,14 @@ def rank_program(g, core, T, topo):
             arrive(slot, v("Di%d%d" % (t, t2)), slot, 4.0)
 
     def helper(t):
-        gcp(v("WE", 0, 2048), v("WH%d" % t))
+        if t == 0:
+            gcp(v("WD", 0, 2048), v("W16"))
+            gcp(v("WD", 2048, 2560), v("Z", 0, 512))
+            gcp(v("WE", 2048, 2176), v("Z", 0, 128))
+        if t < 2:
+            gcp(v("CW", 0, 512), v("Z", 0, 512))
+        for h in (1, 0):
+            gcp(v("WE", *piece(2 * t + 1, h)), v("WH%d" % t, *piece(2 * t + 1, h)))
         hold.append(v("FT", CH[1], CH[2]))
         dma("Y", row("XE%d" % t, 2), v("FI%d" % t))
         hold.pop()
@@ -933,13 +1016,12 @@ def rank_program(g, core, T, topo):
         tt(v("OUT", 0, 128), v("q3", 0, 128), v("HW"), A.add)
         fin.append(dma("Y", None, v("OUT", 0, 128), o=T.yh[:]))
 
-    late_constants()
     lanes(0)
+    tables_out()
+    late_constants()
     fetch(0)
     for t in range(3):
-        slots_reset()
-        if t < 2:
-            gcp(v("CW", 0, 512), v("Z", 0, 512))
+        slots_reset(t)
         check(t)
         helper(t)
         post(t)

@@ -2,10 +2,13 @@ import math
 from concourse.bass import DstId, RemoteDMATransfer
 from concourse.mybir import AluOpType as A, AxisListType, ActivationFunctionType as F
 
-CH = (0, 160, 320, 448, 512)
-BANKS = ("q5", "q3", "q0", "q1")
-FIRST = 160
-TYP = ("SVSS", "SVSS", "SVSS")
+CH = (0, 128, 256, 384, 448, 512)
+BANKS = ("q5", "q3", "q0", "q1", "q6")
+TURNED = 3
+SPLIT = (2, 1, 1, 1, 1)
+MAGIC = 12582912.0
+FIRST = 128
+TYP = ("SSSSS", "SSSSS", "SSSSS")
 SHARE = (128, 112, 112)
 SIGS = 2
 CAND = ("SS", "SS", "SS")
@@ -13,11 +16,14 @@ TBLQ = "S"
 LOADS = ("X", "RI32", "SG", "WI")
 PACE, CUT = 1, 896
 LATE, LAST, SMALL, PATIENCE, WAKE = 2.0, 3.0, 0.0, 0.5, 0.18
-GATHER, SCATTER, MATMUL = 1.56, 3.8, 0.62
-SPEEDS = ((1.1e-3, 1.15, 2.5), (1.0e-3, 1.55, 3.8), (1.0e-3, 2.0, 5.0))
+SOON, LAG, XPB, ENDS = 5.0, 2, "q1", "VVV"
+GATHER, SCATTER, MATMUL = 1.56, 3.8, 0.55
+SPEEDS = ((.85e-3, 1.1, 2.0), (.9e-3, 1.5, 3.8), (1.15e-3, 1.9, 5.0))
 PLAN = ((1.1e-3, 1.08, 2.5), (0.9e-3, 1.45, 3.5), (1.0e-3, 2.0, 5.0)) + ((0.95e-3, 1.56, 3.8), (0.95e-3, 1.3, 3.0), (1.0e-3, 1.7, 4.0))
-PASSES, STEPS, STARTS = 3, 2000, 2
-ORDER, EST = [], []
+PASSES, STEPS, STARTS = 3, 200, 1
+TUNE = ((.85e-3, 1.1, 2.0, .55, .13, .03), (.9e-3, 1.5, 3.8, .5, .15, .02), (1.0e-3, 1.25, 4.5, .62, .2, .02), (1.15e-3, 1.9, 4.5, .5, .15, .04))
+ROUNDS, TRIES, LOSS, BAN, NEAR, GAIN = 5000, 10, 0.03, 8, 0.02, 0.3
+ORDER, EST, LOG = [], [], []
 SCRATCH = {}
 SEMAPHORES = ["cV", "cS", "cP", "cG"]
 
@@ -36,29 +42,31 @@ def _buf(name, cols, dtype, where="sbuf", pool=None):
 
 
 for _n in ("BO", "NBO", "LT", "EQH", "GT", "ID", "NI", "LPB", "NLP", "ZT", "X2D", "K34", "B128", "IDK",
-           "IDF", "ID22", "IDQ", "ON", "ONS", "CWM", "MK12", "C1"):
+           "IDF", "IDQ", "ON", "ONS", "CWM", "MK12", "C1", "ID5", "ID8", "ID10", "ID14", "ID15", "IDN"):
     _buf(_n, 128, BF, pool="PB")
-for _n in ("R1", "RI", "RH", "RX", "R2", "RN", "RU", "RO", "R16"):
+for _n in ("R1", "RI", "RH", "RX", "R2", "RN", "RU", "RO", "R0", "RT"):
     _buf(_n, 144, BF, pool="PB")
-for _n, _c in (("RH3", 32), ("DFB", 128), ("UT", 128), ("SWB", 512), ("KIB", 128)):
+for _n, _c in (("WS", 24), ("WK", 128), ("THD", 256), ("TH2", 1), ("RH3", 32), ("DFB", 128), ("UT", 128), ("SWB", 512), ("KIB", 128)):
     _buf(_n, _c, BF, pool="PB")
 for _n, _c in (("COLS", 128), ("QH", 16), ("CR", 144), ("MG", 128), ("MI", 128), ("JW", 32), ("JC", 32), ("JD", 32), ("J16", 32),
-               ("W8", 8), ("W4", 4), ("S4", 4), ("K3", 3), ("DF", 192), ("ZF", 128), ("TMP", 128)):
+               ("W8", 8), ("W4", 4), ("S4", 4), ("K3", 3), ("DF", 192), ("ZF", 128), ("TMP", 128), ("KB", 128),
+               ("WM", 24), ("IDW", 128)):
     _buf(_n, _c, FP, pool="PF")
 for _n, _c, _d in (
         ("X", 2064, BF), ("WD", 2560, FP), ("WI", 2560, I32), ("W16", 2048, H16), ("RI32", 1032, I32), ("SG", 1040, BF), ("TB", 2688, BF),
-        ("Z", 640, BF), ("UN", 2064, BF), ("PW", 64, FP), ("JI", 512, FP), ("JB", 512, BF),
+        ("Z", 640, BF), ("UN", 2064, BF), ("PW", 64, FP), ("JI", 512, FP), ("JB", 512, BF), ("JF", 512, FP), ("L1", 64, BF),
         ("hyb", 128, I32), ("vfb", 128, I32), ("thi", 1, I32), ("KI", 4, I32), ("ST", 1024, BF), ("SI", 1280, I32),
         ("NW", 128, BF), ("NT", 128, BF), ("VB", 256, H16), ("HW", 128, FP), ("TY", 512, H16), ("POS", 128, FP), ("TTB", 384, BF), ("OFu", 8, U16),
         ("CW", 4224, BF), ("CC", 512, BF), ("CLu", 32, U16), ("OH", 512, BF), ("EX", 32, BF), ("Lf", 32, FP), ("Lu", 32, U16),
         ("TBL", 528, BF), ("Wu", 512, U16), ("Wf", 512, H16), ("Ku", 512, U16), ("KF", 512, H16), ("PM", 512, BF), ("STu", 32, U16),
-        ("HI", 256, I32), ("HF", 64, FP), ("HY", 64, FP), ("TS", 2688, BF), ("FT", 1024, BF), ("FO", 512, BF), ("RD", 256, I32), ("GA", 256, BF), ("PAY", 512, FP),
-        ("sig", 8192, BF), ("mm0", 2560, BF), ("mm1", 2560, BF), ("hg0", 2560, BF), ("hg1", 2560, BF),
+        ("HI", 256, I32), ("HF", 64, FP), ("HY", 64, FP), ("TS", 2688, BF), ("FT", 1024, BF), ("FO", 512, BF), ("RD", 256, I32), ("GA", 512, BF), ("PAY", 512, FP),
+        ("sig", 8192, BF), ("mm0", 2048, BF), ("mm1", 2048, BF), ("hg0", 2048, BF), ("hg1", 2048, BF),
+        ("XP", 2048, FP), ("mf0", 2048, FP), ("mf1", 2048, FP), ("RR", 1152, BF), ("AA", 1152, BF), ("XB", 128, BF), ("XR", 256, FP),
         ("RP", 96, BF), ("LW", 192, FP), ("PFu", 32, U16), ("DL", 224, BF), ("P1W", 1536, FP), ("TBn", 512, BF),
-        ("thB", 4, FP), ("CN", 4, I32), ("BS", 32, FP),
-        ("AI", 256, I32), ("AH", 320, H16), ("T3", 384, BF), ("WB", 24, FP), ("MB", 16, BF), ("Li", 64, I32), ("AF", 352, FP), ("AB", 128, BF), ("AU", 8, U16),
-        ("BI", 640, I32), ("FB", 128, BF), ("TBS", 1536, BF), ("LX", 128, BF), ("OLD", 128, FP), ("BF2", 512, FP), ("SM", 64, I32),
-        ("BU", 256, U16), ("HU", 8, U16), ("WE", 2176, FP), ("OUT", 256, FP),
+        ("thB", 5, FP), ("AS", 256, FP), ("CN", 4, I32), ("BS", 32, FP),
+        ("AI", 256, I32), ("AH", 320, H16), ("WB", 8, FP), ("MB", 8, H16), ("AF", 352, FP), ("AB", 128, BF), ("AU", 16, U16),
+        ("BI", 768, I32), ("TBS", 1536, BF), ("LX", 128, BF), ("BF2", 512, FP), ("CH", 128, H16), ("CT", 128, H16), ("DC", 128, H16),
+        ("NQ", 128, H16), ("UU", 128, H16), ("BU", 256, U16), ("HU", 8, U16), ("WE", 2560, FP), ("OUT", 256, FP),
         ("DW0", 136, FP), ("DW1", 136, FP), ("DW2", 136, FP)):
     _buf(_n, _c, _d)
 for _t in range(3):
@@ -423,6 +431,134 @@ def rank_program(g, core, T, topo):
             EST.append((math.prod(x[0] for x in now) ** (1 / len(now)), left))
             return math.prod(x[0] for x in now), list(order)
 
+        def refine(order):
+            qs = [c["e"] for c in prog]
+            lat = [c["lat"] for c in prog]
+            ms_ = []
+            for cyc, ga, sc, pe, wake, fix in TUNE:
+                cs = []
+                for c in prog:
+                    c = c["cost"]
+                    if isinstance(c, tuple):
+                        c = (c[0] * cyc * pe if c[1] == MATMUL else 0.05 + c[0] * cyc * (ga if c[1] == GATHER else sc) if c[1] in (GATHER, SCATTER)
+                             else fix + max(64, c[0] * c[1]) * cyc)
+                    cs.append(c)
+                pl = [[(p, x and x - WAKE + wake) for p, x in ps.items()] for ps in pred]
+                sl = [[] for _ in range(n)]
+                for k in range(n):
+                    for p, x in pl[k]:
+                        sl[p].append((k, x))
+                ms_.append((cs, pl, sl))
+
+            def full(order):
+                last, before, behind = {}, [-1] * n, [-1] * n
+                for k in order:
+                    e = qs[k]
+                    if e != "R":
+                        j = last.get(e, -1)
+                        before[k] = j
+                        if j >= 0:
+                            behind[j] = k
+                        last[e] = k
+                out, moves, val = [], [], 1.0
+                for cs, pl, sl in ms_:
+                    done, tail = [0.0] * (n + 1), [0.0] * (n + 1)
+                    for k in order:
+                        t0 = done[before[k]]
+                        for p, x in pl[k]:
+                            if done[p] + x > t0:
+                                t0 = done[p] + x
+                        done[k] = t0 + cs[k]
+                    for k in reversed(order):
+                        t0 = max(lat[k], tail[behind[k]])
+                        for s, x in sl[k]:
+                            if tail[s] + x > t0:
+                                t0 = tail[s] + x
+                        tail[k] = t0 + cs[k]
+                    end = max(tail)
+                    val *= end
+                    moves += [(before[k], k) for k in order if before[k] >= 0 and done[before[k]] + tail[k] > end - NEAR]
+                    out.append((done, tail, end))
+                return val, out, moves, before, behind
+
+            def moved(order, at, j, k, late):
+                mid = order[at[j]:at[k] + 1]
+                if late:
+                    need = {j}
+                    for x in mid:
+                        if x in need:
+                            need.update(succ[x])
+                    return None if k in need else [x for x in mid if x not in need] + [x for x in mid if x in need]
+                need = {k}
+                for x in reversed(mid):
+                    if x in need:
+                        need.update(pred[x])
+                return None if j in need else [x for x in mid if x in need] + [x for x in mid if x not in need]
+
+            def judge(old, mid, out, before, behind):
+                head, end_ = {}, {}
+                for x in old:
+                    head.setdefault(qs[x], before[x])
+                    end_[qs[x]] = behind[x]
+                val = 1.0
+                for (cs, pl, sl), (done, tail, end) in zip(ms_, out):
+                    d, free = {}, {e: done[x] for e, x in head.items()}
+                    for k in mid:
+                        t0 = free[qs[k]]
+                        for p, x in pl[k]:
+                            t1 = (d[p] if p in d else done[p]) + x
+                            if t1 > t0:
+                                t0 = t1
+                        d[k] = t0 + cs[k]
+                        if qs[k] != "R":
+                            free[qs[k]] = d[k]
+                    tl, nxt, top = {}, {e: tail[x] for e, x in end_.items()}, 0.0
+                    for k in reversed(mid):
+                        t0 = max(lat[k], nxt[qs[k]])
+                        for s, x in sl[k]:
+                            t1 = (tl[s] if s in tl else tail[s]) + x
+                            if t1 > t0:
+                                t0 = t1
+                        if d[k] + t0 > top:
+                            top = d[k] + t0
+                        tl[k] = t0 + cs[k]
+                        if qs[k] != "R":
+                            nxt[qs[k]] = tl[k]
+                    val *= max(top, end - GAIN)
+                return val
+
+            seed, order = 1, list(order)
+            val, out, moves, before, behind = full(order)
+            best, banned = (val, list(order)), {}
+            for step in range(ROUNDS):
+                at = [0] * n
+                for i, k in enumerate(order):
+                    at[k] = i
+                pick_ = None
+                for _ in range(TRIES):
+                    seed = (seed * 1103515245 + 12345) % 2147483648
+                    j, k = moves[(seed >> 8) % len(moves)]
+                    if banned.get((j, k), -1) > step or at[k] - at[j] > 150:
+                        continue
+                    mid = moved(order, at, j, k, seed >> 7 & 1)
+                    if mid is not None:
+                        x = judge(order[at[j]:at[k] + 1], mid, out, before, behind)
+                        if pick_ is None or x < pick_[0]:
+                            pick_ = (x, j, k, mid)
+                if pick_ is None or pick_[0] > val * (1 + LOSS * (1 - step / ROUNDS)):
+                    continue
+                _, j, k, mid = pick_
+                order[at[j]:at[k] + 1] = mid
+                banned[(k, j)] = step + BAN
+                val, out, moves, before, behind = full(order)
+                LOG.append((step, pick_[0] ** .25, val ** .25))
+                if val < best[0]:
+                    best = (val, list(order))
+            EST.extend((x[2], 0) for x in full(best[1])[1])
+            done, tail, end = full(best[1])[1][1]
+            LOG[:] = [(done[k] - ms_[1][0][k], ms_[1][0][k], qs[k], (prog[k]["w"] + prog[k]["r"])[0][:3], end - (done[k] - ms_[1][0][k] + tail[k])) for k in best[1]]
+            return best[1]
+
         if not ORDER:
             orders = []
             for speed in PLAN:
@@ -443,7 +579,7 @@ def rank_program(g, core, T, topo):
                 costs.append(list(cost))
             some = sorted(range(len(orders)), key=lambda i: total[i])
             some = [i for j, i in enumerate(some) if i // (PASSES + 1) not in [x // (PASSES + 1) for x in some[:j]]][:STARTS]
-            ORDER[:] = min(polish(orders[i], costs) for i in some)[1]
+            ORDER[:] = refine(min(polish(orders[i], costs) for i in some)[1])
         for k in ORDER:
             prog[k]["emit"]()
 
@@ -500,10 +636,10 @@ def rank_program(g, core, T, topo):
     def gtt(o, win, off, b, f):
         op("V", lambda: g.vector.tensor_tensor(ap(o), ind(win, off), ap(b), f), [win, off, b], [o], ew(wid(o), 1.56))
 
-    def scan(o, a, z, f, first=0.0):
+    def scan(o, a, z, f, first=0.0, f2=A.add):
         col_ = isinstance(first, tuple)
-        op("V", lambda: g.vector.tensor_tensor_scan(ap(o), ap(a), ap(z), ap(first) if col_ else first, f, A.add), [a, z] + [first] * col_, [o],
-           ew(wid(o), half(o, a)))
+        op("V", lambda: g.vector.tensor_tensor_scan(ap(o), ap(a), ap(z), ap(first) if col_ else first, f, f2), [a, z] + [first] * col_, [o],
+           ew(wid(o), half(o, a, z)))
 
     def act(o, a, func=F.Copy, bias=None, scale=None, accum_out=None):
         kw = {}
@@ -531,7 +667,7 @@ def rank_program(g, core, T, topo):
             op("G", lambda: g.iota(ap(o), pattern, base, ch, allow_small_or_imprecise_dtypes=True), [], [o], 0.13 + 1.9e-3 * wid(o))
 
     def gcp(o, a):
-        op("G", lambda: g.affine_select(ap(o), ap(a), [[0, wid(o)]], A.is_equal, 0.0, 0, 0), [a], [o, GQ], 0.17 + 1.9e-3 * wid(o))
+        op("G", lambda: g.affine_select(ap(o), ap(a), [[0, wid(o)]], A.is_equal, 0.0, 0, 0), [a], [o], 0.17 + 1.9e-3 * wid(o))
 
     def win(R, i):
         return v(R, 15 - i, 143 - i)
@@ -553,7 +689,8 @@ def rank_program(g, core, T, topo):
         dma("SY"[k & 1], v(name, 0, n), None, i=src[:], lat=at)
     bias[0] = 10.0
     dma("Y", v("FL0"), None, i=T.xs[2:128:16, :], lat=at)
-    dma("S", v("thi"), None, i=T.th[:], lat=at)
+    dma("S", v("thi"), None, i=T.th[:], lat=3.0)
+    dma("S", v("XB"), None, i=T.xs[1:128:16, :], lat=3.0)
     bias[0] = 0.0
     hold.append(v("WI", 0, 2048))
     for t in (1, 2):
@@ -579,14 +716,11 @@ def rank_program(g, core, T, topo):
     def q(k):
         return v("QH", k, k + 1)
 
-    def weights(name, w):
-        last = None
+    def weights(name, w, rest=0.0):
+        last = float(rest)
         for r, x in w.items():
             c = newcol(name)
-            if last is None:
-                act(c, q(r), scale=float(x))
-            else:
-                act(c, q(r), F.Identity, bias=last, scale=float(x))
+            act(c, q(r), F.Identity, bias=last, scale=float(x - rest))
             last = c
         return last
 
@@ -624,7 +758,7 @@ def rank_program(g, core, T, topo):
     for k, (c_, m_) in enumerate(((kf, even), (kp, even), (km, odd), (kf, odd))):
         ts(v("SWB", 128 * k, 128 * k + 128), v("CR", 0, 128), c_, A.is_equal, m_, A.mult)
     act(v("JW"), v("J16"), F.Identity, bias=ki)
-    for name, n, a, b in (("JC", 32, 1.0, 2048.0), ("W8", 8, 1.0, 2048.0), ("JD", 32, 1.0, 1024.0), ("W4", 4, 2.0, 2560.0), ("S4", 4, 4096.0, 1024.0)):
+    for name, n, a, b in (("JC", 32, 1.0, 2048.0), ("JD", 32, 1.0, 1024.0), ("W4", 4, 2.0, 2560.0), ("S4", 4, 4096.0, 1024.0)):
         act(v(name), v("JW", 0, n), F.Identity, bias=b, scale=a)
     act(v("C1"), v("CR", 0, 128), scale=1 / 16)
     ts(v("PW", 0, 16), v("ZF", 0, 16), 2.0, A.add)
@@ -633,7 +767,7 @@ def rank_program(g, core, T, topo):
     op("V", lambda: g.vector.tensor_reduce(ap(v("PW", 48, 49)), ap(v("PW", 32, 48)), AxisListType.X, A.add), [v("PW", 32, 48)], [v("PW", 48, 49)])
     for name, c in (("RI", ki), ("RH", weights("h", {0: 32, 1: 1, 2: 0.25})),
                     ("RU", col["uw"]), ("RX", weights("sx", {0: 1 / 64, 1: 1 / 2048, 3: -64, 4: -1})), ("R2", 2.0), ("RN", -1.0),
-                    ("R16", 16.0), ("RO", weights("ro", {10: 128, 11: 16}))):
+                    ("RO", weights("ro", {10: 128, 11: 16}))):
         act(v(name, 0, 143), v("R1", 0, 143), scale=c)
     weights("rb", {8: 32, 9: 1})
     weights("rs", {5: 64, 6: 2, 12: 1})
@@ -677,15 +811,42 @@ def rank_program(g, core, T, topo):
     for k, r in enumerate((5, 6, 8, 9)):
         dma("Y", row("TB", r), v("ST", 512 + 128 * k, 640 + 128 * k))
     dma("Y", v("TS"), v("TB"), lat=4.0)
+    for h in (0, 1):
+        act(v("XP", 1024 * h, 1024 * h + 1024), v("X", 1024 * h, 1024 * h + 1024))
+    act(v("R0", 0, 143), v("R1", 0, 143), scale=weights("r0", {0: 32768, 1: 0}, 1))
+    mm([(v("q7", 0, 128), win("R0", b), v("X", 128 * b, 128 * b + 128)) for b in range(16)])
+    act(v("XR", 0, 128), v("q7", 0, 128), F.Identity, bias=32768.0)
+    dma("Y", row("XP", 0), v("XR", 0, 128), lat=3.0)
+    act(v("ID5"), v("ID"), scale=32.0)
+    act(v("ID14"), v("ID"), scale=16384.0)
+
+    def types_to_xp(t):
+        o = v(XPB if t else "q7", 384, 512)
+        part = [(o, win("RT", b), v("TB", 128 * b, 128 * b + 128)) for b in range(16)] if t else [(o, v("ID5"), v("ST", 0, 128)), (o, v("ID"), v("ST", 128, 256))]
+        part = [(o, v("ID14"), v("XB"))] + part
+        mms(*[part[k:k + 5] for k in range(0, len(part), 5)])
+        act(v("XR", 128, 256), o, F.Identity, bias=16384.0)
+        dma("Y", row("XP", 1), v("XR", 128, 256), lat=3.0)
+
+    types_to_xp(0)
+    for name, ws in (("WM", (({0: -1, 1: 0}, 2), ({0: 2.0 ** -15}, 0), ({1: 2.0 ** -14}, 0))), ("WS", (({0: 32768, 1: 0}, -1), ({0: -1}, 0), ({1: -1}, 0)))):
+        for k, (w, rest) in enumerate(ws):
+            act(v(name, 8 * k, 8 * k + 8), v("RH3", 8, 16), scale=col["r0"] if w is None else weights("w", w, rest))
+    for name, c in (("WK", 0.125), ("ID8", 256.0), ("ID15", 32768.0), ("IDN", -2.0 ** 36)):
+        act(v(name), v("ID"), scale=c)
+
+    def unwrap_table(k):
+        un, z = v("UN", 16 + 512 * k, 528 + 512 * k), v("Z", 0, 512)
+        op("G", lambda: g.affine_select(ap(un), ap(z), [[-1, 4], [-16, 8], [1000, 16]], A.not_equal, 1.0, -4 * k, 1), [z], [un], 1.15)
 
     def tables_out():
         hand_on(1, "X", 4.0)
         gcp(v("W16"), v("WI", 0, 2048))
         hand_on(3, "W16")
-        op("G", lambda: g.iota(ap(v("UN")), [[0, 2064]], 0, 0, allow_small_or_imprecise_dtypes=True), [], [v("UN"), GQ], 4.1)
         gadd(v("FL0"), row("TB", 2))
-        un = v("UN", 16, 2064)
-        op("G", lambda: g.affine_select(ap(un), ap(un), [[-1, 16], [-16, 8], [1000, 16]], A.not_equal, 1.0, 0, 1), [un], [un, GQ], 4.1)
+        gcp(v("UN", 0, 16), v("Z", 0, 16))
+        for k in range(4):
+            unwrap_table(k)
         send(0, served(1), v("FI0"), v("FL0"))
         arrive(0, v("FI0"), 0, 10.0)
         for k in range(6):
@@ -693,7 +854,7 @@ def rank_program(g, core, T, topo):
                 arrive(10 + 2 * k + h, v(("XE%d", "WH%d")[k & 1] % (k // 2), *piece(k, h)), 3, 10.0 + 12.0 * k)
 
     def late_constants():
-        for n_, src, c in (("NI", "ID", -1.0), ("IDK", "ID", -8388608.0), ("IDF", "ID", 2048.0), ("NBO", "BO", -1.0),
+        for n_, src, c in (("NI", "ID", -1.0), ("IDK", "ID", -8388608.0), ("IDF", "ID", -2048.0), ("NBO", "BO", -1.0),
                            ("B128", "BO", 128.0), ("NLP", "LPB", -1.0)):
             act(v(n_), v(src), scale=c)
         tt(v("ZT"), v("EQH"), v("LT"), A.subtract)
@@ -704,14 +865,31 @@ def rank_program(g, core, T, topo):
         act(v("ONS"), v("Z", 0, 128), F.Identity, bias=1.0 / 4096)
         act(v("CWM"), v("MI"), F.Identity, bias=col["rb"], scale=col["rs"])
         tt(v("CWM"), v("CWM"), v("BO"), A.mult)
-        act(v("MK12"), v("MI"), scale=q(12))
+        act(v("MK12"), v("MI"), scale=weights("m16", {12: 1 / 16}))
         tt(v("MK12"), v("MK12"), v("BO"), A.mult)
         act(v("DF", 0, 128), v("ZF"), F.Identity, bias=weights("df", {9: 1 << 22}))
-        act(v("DF", 128, 192), v("CR", 0, 64), F.Identity, bias=weights("df", {0: (1 << 23) + 2560}), scale=weights("d2", {0: 2}))
+        act(v("DF", 128, 192), v("CR", 0, 64), F.Identity, bias=weights("df", {0: (1 << 23) + 2048 + 2560}), scale=weights("d2", {0: 2}))
         weights("b2", {2: 8192})
         act(v("DFB"), v("Z", 0, 128), F.Identity, bias=col["tl"])
-        ts(v("thB", 0, 1), v("thi"), 0.5, A.add)
-        ts(v("thB", 1, 2), v("thi"), 0.5, A.add)
+        ts(v("thB", 0, 1), v("thi"), -2048.0, A.mult, -1024.0, A.add)
+        ts(v("thB", 1, 2), v("thi"), -2048.0, A.mult, -1024.0, A.add)
+        act(newcol("th"), v("thB", 0, 1), F.Identity, bias=-0.5, scale=-1 / 2048)
+        act(v("thB", 3, 4), v("thB", 1, 2), F.Identity, bias=col["th"], scale=1 / 2048)
+        act(v("thB", 2, 3), v("ZF", 0, 1))
+        act(v("IDW"), v("ID"))
+        act(v("TH2"), col["th"], scale=-1.0)
+        act(newcol("thh"), v("TH2"))
+        act(newcol("thl"), col["th"], F.Identity, bias=col["thh"])
+        act(v("THD", 0, 128), v("ID"), scale=col["thh"])
+        act(v("THD", 128, 256), v("NI"), scale=col["thl"])
+        act(v("RT", 0, 143), v("R1", 0, 143), scale=weights("rt", {0: 32, 1: 1}))
+        act(v("KB"), v("MI"), F.Relu, bias=1048576.0, scale=-1048576.0)
+        gcp(v("DC", 0, 16), v("Z", 0, 16))
+        iota(v("W8"), [[128, 4], [0, 2]], 6144, 4)
+        act(newcol("o64"), odd, scale=64.0)
+        act(newcol("g128"), kg, F.Identity, bias=col["o64"], scale=-64.0)
+        act(v("W8"), v("W8"), F.Identity, bias=col["g128"])
+        act(v("ID10"), v("ID"), scale=-1024.0)
         bias[0] = 12.0
         inv = v("PW", 56, 57)
         op("V", lambda: g.vector.reciprocal(ap(inv), ap(v("PW", 48, 49))), [v("PW", 48, 49)], [inv], 0.25)
@@ -719,7 +897,7 @@ def rank_program(g, core, T, topo):
         ts(v("SI", 0, 512), v("JI"), inv, A.mult, col["cut"], A.subtract)
         bits(v("SI", 0, 512), v("SI", 0, 512), 0, 1)
         gcp(v("JB"), v("SI", 0, 512))
-        act(v("ID22"), v("ID"), scale=4194304.0)
+        act(v("JF"), v("JB"), scale=4194304.0)
         bias[0] = 0.0
 
     def slots_reset(t):
@@ -765,12 +943,12 @@ def rank_program(g, core, T, topo):
             gat(v("Ku", lo, hi), v("RI32"), v("STu", a, z))
             act(v("HY", a, z), v(b, 320 + a, 320 + z))
             act(v("HY", 32 + a, 32 + z), v(b, 320 + a, 320 + z), F.Square, bias=col["c40"])
-        mm([(v("q4", 0, 32), v("ID"), v("EX"))] + wrap(v("q4", 0, 32), "RI", "OH", 0, 512))
-        ts(v("Li", 0, 32), v("CLu"), 16.0, A.mult, 16.0 * c0, A.add)
+        act(v("L1", 0, 32), v("q3", 288, 320), F.Identity, bias=16.0 * c0 - (1024 if t else 0), scale=16.0)
         if t:
-            bits(v("Li", 0, 32), v("Li", 0, 32), 0, 2047)
-        tt(v("Li", 32, 64), v("q4", 0, 32), v("Li", 0, 32), A.add)
-        tt(v("Lf"), v("Li", 32, 64), v("JC"), A.min)
+            act(v("L1", 32, 64), v("q3", 288, 320), F.Sign, bias=c0 - 127.5)
+        mm([(v("q4", 0, 32), v("ID"), v("EX")), (v("q4", 0, 32), v("ID"), v("L1", 0, 32))] + [(v("q4", 0, 32), v("ID10"), v("L1", 32, 64))] * (t > 0)
+           + wrap(v("q4", 0, 32), "RI", "OH", 0, 512))
+        tt(v("Lf"), v("q4", 0, 32), v("JC"), A.min)
         cp(v("Lu"), v("Lf"))
 
     def fetch(t):
@@ -792,7 +970,9 @@ def rank_program(g, core, T, topo):
             return [(v(banks[k], 0, CH[k + 1] - CH[k]), win(R, p), tile(x, k, p)) for p in range(16)]
 
         for k in range(nch):
-            sgat(tile("sg", k), v("SG"), ch("Ku", k))
+            cuts = [CH[k] + (CH[k + 1] - CH[k]) * j // SPLIT[k] for j in range(SPLIT[k] + 1)]
+            for lo, hi_ in zip(cuts, cuts[1:]):
+                sgat(v("sig", 16 * lo, 16 * hi_), v("SG"), v("Ku", lo, hi_))
         ts(v("KF"), v("Ku"), 1023.0, A.min, -1.0 / 2048, A.mult)
         ts(v("PM"), v("Ku"), 1024.0, A.is_ge, 100663296.0, A.mult)
         gat(v("Wu"), v("WI" if t == 0 else "WD"), v("Lu"))
@@ -800,7 +980,7 @@ def rank_program(g, core, T, topo):
         gcp(v("Wf"), v("Wu"))
         bias[0] = 0.0
 
-        mm([(v("q2"), v(l), v(r)) for l, r in (("ID22", "JB"), ("IDK", "KF"), ("ID", "Wf"))[t // 2:]], last=False)
+        mm([(v("q2"), v(l), v(r)) for l, r in (("IDK", "KF"), ("ID", "Wf"))], last=False)
 
         def ft(k, other):
             return ch("FT", k, 512 * other)
@@ -813,24 +993,68 @@ def rank_program(g, core, T, topo):
         ts(hi(4), hi(3), 5, A.arith_shift_right)
         bits(hi(5), hi(3), 0, 31)
         ts(v("HF", 32, 64), hi(4), 1.0 / 32, A.mult)
+        def after(k):
+            j = k - LAG
+            return [v("RR", 384 * j + 256, 384 * j + 384)] if 0 <= j < TURNED else []
+
+        def turned(k):
+            b, mf = banks[k], "mf%d" % (k & 1)
+            r = lambda j, n=1: v(b, 128 * j, 128 * (j + n))
+            u = lambda x, j, n=1: v(x, 384 * k + 128 * j, 384 * k + 128 * (j + n))
+            cuts = [128 * j // SPLIT[k] for j in range(SPLIT[k] + 1)]
+            hold[:] = after(k)
+            for lo, hi_ in zip(cuts, cuts[1:]):
+                gtt(v(mf, 16 * lo, 16 * hi_), v("XP"), v("Wu", CH[k] + lo, CH[k] + hi_), v("sig", 16 * (CH[k] + lo), 16 * (CH[k] + hi_)), A.max)
+            del hold[:]
+            sums = lambda x, w: [(v(b, p, 384, 16), x(p), v(w)) for p in range(16)]
+            last = sums(lambda p: v(mf, p, 2048, 16), "WM")
+            mms(sums(lambda p: tile("sg", k, p), "WS"),
+                [(r(2), ch("KF", k), v("WK")), (r(0), v("ON"), v("THD", 0, 128)), (r(0), v("ON"), v("THD", 128, 256)), (r(2), ch("PM", k), v("ID8"))],
+                last[:8], last[8:])
+            bias[0] = SOON
+            ts(u("RR", 0, 2), r(1, 2), MAGIC, A.add, MAGIC, A.subtract)
+            tt(u("RR", 2), r(2), u("RR", 1), A.is_equal)
+            act(u("AA", 0, 2), u("RR", 0, 2), F.Abs, bias=-1.0)
+            rest = v("AS", 128 * (k & 1), 128 * (k & 1) + 128)
+            more = [(r(3), v(l), x) for l, x in (("ID15", u("RR", 0)), ("ID", u("AA", 0)), ("ID", u("AA", 1)), ("IDN", u("RR", 2)))]
+            if ENDS[k] == "V":
+                act(rest, r(0), F.Identity, bias=v("thB", 2, 3), scale=-1.0)
+                mm(more)
+                tt(u("AA", 2), r(3), rest, A.is_gt)
+            else:
+                act(rest, r(0))
+                mm([(r(3), v("IDW"), rest)] + more)
+                act(u("AA", 2), r(3), F.Sign, bias=v("thB", 3, 4))
+            mm([(r(1), u("AA", 2), v("ID")), (r(2), u("RR", 2), v("NI"))], each=1)
+            act(ft(k, 1), r(2), F.Identity, bias=1.0)
+            act(ft(k, 0), r(1), F.Relu)
+            mm([(r(0), v("ZT"), ft(k, 1))])
+            act(ch("FO", k), r(0), F.Relu, scale=16777216.0)
+            mm([(ch("q2", k), v("IDF"), ft(k, 0)), (ch("q2", k), v("ID"), ch("FO", k))], first=False, last=False)
+            bias[0] = 0.0
+
         for k in range(nch):
+            if k < TURNED:
+                turned(k)
+                continue
             b, n = banks[k], CH[k + 1] - CH[k]
             e = v(b, 0, n)
             cut = min(n, SHARE[t]) if TYP[t][k] == "V" else 0
             for f, lo, hi_ in ((gat, 0, cut), (sgat, cut, n)):
                 if lo < hi_:
-                    hold[:] = [tile("sg", SIGS)] if f is sgat else []
+                    hold[:] = [tile("sg", SIGS)] if f is sgat and SIGS >= 0 else []
                     f(v("hg%d" % (k & 1), 16 * lo, 16 * hi_), v("TB"), v("Wu", CH[k] + lo, CH[k] + hi_))
-            del hold[:]
+            hold[:] = after(k)
             gtt(tile("mm", k), v("X"), ch("Wu", k), tile("sg", k), A.max)
+            del hold[:]
             ends = [part("RX", "hg", k), part("R2", "mm", k)]
             mms(part("RN", "sg", k), [(e, v("ID"), ch("KF", k)), (e, v("ID"), ch("PM", k))], *(ends if TYP[t][k] == "V" else ends[::-1]))
             bias[0] = SMALL
             cp(v("RD", 0, n), e)
             tt(ft(k, 1), e, v("RD", 0, n), A.not_equal)
             mm([(v(b, 256, 256 + n), v("ZT"), ft(k, 1))])
-            ts(v("GA", 0, n), v("RD", 0, n), v("thB", 1, 2), A.is_gt)
-            tt(ft(k, 0), ft(k, 1), v("GA", 0, n), A.mult)
+            act(ch("GA", k), e, F.Relu, bias=v("thB", 1, 2), scale=2048.0)
+            tt(ft(k, 0), ft(k, 1), ch("GA", k), A.min)
             act(ch("FO", k), v(b, 256, 256 + n), F.Relu, scale=16777216.0)
             mm([(ch("q2", k), v("IDF"), ft(k, 0)), (ch("q2", k), v("ID"), ch("FO", k))], first=False, last=k == nch - 1)
             bias[0] = 0.0
@@ -840,7 +1064,7 @@ def rank_program(g, core, T, topo):
         lw = lambda k, n=1: v("LW", 32 * k, 32 * (k + n))
         dl = lambda k: v("DL", 32 * k, 32 * k + 32)
         n_, much, some = v("q3", 0, 32), rp(0), rp(1)
-        act(v("PAY"), v("q2"))
+        act(v("PAY"), v("q2"), F.Identity, bias=2048.0)
         mm(wrap(v("q3", 0, 64), "R1", "FT", 0, 1024))
         ts(rp(1, 2), v("q3", 0, 64), 0.5, A.is_gt)
         ts(much, n_, 3.5, A.is_gt)
@@ -864,19 +1088,25 @@ def rank_program(g, core, T, topo):
             candidates()
             hold.append(v("BU", 128, 256))
             bias[0] = 0.0
-        sca(v("P1W"), v("PFu"), v("PAY"))
+        if t == 2:
+            sca(v("P1W"), v("PFu"), v("PAY"))
+        else:
+            op("V", lambda: g.vector.tensor_tensor(ind(v("P1W"), v("PFu")), ap(v("PAY")), ap(v("JF")), A.add), [v("PAY"), v("JF"), v("PFu")], [v("P1W")],
+               ew(512, SCATTER))
         del hold[:]
         mms([(v("q4"), v("X2D"), v("TBL", 0, 512))],
             [(v("q4", i, 512, 16), v("UN", 16 + 128 * i - r, 144 + 128 * i - r), dl(k)) for r, k in ((1, 4), (2, 6), (0, 3)) for i in range(16)])
         act(v("TBn"), v("q4"))
         if t < 2:
             mm([(v("q2", 0, 32), v("ONS"), v("EX")), (v("q2", 0, 32), v("ON"), some)])
-            act(v("BS"), v("q2", 0, 32), scale=-1.0, accum_out=v("thB", 2, 3))
-            ts(v("CN", 0, 1), v("thB", 2, 3), 4096.0, A.add)
+            act(v("BS"), v("q2", 0, 32), scale=-1.0, accum_out=v("thB", 4, 5))
+            ts(v("CN", 0, 1), v("thB", 4, 5), 4096.0, A.add)
             bits(v("CN", 1, 2), v("CN", 0, 1), 0, 255)
-            tt(v("thB", 1, 2), v("thB", 0, 1), v("CN", 1, 2), A.add)
+            ts(v("thB", 1, 2), v("CN", 1, 2), -2048.0, A.mult, v("thB", 0, 1), A.add)
+            act(v("thB", 3, 4), v("thB", 1, 2), F.Identity, bias=col["th"], scale=1 / 2048)
+            act(v("thB", 2, 3), v("thB", 3, 4), F.Identity, bias=-0.5, scale=-1.0)
         bias[0] = 2.0
-        ts(v("AI", 0, 64), v("P1W", 512, 576), 8388608.0, A.subtract, 0.0, A.max)
+        ts(v("AI", 0, 64), v("P1W", 512, 576), 8388608.0 + 2048.0, A.subtract, 0.0, A.max)
         bits(v("AI", 64, 128), v("AI", 0, 64), 0, 4095)
         cp(v("AH", 0, 64), v("AI", 64, 128))
         cp(v("BI", 0, 128), v("P1W", 0, 128))
@@ -892,9 +1122,7 @@ def rank_program(g, core, T, topo):
         bits(v("AI", 128, 192), v("AI", 0, 64), 17, 31)
         bits(v("AI", 192, 256), v("AI", 0, 64), 12, 31)
         cp(v("AH", 192, 320), v("AI", 128, 256))
-        cp(v("AU", 0, 4), to)
-        if not direct:
-            cp(v("BU", 0, 8), v("q5", 132, 140))
+        cp(v("AU", 0, 4 if direct else 12), v("q5", 128, 132 if direct else 140))
         sgat(v("AB", 0, 64), v("TS"), v("AU", 0, 4))
         sca(v("TB"), v("Lu"), v("TBn"))
         for c in range(4):
@@ -905,8 +1133,8 @@ def rank_program(g, core, T, topo):
         act(v("AB", 64, 128), v("q4", 0, 64), F.Identity, bias=col["b2"])
         tt(v("AF", 268, 272), v("AF", 260, 264), v("W4"), A.min)
         tt(v("AF", 272, 276), to, v("AF", 268, 272), A.max)
-        cp(v("AU", 4, 8), v("AF", 272, 276))
-        sca(v("TB"), v("AU", 4, 8), v("AB", 64, 128))
+        cp(v("AU", 12, 16), v("AF", 272, 276))
+        sca(v("TB"), v("AU", 12, 16), v("AB", 64, 128))
         if t < 2:
             gadd(v("FL%d" % (t + 1)), row("TB", 2))
             send(5 + t, served(2 + t), v("FI%d" % (t + 1)), v("FL%d" % (t + 1)))
@@ -924,17 +1152,17 @@ def rank_program(g, core, T, topo):
     def repairs(t):
         bi = lambda k: v("BI", 128 * k, 128 * k + 128)
         bf = lambda lo, hi: v("BF2", lo, hi)
-        sm = lambda k: v("SM", 8 * k, 8 * k + 8)
         dw = "DW%d" % t
         if t < 2:
-            sgat(v("TBS", 0, 128), v("TBL"), v("BU", 0, 8))
+            sgat(v("TBS", 0, 128), v("TBL"), v("AU", 4, 12))
             candidates()
-        for k, c in enumerate(("rb", "rs")):
-            act(v("T3", 128 * k, 128 * k + 128), v("TBS", 0, 128), scale=col[c])
-        mm(wrap(v("q7", 280, 296), "R1", "T3", 0, 256))
-        act(v("WB"), v("q7", 272, 296))
+        act(v("WB"), v("q7", 272, 280), F.Identity, bias=4096.0)
+        cp(v("CH"), bi(4))
+        turn(v("CT"), v("CH"))
+        tt(v("DC", 1, 128), v("CT", 0, 127), v("CT", 1, 128), A.subtract)
         bits(bi(2), bi(0), 0, 2048)
-        ts(v("FB"), bi(2), -2048.0, A.add)
+        bits(bi(5), bi(0), 0, 4095)
+        ts(bf(384, 512), bi(5), -2048.0, A.add)
         for h in (0, 1):
             pick(CAND[t][h])(v("mm0", 1024 * h, 1024 * h + 1024), v("XE%d" % t), v("BU", 128 + 64 * h, 192 + 64 * h))
         for h in (0, 1):
@@ -947,34 +1175,21 @@ def rank_program(g, core, T, topo):
                 mm(lst, each=2)
                 act(v("hg0", lo, lo + 512), v(qb), F.Abs)
             o = v("q7", 64 * h, 64 * h + 64)
-            mms([(o, v("MK12"), v("TBS", 64 * h, 64 * h + 64))] + [(o, win("R16", m), v("hg0", 1024 * h + 64 * m, 1024 * h + 64 * m + 64)) for m in range(8)],
-                [(o, win("R16", m), v("hg0", 1024 * h + 64 * m, 1024 * h + 64 * m + 64)) for m in range(8, 16)])
-        sgat(v("OLD"), v("WD"), v("BU", 8, 16))
-        tt(bf(384, 512), v("OLD"), bi(2), A.subtract)
+            mms([(o, v("MK12"), v("TBS", 64 * h, 64 * h + 64))] + [(o, win("R1", m), v("hg0", 1024 * h + 64 * m, 1024 * h + 64 * m + 64)) for m in range(8)],
+                [(o, win("R1", m), v("hg0", 1024 * h + 64 * m, 1024 * h + 64 * m + 64)) for m in range(8, 16)])
         changes(t)
         turn(bf(0, 128), v("q7", 0, 128))
-        lo, n, o = 0, 128, 128
-        if t == 2:
-            for k in range(8):
-                least(bf(128 + k, 129 + k), bf(16 * k, 16 * k + 16))
-            lo, n = 128, 8
-        while n > 8:
-            tt(bf(o, o + n // 2), v("BF2", lo, lo + n, 2), v("BF2", lo + 1, lo + n, 2), A.min)
-            lo, n, o = o, n // 2, o + n // 2
-        cp(sm(0), bf(lo, lo + 8))
-        ts(v("MB", 8, 16), bf(lo, lo + 8), 65400.0, A.is_gt)
-        bits(sm(1), sm(0), 0, 15)
-        cp(v("MB", 0, 8), sm(1))
-        mm([(v("q7", 256 + s1, 272, 2), v("SWB", 256 * s1 + 128 * g2, 256 * s1 + 128 * g2 + 128), v("MB", g2, 16, 2))
-            for s1 in (0, 1) for g2 in (0, 1)], each=2)
-        tt(sm(2), v("q7", 256, 264), v("WB", 16, 24), A.mult)
-        tt(sm(3), sm(2), v("WB", 8, 16), A.add)
-        bits(sm(4), sm(3), 0, 2047)
-        cp(v("BU", 24, 32), sm(4))
-        gtt(bf(256, 384), v("WE"), v("BU", 24, 32), v("FB"), A.add)
-        tt(bf(248, 256), v("q7", 264, 272), v("W8"), A.mult)
-        tt(v(dw, 128, 136), v("WB", 0, 8), bf(248, 256), A.max)
-        cp(v("BU", 16, 24), v(dw, 128, 136))
+        scan(bf(128, 256), v("KB"), bf(0, 128), A.add, 0.0, A.min)
+        tt(v("NQ"), bf(0, 128), bf(128, 256), A.not_equal)
+        scan(v("UU"), v("DC"), v("NQ"), A.add, 0.0, A.mult)
+        tt(v("MB"), v("BF2", 143, 256, 16), v("W8"), A.min)
+        swb = lambda s1, g2: v("SWB", 256 * s1 + 128 * g2, 256 * s1 + 128 * g2 + 128)
+        mm([(v("q7", 256 + s1, 264, 2), swb(s1, g2), v(x, 16 * g2 + 15, 128, 32)) for s1 in (0, 1) for x in ("CT", "UU") for g2 in (0, 1)], each=4)
+        mm([(v("q7", 264 + s1, 272, 2), swb(s1, g2), v("MB", g2, 8, 2)) for s1 in (0, 1) for g2 in (0, 1)], each=2)
+        cp(v("BU", 24, 32), v("q7", 256, 264))
+        gtt(bf(256, 384), v("WE"), v("BU", 24, 32), bi(2), A.subtract)
+        tt(v(dw, 128, 136), v("q7", 264, 272), v("WB"), A.max)
+        ts(v("BU", 16, 24), v(dw, 128, 136), -4096.0, A.add)
         if t == 2:
             op("V", lambda: g.vector.tensor_tensor(ind(v("WD"), v("BU", 16, 24)), ap(bf(256, 384)), ap(bf(384, 512)), A.max),
                [bf(256, 512), v("BU", 16, 24)], [v("WD")], ew(128, SCATTER))
@@ -991,7 +1206,7 @@ def rank_program(g, core, T, topo):
         if t == 0:
             gcp(v("WD", 0, 2048), v("W16"))
             gcp(v("WD", 2048, 2560), v("Z", 0, 512))
-            gcp(v("WE", 2048, 2176), v("Z", 0, 128))
+            gcp(v("WE", 2048, 2560), v("Z", 0, 512))
         if t < 2:
             gcp(v("CW", 0, 512), v("Z", 0, 512))
         for h in (1, 0):
@@ -1004,7 +1219,7 @@ def rank_program(g, core, T, topo):
         hold.append(v("BU", 128, 256))
         for s in range(t):
             b = "Di%d%d" % (s, t)
-            cp(v("HU"), v(b, 128, 136))
+            ts(v("HU"), v(b, 128, 136), -4096.0, A.add)
             sca(v("WE"), v("HU"), v(b, 0, 128))
         hold.pop()
 
@@ -1027,6 +1242,7 @@ def rank_program(g, core, T, topo):
         post(t)
         if t < 2:
             lanes(t + 1)
+            types_to_xp(t + 1)
             bias[0] = -LATE
             repairs(t)
             bias[0] = 0.0

@@ -11,18 +11,21 @@ FIRST = 128
 TYP = ("SSSSS", "SSSSS", "SSSSS")
 SHARE = (128, 112, 112)
 SIGS = 2
-CAND = ("SS", "SS", "SS")
+CAND = ("SSSS", "SSSS", "SVSV")
 TBLQ = "S"
 LOADS = ("X", "RI32", "SG", "WI")
 PACE, CUT = 1, 896
 LATE, LAST, SMALL, PATIENCE, WAKE = 2.0, 3.0, 0.0, 0.5, 0.18
-SOON, LAG, XPB, ENDS = 5.0, 2, "q1", "VVV"
+EARLY, PIECE, VSPLIT = 256, 8, (2, 1, 1)
+AFTER = {(2, 0): (("RR", 0),), (3, 0): (("RR", 1),), (4, 0): (("RR", 2),)}
+SOON, LAG, XPB, TTQ, OWN, PARTS, AHEAD = 5.0, 2, "q1", "VVV", 1, 2, 2
 GATHER, SCATTER, MATMUL = 1.56, 3.8, 0.55
 SPEEDS = ((.85e-3, 1.1, 2.0), (.9e-3, 1.5, 3.8), (1.15e-3, 1.9, 5.0))
 PLAN = ((1.1e-3, 1.08, 2.5), (0.9e-3, 1.45, 3.5), (1.0e-3, 2.0, 5.0)) + ((0.95e-3, 1.56, 3.8), (0.95e-3, 1.3, 3.0), (1.0e-3, 1.7, 4.0))
 PASSES, STEPS, STARTS = 3, 200, 1
 TUNE = ((.85e-3, 1.1, 2.0, .55, .13, .03), (.9e-3, 1.5, 3.8, .5, .15, .02), (1.0e-3, 1.25, 4.5, .62, .2, .02), (1.15e-3, 1.9, 4.5, .5, .15, .04))
-ROUNDS, TRIES, LOSS, BAN, NEAR, GAIN = 5000, 10, 0.03, 8, 0.02, 0.3
+ROUNDS, TRIES, LOSS, BAN, NEAR, GAIN = 12000, 10, 1.0, 8, 0.2, 0.6
+JUMP, SEED, EVERY, SLACK = (0, 0, 0, 1, 1, 2, 3, 5), 1, 100, 0.0
 ORDER, EST, LOG = [], [], []
 SCRATCH = {}
 SEMAPHORES = ["cV", "cS", "cP", "cG"]
@@ -41,31 +44,31 @@ def _buf(name, cols, dtype, where="sbuf", pool=None):
         SCRATCH[name] = (where, [128, cols], dtype)
 
 
-for _n in ("BO", "NBO", "LT", "EQH", "GT", "ID", "NI", "LPB", "NLP", "ZT", "X2D", "K34", "B128", "IDK",
-           "IDF", "IDQ", "ON", "ONS", "CWM", "MK12", "C1", "ID5", "ID8", "ID10", "ID14", "ID15", "IDN"):
+for _n in ("BO", "NBO", "LT", "EQH", "GT", "ID", "NI", "LPB", "NLP", "ZT", "X2D", "K34", "B128", "TF", "LPD", "NLD",
+           "IDF", "IDQ", "ON", "ONS", "CWM", "MK12", "C1", "ID5", "IDK", "LPH", "ID10", "ID14", "ID15", "IDN"):
     _buf(_n, 128, BF, pool="PB")
 for _n in ("R1", "RI", "RH", "RX", "R2", "RN", "RU", "RO", "R0", "RT"):
     _buf(_n, 144, BF, pool="PB")
-for _n, _c in (("WS", 24), ("WK", 128), ("THD", 256), ("TH2", 1), ("RH3", 32), ("DFB", 128), ("UT", 128), ("SWB", 512), ("KIB", 128)):
+for _n, _c in (("WS", 24), ("WK", 128), ("B3", 384), ("C3", 384), ("THD", 256), ("TH2", 1), ("RH3", 32), ("UT", 128), ("SWB", 512), ("KIB", 128)):
     _buf(_n, _c, BF, pool="PB")
-for _n, _c in (("COLS", 128), ("QH", 16), ("CR", 144), ("MG", 128), ("MI", 128), ("JW", 32), ("JC", 32), ("JD", 32), ("J16", 32),
+for _n, _c in (("COLS", 128), ("QH", 16), ("CR", 144), ("MG", 128), ("MI", 128), ("JW", 32), ("JC", 32), ("KB3", 96), ("J16", 32),
                ("W8", 8), ("W4", 4), ("S4", 4), ("K3", 3), ("DF", 192), ("ZF", 128), ("TMP", 128), ("KB", 128),
-               ("WM", 24), ("IDW", 128)):
+               ("WM", 24), ("TE", 32)):
     _buf(_n, _c, FP, pool="PF")
 for _n, _c, _d in (
         ("X", 2064, BF), ("WD", 2560, FP), ("WI", 2560, I32), ("W16", 2048, H16), ("RI32", 1032, I32), ("SG", 1040, BF), ("TB", 2688, BF),
-        ("Z", 640, BF), ("UN", 2064, BF), ("PW", 64, FP), ("JI", 512, FP), ("JB", 512, BF), ("JF", 512, FP), ("L1", 64, BF),
+        ("Z", 640, BF), ("UN", 2064, BF), ("JI", 512, FP), ("L1", 64, BF),
         ("hyb", 128, I32), ("vfb", 128, I32), ("thi", 1, I32), ("KI", 4, I32), ("ST", 1024, BF), ("SI", 1280, I32),
         ("NW", 128, BF), ("NT", 128, BF), ("VB", 256, H16), ("HW", 128, FP), ("TY", 512, H16), ("POS", 128, FP), ("TTB", 384, BF), ("OFu", 8, U16),
         ("CW", 4224, BF), ("CC", 512, BF), ("CLu", 32, U16), ("OH", 512, BF), ("EX", 32, BF), ("Lf", 32, FP), ("Lu", 32, U16),
-        ("TBL", 528, BF), ("Wu", 512, U16), ("Wf", 512, H16), ("Ku", 512, U16), ("KF", 512, H16), ("PM", 512, BF), ("STu", 32, U16),
-        ("HI", 256, I32), ("HF", 64, FP), ("HY", 64, FP), ("TS", 2688, BF), ("FT", 1024, BF), ("FO", 512, BF), ("RD", 256, I32), ("GA", 512, BF), ("PAY", 512, FP),
+        ("TBL", 512, BF), ("Wu", 512, U16), ("Wf", 512, H16), ("Ku", 512, U16), ("KF", 512, H16), ("STu", 32, U16),
+        ("HI", 256, I32), ("HF", 64, FP), ("HY", 64, FP), ("TS", 2688, BF), ("FT", 1024, BF), ("FO", 512, BF), ("RD", 256, FP), ("GA", 512, BF), ("PAY", 512, FP),
         ("sig", 8192, BF), ("mm0", 2048, BF), ("mm1", 2048, BF), ("hg0", 2048, BF), ("hg1", 2048, BF),
         ("XP", 2048, FP), ("mf0", 2048, FP), ("mf1", 2048, FP), ("RR", 1152, BF), ("AA", 1152, BF), ("XB", 128, BF), ("XR", 256, FP),
         ("RP", 96, BF), ("LW", 192, FP), ("PFu", 32, U16), ("DL", 224, BF), ("P1W", 1536, FP), ("TBn", 512, BF),
-        ("thB", 5, FP), ("AS", 256, FP), ("CN", 4, I32), ("BS", 32, FP),
-        ("AI", 256, I32), ("AH", 320, H16), ("WB", 8, FP), ("MB", 8, H16), ("AF", 352, FP), ("AB", 128, BF), ("AU", 16, U16),
-        ("BI", 768, I32), ("TBS", 1536, BF), ("LX", 128, BF), ("BF2", 512, FP), ("CH", 128, H16), ("CT", 128, H16), ("DC", 128, H16),
+        ("thB", 6, FP), ("PI", 384, I32), ("AS", 256, FP), ("CN", 4, FP), ("BS", 32, FP),
+        ("AI", 256, I32), ("AH", 320, H16), ("WB", 8, FP), ("MB", 8, H16), ("AF", 416, FP), ("AB", 128, BF), ("AU", 16, U16),
+        ("BI", 768, I32), ("TBS", 128, BF), ("LX", 128, BF), ("NB", 128, FP), ("BF2", 512, FP), ("CH", 128, H16), ("CT", 128, H16), ("DC", 128, H16),
         ("NQ", 128, H16), ("UU", 128, H16), ("BU", 256, U16), ("HU", 8, U16), ("WE", 2560, FP), ("OUT", 256, FP),
         ("DW0", 136, FP), ("DW1", 136, FP), ("DW2", 136, FP)):
     _buf(_n, _c, _d)
@@ -161,6 +164,9 @@ def rank_program(g, core, T, topo):
             if k.get(s, 0) < c:
                 k[s] = c
 
+    def meet(lo, step, x):
+        return step != x[3] or (lo - x[1]) % step == 0
+
     def deps(e, reads, writes):
         need = []
         for lst, wr in ((reads, False), (writes, True)):
@@ -171,7 +177,7 @@ def rank_program(g, core, T, topo):
                         continue
                     if ex and a[4] != e:
                         need.append(a)
-                    elif a[1] < x[2] and x[1] < a[2] and (wr or a[3]) and (a[0] is None or x[4] is None or a[0] == x[4]):
+                    elif a[1] < x[2] and x[1] < a[2] and (wr or a[3]) and (a[0] is None or x[4] is None or a[0] == x[4]) and meet(a[1], a[8], x):
                         need.append(a)
         need.sort(key=lambda a: -a[6])
         for a in need:
@@ -187,7 +193,7 @@ def rank_program(g, core, T, topo):
                     keep = [a for a in old if not (x[1] <= a[1] and a[2] <= x[2] and (x[4] is None or a[0] == x[4]))]
                 else:
                     keep = [a for a in old if a[3] or a[4] != e or a[1:3] != (x[1], x[2]) or a[0] != x[4] or wr]
-                keep.append((x[4], x[1], x[2], wr, e, sem, val, clock))
+                keep.append((x[4], x[1], x[2], wr, e, sem, val, clock, x[3]))
                 acc[x[0]] = keep
 
     prog, hold = [], []
@@ -300,7 +306,7 @@ def rank_program(g, core, T, topo):
                         if x[0] in psum:
                             hit = wr or a[4] or a[5] != c["e"]
                         else:
-                            hit = (wr or a[4]) and a[1] < x[2] and x[1] < a[2] and (a[3] is None or x[4] is None or a[3] == x[4])
+                            hit = (wr or a[4]) and a[1] < x[2] and x[1] < a[2] and (a[3] is None or x[4] is None or a[3] == x[4]) and meet(a[1], a[6], x)
                         if hit:
                             ps[a[0]] = max(ps.get(a[0], 0.0), 0.0 if x in (GQ, LQ) or a[5] == c["e"] == "P" else prog[a[0]]["lat"] + WAKE)
             for lst, wr in ((c["r"], False), (c["w"], True)):
@@ -311,7 +317,7 @@ def rank_program(g, core, T, topo):
                             h[:] = [a for a in h if a[0] == k]
                         else:
                             h[:] = [a for a in h if not (x[1] <= a[1] and a[2] <= x[2] and (x[4] is None or a[3] == x[4]))]
-                    e = (k, x[1], x[2], x[4], wr, c["e"])
+                    e = (k, x[1], x[2], x[4], wr, c["e"], x[3])
                     if e not in h:
                         h.append(e)
             pred.append(ps)
@@ -450,7 +456,7 @@ def rank_program(g, core, T, topo):
                         sl[p].append((k, x))
                 ms_.append((cs, pl, sl))
 
-            def full(order):
+            def full(order, lo=0, hi=n, old=None):
                 last, before, behind = {}, [-1] * n, [-1] * n
                 for k in order:
                     e = qs[k]
@@ -461,15 +467,15 @@ def rank_program(g, core, T, topo):
                             behind[j] = k
                         last[e] = k
                 out, moves, val = [], [], 1.0
-                for cs, pl, sl in ms_:
-                    done, tail = [0.0] * (n + 1), [0.0] * (n + 1)
-                    for k in order:
+                for m, (cs, pl, sl) in enumerate(ms_):
+                    done, tail = old[m][:2] if old else ([0.0] * (n + 1), [0.0] * (n + 1))
+                    for k in order[lo:]:
                         t0 = done[before[k]]
                         for p, x in pl[k]:
                             if done[p] + x > t0:
                                 t0 = done[p] + x
                         done[k] = t0 + cs[k]
-                    for k in reversed(order):
+                    for k in reversed(order[:hi]):
                         t0 = max(lat[k], tail[behind[k]])
                         for s, x in sl[k]:
                             if tail[s] + x > t0:
@@ -500,7 +506,7 @@ def rank_program(g, core, T, topo):
                 for x in old:
                     head.setdefault(qs[x], before[x])
                     end_[qs[x]] = behind[x]
-                val = 1.0
+                val = 0.0
                 for (cs, pl, sl), (done, tail, end) in zip(ms_, out):
                     d, free = {}, {e: done[x] for e, x in head.items()}
                     for k in mid:
@@ -524,34 +530,130 @@ def rank_program(g, core, T, topo):
                         tl[k] = t0 + cs[k]
                         if qs[k] != "R":
                             nxt[qs[k]] = tl[k]
-                    val *= max(top, end - GAIN)
+                    was = max([done[k] - cs[k] + tail[k] for k in mid])
+                    val += math.exp(min(top - end, 3.0) / GAIN) - math.exp((was - end) / GAIN)
                 return val
 
-            seed, order = 1, list(order)
+            def again(order, at, lo, hi, old, out, before, behind, turn_):
+                head, end_ = {}, {}
+                for x in old:
+                    head.setdefault(qs[x], before[x])
+                    end_[qs[x]] = behind[x]
+                for i in range(lo, hi):
+                    k = order[i]
+                    at[k], e = i, qs[k]
+                    if e != "R":
+                        j = before[k] = head[e]
+                        behind[j] = head[e] = k
+                for e, j in head.items():
+                    if e != "R":
+                        behind[j] = end_[e]
+                        before[end_[e]] = j
+                before[n] = behind[n] = -1
+                val = 1.0
+                for m, (cs, pl, sl) in enumerate(ms_):
+                    done, tail = out[m][:2]
+                    far, i = max(hi - 1, max(at[x] if x >= 0 else 0 for x in end_.values())), lo
+                    while i <= far:
+                        k = order[i]
+                        t0 = done[before[k]]
+                        for p, x in pl[k]:
+                            if done[p] + x > t0:
+                                t0 = done[p] + x
+                        t0 += cs[k]
+                        if t0 != done[k]:
+                            done[k] = t0
+                            for s, _ in sl[k]:
+                                if at[s] > far:
+                                    far = at[s]
+                            if behind[k] >= 0 and at[behind[k]] > far:
+                                far = at[behind[k]]
+                        i += 1
+                    far, i = min([lo] + [at[before[x]] for x in order[lo:hi] if before[x] >= 0]), hi - 1
+                    while i >= far:
+                        k = order[i]
+                        t0 = max(lat[k], tail[behind[k]])
+                        for s, x in sl[k]:
+                            if tail[s] + x > t0:
+                                t0 = tail[s] + x
+                        t0 += cs[k]
+                        if t0 != tail[k]:
+                            tail[k] = t0
+                            for p, _ in pl[k]:
+                                if at[p] < far:
+                                    far = at[p]
+                            if before[k] >= 0 and at[before[k]] < far:
+                                far = at[before[k]]
+                        i -= 1
+                    end = max(tail)
+                    val *= end
+                    out[m] = (done, tail, end)
+                done, tail, end = out[turn_ % len(ms_)]
+                end -= NEAR
+                return val, [(before[k], k) for k in order if done[before[k]] + tail[k] > end and before[k] >= 0]
+
+            seed, order = SEED, list(order)
             val, out, moves, before, behind = full(order)
-            best, banned = (val, list(order)), {}
+            before.append(-1)
+            behind.append(-1)
+            best, banned, at = (val, list(order)), {}, [0] * n
+            for i, k in enumerate(order):
+                at[k] = i
+            def sooner(order, m):
+                cs, pl, _ = ms_[m]
+                start, done, busy = [0.0] * n, [0.0] * n, {}
+                for k in order:
+                    t0 = max([done[p] + x for p, x in pl[k]] or [0.0])
+                    if qs[k] != "R":
+                        iv = busy.setdefault(qs[k], [])
+                        j = len(iv)
+                        while j > 0 and iv[j - 1][1] > t0:
+                            j -= 1
+                        while j < len(iv) and iv[j][0] < t0 + cs[k] - 1e-9:
+                            t0 = max(t0, iv[j][1])
+                            j += 1
+                        iv.insert(j, (t0, t0 + cs[k]))
+                    start[k], done[k] = t0, t0 + cs[k]
+                return sorted(order, key=lambda k: (start[k], at[k]))
+
             for step in range(ROUNDS):
-                at = [0] * n
-                for i, k in enumerate(order):
-                    at[k] = i
+                if step % EVERY == 0:
+                    other = sooner(order, step // EVERY % len(ms_))
+                    new = full(other)
+                    if new[0] < val * (1 + SLACK):
+                        order = other
+                        val, out, moves, before, behind = new
+                        before.append(-1)
+                        behind.append(-1)
+                        for i, k in enumerate(order):
+                            at[k] = i
                 pick_ = None
                 for _ in range(TRIES):
                     seed = (seed * 1103515245 + 12345) % 2147483648
                     j, k = moves[(seed >> 8) % len(moves)]
-                    if banned.get((j, k), -1) > step or at[k] - at[j] > 150:
+                    if banned.get((j, k), -1) > step:
                         continue
-                    mid = moved(order, at, j, k, seed >> 7 & 1)
+                    late = seed >> 7 & 1
+                    for _ in range(JUMP[seed >> 4 & 7]):
+                        if late and behind[k] >= 0:
+                            k = behind[k]
+                        elif not late and before[j] >= 0:
+                            j = before[j]
+                    if at[k] - at[j] > 150:
+                        continue
+                    mid = moved(order, at, j, k, late)
                     if mid is not None:
                         x = judge(order[at[j]:at[k] + 1], mid, out, before, behind)
                         if pick_ is None or x < pick_[0]:
                             pick_ = (x, j, k, mid)
-                if pick_ is None or pick_[0] > val * (1 + LOSS * (1 - step / ROUNDS)):
+                if pick_ is None or pick_[0] > LOSS * (1 - step / ROUNDS):
                     continue
                 _, j, k, mid = pick_
-                order[at[j]:at[k] + 1] = mid
+                lo, hi = at[j], at[k] + 1
+                old = order[lo:hi]
+                order[lo:hi] = mid
                 banned[(k, j)] = step + BAN
-                val, out, moves, before, behind = full(order)
-                LOG.append((step, pick_[0] ** .25, val ** .25))
+                val, moves = again(order, at, lo, hi, old, out, before, behind, step)
                 if val < best[0]:
                     best = (val, list(order))
             EST.extend((x[2], 0) for x in full(best[1])[1])
@@ -725,10 +827,11 @@ def rank_program(g, core, T, topo):
         return last
 
     bias[0] = 30.0
-    ms(v("TB", 0, 2048), 0.0)
     ms(v("Z"), 0.0)
     ms(v("ZF"), 0.0)
     bias[0] = 0.0
+    for h in (0, 1):
+        ms(v("TB", 1024 * h, 1024 * h + 1024), 0.0)
     ki, kg, odd = newcol("ki"), newcol("kg"), newcol("odd")
     km, kf, kp = v("K3", 0, 1), v("K3", 1, 2), v("K3", 2, 3)
     ts(v("KI", 1, 2), v("KI", 0, 1), 4, A.arith_shift_right)
@@ -750,6 +853,9 @@ def rank_program(g, core, T, topo):
     tt(v("GT"), v("GT"), v("BO"), A.mult)
     act(v("LPB"), v("ID"), scale=-4096.0)
     tt(v("LPB"), v("LPB"), v("GT"), A.subtract)
+    act(v("LPH"), v("LPB"), scale=0.5)
+    act(newcol("lph"), ki, F.Identity, bias=-2055.5, scale=0.5)
+    act(v("B3", 0, 128), v("BO"), scale=0.5)
     ts(v("RH3", 0, 8), v("CR", 0, 8), kg, A.is_gt)
     ts(v("RH3", 8, 16), v("CR", 0, 8), kg, A.is_equal)
     act(v("RH3", 16, 24), v("RH3", 8, 16), scale=2048.0)
@@ -758,26 +864,18 @@ def rank_program(g, core, T, topo):
     for k, (c_, m_) in enumerate(((kf, even), (kp, even), (km, odd), (kf, odd))):
         ts(v("SWB", 128 * k, 128 * k + 128), v("CR", 0, 128), c_, A.is_equal, m_, A.mult)
     act(v("JW"), v("J16"), F.Identity, bias=ki)
-    for name, n, a, b in (("JC", 32, 1.0, 2048.0), ("JD", 32, 1.0, 1024.0), ("W4", 4, 2.0, 2560.0), ("S4", 4, 4096.0, 1024.0)):
-        act(v(name), v("JW", 0, n), F.Identity, bias=b, scale=a)
+    act(v("JC"), v("JW"), F.Identity, bias=2048.0)
     act(v("C1"), v("CR", 0, 128), scale=1 / 16)
-    ts(v("PW", 0, 16), v("ZF", 0, 16), 2.0, A.add)
-    scan(v("PW", 16, 32), v("PW", 0, 16), v("ZF", 0, 16), A.mult, 0.5)
-    tt(v("PW", 32, 48), v("PW", 16, 32), v("QH"), A.mult)
-    op("V", lambda: g.vector.tensor_reduce(ap(v("PW", 48, 49)), ap(v("PW", 32, 48)), AxisListType.X, A.add), [v("PW", 32, 48)], [v("PW", 48, 49)])
-    for name, c in (("RI", ki), ("RH", weights("h", {0: 32, 1: 1, 2: 0.25})),
-                    ("RU", col["uw"]), ("RX", weights("sx", {0: 1 / 64, 1: 1 / 2048, 3: -64, 4: -1})), ("R2", 2.0), ("RN", -1.0),
-                    ("RO", weights("ro", {10: 128, 11: 16}))):
+    act(newcol("rt"), ki, F.Relu, bias=32.0, scale=-31.0)
+    act(newcol("sx"), col["rt"], F.Identity, bias=weights("s", {3: -1, 4: -1}), scale=1 / 2048)
+    for name, c in (("RI", ki), ("RU", col["uw"]), ("RX", col["sx"]), ("R2", 2.0), ("RN", -1.0)):
         act(v(name, 0, 143), v("R1", 0, 143), scale=c)
-    weights("rb", {8: 32, 9: 1})
-    weights("rs", {5: 64, 6: 2, 12: 1})
     act(v("ON"), v("Z", 0, 128), F.Identity, bias=1.0)
     dma("Y", row("TB", 12), v("ON"))
     ts(v("TB", 2048, 2688), v("Z", 0, 640), weights("tb", {0: 32}), A.add)
-    act(v("TBL", 512, 528), v("Z", 0, 16), F.Identity, bias=weights("tl", {10: 16}))
     ms(v("X", 2048, 2064), 16384.0)
     ms(v("RI32", 1024, 1032), 1024)
-    ms(v("SG", 1024, 1040), 0.0)
+    act(v("SG", 1024, 1040), v("Z", 0, 16), F.Identity, bias=weights("sg", {1: -1.5 * 2.0 ** 34}))
     ts(v("TMP"), v("vfb"), -2048.0, A.mult)
     tt(v("VB", 0, 128), v("TMP"), v("hyb"), A.add)
     act(v("IDQ"), v("ID"), scale=0.25)
@@ -791,40 +889,49 @@ def rank_program(g, core, T, topo):
     act(v("KIB"), v("Z", 0, 128), F.Identity, bias=ki)
     dma("Y", row("TB", 10), v("KIB"))
     dma("Y", row("TB", 11), v("C1"))
-    mm([(v("q6", 0, 128), win("R1", b), v("X", 128 * b, 128 * b + 128)) for b in range(16)])
-    mm([(v("q6", 128, 256), win("RU", b), v("X", 128 * b, 128 * b + 128)) for b in range(16)])
-    si = lambda k: v("SI", 128 * k, 128 * k + 128)
-    cp(v("SI", 256, 512), v("q6", 0, 256))
-    ts(si(4), si(2), 6, A.arith_shift_right)
-    bits(si(5), si(2), 0, 63)
-    cp(v("ST", 256, 512), v("SI", 512, 768))
+    def blocks(o, R, x, more=()):
+        lst = list(more) + [(o, win(R, b), v(x, 128 * b, 128 * b + 128)) for b in range(16)]
+        mms(*[lst[k:k + 4] for k in range(0, 12, 4)], lst[12:])
+
+    def gid(name, c):
+        o, z = v(name, 0, 128), v("Z", 0, 128)
+        op("G", lambda: g.affine_select(ap(o), ap(z), [[-1, 128]], A.not_equal, float(c), 0, 1), [z], [o], 0.42)
+
+    blocks(v("q6", 0, 128), "R1", "X")
+    act(v("ST", 256, 384), v("q6", 0, 128))
+    tt(v("ST", 384, 512), v("q6", 0, 128), v("ST", 256, 384), A.subtract)
     for r in (3, 4):
         dma("Y", row("TB", r), v("ST", 128 * r - 128, 128 * r))
-    bits(si(2), si(3), 0, 2047)
-    ts(si(3), si(2), 32.0, A.add)
-    ts(si(6), si(2), 5, A.arith_shift_right)
-    tt(si(3), si(3), si(2), A.mult)
+    blocks(v("q0", 0, 128), "RU", "X")
+    si = lambda k: v("SI", 128 * k, 128 * k + 128)
+    cp(si(2), v("q0", 0, 128))
+    bits(si(3), si(2), 0, 2047)
+    bits(si(6), si(2), 5, 63)
     bits(si(7), si(2), 0, 31)
-    bits(si(8), si(3), 10, 63)
-    bits(si(9), si(3), 5, 31)
-    cp(v("ST", 512, 1024), v("SI", 768, 1280))
+    gcp(v("BF2", 0, 128), si(3))
+    act(v("BF2", 128, 256), v("BF2", 0, 128), F.Square, bias=16.0)
+    ts(si(4), v("BF2", 128, 256), -256.0, A.add)
+    bits(si(8), si(4), 10, 63)
+    bits(si(9), si(4), 5, 31)
+    gcp(v("ST", 512, 1024), v("SI", 768, 1280))
     for k, r in enumerate((5, 6, 8, 9)):
         dma("Y", row("TB", r), v("ST", 512 + 128 * k, 640 + 128 * k))
     dma("Y", v("TS"), v("TB"), lat=4.0)
     for h in (0, 1):
         act(v("XP", 1024 * h, 1024 * h + 1024), v("X", 1024 * h, 1024 * h + 1024))
     act(v("R0", 0, 143), v("R1", 0, 143), scale=weights("r0", {0: 32768, 1: 0}, 1))
-    mm([(v("q7", 0, 128), win("R0", b), v("X", 128 * b, 128 * b + 128)) for b in range(16)])
+    blocks(v("q7", 0, 128), "R0", "X")
     act(v("XR", 0, 128), v("q7", 0, 128), F.Identity, bias=32768.0)
     dma("Y", row("XP", 0), v("XR", 0, 128), lat=3.0)
     act(v("ID5"), v("ID"), scale=32.0)
     act(v("ID14"), v("ID"), scale=16384.0)
 
     def types_to_xp(t):
-        o = v(XPB if t else "q7", 384, 512)
-        part = [(o, win("RT", b), v("TB", 128 * b, 128 * b + 128)) for b in range(16)] if t else [(o, v("ID5"), v("ST", 0, 128)), (o, v("ID"), v("ST", 128, 256))]
-        part = [(o, v("ID14"), v("XB"))] + part
-        mms(*[part[k:k + 5] for k in range(0, len(part), 5)])
+        o = v(XPB, 384, 512)
+        if t:
+            blocks(o, "RT", "TB", [(o, v("ID14"), v("XB"))])
+        else:
+            mm([(o, v("ID14"), v("XB")), (o, v("ID5"), v("ST", 0, 128)), (o, v("ID"), v("ST", 128, 256))])
         act(v("XR", 128, 256), o, F.Identity, bias=16384.0)
         dma("Y", row("XP", 1), v("XR", 128, 256), lat=3.0)
 
@@ -832,8 +939,9 @@ def rank_program(g, core, T, topo):
     for name, ws in (("WM", (({0: -1, 1: 0}, 2), ({0: 2.0 ** -15}, 0), ({1: 2.0 ** -14}, 0))), ("WS", (({0: 32768, 1: 0}, -1), ({0: -1}, 0), ({1: -1}, 0)))):
         for k, (w, rest) in enumerate(ws):
             act(v(name, 8 * k, 8 * k + 8), v("RH3", 8, 16), scale=col["r0"] if w is None else weights("w", w, rest))
-    for name, c in (("WK", 0.125), ("ID8", 256.0), ("ID15", 32768.0), ("IDN", -2.0 ** 36)):
-        act(v(name), v("ID"), scale=c)
+    for name, c in (("WK", -2.0 ** -14), ("IDK", -2.0 ** -11), ("ID15", 32768.0), ("IDN", -2.0 ** 36),
+                    ("NI", -1.0), ("IDF", -2048.0), ("ID10", -1024.0), ("LPD", -4096.0)):
+        gid(name, c)
 
     def unwrap_table(k):
         un, z = v("UN", 16 + 512 * k, 528 + 512 * k), v("Z", 0, 512)
@@ -854,57 +962,63 @@ def rank_program(g, core, T, topo):
                 arrive(10 + 2 * k + h, v(("XE%d", "WH%d")[k & 1] % (k // 2), *piece(k, h)), 3, 10.0 + 12.0 * k)
 
     def late_constants():
-        for n_, src, c in (("NI", "ID", -1.0), ("IDK", "ID", -8388608.0), ("IDF", "ID", -2048.0), ("NBO", "BO", -1.0),
-                           ("B128", "BO", 128.0), ("NLP", "LPB", -1.0)):
+        for n_, src, c in (("NBO", "BO", -1.0), ("NLP", "LPB", -1.0)):
             act(v(n_), v(src), scale=c)
         tt(v("ZT"), v("EQH"), v("LT"), A.subtract)
         tt(v("ZT"), v("ZT"), v("BO"), A.mult)
-        ts(newcol("keep"), ki, 2.5, A.is_gt)
-        act(v("K34"), v("ID"), scale=col["keep"])
         act(v("X2D"), v("ID"), scale=col["n2"])
-        act(v("ONS"), v("Z", 0, 128), F.Identity, bias=1.0 / 4096)
-        act(v("CWM"), v("MI"), F.Identity, bias=col["rb"], scale=col["rs"])
-        tt(v("CWM"), v("CWM"), v("BO"), A.mult)
-        act(v("MK12"), v("MI"), scale=weights("m16", {12: 1 / 16}))
-        tt(v("MK12"), v("MK12"), v("BO"), A.mult)
-        act(v("DF", 0, 128), v("ZF"), F.Identity, bias=weights("df", {9: 1 << 22}))
-        act(v("DF", 128, 192), v("CR", 0, 64), F.Identity, bias=weights("df", {0: (1 << 23) + 2048 + 2560}), scale=weights("d2", {0: 2}))
-        weights("b2", {2: 8192})
-        act(v("DFB"), v("Z", 0, 128), F.Identity, bias=col["tl"])
+        act(v("DF", 0, 128), v("ZF"), F.Identity, bias=weights("df", {10: 16 * 4096}))
+        act(v("DF", 128, 192), v("CR", 0, 64), F.Identity, bias=weights("df", {0: (1 << 23) + 8 * 4096 + 2048 + 2560}), scale=weights("d2", {0: 2}))
         ts(v("thB", 0, 1), v("thi"), -2048.0, A.mult, -1024.0, A.add)
         ts(v("thB", 1, 2), v("thi"), -2048.0, A.mult, -1024.0, A.add)
         act(newcol("th"), v("thB", 0, 1), F.Identity, bias=-0.5, scale=-1 / 2048)
-        act(v("thB", 3, 4), v("thB", 1, 2), F.Identity, bias=col["th"], scale=1 / 2048)
         act(v("thB", 2, 3), v("ZF", 0, 1))
-        act(v("IDW"), v("ID"))
+        act(v("thB", 5, 6), v("thB", 1, 2), scale=-1.0)
         act(v("TH2"), col["th"], scale=-1.0)
         act(newcol("thh"), v("TH2"))
         act(newcol("thl"), col["th"], F.Identity, bias=col["thh"])
         act(v("THD", 0, 128), v("ID"), scale=col["thh"])
         act(v("THD", 128, 256), v("NI"), scale=col["thl"])
-        act(v("RT", 0, 143), v("R1", 0, 143), scale=weights("rt", {0: 32, 1: 1}))
-        act(v("KB"), v("MI"), F.Relu, bias=1048576.0, scale=-1048576.0)
         gcp(v("DC", 0, 16), v("Z", 0, 16))
         iota(v("W8"), [[128, 4], [0, 2]], 6144, 4)
+        if "S" in TTQ:
+            for k, (src, a, b) in enumerate((("BO", 0.5, 0.0), ("BO", -0.5, 0.0))):
+                act(v("B3", 128 * k + 128, 128 * k + 256), v(src), scale=a)
+            for k, (src, a, b) in enumerate((("LT", 0.0, 8.0), ("LT", 16.0, -8.0), ("EQH", 2.0, -8.0))):
+                act(v("C3", 128 * k, 128 * k + 128), v(src), F.Identity, bias=b, scale=a)
+        act(v("TF"), v("ID"), scale=weights("tf", {2: 0, 3: 0, 4: 0, 11: 65536}, 4096))
+        weights("pay", {0: 2048 + 8 * 4096}, 2048)
+        iota(v("KB3"), [[0, 32], [-16384, 3]], 16384)
+        act(v("KB3"), v("KB3"), F.Relu)
+        act(v("LW", 2, 96, 3), v("JW"), F.Identity, bias=1024.0)
+        tt(v("LPD"), v("LPD"), v("GT"), A.add)
+        act(v("NLD"), v("LPD"), scale=-1.0)
+
+    def last_constants():
+        hold.append(v("FO", CH[-2], CH[-1]))
+        weights("y8", {0: 8})
+        act(v("B128"), v("BO"), scale=128.0)
+        for name, a, b in ((v("TE", 8, 16, 2), 2.0, 2560.0), (v("S4"), 4096.0, 1024.0), (v("TE", 0, 8, 2), 0.0, 0.0)):
+            act(name, v("JW", 0, 4), F.Identity, bias=b, scale=a)
+        act(newcol("keep"), ki, F.Sign, bias=-2.5)
+        act(v("K34"), v("ID"), F.Relu, scale=col["keep"])
+        weights("b2", {2: 8192})
+        act(v("ONS"), v("Z", 0, 128), F.Identity, bias=1.0 / 4096)
+        act(v("CWM"), v("MI"), F.Identity, bias=weights("rb", {8: 32, 9: 1}), scale=weights("rs", {5: 64, 6: 2, 12: 1}))
+        tt(v("CWM"), v("CWM"), v("BO"), A.mult)
+        act(v("MK12"), v("MI"), scale=weights("m16", {12: 1 / 16}))
+        tt(v("MK12"), v("MK12"), v("BO"), A.mult)
+        act(newcol("h"), q(2), F.Identity, bias=col["rt"], scale=0.25)
+        for name, c in (("RO", weights("ro", {10: 128, 11: 1})), ("RH", col["h"]), ("RT", col["rt"])):
+            act(v(name, 0, 143), v("R1", 0, 143), scale=c)
+        act(v("KB"), v("MI"), F.Relu, bias=1048576.0, scale=-1048576.0)
         act(newcol("o64"), odd, scale=64.0)
         act(newcol("g128"), kg, F.Identity, bias=col["o64"], scale=-64.0)
         act(v("W8"), v("W8"), F.Identity, bias=col["g128"])
-        act(v("ID10"), v("ID"), scale=-1024.0)
-        bias[0] = 12.0
-        inv = v("PW", 56, 57)
-        op("V", lambda: g.vector.reciprocal(ap(inv), ap(v("PW", 48, 49))), [v("PW", 48, 49)], [inv], 0.25)
-        act(newcol("cut"), inv, F.Identity, bias=0.499, scale=-4095.0)
-        ts(v("SI", 0, 512), v("JI"), inv, A.mult, col["cut"], A.subtract)
-        bits(v("SI", 0, 512), v("SI", 0, 512), 0, 1)
-        gcp(v("JB"), v("SI", 0, 512))
-        act(v("JF"), v("JB"), scale=4194304.0)
-        bias[0] = 0.0
+        hold.pop()
 
     def slots_reset(t):
-        if t == 2:
-            gcp(v("TBS", 0, 128), v("DFB"))
-        gcp(v("P1W", 0, 128), v("DF", 0, 128))
-        gcp(v("P1W", 512, 576), v("DF", 128, 192))
+        gcp(v("P1W", 384, 576), v("DF"))
 
     def lanes(t):
         c0 = 896 * t % 2048 // 16
@@ -912,22 +1026,26 @@ def rank_program(g, core, T, topo):
             turn(v("VB", 128, 256), v("VB", 0, 128))
             mm([(v("q4", 2 * b + s1, 128, 8), v("SWB", 256 * s1 + 128 * g2, 256 * s1 + 128 * g2 + 128), v("VB", 128 + 32 * b + 16 * g2, 144 + 32 * b + 16 * g2))
                 for b in range(4) for s1 in (0, 1) for g2 in (0, 1)], each=2)
-            ts(v("NW"), v("q4", 0, 128), 0.0, A.is_ge)
-            act(v("HW"), v("q4", 0, 128))
+            parts, mid = ((0, 128, 0),), 0
         else:
             mm(wrap(v("q4", 0, 128), "RH", "TB", 0, 2048))
-            ts(v("NW", 0, 128 - c0), v("q4", c0, 128), 2048.0, A.is_ge)
-            ts(v("NW", 128 - c0, 128), v("q4", 0, c0), 2048.0, A.is_ge)
-            act(v("HW", 0, 128 - c0), v("q4", c0, 128), F.Identity, bias=-2048.0)
-            act(v("HW", 128 - c0, 128), v("q4", 0, c0), F.Identity, bias=-2048.0)
-        mm([(v("q3", 128, 256), v("NW"), v("BO"))])
-        cp(v("TTB", 0, 128), v("q3", 128, 256))
-        tt(v("TTB", 128, 256), v("q3", 128, 256), v("LT"), A.mult)
-        tt(v("TTB", 256, 384), v("q3", 128, 256), v("EQH"), A.is_lt)
+            parts, mid = ((0, 128 - c0, c0), (128 - c0, 128, 0)), 2048
+        for lo, hi, at in parts:
+            act(v("NW", lo, hi), v("q4", at, at + hi - lo), F.Sign, bias=0.5 - mid)
+        if TTQ[t] == "S":
+            mm([(v("q4", 128, 512), v("NW"), v("B3")), (v("q4", 128, 512), v("ID"), v("C3"))])
+            act(v("TTB"), v("q4", 128, 512), F.Relu)
+        for lo, hi, at in parts:
+            act(v("HW", lo, hi), v("q4", at, at + hi - lo), F.Identity, bias=-float(mid))
+        if TTQ[t] == "V":
+            mm([(v("q3", 128, 256), v("NW"), v("B3", 0, 128)), (v("q3", 128, 256), v("ON"), v("B3", 0, 128))])
+            cp(v("TTB", 0, 128), v("q3", 128, 256))
+            tt(v("TTB", 128, 256), v("q3", 128, 256), v("LT"), A.mult)
+            tt(v("TTB", 256, 384), v("q3", 128, 256), v("EQH"), A.is_lt)
         mm([(v("q3", 256, 264), v("TTB", 128 * k, 128 * k + 128), v("RH3", 8 * j, 8 * j + 8)) for j, k in enumerate((0, 1, 2, 2))])
         mm([(v("q3", 264, 265), v("TTB", 0, 128), v("ON", 0, 1))])
-        mm([(v("q5", 0, 128), v("LPB"), v("NW")), (v("q5", 0, 128), v("TTB", 0, 128), v("UT"))])
-        act(v("POS"), v("q5", 0, 128))
+        mm([(v("q5", 0, 128), v("LPH"), v("NW")), (v("q5", 0, 128), v("TTB", 0, 128), v("UT"))])
+        act(v("POS"), v("q5", 0, 128), F.Identity, bias=col["lph"])
         cp(v("OFu"), v("q3", 256, 264))
         sca(v("CW"), v("OFu"), v("C1"))
         ts(v("EX"), v("JW"), v("q3", 264, 265), A.is_ge, 4096.0, A.mult)
@@ -936,8 +1054,11 @@ def rank_program(g, core, T, topo):
         cp(v("CLu"), v("q3", 288, 320))
         for lo, hi, b in ((0, FIRST, "q5"), (FIRST, 512, "q3")):
             a, z = lo // 16, hi // 16
+            hold[:] = [v("TY", 0, FIRST)] if lo and AHEAD else []
             gtt(v("OH", lo, hi), v("POS"), v("CLu", a, z), v("JI", lo, hi), A.is_equal)
+            hold[:] = [v(("STu", "Ku")[AHEAD - 2], 0, a)] if lo and AHEAD > 1 else []
             gtt(v("TY", lo, hi), v("HW"), v("CLu", a, z), v("OH", lo, hi), A.mult)
+            del hold[:]
             mm([(v(b, 320 + a, 320 + z), v("IDQ"), v("EX", a, z))] + wrap(v(b, 320 + a, 320 + z), "R1", "TY", lo, hi))
             cp(v("STu", a, z), v(b, 320 + a, 320 + z))
             gat(v("Ku", lo, hi), v("RI32"), v("STu", a, z))
@@ -953,6 +1074,9 @@ def rank_program(g, core, T, topo):
 
     def fetch(t):
         pick(TBLQ)(v("TBL", 0, 512), v("TB"), v("Lu"))
+
+    def pay(lo, hi):
+        return v("q2", lo, hi) if lo < EARLY else v("q7", lo - EARLY, hi - EARLY)
 
     def check(t):
         nch = len(CH) - 1
@@ -973,17 +1097,23 @@ def rank_program(g, core, T, topo):
             cuts = [CH[k] + (CH[k + 1] - CH[k]) * j // SPLIT[k] for j in range(SPLIT[k] + 1)]
             for lo, hi_ in zip(cuts, cuts[1:]):
                 sgat(v("sig", 16 * lo, 16 * hi_), v("SG"), v("Ku", lo, hi_))
-        ts(v("KF"), v("Ku"), 1023.0, A.min, -1.0 / 2048, A.mult)
-        ts(v("PM"), v("Ku"), 1024.0, A.is_ge, 100663296.0, A.mult)
         gat(v("Wu"), v("WI" if t == 0 else "WD"), v("Lu"))
         bias[0] = 20.0
+        gcp(v("KF", 0, FIRST), v("Ku", 0, FIRST))
+        gcp(v("KF", FIRST, 512), v("Ku", FIRST, 512))
         gcp(v("Wf"), v("Wu"))
         bias[0] = 0.0
 
-        mm([(v("q2"), v(l), v(r)) for l, r in (("IDK", "KF"), ("ID", "Wf"))], last=False)
+        for lo, hi_ in ((0, EARLY), (EARLY, 512)):
+            mm([(pay(lo, hi_), v("ID"), v("Wf", lo, hi_))], last=False)
+            mm([(pay(lo, hi_), v("TF"), v("TBL", lo, hi_))], first=False, last=False)
 
         def ft(k, other):
-            return ch("FT", k, 512 * other)
+            return ch("FT", k, (EARLY, 0)[other] if CH[k] < EARLY else (EARLY, 512)[other])
+
+        def marks(k):
+            o = pay(CH[k], CH[k + 1])
+            mm([(o, v("IDF"), ft(k, 0)), (o, v("ID"), ch("FO", k))], first=False, last=CH[k + 1] in (EARLY, 512))
 
         hi = lambda k: v("HI", 32 * k, 32 * k + 32)
         ts(hi(1), v("HY", 32, 64), -1600.0, A.add)
@@ -993,44 +1123,37 @@ def rank_program(g, core, T, topo):
         ts(hi(4), hi(3), 5, A.arith_shift_right)
         bits(hi(5), hi(3), 0, 31)
         ts(v("HF", 32, 64), hi(4), 1.0 / 32, A.mult)
-        def after(k):
-            j = k - LAG
-            return [v("RR", 384 * j + 256, 384 * j + 384)] if 0 <= j < TURNED else []
+        def after(k, j=0):
+            return [v(x, 384 * i + 256, 384 * i + 384) for x, i in AFTER.get((k, j), ())]
 
         def turned(k):
             b, mf = banks[k], "mf%d" % (k & 1)
             r = lambda j, n=1: v(b, 128 * j, 128 * (j + n))
             u = lambda x, j, n=1: v(x, 384 * k + 128 * j, 384 * k + 128 * (j + n))
-            cuts = [128 * j // SPLIT[k] for j in range(SPLIT[k] + 1)]
-            hold[:] = after(k)
-            for lo, hi_ in zip(cuts, cuts[1:]):
+            cuts = [128 * j // VSPLIT[k] for j in range(VSPLIT[k] + 1)]
+            for j, (lo, hi_) in enumerate(zip(cuts, cuts[1:])):
+                hold[:] = after(k, j) + [v(mf, 16 * lo - 1, 16 * lo)] * (j > 0)
                 gtt(v(mf, 16 * lo, 16 * hi_), v("XP"), v("Wu", CH[k] + lo, CH[k] + hi_), v("sig", 16 * (CH[k] + lo), 16 * (CH[k] + hi_)), A.max)
             del hold[:]
             sums = lambda x, w: [(v(b, p, 384, 16), x(p), v(w)) for p in range(16)]
             last = sums(lambda p: v(mf, p, 2048, 16), "WM")
-            mms(sums(lambda p: tile("sg", k, p), "WS"),
-                [(r(2), ch("KF", k), v("WK")), (r(0), v("ON"), v("THD", 0, 128)), (r(0), v("ON"), v("THD", 128, 256)), (r(2), ch("PM", k), v("ID8"))],
-                last[:8], last[8:])
+            mms(sums(lambda p: tile("sg", k, p), "WS"), [(r(0), v("ON"), v("THD", 0, 128)), (r(0), v("ON"), v("THD", 128, 256))],
+                [(r(2), ch("KF", k), v("WK"))], last[:8], last[8:])
             bias[0] = SOON
             ts(u("RR", 0, 2), r(1, 2), MAGIC, A.add, MAGIC, A.subtract)
             tt(u("RR", 2), r(2), u("RR", 1), A.is_equal)
             act(u("AA", 0, 2), u("RR", 0, 2), F.Abs, bias=-1.0)
             rest = v("AS", 128 * (k & 1), 128 * (k & 1) + 128)
             more = [(r(3), v(l), x) for l, x in (("ID15", u("RR", 0)), ("ID", u("AA", 0)), ("ID", u("AA", 1)), ("IDN", u("RR", 2)))]
-            if ENDS[k] == "V":
-                act(rest, r(0), F.Identity, bias=v("thB", 2, 3), scale=-1.0)
-                mm(more)
-                tt(u("AA", 2), r(3), rest, A.is_gt)
-            else:
-                act(rest, r(0))
-                mm([(r(3), v("IDW"), rest)] + more)
-                act(u("AA", 2), r(3), F.Sign, bias=v("thB", 3, 4))
+            act(rest, r(0), F.Identity, bias=v("thB", 2, 3), scale=-1.0)
+            mm(more)
+            tt(u("AA", 2), r(3), rest, A.is_gt)
             mm([(r(1), u("AA", 2), v("ID")), (r(2), u("RR", 2), v("NI"))], each=1)
             act(ft(k, 1), r(2), F.Identity, bias=1.0)
             act(ft(k, 0), r(1), F.Relu)
             mm([(r(0), v("ZT"), ft(k, 1))])
             act(ch("FO", k), r(0), F.Relu, scale=16777216.0)
-            mm([(ch("q2", k), v("IDF"), ft(k, 0)), (ch("q2", k), v("ID"), ch("FO", k))], first=False, last=False)
+            marks(k)
             bias[0] = 0.0
 
         for k in range(nch):
@@ -1048,92 +1171,95 @@ def rank_program(g, core, T, topo):
             gtt(tile("mm", k), v("X"), ch("Wu", k), tile("sg", k), A.max)
             del hold[:]
             ends = [part("RX", "hg", k), part("R2", "mm", k)]
-            mms(part("RN", "sg", k), [(e, v("ID"), ch("KF", k)), (e, v("ID"), ch("PM", k))], *(ends if TYP[t][k] == "V" else ends[::-1]))
+            mms(part("RN", "sg", k), [(e, v("IDK"), ch("KF", k))], *ends)
             bias[0] = SMALL
-            cp(v("RD", 0, n), e)
+            ts(v("RD", 0, n), e, MAGIC, A.add, MAGIC, A.subtract)
+            if k >= nch - OWN:
+                ts(ch("GA", k), e, 2048.0, A.mult, v("thB", 5, 6), A.is_gt)
             tt(ft(k, 1), e, v("RD", 0, n), A.not_equal)
+            if k < nch - OWN:
+                act(ch("GA", k), e, F.Relu, bias=v("thB", 1, 2), scale=2048.0)
             mm([(v(b, 256, 256 + n), v("ZT"), ft(k, 1))])
-            act(ch("GA", k), e, F.Relu, bias=v("thB", 1, 2), scale=2048.0)
             tt(ft(k, 0), ft(k, 1), ch("GA", k), A.min)
             act(ch("FO", k), v(b, 256, 256 + n), F.Relu, scale=16777216.0)
-            mm([(ch("q2", k), v("IDF"), ft(k, 0)), (ch("q2", k), v("ID"), ch("FO", k))], first=False, last=k == nch - 1)
+            marks(k)
             bias[0] = 0.0
 
     def post(t):
         rp = lambda k, n=1: v("RP", 32 * k, 32 * (k + n))
         lw = lambda k, n=1: v("LW", 32 * k, 32 * (k + n))
         dl = lambda k: v("DL", 32 * k, 32 * k + 32)
-        n_, much, some = v("q3", 0, 32), rp(0), rp(1)
-        act(v("PAY"), v("q2"), F.Identity, bias=2048.0)
-        mm(wrap(v("q3", 0, 64), "R1", "FT", 0, 1024))
-        ts(rp(1, 2), v("q3", 0, 64), 0.5, A.is_gt)
-        ts(much, n_, 3.5, A.is_gt)
-        mm([(v("q5", 0, 64), v(l), rp(k, 2)) for l, k in (("BO", 1), ("NBO", 0), ("LPB", 1), ("NLP", 0))]
-           + [(v("q5", 32 * h + 1, 32 * h + 32), v(l), v("RP", 32 * (h + k), 32 * (h + k) + 31)) for h in (0, 1) for l, k in (("NLP", 1), ("LPB", 0))])
+        a = EARLY // 16
+        n_, much, some = v("q3", a, a + 32), rp(0), rp(1)
+        for lo, hi in ((0, a), (a, 32)):
+            n = hi - lo
+            act(v("PAY", 16 * lo, 16 * hi), pay(16 * lo, 16 * hi), F.Identity, bias=col["pay"])
+            mm(wrap(v("q3", 2 * lo, 2 * hi), "R1", "FT", 32 * lo, 32 * hi))
+            ts(v("RP", 32 + lo, 32 + hi), v("q3", a + lo, a + hi), 0.5, A.is_gt)
+            ts(v("RP", lo, hi), v("q3", a + lo, a + hi), 3.5, A.is_gt)
+            ts(v("RP", 64 + lo, 64 + hi), v("q3", 32 + a, 64) if lo else v("q3", 0, a), 0.5, A.is_gt)
+            one = max(lo, 1)
+            for h, (bo, nbo, lp, nlp) in enumerate((("NBO", "BO", "LPD", "NLD"), ("BO", "NBO", "LPB", "NLP"))):
+                mm([(v("q5", 32 * h + lo, 32 * h + hi), v(l), v("RP", 32 * (h + k) + lo, 32 * (h + k) + hi)) for l, k in ((bo, 1), (nbo, 0), (lp, 1), (nlp, 0))]
+                   + [(v("q5", 32 * h + one, 32 * h + hi), v(l), v("RP", 32 * (h + k) + one - 1, 32 * (h + k) + hi - 1)) for l, k in ((nlp, 1), (lp, 0))])
+            for k in (0, 1):
+                scan(v("LW", 3 * lo + k, 3 * hi, 3), v("q5", 32 * k + lo, 32 * k + hi), v("ZF", 0, n), A.add,
+                     v("LW", 3 * lo - 3 + k, 3 * lo - 2 + k) if lo else 4608.0 - k)
+            scan(v("LW", 96 + 3 * lo, 96 + 3 * hi), v("KB3", 0, 3 * n), v("LW", 3 * lo, 3 * hi), A.add, 0.0, A.min)
+            cp(v("PFu", lo, hi), v("LW", 98 + 3 * lo, 96 + 3 * hi, 3))
+            for x in range(lo, hi, PIECE):
+                sca(v("P1W"), v("PFu", x, min(hi, x + PIECE)), v("PAY", 16 * x, 16 * min(hi, x + PIECE)))
         tt(dl(0), n_, v("HF", 0, 32), A.is_ge)
         tt(dl(2), n_, v("HI", 160, 192), A.add)
-        for k in (0, 1):
-            scan(lw(2 + k), v("q5", 32 * k, 32 * k + 32), v("ZF", 0, 32), A.add, 4095.0 + 512 * k)
-        tt(lw(4), lw(2), lw(3), A.min)
-        tt(lw(5), lw(4), v("JD"), A.min)
-        cp(v("PFu"), lw(5))
         tt(dl(1), v("HF", 32, 64), dl(0), A.subtract)
         act(dl(5), much, scale=32.0)
         act(dl(6), some, scale=8192.0)
         tt(dl(4), dl(2), much, A.mult)
         tt(dl(3), dl(1), dl(5), A.mult)
-        if t == 2:
-            bias[0] = LAST
-            sca(v("TBS"), v("PFu"), v("TBL", 0, 512))
-            candidates()
-            hold.append(v("BU", 128, 256))
-            bias[0] = 0.0
-        if t == 2:
-            sca(v("P1W"), v("PFu"), v("PAY"))
-        else:
-            op("V", lambda: g.vector.tensor_tensor(ind(v("P1W"), v("PFu")), ap(v("PAY")), ap(v("JF")), A.add), [v("PAY"), v("JF"), v("PFu")], [v("P1W")],
-               ew(512, SCATTER))
-        del hold[:]
         mms([(v("q4"), v("X2D"), v("TBL", 0, 512))],
             [(v("q4", i, 512, 16), v("UN", 16 + 128 * i - r, 144 + 128 * i - r), dl(k)) for r, k in ((1, 4), (2, 6), (0, 3)) for i in range(16)])
         act(v("TBn"), v("q4"))
         if t < 2:
             mm([(v("q2", 0, 32), v("ONS"), v("EX")), (v("q2", 0, 32), v("ON"), some)])
             act(v("BS"), v("q2", 0, 32), scale=-1.0, accum_out=v("thB", 4, 5))
-            ts(v("CN", 0, 1), v("thB", 4, 5), 4096.0, A.add)
-            bits(v("CN", 1, 2), v("CN", 0, 1), 0, 255)
-            ts(v("thB", 1, 2), v("CN", 1, 2), -2048.0, A.mult, v("thB", 0, 1), A.add)
-            act(v("thB", 3, 4), v("thB", 1, 2), F.Identity, bias=col["th"], scale=1 / 2048)
-            act(v("thB", 2, 3), v("thB", 3, 4), F.Identity, bias=-0.5, scale=-1.0)
+            cn = lambda k: v("CN", k, k + 1)
+            act(cn(0), v("thB", 4, 5), F.Identity, bias=-255 / 512, scale=1 / 256)
+            act(cn(1), cn(0), F.Identity, bias=MAGIC)
+            act(cn(2), cn(1), F.Identity, bias=256 * MAGIC, scale=-256.0)
+            act(v("thB", 2, 3), cn(2), F.Identity, bias=v("thB", 4, 5))
+            act(v("thB", 1, 2), v("thB", 2, 3), F.Identity, bias=v("thB", 0, 1), scale=-2048.0)
+            act(v("thB", 5, 6), v("thB", 1, 2), scale=-1.0)
         bias[0] = 2.0
         ts(v("AI", 0, 64), v("P1W", 512, 576), 8388608.0 + 2048.0, A.subtract, 0.0, A.max)
         bits(v("AI", 64, 128), v("AI", 0, 64), 0, 4095)
         cp(v("AH", 0, 64), v("AI", 64, 128))
-        cp(v("BI", 0, 128), v("P1W", 0, 128))
-        direct = t == 2
-        if not direct:
-            bits(v("BI", 128, 256), v("BI", 0, 128), 22, 1)
-            ts(v("AH", 64, 192), v("BI", 128, 256), v("PW", 48, 49), A.mult)
+        cp(v("PI", 0, 192), v("P1W", 384, 576))
+        bits(v("PI", 192, 384), v("PI", 0, 192), 12, 255)
+        cp(v("TBS"), v("PI", 192, 320))
+        ts(v("AH", 64, 128), v("PI", 320, 384), col["y8"], A.subtract, col["rt"], A.mult)
         bias[0] = 0.0
         to = v("q5", 128, 132)
-        mm(wrap(to, "R1", "AH", 0, 64) if direct else wrap(v("q5", 128, 140), "R1", "AH", 0, 192))
+        mm(wrap(v("q5", 128, 136), "R1", "AH", 0, 128))
         mm([(v("q3", 64, 128), v("B128"), v("AH", 0, 64)), (v("q3", 64, 128), v("BO"), v("C1", 0, 64))])
         act(v("AF", 256, 260), to, F.Identity, bias=0.5, scale=-128.0)
-        bits(v("AI", 128, 192), v("AI", 0, 64), 17, 31)
-        bits(v("AI", 192, 256), v("AI", 0, 64), 12, 31)
+        act(v("TE", 9, 16, 2), to)
+        cp(v("AU", 0, 8), v("q5", 128, 136))
+        ts(v("AF", 352, 416), v("P1W", 512, 576), 8388608.0, A.is_ge)
+        gtt(v("AI", 0, 64), v("RI32"), v("AU", 4, 8), v("AF", 352, 416), A.mult)
+        bits(v("AI", 128, 192), v("AI", 0, 64), 5, 31)
+        bits(v("AI", 192, 256), v("AI", 0, 64), 0, 31)
         cp(v("AH", 192, 320), v("AI", 128, 256))
-        cp(v("AU", 0, 4 if direct else 12), v("q5", 128, 132 if direct else 140))
         sgat(v("AB", 0, 64), v("TS"), v("AU", 0, 4))
-        sca(v("TB"), v("Lu"), v("TBn"))
+        for k in range(PARTS):
+            sca(v("TB"), v("Lu", 32 * k // PARTS, 32 * (k + 1) // PARTS), v("TBn", 512 * k // PARTS, 512 * (k + 1) // PARTS))
         for c in range(4):
             act(v("AF", 64 * c, 64 * c + 64), v("q3", 64, 128), F.Abs, bias=v("AF", 256 + c, 257 + c))
         for c in range(4):
-            act(v("AF", 288, 352), v("AF", 64 * c, 64 * c + 64), F.Relu, bias=v("S4", c, c + 1), scale=-4096.0, accum_out=v("AF", 260 + c, 261 + c))
+            act(v("AF", 288, 352), v("AF", 64 * c, 64 * c + 64), F.Relu, bias=v("S4", c, c + 1), scale=-4096.0, accum_out=v("TE", 2 * c + 1, 2 * c + 2))
         mm([(v("q4", 0, 64), win("R1", 0), v("AH", 192, 256)), (v("q4", 0, 64), win("R1", 1), v("AH", 256, 320)), (v("q4", 0, 64), v("K34"), v("AB", 0, 64))])
         act(v("AB", 64, 128), v("q4", 0, 64), F.Identity, bias=col["b2"])
-        tt(v("AF", 268, 272), v("AF", 260, 264), v("W4"), A.min)
-        tt(v("AF", 272, 276), to, v("AF", 268, 272), A.max)
-        cp(v("AU", 12, 16), v("AF", 272, 276))
+        scan(v("TE", 16, 24), v("TE", 0, 8), v("TE", 8, 16), A.min, 0.0, A.max)
+        cp(v("AU", 12, 16), v("TE", 17, 24, 2))
         sca(v("TB"), v("AU", 12, 16), v("AB", 64, 128))
         if t < 2:
             gadd(v("FL%d" % (t + 1)), row("TB", 2))
@@ -1153,18 +1279,17 @@ def rank_program(g, core, T, topo):
         bi = lambda k: v("BI", 128 * k, 128 * k + 128)
         bf = lambda lo, hi: v("BF2", lo, hi)
         dw = "DW%d" % t
-        if t < 2:
-            sgat(v("TBS", 0, 128), v("TBL"), v("AU", 4, 12))
-            candidates()
+        candidates()
         act(v("WB"), v("q7", 272, 280), F.Identity, bias=4096.0)
-        cp(v("CH"), bi(4))
+        gcp(v("CH"), bi(4))
         turn(v("CT"), v("CH"))
         tt(v("DC", 1, 128), v("CT", 0, 127), v("CT", 1, 128), A.subtract)
-        bits(bi(2), bi(0), 0, 2048)
-        bits(bi(5), bi(0), 0, 4095)
+        bits(bi(5), v("PI", 0, 128), 0, 4095)
         ts(bf(384, 512), bi(5), -2048.0, A.add)
-        for h in (0, 1):
-            pick(CAND[t][h])(v("mm0", 1024 * h, 1024 * h + 1024), v("XE%d" % t), v("BU", 128 + 64 * h, 192 + 64 * h))
+        act(v("NB"), bf(384, 512), scale=-2048.0)
+        n = len(CAND[t])
+        for h in range(n):
+            pick(CAND[t][h])(v("mm0", 2048 * h // n, 2048 * (h + 1) // n), v("XE%d" % t), v("BU", 128 + 128 * h // n, 128 + 128 * (h + 1) // n))
         for h in (0, 1):
             for b in (0, 1):
                 qb, lo = ("q0", "q1", "q2", "q6")[2 * h + b], 1024 * h + 512 * b
@@ -1187,16 +1312,15 @@ def rank_program(g, core, T, topo):
         mm([(v("q7", 256 + s1, 264, 2), swb(s1, g2), v(x, 16 * g2 + 15, 128, 32)) for s1 in (0, 1) for x in ("CT", "UU") for g2 in (0, 1)], each=4)
         mm([(v("q7", 264 + s1, 272, 2), swb(s1, g2), v("MB", g2, 8, 2)) for s1 in (0, 1) for g2 in (0, 1)], each=2)
         cp(v("BU", 24, 32), v("q7", 256, 264))
-        gtt(bf(256, 384), v("WE"), v("BU", 24, 32), bi(2), A.subtract)
+        gtt(bf(256, 384), v("WE"), v("BU", 24, 32), v("NB"), A.min)
         tt(v(dw, 128, 136), v("q7", 264, 272), v("WB"), A.max)
         ts(v("BU", 16, 24), v(dw, 128, 136), -4096.0, A.add)
+        op("V", lambda: g.vector.tensor_tensor(ind(v("WD"), v("BU", 16, 24)), ap(bf(256, 384)), ap(bf(384, 512)), A.max),
+           [bf(256, 512), v("BU", 16, 24)], [v("WD")], ew(128, SCATTER))
         if t == 2:
-            op("V", lambda: g.vector.tensor_tensor(ind(v("WD"), v("BU", 16, 24)), ap(bf(256, 384)), ap(bf(384, 512)), A.max),
-               [bf(256, 512), v("BU", 16, 24)], [v("WD")], ew(128, SCATTER))
             fin.append(dma("Y", None, v("WD", 0, 2048), o=T.ym[:], lat=6.0))
             return
         tt(v(dw, 0, 128), bf(256, 384), bf(384, 512), A.max)
-        sca(v("WD"), v("BU", 16, 24), v(dw, 0, 128))
         for t2 in range(t + 1, 3):
             slot = 6 + t + t2
             send(slot, served(1 + t2), v("Di%d%d" % (t, t2)), v(dw))
@@ -1211,7 +1335,7 @@ def rank_program(g, core, T, topo):
             gcp(v("CW", 0, 512), v("Z", 0, 512))
         for h in (1, 0):
             gcp(v("WE", *piece(2 * t + 1, h)), v("WH%d" % t, *piece(2 * t + 1, h)))
-        hold.append(v("FT", CH[1], CH[2]))
+        hold.append(v("FO", 0, CH[1]))
         dma("Y", row("XE%d" % t, 2), v("FI%d" % t))
         hold.pop()
 
@@ -1239,6 +1363,8 @@ def rank_program(g, core, T, topo):
         slots_reset(t)
         check(t)
         helper(t)
+        if t == 0:
+            last_constants()
         post(t)
         if t < 2:
             lanes(t + 1)

import math
from concourse.bass import DstId, RemoteDMATransfer
from concourse.mybir import AluOpType as A, AxisListType, ActivationFunctionType as F

CH = (0, 128, 256, 384, 448, 512)
BANKS = ("q5", "q3", "q0", "q1", "q6")
TURNED = 3
SPLIT = (2, 1, 1, 1, 1)
MAGIC = 12582912.0
FIRST = 128
TYP = ("SSSSS", "SSSSS", "SSSSS")
SHARE = (128, 112, 112)
SIGS = 2
CAND = ("SSSS", "SSSS", "SVSV")
TBLQ = "S"
LOADS = ("X", "RI32", "SG", "WI")
PACE, CUT = 1, 896
LATE, LAST, SMALL, PATIENCE, WAKE = 2.0, 3.0, 0.0, 0.5, 0.18
EARLY, PIECE, VSPLIT = 256, 8, (2, 1, 1)
AFTER = {(2, 0): (("RR", 0),), (3, 0): (("RR", 1),), (4, 0): (("RR", 2),)}
SOON, LAG, XPB, TTQ, OWN, PARTS, AHEAD = 5.0, 2, "q1", "VVV", 1, 2, 2
GATHER, SCATTER, MATMUL = 1.56, 3.8, 0.55
SPEEDS = ((.85e-3, 1.1, 2.0), (.9e-3, 1.5, 3.8), (1.15e-3, 1.9, 5.0))
PLAN = ((1.1e-3, 1.08, 2.5), (0.9e-3, 1.45, 3.5), (1.0e-3, 2.0, 5.0)) + ((0.95e-3, 1.56, 3.8), (0.95e-3, 1.3, 3.0), (1.0e-3, 1.7, 4.0))
PASSES, STEPS, STARTS = 3, 200, 1
TUNE = ((.85e-3, 1.1, 2.0, .55, .13, .03), (.9e-3, 1.5, 3.8, .5, .15, .02), (1.0e-3, 1.25, 4.5, .62, .2, .02), (1.15e-3, 1.9, 4.5, .5, .15, .04))
ROUNDS, TRIES, LOSS, BAN, NEAR, GAIN = 12000, 10, 1.0, 8, 0.2, 0.6
JUMP, SEED, EVERY, SLACK = (0, 0, 0, 1, 1, 2, 3, 5), 1, 100, 0.0
ORDER, EST, LOG = [], [], []
SCRATCH = {}
SEMAPHORES = ["cV", "cS", "cP", "cG"]

PLACE = {}
BF, FP, I32, U16, H16 = "bfloat16", "float32", "int32", "uint16", "float16"


def _buf(name, cols, dtype, where="sbuf", pool=None):
    if pool:
        at = SCRATCH[pool][1][1] if pool in SCRATCH else 0
        PLACE[name] = (pool, at, cols, dtype)
        SCRATCH[pool] = ("sbuf", [128, at + (cols + 15) // 16 * 16], dtype)
    else:
        PLACE[name] = (name, 0, cols, dtype)
        SCRATCH[name] = (where, [128, cols], dtype)


for _n in ("BO", "NBO", "LT", "EQH", "GT", "ID", "NI", "LPB", "NLP", "ZT", "X2D", "K34", "B128", "TF", "LPD", "NLD",
           "IDF", "IDQ", "ON", "ONS", "CWM", "MK12", "C1", "ID5", "IDK", "LPH", "ID10", "ID14", "ID15", "IDN"):
    _buf(_n, 128, BF, pool="PB")
for _n in ("R1", "RI", "RH", "RX", "R2", "RN", "RU", "RO", "R0", "RT"):
    _buf(_n, 144, BF, pool="PB")
for _n, _c in (("WS", 24), ("WK", 128), ("B3", 384), ("C3", 384), ("THD", 256), ("TH2", 1), ("RH3", 32), ("UT", 128), ("SWB", 512), ("KIB", 128)):
    _buf(_n, _c, BF, pool="PB")
for _n, _c in (("COLS", 128), ("QH", 16), ("CR", 144), ("MG", 128), ("MI", 128), ("JW", 32), ("JC", 32), ("KB3", 96), ("J16", 32),
               ("W8", 8), ("W4", 4), ("S4", 4), ("K3", 3), ("DF", 192), ("ZF", 128), ("TMP", 128), ("KB", 128),
               ("WM", 24), ("TE", 32)):
    _buf(_n, _c, FP, pool="PF")
for _n, _c, _d in (
        ("X", 2064, BF), ("WD", 2560, FP), ("WI", 2560, I32), ("W16", 2048, H16), ("RI32", 1032, I32), ("SG", 1040, BF), ("TB", 2688, BF),
        ("Z", 640, BF), ("UN", 2064, BF), ("JI", 512, FP), ("L1", 64, BF),
        ("hyb", 128, I32), ("vfb", 128, I32), ("thi", 1, I32), ("KI", 4, I32), ("ST", 1024, BF), ("SI", 1280, I32),
        ("NW", 128, BF), ("NT", 128, BF), ("VB", 256, H16), ("HW", 128, FP), ("TY", 512, H16), ("POS", 128, FP), ("TTB", 384, BF), ("OFu", 8, U16),
        ("CW", 4224, BF), ("CC", 512, BF), ("CLu", 32, U16), ("OH", 512, BF), ("EX", 32, BF), ("Lf", 32, FP), ("Lu", 32, U16),
        ("TBL", 512, BF), ("Wu", 512, U16), ("Wf", 512, H16), ("Ku", 512, U16), ("KF", 512, H16), ("STu", 32, U16),
        ("HI", 256, I32), ("HF", 64, FP), ("HY", 64, FP), ("TS", 2688, BF), ("FT", 1024, BF), ("FO", 512, BF), ("RD", 256, FP), ("GA", 512, BF), ("PAY", 512, FP),
        ("sig", 8192, BF), ("mm0", 2048, BF), ("mm1", 2048, BF), ("hg0", 2048, BF), ("hg1", 2048, BF),
        ("XP", 2048, FP), ("mf0", 2048, FP), ("mf1", 2048, FP), ("RR", 1152, BF), ("AA", 1152, BF), ("XB", 128, BF), ("XR", 256, FP),
        ("RP", 96, BF), ("LW", 192, FP), ("PFu", 32, U16), ("DL", 224, BF), ("P1W", 1536, FP), ("TBn", 512, BF),
        ("thB", 6, FP), ("PI", 384, I32), ("AS", 256, FP), ("CN", 4, FP), ("BS", 32, FP),
        ("AI", 256, I32), ("AH", 320, H16), ("WB", 8, FP), ("MB", 8, H16), ("AF", 416, FP), ("AB", 128, BF), ("AU", 16, U16),
        ("BI", 768, I32), ("TBS", 128, BF), ("LX", 128, BF), ("NB", 128, FP), ("BF2", 512, FP), ("CH", 128, H16), ("CT", 128, H16), ("DC", 128, H16),
        ("NQ", 128, H16), ("UU", 128, H16), ("BU", 256, U16), ("HU", 8, U16), ("WE", 2560, FP), ("OUT", 256, FP),
        ("DW0", 136, FP), ("DW1", 136, FP), ("DW2", 136, FP)):
    _buf(_n, _c, _d)
for _t in range(3):
    _buf("XE%d" % _t, 2048, BF)
    _buf("WH%d" % _t, 2048, H16)
    _buf("FL%d" % _t, 128, BF, "dram")
    _buf("FI%d" % _t, 128, BF, "dram")
for _n in ("i01", "i02", "i12"):
    _buf("D" + _n, 136, FP)
for _b in range(8):
    _buf("q%d" % _b, 512, FP, "psum")
_NDMA, _NREM = 40, 22
SEMAPHORES += ["d%d" % k for k in range(_NDMA)] + ["l%d" % k for k in range(_NREM)] + ["r%d" % k for k in range(_NREM)]


def relays_of(core, T, topo):
    free = [c for c in topo.cores_of(core) if T.rank_of(c) is None and all(topo.may_write(c, d) for d in T.cores)]
    return ([c for c in free if topo.die(c) != topo.die(core)][0], [c for c in free if topo.die(c) == topo.die(core)][0])


def lanes_of(src, dst, T, topo):
    far = topo.engines(src, [d for d in T.cores if topo.chip(d) != topo.chip(src)][0])
    e = [k for k in topo.engines(src, dst) if topo.chip(src) != topo.chip(dst) or k not in far]
    return sum(1 << k for k in e), len(e)


def piece(k, h):
    cut = 1024 if k < 2 else CUT
    return (cut, 2048) if h else (0, cut)


def relay_program(g, core, T, topo):
    own = [c for c in T.cores if topo.chip(c) == topo.chip(core)]
    if not own or core not in relays_of(own[0], T, topo):
        return
    rank, sent = T.rank_of(own[0]), []
    far, near = relays_of(own[0], T, topo)
    n_on = len(topo.engines(own[0], core)) // 2

    def send(slot, dst, name, src, lo=0, hi=2048):
        mask, n = lanes_of(core, dst, T, topo)
        rid, pid, _ = topo.addr(dst)
        g.remote_dma(T[name][:, lo:hi], T[src][:, lo:hi], T.sem["r%d" % slot], T.sem["l%d" % slot], pid, rid, mask)
        sent.append((slot, n))
        return n

    def served(d):
        return T.cores[(rank - d) % len(T.cores)]

    h = 1 if core == far else 0
    for k in range(6):
        t, name, src = k // 2, ("XE%d", "WH%d")[k & 1] % (k // 2), ("X", "W16")[k & 1]
        if k < 2:
            g.wait_ge(T.sem["r%d" % (1 + 2 * k + h)], n_on)
        elif core == near and k >= PACE:
            g.wait_ge(T.sem["l%d" % (10 + 2 * (k - PACE) + h)], n)
        n = send(10 + 2 * k + h, served(1 + t), name, src, *piece(k, h))
    for slot, n in sent:
        g.wait_ge(T.sem["l%d" % slot], n)


def rank_program(g, core, T, topo):
    rank = T.rank_of(core)
    if rank is None:
        relay_program(g, core, T, topo)
        return
    N = len(T.cores)
    GQ = ("gq", 0, 1, 1, None)
    LQ = ("lq", 0, 1, 1, None)
    eng = {"V": g.vector, "S": g.scalar, "P": g.tensor, "G": g, "Y": g.sync}
    cnt = {"cV": 0, "cS": 0, "cP": 0, "cG": 0}
    known = {e: {} for e in eng}
    acc = {}
    nd, sent, fin, bias = [0], [], [], [0.0]
    psum = {"q%d" % b for b in range(8)}

    def v(name, lo=0, hi=None, step=1, rows=None):
        buf, at, cols, _ = PLACE[name]
        return (buf, at + lo, at + (cols if hi is None else hi), step, rows)

    def ap(x):
        name, lo, hi, step, rows = x
        r = slice(None) if rows is None else rows
        return T[name][r, lo:hi] if step == 1 else T[name][r, lo:hi:step]

    def wait(e, sem, val, clock):
        k = known[e]
        if k.get(sem, 0) < val:
            eng[e].wait_ge(T.sem[sem], val)
            k[sem] = val
        for s, c in clock.items():
            if k.get(s, 0) < c:
                k[s] = c

    def meet(lo, step, x):
        return step != x[3] or (lo - x[1]) % step == 0

    def deps(e, reads, writes):
        need = []
        for lst, wr in ((reads, False), (writes, True)):
            for x in lst:
                ex = x[0] in psum
                for a in acc.get(x[0], ()):
                    if ex and e == "P" and a[4] == "P":
                        continue
                    if ex and a[4] != e:
                        need.append(a)
                    elif a[1] < x[2] and x[1] < a[2] and (wr or a[3]) and (a[0] is None or x[4] is None or a[0] == x[4]) and meet(a[1], a[8], x):
                        need.append(a)
        need.sort(key=lambda a: -a[6])
        for a in need:
            wait(e, a[5], a[6], a[7])

    def note(e, reads, writes, sem, val, clock):
        for lst, wr in ((reads, False), (writes, True)):
            for x in lst:
                old = acc.setdefault(x[0], [])
                if x[0] in psum:
                    keep = [a for a in old if a[4] == e and not (wr and x[1] <= a[1] and a[2] <= x[2])]
                elif wr and x[3] == 1:
                    keep = [a for a in old if not (x[1] <= a[1] and a[2] <= x[2] and (x[4] is None or a[0] == x[4]))]
                else:
                    keep = [a for a in old if a[3] or a[4] != e or a[1:3] != (x[1], x[2]) or a[0] != x[4] or wr]
                keep.append((x[4], x[1], x[2], wr, e, sem, val, clock, x[3]))
                acc[x[0]] = keep

    prog, hold = [], []

    def call(e, emit, reads, writes, cost, lat=0.0):
        prog.append({"e": e, "emit": emit, "r": reads + hold, "w": writes, "cost": cost, "lat": lat, "bias": bias[0]})

    def op(e, fn, reads, writes, cost=0.1):
        def emit():
            deps(e, reads, writes)
            sem = "c" + e
            cnt[sem] += 1
            fn().then_inc(T.sem[sem], 1)
            clock = dict(known[e])
            clock[sem] = cnt[sem]
            note(e, reads, writes, sem, cnt[sem], clock)
        call(e, emit, reads, writes, cost)

    def mm(lst, first=True, last=True, each=0):
        cyc = sum(max(64, wid(r)) * (4 if SCRATCH[r[0]][2] == FP else 1) for _, _, r in lst)
        n = each or len(lst)

        def emit():
            val = cnt["cP"] + 1
            for k, (o, l, r) in enumerate(lst):
                deps("P", [l, r], [o] if k == 0 else [])
                m = g.tensor.matmul(ap(o), ap(l), ap(r), first and k % n == 0, last and k % n == n - 1)
            m.then_inc(T.sem["cP"], 1)
            cnt["cP"] = val
            clock = dict(known["P"])
            clock["cP"] = val
            note("P", [x[1] for x in lst] + [x[2] for x in lst], [x[0] for x in lst], "cP", val, clock)
        call("P", emit, [x[1] for x in lst] + [x[2] for x in lst], [x[0] for x in lst], (cyc, MATMUL))

    def mms(*parts):
        for n, lst in enumerate(parts):
            mm(lst, n == 0, n == len(parts) - 1)

    def dma(e, out, in_, o=None, i=None, lat=None):
        sem = "d%d" % nd[0]
        nd[0] += 1
        rd, wr = ([] if in_ is None else [in_]), ([] if out is None else [out])

        def emit():
            deps(e, rd, wr)
            eng[e].dma_start(ap(out) if o is None else o, ap(in_) if i is None else i).then_inc(T.sem[sem], 16)
            clock = dict(known[e])
            clock[sem] = 16
            note("D" + sem, rd, wr, sem, 16, clock)
        call(e, emit, rd, wr + ([] if i is None else [LQ]), 0.06, lat or (4.0 if out is not None and out[0] == "TB" else 2.3))
        return sem

    def gadd(out, in_):
        sem = "d%d" % nd[0]
        nd[0] += 1

        def emit():
            deps("G", [in_], [out])
            g.dma_start(ap(out), ap(in_), accum_op=A.add).then_inc(T.sem[sem], 16)
            clock = dict(known["G"])
            clock[sem] = 16
            note("D" + sem, [in_], [out], sem, 16, clock)
        call("G", emit, [in_], [out, GQ], 1.0, 2.3)

    def send(slot, dst, out, in_, cost=1.2):
        mask, n = lanes_of(core, dst, T, topo)
        sent.append(("l%d" % slot, n))

        def emit():
            deps("G", [in_], [])
            rid, pid, _ = topo.addr(dst)
            g.remote_dma(ap(out), ap(in_), T.sem["r%d" % slot], T.sem["l%d" % slot], pid, rid, mask)
            note("Dl%d" % slot, [in_], [], "l%d" % slot, n, {"l%d" % slot: n})
        call("G", emit, [in_], [(slot, 0, 1, 1, None), GQ], cost, 0.0)

    def hand_on(slot, name, cost=1.2):
        wide = 2048 - CUT
        far, near = relays_of(core, T, topo)
        e = topo.engines(core, near)
        sent.append(("l%d" % slot, len(e)))

        def emit():
            deps("G", [v(name, 0, 2048)], [])
            tr = []
            for h, (dst, lo) in enumerate(((near, 0), (far, CUT))):
                rid, pid, _ = topo.addr(dst)
                tr.append(RemoteDMATransfer(dst_ids=[DstId(rid=rid, pnc=pid)], dma_engine_mask=sum(1 << k for k in e[h * len(e) // 2:(h + 1) * len(e) // 2]),
                                            remote_sem=T.sem["r%d" % (slot + h)], src=ap(v(name, lo, lo + wide)), dst=ap(v(name, lo, lo + wide))))
            g.remote_dma_fused(tr, local_sem=T.sem["l%d" % slot])
            note("Dl%d" % slot, [v(name, 0, 2048)], [], "l%d" % slot, len(e), {"l%d" % slot: len(e)})
        call("G", emit, [v(name, 0, 2048)], [(slot, 0, 1, 1, None), GQ], cost, 0.0)

    def served(d):
        return T.cores[(rank - d) % N]

    def arrive(slot, buf, left, way):
        n = lanes_of(served(-1), core, T, topo)[1]
        call("R", lambda: note("Dr%d" % slot, [], [buf], "r%d" % slot, n, {"r%d" % slot: n}), [(left, 0, 1, 1, None)], [buf], way)

    def issue():
        hist, pred = {}, []
        for k, c in enumerate(prog):
            ps = {}
            for lst, wr in ((c["r"], False), (c["w"], True)):
                for x in lst:
                    h = hist.setdefault(x[0], [])
                    for a in h:
                        if a[0] == k:
                            continue
                        if x[0] in psum:
                            hit = wr or a[4] or a[5] != c["e"]
                        else:
                            hit = (wr or a[4]) and a[1] < x[2] and x[1] < a[2] and (a[3] is None or x[4] is None or a[3] == x[4]) and meet(a[1], a[6], x)
                        if hit:
                            ps[a[0]] = max(ps.get(a[0], 0.0), 0.0 if x in (GQ, LQ) or a[5] == c["e"] == "P" else prog[a[0]]["lat"] + WAKE)
            for lst, wr in ((c["r"], False), (c["w"], True)):
                for x in lst:
                    h = hist[x[0]]
                    if wr and x[3] == 1:
                        if x[0] in psum:
                            h[:] = [a for a in h if a[0] == k]
                        else:
                            h[:] = [a for a in h if not (x[1] <= a[1] and a[2] <= x[2] and (x[4] is None or a[3] == x[4]))]
                    e = (k, x[1], x[2], x[4], wr, c["e"], x[3])
                    if e not in h:
                        h.append(e)
            pred.append(ps)
        n = len(prog)
        rank_, cost, succ = [0.0] * n, [0.0] * n, [[] for _ in range(n)]
        for k in range(n):
            for p in pred[k]:
                succ[p].append(k)

        def assume(speed):
            cyc, ga, sc = speed
            for k in range(n - 1, -1, -1):
                c = prog[k]["cost"]
                if isinstance(c, tuple):
                    if c[1] == MATMUL:
                        c = c[0] * cyc * MATMUL
                    elif c[1] in (GATHER, SCATTER):
                        c = 0.05 + c[0] * cyc * (ga if c[1] == GATHER else sc)
                    else:
                        c = 0.03 + max(64, c[0] * c[1]) * cyc
                cost[k] = c
                rank_[k] = c + max([rank_[s] + pred[s][k] for s in succ[k]] or [prog[k]["lat"]])
            for k in range(n):
                rank_[k] += prog[k]["bias"]

        def length(order):
            free, done = {}, [0.0] * n
            for k in order:
                e = prog[k]["e"]
                t0 = max([done[p] + x for p, x in pred[k].items()] + [0.0 if e == "R" else free.get(e, 0.0)])
                done[k] = free[e] = t0 + cost[k]
            return max(done[k] + prog[k]["lat"] for k in range(n))

        def place(order, before, lag, head):
            start, busy = [0.0] * n, {}
            for k in order:
                t0 = max([start[p] + cost[p] + lag(p, k) for p in before[k]] or [head[k]])
                if prog[k]["e"] != "R":
                    iv = busy.setdefault(prog[k]["e"], [])
                    j = len(iv)
                    while j > 0 and iv[j - 1][1] > t0:
                        j -= 1
                    while j < len(iv) and iv[j][0] < t0 + cost[k] - 1e-9:
                        t0 = max(t0, iv[j][1])
                        j += 1
                    iv.insert(j, (t0, t0 + cost[k]))
                start[k] = t0
            return start

        def greedy():
            left = [len(p) for p in pred]
            at, free, start = [0.0] * n, {}, [0.0] * n
            ready = {k for k in range(n) if left[k] == 0}
            while ready:
                t0, _, k = min((at[k] if prog[k]["e"] == "R" else max(at[k], free.get(prog[k]["e"], 0.0)), -rank_[k], k) for k in ready)
                e, late = prog[k]["e"], t0 + PATIENCE * cost[k]
                if e in ("V", "S", "P", "G"):
                    for j in ready:
                        if prog[j]["e"] == e and at[j] < late and (rank_[j], -j) > (rank_[k], -k):
                            k = j
                    t0 = max(at[k], free.get(e, 0.0))
                ready.remove(k)
                start[k] = t0
                free[e] = t0 + cost[k]
                for s in succ[k]:
                    at[s] = max(at[s], t0 + cost[k] + pred[s][k])
                    left[s] -= 1
                    if left[s] == 0:
                        ready.add(s)
            return start

        def polish(order, costs):
            pl, lat = [list(p.items()) for p in pred], [c["lat"] for c in prog]

            def run(order, cs):
                free, last, done, why = {}, {}, [0.0] * n, [None] * n
                for k in order:
                    t0, e = 0.0, prog[k]["e"]
                    for p, x in pl[k]:
                        if done[p] + x > t0:
                            t0, why[k] = done[p] + x, (p, False)
                    if e != "R":
                        if free.get(e, 0.0) > t0:
                            t0, why[k] = free[e], (last[e], True)
                        last[e] = k
                    done[k] = free[e] = t0 + cs[k]
                end = max(range(n), key=lambda k: done[k] + lat[k])
                return done[end] + lat[end], end, why

            def ahead(order, k, j):
                lo, hi = order.index(j), order.index(k)
                need = {k}
                for x in order[lo:hi + 1][::-1]:
                    if x in need:
                        need.update(p for p, _ in pl[x])
                mid = order[lo:hi + 1]
                return None if j in need else order[:lo] + [x for x in mid if x in need] + [x for x in mid if x not in need] + order[hi + 1:]

            now, left = [run(order, cs) for cs in costs], STEPS
            while left > 0:
                moves = {}
                for _, k, why in now:
                    while why[k] is not None:
                        if why[k][1]:
                            moves[(k, why[k][0])] = True
                        k = why[k][0]
                for k, j in moves:
                    left -= 1
                    other = ahead(order, k, j)
                    if other is not None:
                        new = [run(other, cs) for cs in costs]
                        if math.prod(x[0] for x in new) < math.prod(x[0] for x in now) * (1 - 1e-6):
                            order, now = other, new
                            break
                else:
                    break
            EST.append((math.prod(x[0] for x in now) ** (1 / len(now)), left))
            return math.prod(x[0] for x in now), list(order)

        def refine(order):
            qs = [c["e"] for c in prog]
            lat = [c["lat"] for c in prog]
            ms_ = []
            for cyc, ga, sc, pe, wake, fix in TUNE:
                cs = []
                for c in prog:
                    c = c["cost"]
                    if isinstance(c, tuple):
                        c = (c[0] * cyc * pe if c[1] == MATMUL else 0.05 + c[0] * cyc * (ga if c[1] == GATHER else sc) if c[1] in (GATHER, SCATTER)
                             else fix + max(64, c[0] * c[1]) * cyc)
                    cs.append(c)
                pl = [[(p, x and x - WAKE + wake) for p, x in ps.items()] for ps in pred]
                sl = [[] for _ in range(n)]
                for k in range(n):
                    for p, x in pl[k]:
                        sl[p].append((k, x))
                ms_.append((cs, pl, sl))

            def full(order, lo=0, hi=n, old=None):
                last, before, behind = {}, [-1] * n, [-1] * n
                for k in order:
                    e = qs[k]
                    if e != "R":
                        j = last.get(e, -1)
                        before[k] = j
                        if j >= 0:
                            behind[j] = k
                        last[e] = k
                out, moves, val = [], [], 1.0
                for m, (cs, pl, sl) in enumerate(ms_):
                    done, tail = old[m][:2] if old else ([0.0] * (n + 1), [0.0] * (n + 1))
                    for k in order[lo:]:
                        t0 = done[before[k]]
                        for p, x in pl[k]:
                            if done[p] + x > t0:
                                t0 = done[p] + x
                        done[k] = t0 + cs[k]
                    for k in reversed(order[:hi]):
                        t0 = max(lat[k], tail[behind[k]])
                        for s, x in sl[k]:
                            if tail[s] + x > t0:
                                t0 = tail[s] + x
                        tail[k] = t0 + cs[k]
                    end = max(tail)
                    val *= end
                    moves += [(before[k], k) for k in order if before[k] >= 0 and done[before[k]] + tail[k] > end - NEAR]
                    out.append((done, tail, end))
                return val, out, moves, before, behind

            def moved(order, at, j, k, late):
                mid = order[at[j]:at[k] + 1]
                if late:
                    need = {j}
                    for x in mid:
                        if x in need:
                            need.update(succ[x])
                    return None if k in need else [x for x in mid if x not in need] + [x for x in mid if x in need]
                need = {k}
                for x in reversed(mid):
                    if x in need:
                        need.update(pred[x])
                return None if j in need else [x for x in mid if x in need] + [x for x in mid if x not in need]

            def judge(old, mid, out, before, behind):
                head, end_ = {}, {}
                for x in old:
                    head.setdefault(qs[x], before[x])
                    end_[qs[x]] = behind[x]
                val = 0.0
                for (cs, pl, sl), (done, tail, end) in zip(ms_, out):
                    d, free = {}, {e: done[x] for e, x in head.items()}
                    for k in mid:
                        t0 = free[qs[k]]
                        for p, x in pl[k]:
                            t1 = (d[p] if p in d else done[p]) + x
                            if t1 > t0:
                                t0 = t1
                        d[k] = t0 + cs[k]
                        if qs[k] != "R":
                            free[qs[k]] = d[k]
                    tl, nxt, top = {}, {e: tail[x] for e, x in end_.items()}, 0.0
                    for k in reversed(mid):
                        t0 = max(lat[k], nxt[qs[k]])
                        for s, x in sl[k]:
                            t1 = (tl[s] if s in tl else tail[s]) + x
                            if t1 > t0:
                                t0 = t1
                        if d[k] + t0 > top:
                            top = d[k] + t0
                        tl[k] = t0 + cs[k]
                        if qs[k] != "R":
                            nxt[qs[k]] = tl[k]
                    was = max([done[k] - cs[k] + tail[k] for k in mid])
                    val += math.exp(min(top - end, 3.0) / GAIN) - math.exp((was - end) / GAIN)
                return val

            def again(order, at, lo, hi, old, out, before, behind, turn_):
                head, end_ = {}, {}
                for x in old:
                    head.setdefault(qs[x], before[x])
                    end_[qs[x]] = behind[x]
                for i in range(lo, hi):
                    k = order[i]
                    at[k], e = i, qs[k]
                    if e != "R":
                        j = before[k] = head[e]
                        behind[j] = head[e] = k
                for e, j in head.items():
                    if e != "R":
                        behind[j] = end_[e]
                        before[end_[e]] = j
                before[n] = behind[n] = -1
                val = 1.0
                for m, (cs, pl, sl) in enumerate(ms_):
                    done, tail = out[m][:2]
                    far, i = max(hi - 1, max(at[x] if x >= 0 else 0 for x in end_.values())), lo
                    while i <= far:
                        k = order[i]
                        t0 = done[before[k]]
                        for p, x in pl[k]:
                            if done[p] + x > t0:
                                t0 = done[p] + x
                        t0 += cs[k]
                        if t0 != done[k]:
                            done[k] = t0
                            for s, _ in sl[k]:
                                if at[s] > far:
                                    far = at[s]
                            if behind[k] >= 0 and at[behind[k]] > far:
                                far = at[behind[k]]
                        i += 1
                    far, i = min([lo] + [at[before[x]] for x in order[lo:hi] if before[x] >= 0]), hi - 1
                    while i >= far:
                        k = order[i]
                        t0 = max(lat[k], tail[behind[k]])
                        for s, x in sl[k]:
                            if tail[s] + x > t0:
                                t0 = tail[s] + x
                        t0 += cs[k]
                        if t0 != tail[k]:
                            tail[k] = t0
                            for p, _ in pl[k]:
                                if at[p] < far:
                                    far = at[p]
                            if before[k] >= 0 and at[before[k]] < far:
                                far = at[before[k]]
                        i -= 1
                    end = max(tail)
                    val *= end
                    out[m] = (done, tail, end)
                done, tail, end = out[turn_ % len(ms_)]
                end -= NEAR
                return val, [(before[k], k) for k in order if done[before[k]] + tail[k] > end and before[k] >= 0]

            seed, order = SEED, list(order)
            val, out, moves, before, behind = full(order)
            before.append(-1)
            behind.append(-1)
            best, banned, at = (val, list(order)), {}, [0] * n
            for i, k in enumerate(order):
                at[k] = i
            def sooner(order, m):
                cs, pl, _ = ms_[m]
                start, done, busy = [0.0] * n, [0.0] * n, {}
                for k in order:
                    t0 = max([done[p] + x for p, x in pl[k]] or [0.0])
                    if qs[k] != "R":
                        iv = busy.setdefault(qs[k], [])
                        j = len(iv)
                        while j > 0 and iv[j - 1][1] > t0:
                            j -= 1
                        while j < len(iv) and iv[j][0] < t0 + cs[k] - 1e-9:
                            t0 = max(t0, iv[j][1])
                            j += 1
                        iv.insert(j, (t0, t0 + cs[k]))
                    start[k], done[k] = t0, t0 + cs[k]
                return sorted(order, key=lambda k: (start[k], at[k]))

            for step in range(ROUNDS):
                if step % EVERY == 0:
                    other = sooner(order, step // EVERY % len(ms_))
                    new = full(other)
                    if new[0] < val * (1 + SLACK):
                        order = other
                        val, out, moves, before, behind = new
                        before.append(-1)
                        behind.append(-1)
                        for i, k in enumerate(order):
                            at[k] = i
                pick_ = None
                for _ in range(TRIES):
                    seed = (seed * 1103515245 + 12345) % 2147483648
                    j, k = moves[(seed >> 8) % len(moves)]
                    if banned.get((j, k), -1) > step:
                        continue
                    late = seed >> 7 & 1
                    for _ in range(JUMP[seed >> 4 & 7]):
                        if late and behind[k] >= 0:
                            k = behind[k]
                        elif not late and before[j] >= 0:
                            j = before[j]
                    if at[k] - at[j] > 150:
                        continue
                    mid = moved(order, at, j, k, late)
                    if mid is not None:
                        x = judge(order[at[j]:at[k] + 1], mid, out, before, behind)
                        if pick_ is None or x < pick_[0]:
                            pick_ = (x, j, k, mid)
                if pick_ is None or pick_[0] > LOSS * (1 - step / ROUNDS):
                    continue
                _, j, k, mid = pick_
                lo, hi = at[j], at[k] + 1
                old = order[lo:hi]
                order[lo:hi] = mid
                banned[(k, j)] = step + BAN
                val, moves = again(order, at, lo, hi, old, out, before, behind, step)
                if val < best[0]:
                    best = (val, list(order))
            EST.extend((x[2], 0) for x in full(best[1])[1])
            done, tail, end = full(best[1])[1][1]
            LOG[:] = [(done[k] - ms_[1][0][k], ms_[1][0][k], qs[k], (prog[k]["w"] + prog[k]["r"])[0][:3], end - (done[k] - ms_[1][0][k] + tail[k])) for k in best[1]]
            return best[1]

        if not ORDER:
            orders = []
            for speed in PLAN:
                assume(speed)
                fore = greedy()
                for _ in range(PASSES + 1):
                    orders.append(sorted(range(n), key=lambda k: (fore[k], k)))
                    back = place(sorted(range(n), key=lambda k: (-fore[k] - cost[k], -k)), succ, lambda p, k: pred[p][k], [c["lat"] for c in prog])
                    fore = place(sorted(range(n), key=lambda k: (-back[k] - cost[k], k)), pred, lambda p, k: pred[k][p], [0.0] * n)
            total = [1.0] * len(orders)
            for speed in SPEEDS:
                assume(speed)
                total = [x * length(o) for x, o in zip(total, orders)]
            ORDER[:] = orders[total.index(min(total))]
            costs = []
            for speed in SPEEDS:
                assume(speed)
                costs.append(list(cost))
            some = sorted(range(len(orders)), key=lambda i: total[i])
            some = [i for j, i in enumerate(some) if i // (PASSES + 1) not in [x // (PASSES + 1) for x in some[:j]]][:STARTS]
            ORDER[:] = refine(min(polish(orders[i], costs) for i in some)[1])
        for k in ORDER:
            prog[k]["emit"]()

    def wid(x):
        return (x[2] - x[1] + x[3] - 1) // x[3]

    def half(*xs):
        return 0.5 if all(SCRATCH[x[0]][2] in (BF, U16, H16) for x in xs) else 1.0

    def ew(w, f=1.0):
        return (w, f)

    def ind(win, off):
        return ap(win).indirect(ap(off))

    def tt(o, a, b, f):
        k = 1 if a[0] in psum or b[0] in psum else 2 * half(o, a, b)
        op("V", lambda: g.vector.tensor_tensor(ap(o), ap(a), ap(b), f), [a, b], [o], ew(wid(o), k))

    def ts(o, a, s1, f, s2=None, f2=None):
        rd = [a] + [x for x in (s1, s2) if isinstance(x, tuple)]
        p1 = ap(s1) if isinstance(s1, tuple) else s1
        p2 = ap(s2) if isinstance(s2, tuple) else s2
        w = ew(wid(o), half(o, a))
        if f2 is None:
            op("V", lambda: g.vector.tensor_scalar(ap(o), ap(a), p1, None, f), rd, [o], w)
        else:
            op("V", lambda: g.vector.tensor_scalar(ap(o), ap(a), p1, p2, f, f2), rd, [o], w)

    def bits(o, a, shift, mask):
        if shift:
            ts(o, a, shift, A.arith_shift_right, mask, A.bitwise_and)
        else:
            ts(o, a, mask, A.bitwise_and)

    def cp(o, a):
        op("V", lambda: g.vector.tensor_copy(ap(o), ap(a)), [a], [o], ew(wid(o), half(o, a)))

    def ms(o, c):
        op("V", lambda: g.vector.memset(ap(o), c), [], [o], ew(wid(o), half(o)))

    def least(o, a):
        op("V", lambda: g.vector.tensor_reduce(ap(o), ap(a), AxisListType.X, A.min), [a], [o], ew(wid(a)))

    def turn(o, a):
        op("V", lambda: g.vector.transpose(ap(o), ap(a)), [a], [o], ew(wid(o), half(o, a)))

    def gat(o, win, off):
        op("V", lambda: g.vector.tensor_copy(ap(o), ind(win, off)), [win, off], [o], ew(wid(o), 1.56))

    def sca(win, off, a):
        op("V", lambda: g.vector.tensor_copy(ind(win, off), ap(a)), [a, off], [win], ew(wid(a), 3.8))

    def gtt(o, win, off, b, f):
        op("V", lambda: g.vector.tensor_tensor(ap(o), ind(win, off), ap(b), f), [win, off, b], [o], ew(wid(o), 1.56))

    def scan(o, a, z, f, first=0.0, f2=A.add):
        col_ = isinstance(first, tuple)
        op("V", lambda: g.vector.tensor_tensor_scan(ap(o), ap(a), ap(z), ap(first) if col_ else first, f, f2), [a, z] + [first] * col_, [o],
           ew(wid(o), half(o, a, z)))

    def act(o, a, func=F.Copy, bias=None, scale=None, accum_out=None):
        kw = {}
        rd = [a]
        for k, x in (("bias", bias), ("scale", scale)):
            if isinstance(x, tuple):
                rd += [x]
                kw[k] = ap(x)
            elif x is not None:
                kw[k] = x
        if accum_out is not None:
            kw["accum_out"] = ap(accum_out)
        op("S", lambda: g.scalar.activation(ap(o), ap(a), func, **kw), rd, [o] + ([] if accum_out is None else [accum_out]), ew(wid(o)))

    def sgat(o, win, off):
        op("S", lambda: g.scalar.activation(ap(o), ind(win, off), F.Copy), [win, off], [o], ew(wid(o), 1.56))

    def pick(e):
        return gat if e == "V" else sgat

    def iota(o, pattern, base, ch=0):
        if SCRATCH[o[0]][2] == I32:
            op("G", lambda: g.iota(ap(o), pattern, base, ch), [], [o], 0.13 + 1.9e-3 * wid(o))
        else:
            op("G", lambda: g.iota(ap(o), pattern, base, ch, allow_small_or_imprecise_dtypes=True), [], [o], 0.13 + 1.9e-3 * wid(o))

    def gcp(o, a):
        op("G", lambda: g.affine_select(ap(o), ap(a), [[0, wid(o)]], A.is_equal, 0.0, 0, 0), [a], [o], 0.17 + 1.9e-3 * wid(o))

    def win(R, i):
        return v(R, 15 - i, 143 - i)

    def wrap(o, R, x, lo, hi):
        return [(o, win(R, i), v(x, lo + i, hi, 16)) for i in range(16)]

    def row(name, q):
        return v(name, 0, 2048, 1, slice(q, 128, 16))

    bias[0] = 500.0
    dma("Y", v("vfb"), None, i=T.vf[:])
    dma("S", v("hyb"), None, i=T.hy[:])
    at = 3.0
    for k, name in enumerate(LOADS):
        src, n, us = {"X": (T.xs, 2048, 1.8), "WI": (T.wd, 2048, 3.6), "RI32": (T.rq, 1024, 1.8), "SG": (T.sg, 1024, 0.9)}[name]
        at += us
        bias[0] = 400.0 - 50 * k
        dma("SY"[k & 1], v(name, 0, n), None, i=src[:], lat=at)
    bias[0] = 10.0
    dma("Y", v("FL0"), None, i=T.xs[2:128:16, :], lat=at)
    dma("S", v("thi"), None, i=T.th[:], lat=3.0)
    dma("S", v("XB"), None, i=T.xs[1:128:16, :], lat=3.0)
    bias[0] = 0.0
    hold.append(v("WI", 0, 2048))
    for t in (1, 2):
        dma("Y", v("FL%d" % t), None, i=T.xs[2:128:16, :])
    hold.pop()

    iota(v("KI", 0, 1), [[1, 1]], 0, 1)
    iota(v("CR"), [[1, 144]], 0)
    iota(v("MG"), [[1, 8], [0, 16]], 0)
    iota(v("MI"), [[0, 8], [1, 16]], 0)
    iota(v("J16"), [[16, 32]], 0)
    iota(v("K3", 0, 3), [[16, 3]], -16, 1)
    iota(v("CW", 0, 512), [[0, 512]], 0)
    iota(v("JI"), [[1, 512]], -4095)
    iota(v("WI", 2048, 2560), [[0, 512]], 0)
    col, ncol = {}, [0]

    def newcol(name=None):
        ncol[0] += 1
        col[name] = v("COLS", ncol[0] - 1, ncol[0])
        return col[name]

    def q(k):
        return v("QH", k, k + 1)

    def weights(name, w, rest=0.0):
        last = float(rest)
        for r, x in w.items():
            c = newcol(name)
            act(c, q(r), F.Identity, bias=last, scale=float(x - rest))
            last = c
        return last

    bias[0] = 30.0
    ms(v("Z"), 0.0)
    ms(v("ZF"), 0.0)
    bias[0] = 0.0
    for h in (0, 1):
        ms(v("TB", 1024 * h, 1024 * h + 1024), 0.0)
    ki, kg, odd = newcol("ki"), newcol("kg"), newcol("odd")
    km, kf, kp = v("K3", 0, 1), v("K3", 1, 2), v("K3", 2, 3)
    ts(v("KI", 1, 2), v("KI", 0, 1), 4, A.arith_shift_right)
    bits(v("KI", 2, 3), v("KI", 0, 1), 0, 15)
    bits(v("KI", 3, 4), v("KI", 0, 1), 4, 1)
    cp(ki, v("KI", 2, 3))
    cp(kg, v("KI", 1, 2))
    cp(odd, v("KI", 3, 4))
    ts(v("QH"), v("CR", 0, 16), ki, A.is_equal)
    for name, src, a, b in (("even2", odd, -1.0, 1.0), ("g15", kg, 16.0, 15.0), ("uw", ki, 10.0, 1.0), ("n2", q(2), -1.0, 1.0), ("c40", ki, 0.0, 40.0)):
        act(newcol(name), src, F.Identity, bias=b, scale=a)
    even = col["even2"]
    ts(v("R1", 0, 143), v("CR", 0, 143), col["g15"], A.is_equal)
    ts(v("BO"), v("MG"), kg, A.is_equal)
    ts(v("ID"), v("CR", 0, 128), kf, A.is_equal)
    ts(v("LT"), v("MI"), ki, A.is_gt)
    ts(v("EQH"), v("MI"), ki, A.is_equal, 0.5, A.mult)
    ts(v("GT"), v("MI"), ki, A.is_lt)
    tt(v("GT"), v("GT"), v("BO"), A.mult)
    act(v("LPB"), v("ID"), scale=-4096.0)
    tt(v("LPB"), v("LPB"), v("GT"), A.subtract)
    act(v("LPH"), v("LPB"), scale=0.5)
    act(newcol("lph"), ki, F.Identity, bias=-2055.5, scale=0.5)
    act(v("B3", 0, 128), v("BO"), scale=0.5)
    ts(v("RH3", 0, 8), v("CR", 0, 8), kg, A.is_gt)
    ts(v("RH3", 8, 16), v("CR", 0, 8), kg, A.is_equal)
    act(v("RH3", 16, 24), v("RH3", 8, 16), scale=2048.0)
    act(v("RH3", 24, 32), v("RH3", 8, 16), scale=kf)
    ts(v("UT"), v("CR", 0, 128), kf, A.is_ge)
    for k, (c_, m_) in enumerate(((kf, even), (kp, even), (km, odd), (kf, odd))):
        ts(v("SWB", 128 * k, 128 * k + 128), v("CR", 0, 128), c_, A.is_equal, m_, A.mult)
    act(v("JW"), v("J16"), F.Identity, bias=ki)
    act(v("JC"), v("JW"), F.Identity, bias=2048.0)
    act(v("C1"), v("CR", 0, 128), scale=1 / 16)
    act(newcol("rt"), ki, F.Relu, bias=32.0, scale=-31.0)
    act(newcol("sx"), col["rt"], F.Identity, bias=weights("s", {3: -1, 4: -1}), scale=1 / 2048)
    for name, c in (("RI", ki), ("RU", col["uw"]), ("RX", col["sx"]), ("R2", 2.0), ("RN", -1.0)):
        act(v(name, 0, 143), v("R1", 0, 143), scale=c)
    act(v("ON"), v("Z", 0, 128), F.Identity, bias=1.0)
    dma("Y", row("TB", 12), v("ON"))
    ts(v("TB", 2048, 2688), v("Z", 0, 640), weights("tb", {0: 32}), A.add)
    ms(v("X", 2048, 2064), 16384.0)
    ms(v("RI32", 1024, 1032), 1024)
    act(v("SG", 1024, 1040), v("Z", 0, 16), F.Identity, bias=weights("sg", {1: -1.5 * 2.0 ** 34}))
    ts(v("TMP"), v("vfb"), -2048.0, A.mult)
    tt(v("VB", 0, 128), v("TMP"), v("hyb"), A.add)
    act(v("IDQ"), v("ID"), scale=0.25)
    ts(v("SI", 0, 128), v("hyb"), 5, A.arith_shift_right)
    bits(v("SI", 128, 256), v("hyb"), 0, 31)
    cp(v("ST", 0, 256), v("SI", 0, 256))
    dma("Y", row("TB", 0), v("ST", 0, 128))
    dma("Y", row("TB", 1), v("ST", 128, 256))
    act(v("NT"), v("TMP"), F.Identity, bias=8192.0, scale=4.0)
    dma("Y", row("TB", 2), v("NT"))
    act(v("KIB"), v("Z", 0, 128), F.Identity, bias=ki)
    dma("Y", row("TB", 10), v("KIB"))
    dma("Y", row("TB", 11), v("C1"))
    def blocks(o, R, x, more=()):
        lst = list(more) + [(o, win(R, b), v(x, 128 * b, 128 * b + 128)) for b in range(16)]
        mms(*[lst[k:k + 4] for k in range(0, 12, 4)], lst[12:])

    def gid(name, c):
        o, z = v(name, 0, 128), v("Z", 0, 128)
        op("G", lambda: g.affine_select(ap(o), ap(z), [[-1, 128]], A.not_equal, float(c), 0, 1), [z], [o], 0.42)

    blocks(v("q6", 0, 128), "R1", "X")
    act(v("ST", 256, 384), v("q6", 0, 128))
    tt(v("ST", 384, 512), v("q6", 0, 128), v("ST", 256, 384), A.subtract)
    for r in (3, 4):
        dma("Y", row("TB", r), v("ST", 128 * r - 128, 128 * r))
    blocks(v("q0", 0, 128), "RU", "X")
    si = lambda k: v("SI", 128 * k, 128 * k + 128)
    cp(si(2), v("q0", 0, 128))
    bits(si(3), si(2), 0, 2047)
    bits(si(6), si(2), 5, 63)
    bits(si(7), si(2), 0, 31)
    gcp(v("BF2", 0, 128), si(3))
    act(v("BF2", 128, 256), v("BF2", 0, 128), F.Square, bias=16.0)
    ts(si(4), v("BF2", 128, 256), -256.0, A.add)
    bits(si(8), si(4), 10, 63)
    bits(si(9), si(4), 5, 31)
    gcp(v("ST", 512, 1024), v("SI", 768, 1280))
    for k, r in enumerate((5, 6, 8, 9)):
        dma("Y", row("TB", r), v("ST", 512 + 128 * k, 640 + 128 * k))
    dma("Y", v("TS"), v("TB"), lat=4.0)
    for h in (0, 1):
        act(v("XP", 1024 * h, 1024 * h + 1024), v("X", 1024 * h, 1024 * h + 1024))
    act(v("R0", 0, 143), v("R1", 0, 143), scale=weights("r0", {0: 32768, 1: 0}, 1))
    blocks(v("q7", 0, 128), "R0", "X")
    act(v("XR", 0, 128), v("q7", 0, 128), F.Identity, bias=32768.0)
    dma("Y", row("XP", 0), v("XR", 0, 128), lat=3.0)
    act(v("ID5"), v("ID"), scale=32.0)
    act(v("ID14"), v("ID"), scale=16384.0)

    def types_to_xp(t):
        o = v(XPB, 384, 512)
        if t:
            blocks(o, "RT", "TB", [(o, v("ID14"), v("XB"))])
        else:
            mm([(o, v("ID14"), v("XB")), (o, v("ID5"), v("ST", 0, 128)), (o, v("ID"), v("ST", 128, 256))])
        act(v("XR", 128, 256), o, F.Identity, bias=16384.0)
        dma("Y", row("XP", 1), v("XR", 128, 256), lat=3.0)

    types_to_xp(0)
    for name, ws in (("WM", (({0: -1, 1: 0}, 2), ({0: 2.0 ** -15}, 0), ({1: 2.0 ** -14}, 0))), ("WS", (({0: 32768, 1: 0}, -1), ({0: -1}, 0), ({1: -1}, 0)))):
        for k, (w, rest) in enumerate(ws):
            act(v(name, 8 * k, 8 * k + 8), v("RH3", 8, 16), scale=col["r0"] if w is None else weights("w", w, rest))
    for name, c in (("WK", -2.0 ** -14), ("IDK", -2.0 ** -11), ("ID15", 32768.0), ("IDN", -2.0 ** 36),
                    ("NI", -1.0), ("IDF", -2048.0), ("ID10", -1024.0), ("LPD", -4096.0)):
        gid(name, c)

    def unwrap_table(k):
        un, z = v("UN", 16 + 512 * k, 528 + 512 * k), v("Z", 0, 512)
        op("G", lambda: g.affine_select(ap(un), ap(z), [[-1, 4], [-16, 8], [1000, 16]], A.not_equal, 1.0, -4 * k, 1), [z], [un], 1.15)

    def tables_out():
        hand_on(1, "X", 4.0)
        gcp(v("W16"), v("WI", 0, 2048))
        hand_on(3, "W16")
        gadd(v("FL0"), row("TB", 2))
        gcp(v("UN", 0, 16), v("Z", 0, 16))
        for k in range(4):
            unwrap_table(k)
        send(0, served(1), v("FI0"), v("FL0"))
        arrive(0, v("FI0"), 0, 10.0)
        for k in range(6):
            for h in (0, 1):
                arrive(10 + 2 * k + h, v(("XE%d", "WH%d")[k & 1] % (k // 2), *piece(k, h)), 3, 10.0 + 12.0 * k)

    def late_constants():
        for n_, src, c in (("NBO", "BO", -1.0), ("NLP", "LPB", -1.0)):
            act(v(n_), v(src), scale=c)
        tt(v("ZT"), v("EQH"), v("LT"), A.subtract)
        tt(v("ZT"), v("ZT"), v("BO"), A.mult)
        act(v("X2D"), v("ID"), scale=col["n2"])
        act(v("DF", 0, 128), v("ZF"), F.Identity, bias=weights("df", {10: 16 * 4096}))
        act(v("DF", 128, 192), v("CR", 0, 64), F.Identity, bias=weights("df", {0: (1 << 23) + 8 * 4096 + 2048 + 2560}), scale=weights("d2", {0: 2}))
        ts(v("thB", 0, 1), v("thi"), -2048.0, A.mult, -1024.0, A.add)
        ts(v("thB", 1, 2), v("thi"), -2048.0, A.mult, -1024.0, A.add)
        act(newcol("th"), v("thB", 0, 1), F.Identity, bias=-0.5, scale=-1 / 2048)
        act(v("thB", 2, 3), v("ZF", 0, 1))
        act(v("thB", 5, 6), v("thB", 1, 2), scale=-1.0)
        act(v("TH2"), col["th"], scale=-1.0)
        act(newcol("thh"), v("TH2"))
        act(newcol("thl"), col["th"], F.Identity, bias=col["thh"])
        act(v("THD", 0, 128), v("ID"), scale=col["thh"])
        act(v("THD", 128, 256), v("NI"), scale=col["thl"])
        gcp(v("DC", 0, 16), v("Z", 0, 16))
        iota(v("W8"), [[128, 4], [0, 2]], 6144, 4)
        if "S" in TTQ:
            for k, (src, a, b) in enumerate((("BO", 0.5, 0.0), ("BO", -0.5, 0.0))):
                act(v("B3", 128 * k + 128, 128 * k + 256), v(src), scale=a)
            for k, (src, a, b) in enumerate((("LT", 0.0, 8.0), ("LT", 16.0, -8.0), ("EQH", 2.0, -8.0))):
                act(v("C3", 128 * k, 128 * k + 128), v(src), F.Identity, bias=b, scale=a)
        act(v("TF"), v("ID"), scale=weights("tf", {2: 0, 3: 0, 4: 0, 11: 65536}, 4096))
        weights("pay", {0: 2048 + 8 * 4096}, 2048)
        iota(v("KB3"), [[0, 32], [-16384, 3]], 16384)
        act(v("KB3"), v("KB3"), F.Relu)
        act(v("LW", 2, 96, 3), v("JW"), F.Identity, bias=1024.0)
        tt(v("LPD"), v("LPD"), v("GT"), A.add)
        act(v("NLD"), v("LPD"), scale=-1.0)

    def last_constants():
        hold.append(v("FO", CH[-2], CH[-1]))
        weights("y8", {0: 8})
        act(v("B128"), v("BO"), scale=128.0)
        for name, a, b in ((v("TE", 8, 16, 2), 2.0, 2560.0), (v("S4"), 4096.0, 1024.0), (v("TE", 0, 8, 2), 0.0, 0.0)):
            act(name, v("JW", 0, 4), F.Identity, bias=b, scale=a)
        act(newcol("keep"), ki, F.Sign, bias=-2.5)
        act(v("K34"), v("ID"), F.Relu, scale=col["keep"])
        weights("b2", {2: 8192})
        act(v("ONS"), v("Z", 0, 128), F.Identity, bias=1.0 / 4096)
        act(v("CWM"), v("MI"), F.Identity, bias=weights("rb", {8: 32, 9: 1}), scale=weights("rs", {5: 64, 6: 2, 12: 1}))
        tt(v("CWM"), v("CWM"), v("BO"), A.mult)
        act(v("MK12"), v("MI"), scale=weights("m16", {12: 1 / 16}))
        tt(v("MK12"), v("MK12"), v("BO"), A.mult)
        act(newcol("h"), q(2), F.Identity, bias=col["rt"], scale=0.25)
        for name, c in (("RO", weights("ro", {10: 128, 11: 1})), ("RH", col["h"]), ("RT", col["rt"])):
            act(v(name, 0, 143), v("R1", 0, 143), scale=c)
        act(v("KB"), v("MI"), F.Relu, bias=1048576.0, scale=-1048576.0)
        act(newcol("o64"), odd, scale=64.0)
        act(newcol("g128"), kg, F.Identity, bias=col["o64"], scale=-64.0)
        act(v("W8"), v("W8"), F.Identity, bias=col["g128"])
        hold.pop()

    def slots_reset(t):
        gcp(v("P1W", 384, 576), v("DF"))

    def lanes(t):
        c0 = 896 * t % 2048 // 16
        if t == 0:
            turn(v("VB", 128, 256), v("VB", 0, 128))
            mm([(v("q4", 2 * b + s1, 128, 8), v("SWB", 256 * s1 + 128 * g2, 256 * s1 + 128 * g2 + 128), v("VB", 128 + 32 * b + 16 * g2, 144 + 32 * b + 16 * g2))
                for b in range(4) for s1 in (0, 1) for g2 in (0, 1)], each=2)
            parts, mid = ((0, 128, 0),), 0
        else:
            mm(wrap(v("q4", 0, 128), "RH", "TB", 0, 2048))
            parts, mid = ((0, 128 - c0, c0), (128 - c0, 128, 0)), 2048
        for lo, hi, at in parts:
            act(v("NW", lo, hi), v("q4", at, at + hi - lo), F.Sign, bias=0.5 - mid)
        if TTQ[t] == "S":
            mm([(v("q4", 128, 512), v("NW"), v("B3")), (v("q4", 128, 512), v("ID"), v("C3"))])
            act(v("TTB"), v("q4", 128, 512), F.Relu)
        for lo, hi, at in parts:
            act(v("HW", lo, hi), v("q4", at, at + hi - lo), F.Identity, bias=-float(mid))
        if TTQ[t] == "V":
            mm([(v("q3", 128, 256), v("NW"), v("B3", 0, 128)), (v("q3", 128, 256), v("ON"), v("B3", 0, 128))])
            cp(v("TTB", 0, 128), v("q3", 128, 256))
            tt(v("TTB", 128, 256), v("q3", 128, 256), v("LT"), A.mult)
            tt(v("TTB", 256, 384), v("q3", 128, 256), v("EQH"), A.is_lt)
        mm([(v("q3", 256, 264), v("TTB", 128 * k, 128 * k + 128), v("RH3", 8 * j, 8 * j + 8)) for j, k in enumerate((0, 1, 2, 2))])
        mm([(v("q3", 264, 265), v("TTB", 0, 128), v("ON", 0, 1))])
        mm([(v("q5", 0, 128), v("LPH"), v("NW")), (v("q5", 0, 128), v("TTB", 0, 128), v("UT"))])
        act(v("POS"), v("q5", 0, 128), F.Identity, bias=col["lph"])
        cp(v("OFu"), v("q3", 256, 264))
        sca(v("CW"), v("OFu"), v("C1"))
        ts(v("EX"), v("JW"), v("q3", 264, 265), A.is_ge, 4096.0, A.mult)
        scan(v("CC"), v("CW", 0, 512), v("Z", 0, 512), A.max)
        mm(wrap(v("q3", 288, 320), "R1", "CC", 0, 512))
        cp(v("CLu"), v("q3", 288, 320))
        for lo, hi, b in ((0, FIRST, "q5"), (FIRST, 512, "q3")):
            a, z = lo // 16, hi // 16
            hold[:] = [v("TY", 0, FIRST)] if lo and AHEAD else []
            gtt(v("OH", lo, hi), v("POS"), v("CLu", a, z), v("JI", lo, hi), A.is_equal)
            hold[:] = [v(("STu", "Ku")[AHEAD - 2], 0, a)] if lo and AHEAD > 1 else []
            gtt(v("TY", lo, hi), v("HW"), v("CLu", a, z), v("OH", lo, hi), A.mult)
            del hold[:]
            mm([(v(b, 320 + a, 320 + z), v("IDQ"), v("EX", a, z))] + wrap(v(b, 320 + a, 320 + z), "R1", "TY", lo, hi))
            cp(v("STu", a, z), v(b, 320 + a, 320 + z))
            gat(v("Ku", lo, hi), v("RI32"), v("STu", a, z))
            act(v("HY", a, z), v(b, 320 + a, 320 + z))
            act(v("HY", 32 + a, 32 + z), v(b, 320 + a, 320 + z), F.Square, bias=col["c40"])
        act(v("L1", 0, 32), v("q3", 288, 320), F.Identity, bias=16.0 * c0 - (1024 if t else 0), scale=16.0)
        if t:
            act(v("L1", 32, 64), v("q3", 288, 320), F.Sign, bias=c0 - 127.5)
        mm([(v("q4", 0, 32), v("ID"), v("EX")), (v("q4", 0, 32), v("ID"), v("L1", 0, 32))] + [(v("q4", 0, 32), v("ID10"), v("L1", 32, 64))] * (t > 0)
           + wrap(v("q4", 0, 32), "RI", "OH", 0, 512))
        tt(v("Lf"), v("q4", 0, 32), v("JC"), A.min)
        cp(v("Lu"), v("Lf"))

    def fetch(t):
        pick(TBLQ)(v("TBL", 0, 512), v("TB"), v("Lu"))

    def pay(lo, hi):
        return v("q2", lo, hi) if lo < EARLY else v("q7", lo - EARLY, hi - EARLY)

    def check(t):
        nch = len(CH) - 1
        banks = BANKS

        def ch(x, k, at=0):
            return v(x, at + CH[k], at + CH[k + 1])

        def tile(x, k, p=None):
            n = 16 * (CH[k + 1] - CH[k])
            name, at = ("sig", 16 * CH[k]) if x == "sg" else ("%s%d" % (x, k & 1), 0)
            return v(name, at, at + n) if p is None else v(name, at + p, at + n, 16)

        def part(R, x, k):
            return [(v(banks[k], 0, CH[k + 1] - CH[k]), win(R, p), tile(x, k, p)) for p in range(16)]

        for k in range(nch):
            cuts = [CH[k] + (CH[k + 1] - CH[k]) * j // SPLIT[k] for j in range(SPLIT[k] + 1)]
            for lo, hi_ in zip(cuts, cuts[1:]):
                sgat(v("sig", 16 * lo, 16 * hi_), v("SG"), v("Ku", lo, hi_))
        gat(v("Wu"), v("WI" if t == 0 else "WD"), v("Lu"))
        bias[0] = 20.0
        gcp(v("KF", 0, FIRST), v("Ku", 0, FIRST))
        gcp(v("KF", FIRST, 512), v("Ku", FIRST, 512))
        gcp(v("Wf"), v("Wu"))
        bias[0] = 0.0

        for lo, hi_ in ((0, EARLY), (EARLY, 512)):
            mm([(pay(lo, hi_), v("ID"), v("Wf", lo, hi_))], last=False)
            mm([(pay(lo, hi_), v("TF"), v("TBL", lo, hi_))], first=False, last=False)

        def ft(k, other):
            return ch("FT", k, (EARLY, 0)[other] if CH[k] < EARLY else (EARLY, 512)[other])

        def marks(k):
            o = pay(CH[k], CH[k + 1])
            mm([(o, v("IDF"), ft(k, 0)), (o, v("ID"), ch("FO", k))], first=False, last=CH[k + 1] in (EARLY, 512))

        hi = lambda k: v("HI", 32 * k, 32 * k + 32)
        ts(hi(1), v("HY", 32, 64), -1600.0, A.add)
        bits(hi(2), hi(1), 4, 1023)
        tt(hi(3), hi(2), v("HY", 0, 32), A.subtract)
        ts(v("HF", 0, 32), hi(2), 1024.0, A.subtract, -1.0, A.mult)
        ts(hi(4), hi(3), 5, A.arith_shift_right)
        bits(hi(5), hi(3), 0, 31)
        ts(v("HF", 32, 64), hi(4), 1.0 / 32, A.mult)
        def after(k, j=0):
            return [v(x, 384 * i + 256, 384 * i + 384) for x, i in AFTER.get((k, j), ())]

        def turned(k):
            b, mf = banks[k], "mf%d" % (k & 1)
            r = lambda j, n=1: v(b, 128 * j, 128 * (j + n))
            u = lambda x, j, n=1: v(x, 384 * k + 128 * j, 384 * k + 128 * (j + n))
            cuts = [128 * j // VSPLIT[k] for j in range(VSPLIT[k] + 1)]
            for j, (lo, hi_) in enumerate(zip(cuts, cuts[1:])):
                hold[:] = after(k, j) + [v(mf, 16 * lo - 1, 16 * lo)] * (j > 0)
                gtt(v(mf, 16 * lo, 16 * hi_), v("XP"), v("Wu", CH[k] + lo, CH[k] + hi_), v("sig", 16 * (CH[k] + lo), 16 * (CH[k] + hi_)), A.max)
            del hold[:]
            sums = lambda x, w: [(v(b, p, 384, 16), x(p), v(w)) for p in range(16)]
            last = sums(lambda p: v(mf, p, 2048, 16), "WM")
            mms(sums(lambda p: tile("sg", k, p), "WS"), [(r(0), v("ON"), v("THD", 0, 128)), (r(0), v("ON"), v("THD", 128, 256))],
                [(r(2), ch("KF", k), v("WK"))], last[:8], last[8:])
            bias[0] = SOON
            ts(u("RR", 0, 2), r(1, 2), MAGIC, A.add, MAGIC, A.subtract)
            tt(u("RR", 2), r(2), u("RR", 1), A.is_equal)
            act(u("AA", 0, 2), u("RR", 0, 2), F.Abs, bias=-1.0)
            rest = v("AS", 128 * (k & 1), 128 * (k & 1) + 128)
            more = [(r(3), v(l), x) for l, x in (("ID15", u("RR", 0)), ("ID", u("AA", 0)), ("ID", u("AA", 1)), ("IDN", u("RR", 2)))]
            act(rest, r(0), F.Identity, bias=v("thB", 2, 3), scale=-1.0)
            mm(more)
            tt(u("AA", 2), r(3), rest, A.is_gt)
            mm([(r(1), u("AA", 2), v("ID")), (r(2), u("RR", 2), v("NI"))], each=1)
            act(ft(k, 1), r(2), F.Identity, bias=1.0)
            act(ft(k, 0), r(1), F.Relu)
            mm([(r(0), v("ZT"), ft(k, 1))])
            act(ch("FO", k), r(0), F.Relu, scale=16777216.0)
            marks(k)
            bias[0] = 0.0

        for k in range(nch):
            if k < TURNED:
                turned(k)
                continue
            b, n = banks[k], CH[k + 1] - CH[k]
            e = v(b, 0, n)
            cut = min(n, SHARE[t]) if TYP[t][k] == "V" else 0
            for f, lo, hi_ in ((gat, 0, cut), (sgat, cut, n)):
                if lo < hi_:
                    hold[:] = [tile("sg", SIGS)] if f is sgat and SIGS >= 0 else []
                    f(v("hg%d" % (k & 1), 16 * lo, 16 * hi_), v("TB"), v("Wu", CH[k] + lo, CH[k] + hi_))
            hold[:] = after(k)
            gtt(tile("mm", k), v("X"), ch("Wu", k), tile("sg", k), A.max)
            del hold[:]
            ends = [part("RX", "hg", k), part("R2", "mm", k)]
            mms(part("RN", "sg", k), [(e, v("IDK"), ch("KF", k))], *ends)
            bias[0] = SMALL
            ts(v("RD", 0, n), e, MAGIC, A.add, MAGIC, A.subtract)
            if k >= nch - OWN:
                ts(ch("GA", k), e, 2048.0, A.mult, v("thB", 5, 6), A.is_gt)
            tt(ft(k, 1), e, v("RD", 0, n), A.not_equal)
            if k < nch - OWN:
                act(ch("GA", k), e, F.Relu, bias=v("thB", 1, 2), scale=2048.0)
            mm([(v(b, 256, 256 + n), v("ZT"), ft(k, 1))])
            tt(ft(k, 0), ft(k, 1), ch("GA", k), A.min)
            act(ch("FO", k), v(b, 256, 256 + n), F.Relu, scale=16777216.0)
            marks(k)
            bias[0] = 0.0

    def post(t):
        rp = lambda k, n=1: v("RP", 32 * k, 32 * (k + n))
        lw = lambda k, n=1: v("LW", 32 * k, 32 * (k + n))
        dl = lambda k: v("DL", 32 * k, 32 * k + 32)
        a = EARLY // 16
        n_, much, some = v("q3", a, a + 32), rp(0), rp(1)
        for lo, hi in ((0, a), (a, 32)):
            n = hi - lo
            act(v("PAY", 16 * lo, 16 * hi), pay(16 * lo, 16 * hi), F.Identity, bias=col["pay"])
            mm(wrap(v("q3", 2 * lo, 2 * hi), "R1", "FT", 32 * lo, 32 * hi))
            ts(v("RP", 32 + lo, 32 + hi), v("q3", a + lo, a + hi), 0.5, A.is_gt)
            ts(v("RP", lo, hi), v("q3", a + lo, a + hi), 3.5, A.is_gt)
            ts(v("RP", 64 + lo, 64 + hi), v("q3", 32 + a, 64) if lo else v("q3", 0, a), 0.5, A.is_gt)
            one = max(lo, 1)
            for h, (bo, nbo, lp, nlp) in enumerate((("NBO", "BO", "LPD", "NLD"), ("BO", "NBO", "LPB", "NLP"))):
                mm([(v("q5", 32 * h + lo, 32 * h + hi), v(l), v("RP", 32 * (h + k) + lo, 32 * (h + k) + hi)) for l, k in ((bo, 1), (nbo, 0), (lp, 1), (nlp, 0))]
                   + [(v("q5", 32 * h + one, 32 * h + hi), v(l), v("RP", 32 * (h + k) + one - 1, 32 * (h + k) + hi - 1)) for l, k in ((nlp, 1), (lp, 0))])
            for k in (0, 1):
                scan(v("LW", 3 * lo + k, 3 * hi, 3), v("q5", 32 * k + lo, 32 * k + hi), v("ZF", 0, n), A.add,
                     v("LW", 3 * lo - 3 + k, 3 * lo - 2 + k) if lo else 4608.0 - k)
            scan(v("LW", 96 + 3 * lo, 96 + 3 * hi), v("KB3", 0, 3 * n), v("LW", 3 * lo, 3 * hi), A.add, 0.0, A.min)
            cp(v("PFu", lo, hi), v("LW", 98 + 3 * lo, 96 + 3 * hi, 3))
            for x in range(lo, hi, PIECE):
                sca(v("P1W"), v("PFu", x, min(hi, x + PIECE)), v("PAY", 16 * x, 16 * min(hi, x + PIECE)))
        tt(dl(0), n_, v("HF", 0, 32), A.is_ge)
        tt(dl(2), n_, v("HI", 160, 192), A.add)
        tt(dl(1), v("HF", 32, 64), dl(0), A.subtract)
        act(dl(5), much, scale=32.0)
        act(dl(6), some, scale=8192.0)
        tt(dl(4), dl(2), much, A.mult)
        tt(dl(3), dl(1), dl(5), A.mult)
        mms([(v("q4"), v("X2D"), v("TBL", 0, 512))],
            [(v("q4", i, 512, 16), v("UN", 16 + 128 * i - r, 144 + 128 * i - r), dl(k)) for r, k in ((1, 4), (2, 6), (0, 3)) for i in range(16)])
        act(v("TBn"), v("q4"))
        if t < 2:
            mm([(v("q2", 0, 32), v("ONS"), v("EX")), (v("q2", 0, 32), v("ON"), some)])
            act(v("BS"), v("q2", 0, 32), scale=-1.0, accum_out=v("thB", 4, 5))
            cn = lambda k: v("CN", k, k + 1)
            act(cn(0), v("thB", 4, 5), F.Identity, bias=-255 / 512, scale=1 / 256)
            act(cn(1), cn(0), F.Identity, bias=MAGIC)
            act(cn(2), cn(1), F.Identity, bias=256 * MAGIC, scale=-256.0)
            act(v("thB", 2, 3), cn(2), F.Identity, bias=v("thB", 4, 5))
            act(v("thB", 1, 2), v("thB", 2, 3), F.Identity, bias=v("thB", 0, 1), scale=-2048.0)
            act(v("thB", 5, 6), v("thB", 1, 2), scale=-1.0)
        bias[0] = 2.0
        ts(v("AI", 0, 64), v("P1W", 512, 576), 8388608.0 + 2048.0, A.subtract, 0.0, A.max)
        bits(v("AI", 64, 128), v("AI", 0, 64), 0, 4095)
        cp(v("AH", 0, 64), v("AI", 64, 128))
        cp(v("PI", 0, 192), v("P1W", 384, 576))
        bits(v("PI", 192, 384), v("PI", 0, 192), 12, 255)
        cp(v("TBS"), v("PI", 192, 320))
        ts(v("AH", 64, 128), v("PI", 320, 384), col["y8"], A.subtract, col["rt"], A.mult)
        bias[0] = 0.0
        to = v("q5", 128, 132)
        mm(wrap(v("q5", 128, 136), "R1", "AH", 0, 128))
        mm([(v("q3", 64, 128), v("B128"), v("AH", 0, 64)), (v("q3", 64, 128), v("BO"), v("C1", 0, 64))])
        act(v("AF", 256, 260), to, F.Identity, bias=0.5, scale=-128.0)
        act(v("TE", 9, 16, 2), to)
        cp(v("AU", 0, 8), v("q5", 128, 136))
        ts(v("AF", 352, 416), v("P1W", 512, 576), 8388608.0, A.is_ge)
        gtt(v("AI", 0, 64), v("RI32"), v("AU", 4, 8), v("AF", 352, 416), A.mult)
        bits(v("AI", 128, 192), v("AI", 0, 64), 5, 31)
        bits(v("AI", 192, 256), v("AI", 0, 64), 0, 31)
        cp(v("AH", 192, 320), v("AI", 128, 256))
        sgat(v("AB", 0, 64), v("TS"), v("AU", 0, 4))
        for k in range(PARTS):
            sca(v("TB"), v("Lu", 32 * k // PARTS, 32 * (k + 1) // PARTS), v("TBn", 512 * k // PARTS, 512 * (k + 1) // PARTS))
        for c in range(4):
            act(v("AF", 64 * c, 64 * c + 64), v("q3", 64, 128), F.Abs, bias=v("AF", 256 + c, 257 + c))
        for c in range(4):
            act(v("AF", 288, 352), v("AF", 64 * c, 64 * c + 64), F.Relu, bias=v("S4", c, c + 1), scale=-4096.0, accum_out=v("TE", 2 * c + 1, 2 * c + 2))
        mm([(v("q4", 0, 64), win("R1", 0), v("AH", 192, 256)), (v("q4", 0, 64), win("R1", 1), v("AH", 256, 320)), (v("q4", 0, 64), v("K34"), v("AB", 0, 64))])
        act(v("AB", 64, 128), v("q4", 0, 64), F.Identity, bias=col["b2"])
        scan(v("TE", 16, 24), v("TE", 0, 8), v("TE", 8, 16), A.min, 0.0, A.max)
        cp(v("AU", 12, 16), v("TE", 17, 24, 2))
        sca(v("TB"), v("AU", 12, 16), v("AB", 64, 128))
        if t < 2:
            gadd(v("FL%d" % (t + 1)), row("TB", 2))
            send(5 + t, served(2 + t), v("FI%d" % (t + 1)), v("FL%d" % (t + 1)))
            arrive(5 + t, v("FI%d" % (t + 1)), 5 + t, 4.0)

    def candidates():
        mm([(v("q6", 128, 256), v("CWM"), v("TBS", 0, 128))])
        mm(wrap(v("q7", 272, 280), "RO", "TBS", 0, 128))
        cp(v("BI", 384, 512), v("q6", 128, 256))
        cp(v("BU", 8, 16), v("q7", 272, 280))
        sgat(v("LX"), v("X"), v("BU", 8, 16))
        bits(v("BI", 512, 640), v("BI", 384, 512), 0, 2047)
        cp(v("BU", 128, 256), v("BI", 512, 640))

    def repairs(t):
        bi = lambda k: v("BI", 128 * k, 128 * k + 128)
        bf = lambda lo, hi: v("BF2", lo, hi)
        dw = "DW%d" % t
        candidates()
        act(v("WB"), v("q7", 272, 280), F.Identity, bias=4096.0)
        gcp(v("CH"), bi(4))
        turn(v("CT"), v("CH"))
        tt(v("DC", 1, 128), v("CT", 0, 127), v("CT", 1, 128), A.subtract)
        bits(bi(5), v("PI", 0, 128), 0, 4095)
        ts(bf(384, 512), bi(5), -2048.0, A.add)
        act(v("NB"), bf(384, 512), scale=-2048.0)
        n = len(CAND[t])
        for h in range(n):
            pick(CAND[t][h])(v("mm0", 2048 * h // n, 2048 * (h + 1) // n), v("XE%d" % t), v("BU", 128 + 128 * h // n, 128 + 128 * (h + 1) // n))
        for h in (0, 1):
            for b in (0, 1):
                qb, lo = ("q0", "q1", "q2", "q6")[2 * h + b], 1024 * h + 512 * b
                lst = []
                for m in range(8):
                    o = v(qb, 64 * m, 64 * m + 64)
                    lst += [(o, v("NI"), v("LX", 64 * h, 64 * h + 64)), (o, v("ID"), v("mm0", 1024 * h + 8 * b + m, 1024 * h + 1024, 16))]
                mm(lst, each=2)
                act(v("hg0", lo, lo + 512), v(qb), F.Abs)
            o = v("q7", 64 * h, 64 * h + 64)
            mms([(o, v("MK12"), v("TBS", 64 * h, 64 * h + 64))] + [(o, win("R1", m), v("hg0", 1024 * h + 64 * m, 1024 * h + 64 * m + 64)) for m in range(8)],
                [(o, win("R1", m), v("hg0", 1024 * h + 64 * m, 1024 * h + 64 * m + 64)) for m in range(8, 16)])
        changes(t)
        turn(bf(0, 128), v("q7", 0, 128))
        scan(bf(128, 256), v("KB"), bf(0, 128), A.add, 0.0, A.min)
        tt(v("NQ"), bf(0, 128), bf(128, 256), A.not_equal)
        scan(v("UU"), v("DC"), v("NQ"), A.add, 0.0, A.mult)
        tt(v("MB"), v("BF2", 143, 256, 16), v("W8"), A.min)
        swb = lambda s1, g2: v("SWB", 256 * s1 + 128 * g2, 256 * s1 + 128 * g2 + 128)
        mm([(v("q7", 256 + s1, 264, 2), swb(s1, g2), v(x, 16 * g2 + 15, 128, 32)) for s1 in (0, 1) for x in ("CT", "UU") for g2 in (0, 1)], each=4)
        mm([(v("q7", 264 + s1, 272, 2), swb(s1, g2), v("MB", g2, 8, 2)) for s1 in (0, 1) for g2 in (0, 1)], each=2)
        cp(v("BU", 24, 32), v("q7", 256, 264))
        gtt(bf(256, 384), v("WE"), v("BU", 24, 32), v("NB"), A.min)
        tt(v(dw, 128, 136), v("q7", 264, 272), v("WB"), A.max)
        ts(v("BU", 16, 24), v(dw, 128, 136), -4096.0, A.add)
        op("V", lambda: g.vector.tensor_tensor(ind(v("WD"), v("BU", 16, 24)), ap(bf(256, 384)), ap(bf(384, 512)), A.max),
           [bf(256, 512), v("BU", 16, 24)], [v("WD")], ew(128, SCATTER))
        if t == 2:
            fin.append(dma("Y", None, v("WD", 0, 2048), o=T.ym[:], lat=6.0))
            return
        tt(v(dw, 0, 128), bf(256, 384), bf(384, 512), A.max)
        for t2 in range(t + 1, 3):
            slot = 6 + t + t2
            send(slot, served(1 + t2), v("Di%d%d" % (t, t2)), v(dw))
            arrive(slot, v("Di%d%d" % (t, t2)), slot, 4.0)

    def helper(t):
        if t == 0:
            gcp(v("WD", 0, 2048), v("W16"))
            gcp(v("WD", 2048, 2560), v("Z", 0, 512))
            gcp(v("WE", 2048, 2560), v("Z", 0, 512))
        if t < 2:
            gcp(v("CW", 0, 512), v("Z", 0, 512))
        for h in (1, 0):
            gcp(v("WE", *piece(2 * t + 1, h)), v("WH%d" % t, *piece(2 * t + 1, h)))
        hold.append(v("FO", 0, CH[1]))
        dma("Y", row("XE%d" % t, 2), v("FI%d" % t))
        hold.pop()

    def changes(t):
        hold.append(v("BU", 128, 256))
        for s in range(t):
            b = "Di%d%d" % (s, t)
            ts(v("HU"), v(b, 128, 136), -4096.0, A.add)
            sca(v("WE"), v("HU"), v(b, 0, 128))
        hold.pop()

    def flags_out():
        mm([(v("q3", 0, 128), win("RH", b), v("TB", 128 * b, 128 * b + 128)) for b in range(16)])
        ts(v("OUT", 128, 256), v("q3", 0, 128), 2048.0, A.is_lt)
        fin.append(dma("Y", None, v("OUT", 128, 256), o=T.yv[:]))
        act(v("HW"), v("OUT", 128, 256), F.Identity, bias=-2048.0, scale=2048.0)
        tt(v("OUT", 0, 128), v("q3", 0, 128), v("HW"), A.add)
        fin.append(dma("Y", None, v("OUT", 0, 128), o=T.yh[:]))

    lanes(0)
    tables_out()
    late_constants()
    fetch(0)
    for t in range(3):
        slots_reset(t)
        check(t)
        helper(t)
        if t == 0:
            last_constants()
        post(t)
        if t < 2:
            lanes(t + 1)
            types_to_xp(t + 1)
            bias[0] = -LATE
            repairs(t)
            bias[0] = 0.0
            fetch(t + 1)
        else:
            bias[0] = LAST
            repairs(t)
            bias[0] = 0.0
            flags_out()
    issue()
    for sem in fin:
        wait("Y", sem, 16, {})
    for sem, n in sent:
        wait("G", sem, n, {})
    for sem in cnt:
        wait("G", sem, cnt[sem], {})
